import numpy as np, ml_dtypes
CORES = [23,119,17,113]
N = 4
BF = ml_dtypes.bfloat16
def gentries(a):
    return np.ascontiguousarray(a.reshape(8, 16, -1).transpose(0, 2, 1)).reshape(8, -1)
def gtable(e):
    e = np.asarray(e); return np.ascontiguousarray(e.reshape(8, -1, 16).transpose(0, 2, 1)).reshape(128, -1).astype(np.int32)
W, NB, P, Q, RO, ST, LO, HI, OWN = 8192, 512, 256, 32, 5, 1, 4, 9, 0
def sites(rng):
    b = np.argsort(rng.random((N, 8, NB)), axis=-1); o = np.argsort(rng.random((N, 8, NB)), axis=-1)
    return b, np.ascontiguousarray(o[..., :P]), np.take_along_axis(b, o[..., P:], -1)
def some(rng):
    x = rng.integers(0, 256, (N, 8, 16, W), dtype=np.int16); c = rng.integers(0, W, (N, 8, 16, NB))
    pf = rng.integers(0, 256, (N, 8, 16, P)); pn = rng.integers(0, 256, (N, 8, 16, P))
    th = (rng.choice(np.array([1, 60, 400]), (N, 8, 1)) * rng.random((N, 8, 16))).astype(np.int64)
    return x, c, pf, pn, th
def lay(b, fl, nu, ca, ch):
    c = np.zeros((N, 8, 16, NB), np.int64); a = np.take_along_axis(b, fl, -1)
    np.put_along_axis(c, a[:, :, None, :], ca, 3); np.put_along_axis(c, nu[:, :, None, :], ch, 3)
    return c
def pack(x, c, b, fl, nu, pf, pn, th):
    return {"xf": x.reshape(N, 128, W).astype(np.float32).astype(BF), "cb": np.ascontiguousarray(c.reshape(N, 128, NB)).astype(np.int32), "bs": np.stack([gtable(v) for v in b]),
            "fs": np.stack([gtable(v) for v in fl]), "nb": np.stack([gtable(v) for v in nu]), "pf": pf.reshape(N, 128, P).astype(np.float32).astype(BF),
            "pn": pn.reshape(N, 128, P).astype(np.float32).astype(BF), "th": np.ascontiguousarray(th.reshape(N, 128, 1)).astype(np.int32)}
def setup_inputs(rng):
    b, fl, nu = sites(rng); x, c, pf, pn, th = some(rng)
    return pack(x, c, b, fl, nu, pf, pn, th)
def setup_inputs_corners(rng):
    b, fl, nu = sites(rng)
    for q in range(N):
        for g in range(8):
            if g in (0, 3): b[q, g] = np.arange(NB)
            if g == 1: b[q, g] = np.arange(NB)[::-1]
            o = np.concatenate([fl[q, g], np.setdiff1d(np.arange(NB), fl[q, g])])
            if g == 2: o = np.concatenate([np.arange(0, NB, 2), rng.permutation(np.arange(1, NB, 2))])
            if g == 3: o = np.arange(NB)
            if g == 4: o = np.arange(NB)[::-1]
            if g == 5: o = np.concatenate([rng.permutation(P), P + rng.permutation(P)])
            fl[q, g] = o[:P]; nu[q, g] = b[q, g][o[P:]]
    order = np.argsort(rng.random((N, 8, W)), axis=-1)
    order[:, 6:] = order[0, 6:].copy()
    tot = np.concatenate([np.broadcast_to(np.arange(4081), (N, 8, 4081)), rng.integers(0, 4081, (N, 8, W - 4081))], axis=2)
    sg = np.zeros((N, 8, W), np.int64); np.put_along_axis(sg, order, tot, 2); sg = sg[:, :, None, :]
    ln = (np.arange(16)[:, None] + np.arange(W)[None, :]) % 16
    x = (sg // 16 + (ln[None, None] < sg % 16)).astype(np.int16); loc = order[:, :, None, :4081]
    th = rng.choice(np.array([0, 1, 2, 7, 300, 1001, 4095, 4096, 6001, 8158, 8159]), (N, 8, 16)); th[:, 6:] = rng.integers(1002, 4160, (N, 2, 16))
    want = rng.choice(np.array([0, LO, LO + 1, HI - 1, HI, 16]), (N, 8, P))
    for q in range(N):
        for g in range(8):
            m = (g + q) % 8
            if m < 4: want[q, g] = rng.choice(np.array(((HI, 16), (0, LO), (LO + 1, HI - 1), (16, 16))[m]), P)
    sw = np.argsort(np.argsort(rng.random((N, 8, 16, P)), axis=2), axis=2) < want[:, :, None, :]
    d = th[..., None] // 2 + sw; lo = (rng.random((N, 8, 16, P)) * (4081 - d)).astype(np.int64)
    ch = np.take_along_axis(loc, lo + d, 3); cl = np.take_along_axis(loc, lo, 3)
    u = rng.integers(0, 2, (N, 8, 1, P)); z = np.zeros((N, 8, 16, P), np.int64)
    ca = np.where(u == 0, ch, cl); cc = np.where(u == 0, cl, ch)
    mv = rng.random(P) < 0.5; mv[0] = True; mv[P - 1] = False
    u[:, 6, 0] = np.where(mv, rng.integers(0, 2, P), np.arange(N)[:, None] % 2); u[:, 7] = rng.integers(0, 2)
    for g in (6, 7):
        small, large = [w[(w & (min(Q, 16) - 1)) > 0] for w in (order[0, g, :1001], order[0, g, 3080:4081])]
        small = rng.choice(small, (N, 16, P)); large = rng.choice(large, (N, 16, P)); up = u[:, g] == 0
        if g == 6: up = up != mv
        ca[:, g] = np.where(up, large, small); cc[:, g] = np.where(up, small, large)
    return pack(x, lay(b, fl, nu, ca, cc), b, fl, nu, z + 255 * u, z + 255 * (1 - u), th)
def setup_inputs_ends(rng):
    o = 1 + np.argsort(rng.random((N, 8, NB - 2)), axis=-1); k = 1 + np.argsort(rng.random((N, 8, NB - 2)), axis=-1)
    z = np.zeros((N, 8, 1), np.int64); fl = np.concatenate([z, o[..., :P - 2], z + NB - 1], axis=2); nu = np.concatenate([z, k[..., :P - 2], z + NB - 1], axis=2)
    b = np.zeros((N, 8, NB), np.int64); np.put_along_axis(b, fl, k[..., P - 2:], 2); np.put_along_axis(b, o[..., P - 2:], nu, 2)
    rk = 1 + np.argsort(rng.random((N, 8, W - 2)), axis=-1); n = 2 * W // 5; low = rk[:, :, None, :n]; high = rk[:, :, None, n:2 * n]
    x = rng.integers(0, 2, (N, 8, 16, W), dtype=np.int16) * np.int16(255)
    np.put_along_axis(x, low, 0, 3); np.put_along_axis(x, high, 255, 3)
    e = rng.integers(0, 2, (N, 8)); e[N - 1, 7] = 0
    x[..., 0] = 255 * e[:, :, None]; x[..., W - 1] = 255 * (1 - e)[:, :, None]
    eh = np.where(e == 1, 0, W - 1)[:, :, None, None]; el = W - 1 - eh; sh = (N, 8, 16, P)
    ch = np.where(rng.random(sh) < 0.75, eh, np.take_along_axis(high, rng.integers(0, n, sh), 3))
    cl = np.where(rng.random(sh) < 0.75, el, np.take_along_axis(low, rng.integers(0, n, sh), 3))
    u = rng.choice(np.array([0, 0, 1, 1, 2]), (N, 8, 1, P)); u[0] = rng.integers(0, 2, (8, 1, P)); u[N - 1] = rng.integers(0, 2, (8, 1, P)); u[N - 1, 7, 0, P - 1] = 0
    pf = np.where(u == 0, 0, np.where(u == 1, 255, 255 * rng.integers(0, 2, sh))); pn = np.where(u == 0, 255, np.where(u == 1, 0, 255 * rng.integers(0, 2, sh)))
    th = 8159 * rng.integers(0, 2, (N, 8, 16)); th[:, 0, 0] = 0; th[:, 7, 15] = 8159
    w = rng.choice(np.array([0.0, 0.3, 0.6, 0.8, 1.0]), (N, 8, 1, P)); w[0] = 0.0; w[N - 1] = 1.0
    up = (rng.random(sh) < w) == (u == 0); ca = np.where(up, ch, cl); cc = np.where(up, cl, ch)
    tie = rng.random(sh) < 0.1; tie[0] = False; tie[N - 1] = False
    return pack(x, lay(b, fl, nu, ca, np.where(tie, ca, cc)), b, fl, nu, pf, pn, th)
def setup_inputs_fresh(rng):
    b, fl, nu = sites(rng); x, c, pf, pn, th = some(rng); sh = (N, 8, 16, NB)
    sm = np.add.reduce(pf, axis=2); i = rng.integers(0, P, sh); r = np.arange(N)[:, None, None, None]; g = np.arange(8)[None, :, None, None]
    q = (r + ST * rng.integers(0, RO, sh)) % N
    c = np.where(rng.random(sh) < 0.9, Q * i + ((sm[q, g, i] + rng.integers(3, 11, sh)) & (Q - 1)), c)
    return pack(x, c, b, fl, nu, pf, pn, th)
def setup_inputs_spread(rng):
    b, fl, nu = sites(rng)
    x = np.minimum(np.exp2(8.01 * rng.random((N, 8, 1, W), dtype=np.float32)) * rng.random((N, 8, 16, W), dtype=np.float32), 255).astype(np.int16)
    pf = np.minimum(np.exp2(2 + 6.01 * rng.random((N, 8, 1, P))) * rng.random((N, 8, 16, P)), 255).astype(np.int64)
    pn = np.minimum(np.exp2(2 + 6.01 * rng.random((N, 8, 1, P))) * rng.random((N, 8, 16, P)), 255).astype(np.int64)
    c = np.minimum((W * rng.random((N, 8, 16, NB)) ** 3).astype(np.int64), W - 1); c = np.where(rng.random((N, 8, 1, NB)) < 0.5, c, W - 1 - c)
    kind = rng.choice(np.array([0.25, 0.25, 0.5, 1.0]), (N, 8, 1))
    th = np.minimum(np.exp2(13 * kind * rng.random((N, 8, 16))).astype(np.int64) - 1, 8159)
    return pack(x, c, b, fl, nu, pf, pn, th)
def check_inputs(d):
    bad = []
    for k, lo, hi in (("xf", 0, 255), ("cb", 0, W - 1), ("bs", 0, NB - 1), ("fs", 0, NB - 1), ("nb", 0, NB - 1), ("pf", 0, 255), ("pn", 0, 255), ("th", 0, 8159)):
        v = np.asarray(d[k]).astype(np.float32)
        if not (np.all(v >= lo) and np.all(v <= hi)): bad.append("range of " + k)
        elif np.any(v != np.floor(v)): bad.append("whole numbers of " + k)
    b, fl, nu = [np.stack([gentries(np.clip(np.asarray(v), 0, NB - 1).astype(np.int64)) for v in d[k]]) for k in ("bs", "fs", "nb")]
    if np.any(np.sort(b, axis=-1) != np.arange(NB)): bad.append("bs: a permutation of the boxes in every group")
    if np.any(np.sort(np.concatenate([np.take_along_axis(b, fl, -1), nu], axis=2), axis=-1) != np.arange(NB)): bad.append("fs, nb: the flyers' boxes and the nurses' boxes are all boxes, each once")
    return bad
def reference(xf, cb, bs, fs, nb, pf, pn, th):
    x = xf.astype(np.float32).astype(np.int32).reshape(N, 8, 16, W); c = cb.astype(np.int64).reshape(N, 8, 16, NB)
    b, fl, nu = [np.stack([gentries(v) for v in k]).astype(np.int64) for k in (bs, fs, nb)]
    rf = pf.astype(np.float32).astype(np.int32).reshape(N, 8, 16, P); rn = pn.astype(np.float32).astype(np.int32).reshape(N, 8, 16, P); lim = th.astype(np.int64).reshape(N, 8, 16, 1)
    for t in range(RO):
        for r in range(N):
            q = (r + ST * t) % N
            box = np.take_along_axis(b[r], fl[r], 1); nur = nu[r].copy()
            ca = np.take_along_axis(c[r], box[:, None, :], 2); ch = np.take_along_axis(c[r], nur[:, None, :], 2)
            xa = np.take_along_axis(x[q], ca.reshape(8, 1, 16 * P), 2).reshape(8, 16, 16, P)
            xh = np.take_along_axis(x[q], ch.reshape(8, 1, 16 * P), 2).reshape(8, 16, 16, P)
            u = rf[q][:, :, None, :]; v = rn[q][:, :, None, :]
            score = np.add.reduce(np.abs(xa - u) + np.abs(xh - v) - np.abs(xh - u) - np.abs(xa - v), axis=1)
            sw = score > lim[q]; s = np.add.reduce(sw.astype(np.int64), axis=1)
            np.put_along_axis(c[r], box[:, None, :], np.where(sw, ch, ca), 2); np.put_along_axis(c[r], nur[:, None, :], np.where(sw, ca, ch), 2)
            flag = np.zeros((8, NB), bool); np.put_along_axis(flag, fl[r], s >= HI, 1)
            inv = np.argsort(b[r], axis=1); turn = s <= LO
            fl[r] = np.where(turn, np.take_along_axis(inv, nur, 1), fl[r]); nu[r] = np.where(turn, box, nur)
            total = np.add.reduce(s, axis=1)[:, None]
            if not OWN: total = np.zeros((8, 1), np.int64) + np.add.reduce(total, axis=None)
            mate = np.arange(NB)[None, :] ^ ((total & (NB - 1)) | 1)
            both = flag & np.take_along_axis(flag, mate, 1)
            b[r] = np.where(both, np.take_along_axis(b[r], mate, 1), b[r])
            col = Q * np.arange(P)[None, :] + ((np.add.reduce(rf[q].astype(np.int64), axis=1) + s) & (Q - 1))
            np.put_along_axis(x[q], col[:, None, :], rf[q], 2)
    who = [(q - ST * (RO - 1)) % N for q in range(N)]
    return {"yc": c[who].reshape(N, 128, NB).astype(np.float32), "yb": np.stack([gtable(b[r]) for r in who]).astype(np.float32),
            "yf": np.stack([gtable(fl[r]) for r in who]).astype(np.float32), "yn": np.stack([gtable(nu[r]) for r in who]).astype(np.float32)}

@@ -1,0 +1,596 @@
+from concourse.mybir import AluOpType as A, AxisListType, ActivationFunctionType as AF
+
+NS = ((), (5, 6, 7))
+NSET = (5, 6, 7)
+NXG, NT = 8, 2
+LG = 7
+JF, JD, JC, JS = 9, 14, 14, 14
+LP = 2
+WCOL = 544
+FL, BF, I32, U16 = "float32", "bfloat16", "int32", "uint16"
+
+
+def _scratch():
+    s = {}
+
+    def sb(names, cols, dt):
+        for n in names.split():
+            s[n] = ("sbuf", [128, cols], dt)
+    sb("xfs", 8192, BF)
+    sb("F16 N16", 4096, BF)
+    sb("FMN NNEG", 512 * len(NSET), BF)
+    sb("pfs pns FLB MROW IDX1 XN", 256, BF)
+    sb("cbs", 512, I32)
+    sb("CBF CS YC", 512, FL)
+    sb("bss", 32, I32)
+    sb("fss nbs OI1 OI2 BASE LI", 16, I32)
+    sb("ths TI PI PM UI UB", 2, I32)
+    sb("BITS", 16, I32)
+    sb("IDF NIDF", 128, FL)
+    sb("NB thh PMF RTOT CF AB C128", 2, FL)
+    sb("ONES", 128, BF)
+    sb("IDENT G16", 128, BF)
+    sb("SELP", 2048, BF)
+    sb("SWT THH THL", 128, BF)
+    sb("GN8", 8, BF)
+    sb("XG", 512 * NXG, BF)
+    sb("TF TN", 2048 * NT, BF)
+    sb("OH OA", 256, U16)
+    sb("CAf CHf", 256, FL)
+    sb("SW", 256, BF)
+    sb("WI1 WI2 WI3 WI4 WO0 WO1 WO2 WO3 WO4", WCOL, FL)
+    sb("MI0 MI1 MI2 MI3 MI4 MO0 MO1 MO2 MO3 MO4", 64, FL)
+    sb("HI1 HI2", 32, FL)
+    sb("bsU XLU XLS YL GU", 32, U16)
+    sb("fsU nbU FU ETAU ALU OFFU E4U", 16, U16)
+    sb("DFG TRN XX TD FL16 ABS Z1 Z2 Z3 LIF LI1 AB0 ELS", 16, FL)
+    sb("U", 1536, BF)
+    sb("IOTC BROW BROW4", 512, BF)
+    sb("XB0 XB1", WCOL, BF)
+    sb("GROW", 256, BF)
+    sb("RS RC", 32, BF)
+    sb("LB", 128, BF)
+    sb("LTB RTB", 16, BF)
+    sb("PAB", 48, FL)
+    sb("BL B1 B2 B3 B4 YB", 32, FL)
+    for n in ["PX0", "PX1", "PX2", "PX3", "PSC0", "PSC1", "PL", "PM2"]:
+        s[n] = ("psum", [128, 512], FL)
+    return s
+
+
+SCRATCH = _scratch()
+LOADS = ["pf", "pn", "fs", "bs", "nb", "th", "cb", "xa", "xb"]
+SEMAPHORES = (["qV", "qS", "qP", "qG", "loc"] + ["d_" + n for n in LOADS] + ["o_yc", "o_yb", "o_yf", "o_yn"]
+              + ["a%d_%d" % (k, t) for k in range(5) for t in range(1, 5)] + ["ah1", "ah2"])
+
+
+def rank_program(g, core, T, topo):
+    rank = T.rank_of(core)
+    if rank is None:
+        return
+    N = len(T.cores)
+    Q = {"V": g.vector, "S": g.scalar, "P": g.tensor, "G": g, "D": g.sync}
+    cnt = {"V": 0, "S": 0, "P": 0, "G": 0}
+    seen = {q: {} for q in Q}
+    snap = {}
+    wr, wp, rd = {}, {}, {}
+
+    def need(q, R, W):
+        toks = []
+        for k in R:
+            if k in wr:
+                toks.append(wr[k])
+            if k[0] == "P":
+                toks += [t for qq, t in rd.get(k, {}).items() if qq != q]
+        for k in W:
+            w = wr if k[0] != "+" else wp
+            k = k.lstrip("+")
+            if k in w and (q != "P" or w[k][0] != "qP"):
+                toks.append(w[k])
+            toks += [t for qq, t in rd.get(k, {}).items() if q != "P" or qq != q]
+        best = {}
+        for s, v in toks:
+            if v > seen[q].get(s, 0):
+                best[s] = max(best.get(s, 0), v)
+        for s in sorted(best, key=lambda s: -best[s]):
+            v = best[s]
+            if v <= seen[q].get(s, 0):
+                continue
+            Q[q].wait_ge(T.sem[s], v)
+            for s2, v2 in snap.get((s, v), {}).items():
+                seen[q][s2] = max(seen[q].get(s2, 0), v2)
+            seen[q][s] = max(seen[q].get(s, 0), v)
+
+    def done(q, R, W, tok):
+        snap[tok] = dict(seen[q])
+        for k in R:
+            rd.setdefault(k, {})[q] = tok
+        for k in W:
+            wr[k.lstrip("+")] = tok
+            if k[0] != "+":
+                wp[k] = tok
+                rd[k] = {}
+
+    def op(q, fn, R, W):
+        R, W = R.split(), W.split()
+        need(q, R, W)
+        fn(Q[q]).then_inc(T.sem["q" + q], 1)
+        cnt[q] += 1
+        done(q, R, W, ("q" + q, cnt[q]))
+
+    def dma(q, out, in_, R, W, sem):
+        R, W = R.split(), W.split()
+        need(q, R, W)
+        Q[q].dma_start(out, in_).then_inc(T.sem[sem], 16)
+        done(q, R, W, (sem, 16))
+
+    nloc = [0]
+
+    def send(dst, out, in_, R, sem):
+        need("G", R.split(), [])
+        m = topo.mask(core, dst)
+        rid, pid, _s = topo.addr(dst)
+        g.remote_dma(out, in_, T.sem[sem], T.sem.loc, pid, rid, m)
+        nloc[0] += len(topo.engines(core, dst))
+
+    for t in range(1, 5):
+        src = T.cores[(rank - 1) % N]
+        ne = len(topo.engines(src, core))
+        wr["WI%da" % t] = ("a0_%d" % t, ne)
+        wr["WI%db" % t] = ("a1_%d" % t, ne)
+        wr["WI%de0" % t] = ("a3_%d" % t, ne)
+        wr["WI%de1" % t] = ("a4_%d" % t, ne)
+        wr["MI%d" % t] = ("a2_%d" % t, ne)
+    wr["HI1"] = ("ah1", len(topo.engines(T.cores[(rank + 1) % N], core)))
+    wr["HI2"] = ("ah2", len(topo.engines(T.cores[(rank + 2) % N], core)))
+
+    def tt(o, a, b, o_, R, W):
+        op("V", lambda e: e.tensor_tensor(o, a, b, o_), R, W)
+
+    def ts(o, a, s1, s2, o0, o1, R, W):
+        if o1 is None:
+            op("V", lambda e: e.tensor_scalar(o, a, s1, None, o0), R, W)
+        else:
+            op("V", lambda e: e.tensor_scalar(o, a, s1, s2, o0, o1), R, W)
+
+    def cp(o, a, R, W):
+        op("V", lambda e: e.tensor_copy(o, a), R, W)
+
+    def ms(o, c, W):
+        op("V", lambda e: e.memset(o, c), "", W)
+
+    def act(o, a, R, W, f=AF.Copy, **kw):
+        op("S", lambda e: e.activation(o, a, f, **kw), R, W)
+
+    def mm(o, l, r, st, sp, R, W):
+        op("P", lambda e: e.matmul(o, l, r, st, sp), R, W)
+
+    def sel(k):
+        return T.SELP[:, 128 * k:128 * k + 128]
+
+    def conv(out, row, a, n, R, W):
+        for l in range(16):
+            mm(out, sel(l), row[:, a + l:a + 16 * (n - 1) + l + 1:16], l == 0, l == 15, R + " SELP", W)
+
+    dma("D", T.nbs[:], T.nb[:], "", "nbs", "d_nb")
+    dma("S", T.cbs[:], T.cb[:], "", "cbs", "d_cb")
+    dma("D", T.bss[:], T.bs[:], "", "bss", "d_bs")
+    dma("S", T.pns[:], T.pn[:], "", "pns", "d_pn")
+    dma("D", T.fss[:], T.fs[:], "", "fss", "d_fs")
+    dma("S", T.pfs[:], T.pf[:], "", "pfs", "d_pf")
+    dma("D", T.ths[:, 0:1], T.th[:], "", "ths", "d_th")
+    dma("S", T.xfs[:, 0:4096], T.xf[:, 0:4096], "", "xfs", "d_xa")
+    dma("D", T.xfs[:, 4096:8192], T.xf[:, 4096:8192], "", "xfsb", "d_xb")
+
+    def gop(fn, R, W):
+        op("G", fn, R, W)
+    ms(T.ONES[:], 1.0, "ONES")
+    ms(T.NB[:, 0:1], -8.5, "NB")
+    gop(lambda e: e.affine_select(T.SWT[:], T.ONES[:], [[-16, 8], [0, 16]], A.is_ge, 0.0, 0, 1), "ONES", "SWT")
+    gop(lambda e: e.affine_select(T.G16[:], T.SWT[:], [[16, 8], [0, 16]], A.is_ge, 0.0, 15, -1), "SWT", "G16")
+    gop(lambda e: e.affine_select(T.IDENT[:], T.ONES[:], [[-1, 128]], A.is_equal, 0.0, 0, 1), "ONES", "IDENT")
+    gop(lambda e: e.iota(T.PI[:, 0:1], [[1, 1]], 0, 1), "", "PI")
+    gop(lambda e: e.iota(T.LI[:], [[16, 16]], 0, 0), "", "LI")
+    gop(lambda e: e.iota(T.IOTC[:], [[1, 512]], -256, 0, allow_small_or_imprecise_dtypes=True), "", "IOTC")
+    for x in ("XB0", "XB1"):
+        for c in (0, 528):
+            gop(lambda e: e.iota(T[x][:, c:c + 16], [[0, 16]], 0, 0, allow_small_or_imprecise_dtypes=True), "", "+" + x)
+    for k in range(16):
+        gop(lambda e: e.affine_select(T.SELP[:, 128 * k:128 * k + 128], T.G16[:], [[0, 8], [1, 16]], A.is_equal, 0.0, -k, 0), "G16", "+SELP")
+    for b in range(9):
+        for c, v in ((b, 2 ** (8 - b)), (16 + b, 2 ** b if b else 0), (32 + b, -2 ** b if b else 1)):
+            gop(lambda e: e.iota(T.PAB[:, c:c + 1], [[0, 1]], v, 0, allow_small_or_imprecise_dtypes=True), "", "+PAB")
+    gop(lambda e: e.iota(T.IDX1[:], [[1, 256]], 1, 0, allow_small_or_imprecise_dtypes=True), "", "IDX1")
+    for t in range(5):
+        for c in (8, 536):
+            gop(lambda e: e.iota(T["WO%d" % t][:, c:c + 8], [[0, 8]], 0, 0, allow_small_or_imprecise_dtypes=True), "", "WO%dp" % t)
+    cp(T.fsU[:], T.fss[:], "fss", "fsU")
+    cp(T.bsU[:], T.bss[:], "bss", "bsU")
+    cp(T.nbU[:], T.nbs[:], "nbs", "nbU")
+    cp(T.CBF[:], T.cbs[:], "cbs", "CBF")
+    cp(T.OH[:], T.CBF[:].indirect(T.nbU[:]), "CBF nbU", "OHa OHb")
+    act(T.CS[:], T.CBF[:].indirect(T.bsU[:]), "CBF bsU", "CS")
+    p = 32 * NSET[0]
+    tt(T.XN[:, 0:256 - p], T.pfs[:, p:256], T.pns[:, p:256], A.subtract, "pfs pns", "XN")
+    for k in range(16):
+        act(T.NNEG[:, k::16], T.pns[:, p:256], "pns", "+NNEG", scale=-1.0)
+        act(T.FMN[:, k::16], T.XN[:, 0:256 - p], "XN", "+FMN")
+    act(T.IDF[:], T.IDENT[:], "IDENT", "IDF")
+    act(T.NIDF[:], T.IDENT[:], "IDENT", "NIDF", scale=-1.0)
+    for k in range(16):
+        cp(T.F16[:, k::16], T.pfs[:], "pfs", "+F16")
+    for k in range(16):
+        cp(T.N16[:, k::16], T.pns[:], "pns", "+N16")
+    cp(T.OA[:], T.CS[:].indirect(T.fsU[:]), "CS fsU", "OA")
+    ts(T.GN8[:], T.G16[:, ::16], -1.0, None, A.mult, None, "G16", "GN8")
+    for n, bits in enumerate((4032, 63)):
+        op("V", lambda e: e.tensor_scalar(T.TI[:, n:n + 1], T.ths[:, 0:1], 1, bits, A.arith_shift_right, A.bitwise_and), "ths", "TI%d" % n)
+    for n in range(2):
+        cp(T.thh[:, n:n + 1], T.TI[:, n:n + 1], "TI%d" % n, "thh%d" % n)
+    for n, c in enumerate(("THH", "THL")):
+        ts(T[c][:], T.ONES[:], T.thh[:, n:n + 1], -1.0, A.mult, A.mult, "ONES thh%d" % n, c)
+
+    def setup_lists():
+        op("V", lambda e: e.tensor_scalar(T.PM[:, 0:1], T.PI[:, 0:1], 15, None, A.bitwise_and), "PI", "PM")
+        cp(T.PMF[:, 0:1], T.PM[:, 0:1], "PM", "PMF")
+        ts(T.LIF[:], T.LI[:], T.PMF[:, 0:1], None, A.add, None, "LI PMF", "LIF")
+        ts(T.BASE[:], T.LI[:], 32.0, None, A.mult, None, "LI", "BASE")
+        ts(T.PMF[:, 1:2], T.PM[:, 0:1], 32.0, None, A.mult, None, "PM", "PMF1")
+        ts(T.LI1[:], T.LIF[:], 1.0, None, A.add, None, "LIF", "LI1")
+        ts(T.AB0[:], T.LIF[:], 144.0, None, A.add, None, "LIF", "AB0")
+        cp(T.BROW4[:].indirect(T.bsU[:]), T.IOTC[:], "IOTC bsU", "BROW4")
+        cp(T.MI0[:, 0:16], T.fss[:], "fss", "MI0")
+
+    def setup_sums():
+        cp(T.OI1[:], T.PL[:, 0:16], "PL", "OI1")
+        op("V", lambda e: e.tensor_scalar(T.OI2[:], T.OI1[:], 31, None, A.bitwise_and), "OI1", "OI2")
+        tt(T.ELS[:], T.OI2[:], T.BASE[:], A.add, "OI2 BASE", "ELS")
+
+    def setup_sites():
+        ts(T.MI0[:, 16:32], T.PL[:, 16:32], 0.0625, 256.0, A.mult, A.add, "PL", "MI0")
+
+    def setup_xor():
+        for b in range(4):
+            op("V", lambda e: e.tensor_scalar(T.BITS[:, b:b + 1], T.PM[:, 0:1], b, 1, A.arith_shift_right, A.bitwise_and), "PM", "+BITS")
+        for b in range(5):
+            op("V", lambda e: e.tensor_scalar(T.BITS[:, 4 + b:5 + b], T.PI[:, 0:1], b, 1, A.arith_shift_right, A.bitwise_and), "PI", "+BITS")
+        ms(T.LTB[:], 1.0, "LTB")
+        ms(T.RTB[:], 1.0, "RTB")
+        ts(T.LTB[:, 0:4], T.BITS[:, 0:4], -2.0, 1.0, A.mult, A.add, "BITS", "LTB")
+        ts(T.RTB[:, 4:9], T.BITS[:, 4:9], -2.0, 1.0, A.mult, A.add, "BITS", "RTB")
+        ms(T.C128[:, 0:1], 1.0 / 32768, "C128a")
+        ms(T.C128[:, 1:2], 1.0 / 256, "C128b")
+
+    def setup_signs():
+        mm(T.PM2[0:9, 0:128], T.LTB[:, 0:9], T.IDENT[:], True, True, "LTB IDENT", "PM2")
+        mm(T.PM2[0:9, 128:160], T.RTB[0:32, 0:9], T.IDENT[0:32, 0:32], True, True, "RTB IDENT", "PM2")
+        mm(T.PM2[0:9, 160:161], T.PAB[:, 16:25], T.C128[:, 0:1], True, True, "PAB C128a", "PM2")
+        mm(T.PM2[0:9, 161:162], T.PAB[:, 32:41], T.C128[:, 1:2], True, True, "PAB C128b", "PM2")
+
+    def setup_signs2():
+        cp(T.LB[0:9, :], T.PM2[0:9, 0:128], "PM2", "LB")
+        cp(T.RC[0:9, :], T.PM2[0:9, 128:160], "PM2", "RC")
+        cp(T.AB[0:9, 0:2], T.PM2[0:9, 160:162], "PM2", "AB")
+
+    def setup_boxes():
+        act(T.BROW[:], T.IOTC[:].indirect(T.bsU[:]), "IOTC bsU", "BROW")
+        act(T.XB0[:, 144:400], T.BROW[:].indirect(T.fsU[:]), "BROW fsU", "XB0")
+        act(T.XB0[:, 16:144], T.IOTC[:].indirect(T.nbU[:, 0:8]), "IOTC nbU", "XB0")
+        act(T.XB0[:, 400:528], T.IOTC[:].indirect(T.nbU[:, 8:16]), "IOTC nbU", "XB0")
+
+    def xg(j):
+        return T.XG[:, 512 * (j % NXG):512 * (j % NXG) + 512]
+
+    def gather(j):
+        off = T.OH if j < 8 else T.OA
+        key = ("OHa" if j < 4 else "OHb") if j < 8 else "OA"
+        c = j % 8
+        act(xg(j), T.xfs[:].indirect(off[:, 32 * c:32 * c + 32]), "xfs xfsb " + key, "XG%d" % (j % NXG))
+
+    def ident(j):
+        c, b = j % 8, "PX%d" % (j % 4)
+        x = "XG%d" % (j % NXG)
+        if c in NS[j // 8]:
+            n = NSET.index(c)
+            mm(T[b][:], T.IDENT[:], xg(j), True, False, "IDENT " + x, b)
+            mm(T[b][:], T.IDENT[:], T.NNEG[:, 512 * n:512 * n + 512], False, True, "IDENT NNEG", b)
+        else:
+            mm(T[b][:], T.IDENT[:], xg(j), True, True, "IDENT " + x, b)
+
+    def term_f(j):
+        c, b, n = j % 8, "PX%d" % (j % 4), (j // 4) % NT
+        o = T.TF[:, 512 * (j % 8):512 * (j % 8) + 512]
+        if c in NS[j // 8]:
+            tab, key, a = T.FMN, "FMN", NSET.index(c)
+        else:
+            tab, key, a = T.F16, "F16", c
+        tt(o, T[b][:], tab[:, 512 * a:512 * a + 512], A.max, b + " " + key, "TF%d_%d" % (n, j % 4))
+
+    def term_n(j):
+        c, b, n = j % 8, "PX%d" % (j % 4), (j // 4) % NT
+        o = T.TN[:, 512 * (j % 8):512 * (j % 8) + 512]
+        if c in NS[j // 8]:
+            act(o, T[b][:], b, "TN%d_%d" % (n, j % 4), f=AF.Relu)
+        else:
+            tt(o, T[b][:], T.N16[:, 512 * c:512 * c + 512], A.max, b + " N16", "TN%d_%d" % (n, j % 4))
+
+    def lanes(blk, which):
+        a, h = blk >= 2, blk % 2
+        nm = "%s%d" % (("TF", "TN")[which], blk % NT)
+        P = "PSC%d" % h
+        if not a and which == 0:
+            mm(T[P][:, 0:128], T.THH[:], T.IDENT[:], True, False, "THH IDENT", P)
+            mm(T[P][:, 0:128], T.THL[:], T.IDENT[:], False, False, "THL IDENT", P)
+        tab, key = (T.G16[:, ::16], "G16") if a == (which == 0) else (T.GN8[:], "GN8")
+        for k in range(16):
+            o = 2048 * (blk % NT)
+            mm(T[P][:, k:128:16], T[nm[0:2]][:, o + k:o + 2048:16], tab, False, a and which == 1 and k == 15,
+               "%s_0 %s_1 %s_2 %s_3 %s" % (nm, nm, nm, nm, key), P)
+
+    def half_cmp(h):
+        ts(T.SWT[:], T["PSC%d" % h][:, 0:128], 0.0, None, A.is_gt, None, "PSC%d" % h, "SWT")
+        mm(T.PM2[:, 256:384], T.SWT[:], T.IDENT[:], True, True, "SWT IDENT", "PM2")
+
+    def half_sum(h):
+        cp(T.SW[:, 128 * h:128 * h + 128], T.PM2[:, 256:384], "PM2", "SW%d" % h)
+        conv(T.PL[:, 8 * h:8 * h + 8], T.SW, 128 * h, 8, "SW%d" % h, "PL")
+        if h:
+            mm(T.PSC1[:, 128:384], T.G16[:], T.SW[:], True, True, "G16 SW0 SW1", "PSC1")
+            act(T.FLB[:], T.PSC1[:, 128:384], "PSC1 NB", "FLB", f=AF.Sign, bias=T.NB[:, 0:1])
+
+    def half_rows(t, h):
+        s = slice(128 * h, 128 * h + 128)
+        wo, key = T["WO%d" % t], "WO%d%s" % (t, "ab"[h])
+        p = T.PM2[:, 256:384]
+        tt(p, T.PM2[:, s], T.SW[:, s], A.mult, "PM2 SW%d" % h, "PM2")
+        a = slice(144 + 128 * h, 272 + 128 * h)
+        hh = slice(16 + 384 * h, 144 + 384 * h)
+        tt(wo[:, a], p, T.CAf[:, s], A.add, "PM2 CAf", "+" + key)
+        tt(wo[:, hh], T.CHf[:, s], p, A.subtract, "PM2 CHf%d" % h, "+" + key)
+        if t < 4:
+            w = slice(16 + 256 * h, 272 + 256 * h)
+            send(T.cores[(rank + 1) % N], T["WI%d" % (t + 1)][:, w], wo[:, w], key, "a%d_%d" % (h, t + 1))
+
+    def half_off(h):
+        s = slice(8 * h, 8 * h + 8)
+        tt(T.OI1[:, s], T.PL[:, s], T.ELS[:, s], A.add, "PL ELS", "OI1")
+        op("V", lambda e: e.tensor_scalar(T.OI2[:, s], T.OI1[:, s], 8191 - 32, None, A.bitwise_and), "OI1", "OI2")
+        ts(T.OFFU[:, s], T.OI2[:, s], T.PMF[:, 1:2], None, A.add, None, "OI2 PMF1", "OFFU%d" % h)
+
+    def half_put(h):
+        s, r = slice(8 * h, 8 * h + 8), slice(128 * h, 128 * h + 128)
+        cp(T.xfs[:].indirect(T.OFFU[:, s]), T.pfs[:, r], "pfs OFFU%d" % h, "xfs xfsb")
+
+    def half_eta(t, h):
+        s = slice(8 * h, 8 * h + 8)
+        wo, key = T["WO%d" % t], "WO%d%s" % (t, "ab"[h])
+        e = slice(528 * h, 528 * h + 16)
+        ts(T.TD[:, s], T.PL[:, s], 4.5, (-128.0, 128.0)[h], A.is_lt, A.mult, "PL", "TD%d" % h)
+        tt(wo[:, 528 * h:528 * h + 8], T.LIF[:, s], T.TD[:, s], A.subtract, "LIF TD%d" % h, "WO%de%d" % (t, h))
+        if t < 4:
+            send(T.cores[(rank + 1) % N], T["WI%d" % (t + 1)][:, e], wo[:, e], "WO%de%d WO%dp" % (t, h, t), "a%d_%d" % (3 + h, t + 1))
+            act(T["MO%d" % t][:, 32 + 24 * h:40 + 24 * h], wo[:, 528 * h:528 * h + 8], "WO%de%d" % (t, h), "MO%de%d" % (t, h),
+                f=AF.Identity, bias=(16.0, 272.0)[h])
+
+    def win(t, h):
+        return T["WI%d" % t][:, 16 + 256 * h:272 + 256 * h]
+
+    def take_h(t, h):
+        s = slice(8 * h, 8 * h + 8)
+        cp(T.ETAU[:, s], T["WI%d" % t][:, 528 * h:528 * h + 8], "WI%de%d" % (t, h), "ETAU%d" % h)
+        cp(T.OH[:, 128 * h:128 * h + 128], win(t, h).indirect(T.ETAU[:, s]), "WI%d%s ETAU%d" % (t, "ab"[h], h), "OH" + "ab"[h])
+
+    def all_in(t):
+        return "WI%da WI%db WI%de0 WI%de1 " % (t, t, t, t)
+
+    def take_a(t):
+        cp(T.ALU[:], T["MI%d" % t][:, 40:56], "MI%d" % t, "ALU")
+        cp(T.OA[:], T["WI%d" % t][:].indirect(T.ALU[:]), all_in(t) + "ALU", "OA")
+
+    def floats(t, part):
+        if t == 0:
+            if part < 2:
+                h = part
+                act(T.CHf[:, 128 * h:128 * h + 128], T.CBF[:].indirect(T.nbU[:, 8 * h:8 * h + 8]), "CBF nbU", "CHf%d" % h)
+            else:
+                act(T.CAf[:], T.CS[:].indirect(T.fsU[:]), "CS fsU", "CAf")
+        elif part < 2:
+            h = part
+            act(T.CHf[:, 128 * h:128 * h + 128], win(t, h).indirect(T.ETAU[:, 8 * h:8 * h + 8]), "WI%d%s ETAU%d" % (t, "ab"[h], h), "CHf%d" % h)
+        else:
+            act(T.CAf[:], T["WI%d" % t][:].indirect(T.ALU[:]), all_in(t) + "ALU", "CAf")
+
+    def diff(h):
+        s = slice(128 * h, 128 * h + 128)
+        mm(T.PM2[:, s], T.IDF[:], T.CHf[:, s], True, False, "IDF CHf%d" % h, "PM2")
+        mm(T.PM2[:, s], T.NIDF[:], T.CAf[:, s], False, True, "NIDF CAf", "PM2")
+
+    def sites_in(t):
+        m = "MI%d" % t
+        cp(T.FU[:], T[m][:, 0:16], m, "FU")
+        tt(T.DFG[:], T[m][:, 16:32], T[m][:, 0:16], A.subtract, m, "DFG")
+
+    def chain(t):
+        op("V", lambda e: e.tensor_reduce(T.RTOT[:, 0:1], T.PL[:, 0:16], AxisListType.X, A.add), "PL", "RTOT")
+        mm(T.PM2[0:9, 384:385], T.PAB[:, 0:9], T.RTOT[:, 0:1], True, True, "PAB RTOT", "PM2")
+        ts(T.TRN[:], T.PL[:, 0:16], 4.5, None, A.is_lt, None, "PL", "TRN")
+        cp(T.UI[0:9, 0:1], T.PM2[0:9, 384:385], "PM2", "UI")
+        op("V", lambda e: e.tensor_scalar(T.UB[0:9, 0:1], T.UI[0:9, 0:1], 256, None, A.bitwise_and), "UI", "UB")
+        if t < 4:
+            ts(T.FL16[:], T.PL[:, 0:16], 8.5, 0.0625, A.is_gt, A.mult, "PL", "FL16")
+        ts(T.CF[0:9, 0:1], T.UB[0:9, 0:1], T.AB[0:9, 0:1], T.AB[0:9, 1:2], A.mult, A.add, "UB AB", "CF")
+        tt(T.XX[:], T.TRN[:], T.DFG[:], A.mult, "TRN DFG", "XX")
+        ts(T.RS[0:9, :], T.RC[0:9, :], T.CF[0:9, 0:1], None, A.mult, None, "RC CF", "RS")
+        mm(T.PM2[:, 400:432], T.LB[0:9, :], T.RS[0:9, :], True, True, "LB RS", "PM2")
+        m, mo = "MI%d" % t, "MO%d" % t
+        tt(T[mo][:, 0:16], T[m][:, 0:16], T.XX[:], A.add, m + " XX", mo)
+        ts(T.XLU[:], T.PM2[:, 400:432], 255.5, None, A.add, None, "PM2", "XLU")
+        tt(T.U[:, 0:512].indirect(T.FU[:]), T.FLB[:], T.IDX1[:], A.mult, "FLB IDX1 FU", "U0")
+        if t < 4:
+            tt(T[mo][:, 16:32], T[m][:, 16:32], T.XX[:], A.subtract, m + " XX", mo)
+            tt(T.ABS[:], T.AB0[:], T.TD[:], A.add, "AB0 TD0 TD1", "ABS")
+
+    def partner(t):
+        act(T.U[:, 512:1024], T.U[:, 0:512].indirect(T.XLU[:]), "U0 XLU", "U1")
+        act(T.MROW[:], T.U[:, 512:1024].indirect(T.FU[:]), "U1 FU", "MROW", f=AF.Relu)
+        conv(T.PL[:, 32:48], T.MROW, 0, 16, "MROW", "PL")
+
+    def alpha(t):
+        mo = "MO%d" % t
+        tt(T.Z1[:], T.PL[:, 32:48], T.FL16[:], A.mult, "PL FL16", "Z1")
+        ts(T.Z2[:], T.Z1[:], 256.0, None, A.mult, None, "Z1", "Z2")
+        tt(T.Z1[:], T.Z1[:], T.ABS[:], A.add, "Z1 ABS", "Z1")
+        tt(T.Z3[:], T.Z2[:], T.LI1[:], A.min, "Z2 LI1", "Z3")
+        tt(T[mo][:, 40:56], T.Z1[:], T.Z3[:], A.subtract, "Z1 Z3", mo)
+        mo += " %se0 %se1" % (mo, mo)
+        send(T.cores[(rank + 1) % N], T["MI%d" % (t + 1)][:], T["MO%d" % t][:], mo, "a2_%d" % (t + 1))
+        if t in (1, 2):
+            send(T.cores[(rank - t) % N], T["HI%d" % t][:], T["MO%d" % t][:, 32:64], mo, "ah%d" % t)
+
+    def boxes(n, lists, key):
+        a, b = "XB%d" % (n % 2), "XB%d" % (1 - n % 2)
+        cp(T.XLS[:], lists, key, "XLS")
+        act(T[b][:, 16:528], T[a][:].indirect(T.XLS[:]), a + " XLS", b)
+
+    def box_lists():
+        ts(T.YL[:], T.PL[:, 64:96], 0.0625, 256.0, A.mult, A.add, "PL", "YL")
+        cp(T.GU[:, 0:8], T.MI4[:, 16:24], "MI4", "GU")
+        cp(T.GU[:, 8:24], T.MI4[:, 0:16], "MI4", "+GU")
+        cp(T.GU[:, 24:32], T.MI4[:, 24:32], "MI4", "+GU")
+        cp(T.BROW4[:].indirect(T.GU[:]), T.XB0[:, 16:528], "XB0 GU", "BROW4")
+        conv(T.PL[:, 128:160], T.BROW4, 0, 32, "BROW4", "PL")
+
+    def put_yc(h):
+        k = "WO4" + "ab"[h]
+        cp(T.YC[:].indirect(T.YL[:, 16 * h:16 * h + 16]), T.WO4[:, 16 + 256 * h:272 + 256 * h], k + " YL", "YC")
+
+    def main(t):
+        st = {"g": 0, "p": 0}
+
+        def ahead(j):
+            lim = 4 if not st.get("oh1") else (8 if not st.get("oa") else 16)
+            while st["g"] < min(lim, j + LG if j else 3):
+                gather(st["g"])
+                st["g"] += 1
+            while st["p"] < min(st["g"], j + LP + 1, 16):
+                ident(st["p"])
+                if st["p"] in NS[0]:
+                    term_n(st["p"])
+                st["p"] += 1
+        if t == 0:
+            st["oh1"] = st["oa"] = True
+        for j in range(16):
+            ahead(j)
+            if j == 0 and t:
+                partner(t - 1)
+            if j == 3 and t:
+                alpha(t - 1)
+            if j == 2 and t:
+                take_h(t, 1)
+                st["oh1"] = True
+                ahead(j)
+            if t == 0 and j == 4:
+                conv(T.PL[:, 0:16], T.pfs, 0, 16, "pfs", "PL")
+                act(T.GROW[:], T.BROW4[:].indirect(T.nbU[:]), "BROW4 nbU", "GROW")
+            if t == 0 and j == 6:
+                setup_sums()
+                conv(T.PL[:, 16:32], T.GROW, 0, 16, "GROW", "PL")
+                setup_signs()
+            if t == 0 and j == 9:
+                setup_sites()
+                setup_signs2()
+            if j == 7:
+                gop(lambda e: e.iota(T.U[:, 0:512], [[0, 512]], 0, 0, allow_small_or_imprecise_dtypes=True), "", "U0")
+            if j == 10:
+                floats(t, 0)
+                floats(t, 1)
+            if j == 6 and t:
+                take_a(t)
+                st["oa"] = True
+                ahead(j)
+            if j == JF:
+                floats(t, 2)
+            if j == 9:
+                sites_in(t)
+            if j == JD:
+                diff(0)
+            if t == 1 and j == 10:
+                boxes(0, T.MO0[:, 32:64], "MO0 MO0e0 MO0e1")
+            if t == 3 and j == 4:
+                boxes(1, T.HI1[:], "HI1")
+            if t == 4 and j == 3:
+                boxes(2, T.HI2[:], "HI2")
+            if t == 4 and j == 8:
+                boxes(3, T.MI4[:, 32:64], "MI4")
+            if t == 4 and j == 12:
+                conv(T.PL[:, 64:96], T.XB0, 16, 32, "XB0", "PL")
+            if t == 4 and j == 13:
+                box_lists()
+            if j == JC:
+                half_cmp(0)
+            term_f(j)
+            if j == JS:
+                half_sum(0)
+                half_rows(t, 0)
+                diff(1)
+            if j not in NS[0]:
+                term_n(j)
+            if j < 12:
+                if j % 4 == 3:
+                    lanes(j // 4, 0)
+                    lanes(j // 4, 1)
+        lanes(3, 0)
+        lanes(3, 1)
+        half_eta(t, 0)
+        if t < 4:
+            half_off(0)
+            half_put(0)
+        else:
+            put_yc(0)
+        half_cmp(1)
+        half_sum(1)
+        half_rows(t, 1)
+        if t < 4:
+            half_off(1)
+            half_eta(t, 1)
+            half_put(1)
+        else:
+            half_eta(t, 1)
+            put_yc(1)
+            dma("D", T.yc[:], T.YC[:], "YC", "yc", "o_yc")
+            ts(T.E4U[:, 0:8], T.WO4[:, 0:8], 16.0, None, A.add, None, "WO4e0", "E4U")
+            ts(T.E4U[:, 8:16], T.WO4[:, 528:536], 272.0, None, A.add, None, "WO4e1", "+E4U")
+            act(T.XN[:], T.XB0[:].indirect(T.E4U[:]), "XB0 E4U", "XN")
+        if t < 4:
+            take_h(t + 1, 0)
+        chain(t)
+
+    setup_lists()
+    setup_boxes()
+    setup_xor()
+    for t in range(5):
+        main(t)
+
+    dma("D", T.yf[:], T.MO4[:, 0:16], "MO4", "yf", "o_yf")
+    conv(T.PL[:, 320:336], T.XN, 0, 16, "XN", "PL")
+    act(T.U[:, 1024:1536], T.BROW4[:].indirect(T.XLU[:]), "BROW4 XLU", "U2")
+    act(T.U[:, 512:1024], T.U[:, 0:512].indirect(T.XLU[:]), "U0 XLU", "U1")
+    ts(T.Z3[:], T.PL[:, 320:336], 0.0625, 256.0, A.mult, A.add, "PL", "Z3")
+    dma("D", T.yn[:], T.Z3[:], "Z3", "yn", "o_yn")
+    ts(T.BL[:], T.PL[:, 128:160], 0.0625, 256.0, A.mult, A.add, "PL", "BL")
+    conv(T.PL[:, 256:288], T.U, 1024, 32, "U2", "PL")
+    conv(T.PL[:, 192:224], T.U, 0, 32, "U0", "PL")
+    conv(T.PL[:, 224:256], T.U, 512, 32, "U1", "PL")
+    ts(T.B1[:], T.PL[:, 192:224], 0.5, None, A.is_gt, None, "PL", "B1")
+    ts(T.B2[:], T.PL[:, 224:256], 0.5, None, A.is_gt, None, "PL", "B2")
+    ts(T.B3[:], T.PL[:, 256:288], 0.0625, 256.0, A.mult, A.add, "PL", "B3")
+    tt(T.B1[:], T.B1[:], T.B2[:], A.mult, "B1 B2", "B1")
+    tt(T.B3[:], T.B3[:], T.BL[:], A.subtract, "B3 BL", "B3")
+    tt(T.B4[:], T.B3[:], T.B1[:], A.mult, "B3 B1", "B4")
+    tt(T.YB[:], T.BL[:], T.B4[:], A.add, "BL B4", "YB")
+    dma("D", T.yb[:], T.YB[:], "YB", "yb", "o_yb")
+    for q in ("V", "S", "P", "G"):
+        g.wait_ge(T.sem["q" + q], cnt[q])
+    for n in ("yc", "yb", "yf", "yn"):
+        g.wait_ge(T.sem["o_" + n], 16)
+    g.wait_ge(T.sem.loc, nloc[0])

@@ -1,12 +1,13 @@
-from concourse.mybir import AluOpType as A, AxisListType, ActivationFunctionType as AF
+from concourse.mybir import AluOpType as A, ActivationFunctionType as AF
 
-NS = ((), (5, 6, 7))
-NSET = (5, 6, 7)
-NXG, NT = 8, 2
-LG = 7
-JF, JD, JC, JS = 9, 14, 14, 14
-LP = 2
-WCOL = 544
+NXG, NCL = 6, 4
+VG = ((1, 5, 9, 12), (1, 6, 9, 12), (1, 6, 9, 12), (1, 6, 9, 12), (1, 6))
+FLAGS = ((0, 8), (8, 12), (12, 16))
+OFFS = ((0, 12), (12, 16))
+HCOL, ACOL = (64, 128, 0, 448), 192
+SENDS = ((64, 128, "h0"), (128, 320, "h1 a0 a1"), (0, 64, "h2"), (320, 512, "a2 a3 h3"))
+CYC, GAT, SCA, PEC, HOP, FAR = 0.83, 1.3, 3.2, 0.5, 220, 3000
+PASSES = 4
 FL, BF, I32, U16 = "float32", "bfloat16", "int32", "uint16"
 
 
@@ -16,52 +17,86 @@ def _scratch():
     def sb(names, cols, dt):
         for n in names.split():
             s[n] = ("sbuf", [128, cols], dt)
-    sb("xfs", 8192, BF)
-    sb("F16 N16", 4096, BF)
-    sb("FMN NNEG", 512 * len(NSET), BF)
-    sb("pfs pns FLB MROW IDX1 XN", 256, BF)
+    sb("xfs D1", 8192, BF)
+    sb("XG", 1024 * NXG, BF)
+    sb("CL", 1024 * NCL, BF)
+    for n in ("WH", "WA", "Z"):
+        s[n] = ("sbuf", [128, 16, 8, 16], BF)
+    sb("pfs pns LO HI DF SG AB MM TROW MROW IDX GROW", 256, BF)
     sb("cbs", 512, I32)
     sb("CBF CS YC", 512, FL)
+    sb("AFL PS", 256, FL)
+    sb("WI WO", 512 * 5, FL)
+    sb("MI", 64 * 5, I32)
+    sb("MO", 80 * 4, I32)
+    sb("HM", 32 * 4, I32)
     sb("bss", 32, I32)
-    sb("fss nbs OI1 OI2 BASE LI", 16, I32)
-    sb("ths TI PI PM UI UB", 2, I32)
-    sb("BITS", 16, I32)
+    sb("fss nbs OI1 OI2 EI1 EI2 BASE LI ELS AL BI1 BI2", 16, I32)
+    sb("ths TH PI PM RI", 2, I32)
     sb("IDF NIDF", 128, FL)
-    sb("NB thh PMF RTOT CF AB C128", 2, FL)
-    sb("ONES", 128, BF)
-    sb("IDENT G16", 128, BF)
-    sb("SELP", 2048, BF)
-    sb("SWT THH THL", 128, BF)
-    sb("GN8", 8, BF)
-    sb("XG", 512 * NXG, BF)
-    sb("TF TN", 2048 * NT, BF)
-    sb("OH OA", 256, U16)
-    sb("CAf CHf", 256, FL)
-    sb("SW", 256, BF)
-    sb("WI1 WI2 WI3 WI4 WO0 WO1 WO2 WO3 WO4", WCOL, FL)
-    sb("MI0 MI1 MI2 MI3 MI4 MO0 MO1 MO2 MO3 MO4", 64, FL)
-    sb("HI1 HI2", 32, FL)
-    sb("bsU XLU XLS YL GU", 32, U16)
-    sb("fsU nbU FU ETAU ALU OFFU E4U", 16, U16)
-    sb("DFG TRN XX TD FL16 ABS Z1 Z2 Z3 LIF LI1 AB0 ELS", 16, FL)
+    sb("THN PMF PIF DD LX1", 2, FL)
+    sb("ACC", 8, FL)
+    sb("ONES IDENT G16 SWT KK K16 TI LB", 128, BF)
+    sb("SELW NSELW", 144, BF)
+    sb("EUW ESW", 240, BF)
+    sb("TR IOTC BROW BROW4 XB0 XB1", 512, BF)
+    sb("LL", 48, BF)
+    sb("HALF", 2, BF)
+    sb("LTB RTB SB9 P2", 16, BF)
+    sb("RS RX", 32, BF)
+    sb("UH UA", 256, U16)
+    sb("bsU XLU XLS YL", 32, U16)
+    sb("FA", 64, U16)
+    sb("fsU nbU OFFU GU", 16, U16)
+    sb("L256 PABI PAB DA YF YN", 16, FL)
+    sb("TRN DF2 XX YL32 BL B1 B2 YB", 32, FL)
     sb("U", 1536, BF)
-    sb("IOTC BROW BROW4", 512, BF)
-    sb("XB0 XB1", WCOL, BF)
-    sb("GROW", 256, BF)
-    sb("RS RC", 32, BF)
-    sb("LB", 128, BF)
-    sb("LTB RTB", 16, BF)
-    sb("PAB", 48, FL)
-    sb("BL B1 B2 B3 B4 YB", 32, FL)
-    for n in ["PX0", "PX1", "PX2", "PX3", "PSC0", "PSC1", "PL", "PM2"]:
+    for n in ("PB0", "PB1", "PB2", "PB3"):
+        s[n] = ("psum", [128, 4, 8, 16], FL)
+    for n in ("PD0", "PD1", "PL", "PN"):
         s[n] = ("psum", [128, 512], FL)
     return s
 
 
 SCRATCH = _scratch()
+BANKS = ("PB0", "PB1", "PB2", "PB3", "PD0", "PD1", "PL", "PN")
 LOADS = ["pf", "pn", "fs", "bs", "nb", "th", "cb", "xa", "xb"]
 SEMAPHORES = (["qV", "qS", "qP", "qG", "loc"] + ["d_" + n for n in LOADS] + ["o_yc", "o_yb", "o_yf", "o_yn"]
-              + ["a%d_%d" % (k, t) for k in range(5) for t in range(1, 5)] + ["ah1", "ah2"])
+              + ["a%d_%d" % (k, t) for k in range(5) for t in range(1, 5)] + ["ah1", "ah2", "ah3"])
+
+
+def issue_order(calls):
+    n = len(calls)
+    pre = [c["pre"] for c in calls]
+    after = [[] for _ in range(n)]
+    for i in range(n):
+        for p in pre[i]:
+            after[p].append(i)
+
+    def gap(i, j):
+        return 0 if calls[i]["q"] == calls[j]["q"] == "P" else calls[min(i, j)]["late"]
+
+    def walk(before, behind, urgent, start):
+        left = [len(b) for b in before]
+        ready = {i: start(i) for i in range(n) if not left[i]}
+        free, end, order = {}, [0.0] * n, []
+        while ready:
+            t0, q = min((max(r, free.get(calls[i]["q"], 0.0)), calls[i]["q"]) for i, r in ready.items())
+            i = max((i for i, r in ready.items() if calls[i]["q"] == q and r <= t0 + HOP / 2), key=urgent)
+            end[i] = free[q] = max(t0, ready.pop(i)) + calls[i]["ns"]
+            order.append(i)
+            for j in behind[i]:
+                left[j] -= 1
+                if not left[j]:
+                    ready[j] = max(end[p] + gap(p, j) for p in before[j])
+        return end, order
+    end, best = list(range(n)), None
+    for _ in range(PASSES):
+        back, _o = walk(after, pre, lambda i: end[i], lambda i: calls[i]["late"])
+        end, order = walk(pre, after, lambda i: (i < len(LOADS), -i if i < len(LOADS) else back[i]), lambda i: 0.0)
+        if best is None or max(end) < best[0]:
+            best = (max(end), order)
+    return best[1]
 
 
 def rank_program(g, core, T, topo):
@@ -70,527 +105,406 @@ def rank_program(g, core, T, topo):
         return
     N = len(T.cores)
     Q = {"V": g.vector, "S": g.scalar, "P": g.tensor, "G": g, "D": g.sync}
-    cnt = {"V": 0, "S": 0, "P": 0, "G": 0}
-    seen = {q: {} for q in Q}
-    snap = {}
-    wr, wp, rd = {}, {}, {}
+    calls = []
+    whole, parts, rd = {}, {}, {}
 
-    def need(q, R, W):
-        toks = []
+    def record(q, fns, R, W, ns, late=HOP, tok=None, far=False):
+        R, W, pre = R.split(), W.split(), set()
         for k in R:
-            if k in wr:
-                toks.append(wr[k])
-            if k[0] == "P":
-                toks += [t for qq, t in rd.get(k, {}).items() if qq != q]
+            pre.update(parts.get(k, []))
+            if k in BANKS:
+                pre.update(i for i in rd.get(k, []) if calls[i]["q"] != q)
         for k in W:
-            w = wr if k[0] != "+" else wp
-            k = k.lstrip("+")
-            if k in w and (q != "P" or w[k][0] != "qP"):
-                toks.append(w[k])
-            toks += [t for qq, t in rd.get(k, {}).items() if q != "P" or qq != q]
-        best = {}
-        for s, v in toks:
-            if v > seen[q].get(s, 0):
-                best[s] = max(best.get(s, 0), v)
-        for s in sorted(best, key=lambda s: -best[s]):
-            v = best[s]
-            if v <= seen[q].get(s, 0):
-                continue
-            Q[q].wait_ge(T.sem[s], v)
-            for s2, v2 in snap.get((s, v), {}).items():
-                seen[q][s2] = max(seen[q].get(s2, 0), v2)
-            seen[q][s] = max(seen[q].get(s, 0), v)
-
-    def done(q, R, W, tok):
-        snap[tok] = dict(seen[q])
+            pre.update(parts.get(k, []) if k[0] != "+" else whole.get(k[1:], []))
+            pre.update(rd.get(k.lstrip("+"), []))
+        i = len(calls)
+        calls.append({"q": q, "fns": fns, "pre": pre, "ns": ns, "late": late, "tok": tok, "far": far})
         for k in R:
-            rd.setdefault(k, {})[q] = tok
+            rd.setdefault(k, []).append(i)
         for k in W:
-            wr[k.lstrip("+")] = tok
-            if k[0] != "+":
-                wp[k] = tok
-                rd[k] = {}
+            if k[0] == "+":
+                parts.setdefault(k[1:], []).append(i)
+            else:
+                whole[k], parts[k], rd[k] = [i], [i], []
 
-    def op(q, fn, R, W):
-        R, W = R.split(), W.split()
-        need(q, R, W)
-        fn(Q[q]).then_inc(T.sem["q" + q], 1)
-        cnt[q] += 1
-        done(q, R, W, ("q" + q, cnt[q]))
+    def emit():
+        cnt = {"V": 0, "S": 0, "P": 0, "G": 0}
+        seen = {q: {} for q in Q}
+        snap, tok = {}, {}
+        for i in issue_order(calls):
+            c = calls[i]
+            q, best = c["q"], {}
+            for p in c["pre"]:
+                if q != "P" or calls[p]["q"] != "P":
+                    s, v = tok[p]
+                    best[s] = max(best.get(s, 0), v)
+            for s in sorted(best, key=lambda s: -best[s]):
+                v = best[s]
+                if v > seen[q].get(s, 0):
+                    Q[q].wait_ge(T.sem[s], v)
+                    for s2, v2 in snap.get((s, v), {}).items():
+                        seen[q][s2] = max(seen[q].get(s2, 0), v2)
+                    seen[q][s] = v
+            for fn in c["fns"]:
+                if c["tok"]:
+                    fn(Q[q])
+                else:
+                    fn(Q[q]).then_inc(T.sem["q" + q], 1)
+                    cnt[q] += 1
+            tok[i] = c["tok"] or ("q" + q, cnt[q])
+            if not c["far"]:
+                snap[tok[i]] = dict(seen[q])
+        for q in cnt:
+            g.wait_ge(T.sem["q" + q], cnt[q])
 
-    def dma(q, out, in_, R, W, sem):
-        R, W = R.split(), W.split()
-        need(q, R, W)
-        Q[q].dma_start(out, in_).then_inc(T.sem[sem], 16)
-        done(q, R, W, (sem, 16))
+    def dma(q, out, in_, R, W, sem, late=2500):
+        record(q, [lambda e: e.dma_start(out, in_).then_inc(T.sem[sem], 16)], R, W, 60, late, (sem, 16))
 
     nloc = [0]
 
-    def send(dst, out, in_, R, sem):
-        need("G", R.split(), [])
-        m = topo.mask(core, dst)
+    def send(hops, out, in_, R, W, sem, cols):
+        dst, src = T.cores[(rank + hops) % N], T.cores[(rank - hops) % N]
         rid, pid, _s = topo.addr(dst)
-        g.remote_dma(out, in_, T.sem[sem], T.sem.loc, pid, rid, m)
+        record("G", [lambda e: e.remote_dma(out, in_, T.sem[sem], T.sem.loc, pid, rid, topo.mask(core, dst))], R, W,
+               400, FAR + 6 * cols, (sem, len(topo.engines(src, core))), True)
         nloc[0] += len(topo.engines(core, dst))
 
-    for t in range(1, 5):
-        src = T.cores[(rank - 1) % N]
-        ne = len(topo.engines(src, core))
-        wr["WI%da" % t] = ("a0_%d" % t, ne)
-        wr["WI%db" % t] = ("a1_%d" % t, ne)
-        wr["WI%de0" % t] = ("a3_%d" % t, ne)
-        wr["WI%de1" % t] = ("a4_%d" % t, ne)
-        wr["MI%d" % t] = ("a2_%d" % t, ne)
-    wr["HI1"] = ("ah1", len(topo.engines(T.cores[(rank + 1) % N], core)))
-    wr["HI2"] = ("ah2", len(topo.engines(T.cores[(rank + 2) % N], core)))
+    def vec(fn, R, W, n):
+        record("V", [fn], R, W, max(n, 64 * CYC))
 
-    def tt(o, a, b, o_, R, W):
-        op("V", lambda e: e.tensor_tensor(o, a, b, o_), R, W)
+    def tt(o, a, b, o_, R, W, n=0):
+        vec(lambda e: e.tensor_tensor(o, a, b, o_), R, W, n)
 
-    def ts(o, a, s1, s2, o0, o1, R, W):
+    def ts(o, a, s1, s2, o0, o1, R, W, n=0):
         if o1 is None:
-            op("V", lambda e: e.tensor_scalar(o, a, s1, None, o0), R, W)
+            vec(lambda e: e.tensor_scalar(o, a, s1, None, o0), R, W, n)
         else:
-            op("V", lambda e: e.tensor_scalar(o, a, s1, s2, o0, o1), R, W)
+            vec(lambda e: e.tensor_scalar(o, a, s1, s2, o0, o1), R, W, n)
 
-    def cp(o, a, R, W):
-        op("V", lambda e: e.tensor_copy(o, a), R, W)
+    def cp(o, a, R, W, n=0):
+        vec(lambda e: e.tensor_copy(o, a), R, W, n)
 
-    def ms(o, c, W):
-        op("V", lambda e: e.memset(o, c), "", W)
+    def ms(o, c, W, n=0):
+        vec(lambda e: e.memset(o, c), "", W, n)
 
-    def act(o, a, R, W, f=AF.Copy, **kw):
-        op("S", lambda e: e.activation(o, a, f, **kw), R, W)
+    def act(o, a, R, W, n=0, f=AF.Copy, **kw):
+        record("S", [lambda e: e.activation(o, a, f, **kw)], R, W, max(n, 64 * CYC))
 
-    def mm(o, l, r, st, sp, R, W):
-        op("P", lambda e: e.matmul(o, l, r, st, sp), R, W)
+    def mms(l, R, W, n):
+        record("P", [lambda e, m=m: e.matmul(*m) for m in l], R, W, n * PEC)
 
-    def sel(k):
-        return T.SELP[:, 128 * k:128 * k + 128]
+    def iota(o, pat, base, cm, W, n=16, **kw):
+        record("G", [lambda e: e.iota(o, pat, base, cm, **kw)], "", W, 130 + 2 * n * CYC)
 
-    def conv(out, row, a, n, R, W):
-        for l in range(16):
-            mm(out, sel(l), row[:, a + l:a + 16 * (n - 1) + l + 1:16], l == 0, l == 15, R + " SELP", W)
+    def fiota(o, pat, base, cm, W, n=16):
+        iota(o, pat, base, cm, W, n, allow_small_or_imprecise_dtypes=True)
 
-    dma("D", T.nbs[:], T.nb[:], "", "nbs", "d_nb")
-    dma("S", T.cbs[:], T.cb[:], "", "cbs", "d_cb")
-    dma("D", T.bss[:], T.bs[:], "", "bss", "d_bs")
+    def sel(o, a, pat, cmp_, fill, base, cm, R, W):
+        record("G", [lambda e: e.affine_select(o, a, pat, cmp_, fill, base, cm)], R, W, 170 + 256 * CYC)
+
+    def gat(n):
+        return 60 + GAT * n
+
+    def sca(n):
+        return 50 + SCA * n
+
+    def conv(out, row, a, n, R, W, st=True, sp=True, tab="SELW"):
+        mms([(out, T[tab][:, 15 - l:143 - l], row[:, a + l:a + 16 * (n - 1) + l + 1:16], st and l == 0, sp and l == 15)
+             for l in range(16)], R + " " + tab, W, 1024)
+
+    def wi(t, a, b):
+        return T.WI[:, 512 * t + a:512 * t + b]
+
+    def wo(t, a, b):
+        return T.WO[:, 512 * t + a:512 * t + b]
+
+    def mi(t, a, b):
+        return T.MI[:, 64 * t + a:64 * t + b]
+
+    def mo(t, a, b):
+        return T.MO[:, 80 * t + a:80 * t + b]
+
+    def fa(t, a, b):
+        return T.FA[:, 32 * (t % 2) + a:32 * (t % 2) + b]
+
+    dma("D", T.pfs[:], T.pf[:], "", "pfs", "d_pf")
     dma("S", T.pns[:], T.pn[:], "", "pns", "d_pn")
-    dma("D", T.fss[:], T.fs[:], "", "fss", "d_fs")
-    dma("S", T.pfs[:], T.pf[:], "", "pfs", "d_pf")
-    dma("D", T.ths[:, 0:1], T.th[:], "", "ths", "d_th")
-    dma("S", T.xfs[:, 0:4096], T.xf[:, 0:4096], "", "xfs", "d_xa")
-    dma("D", T.xfs[:, 4096:8192], T.xf[:, 4096:8192], "", "xfsb", "d_xb")
+    dma("D", T.nbs[:], T.nb[:], "", "nbs", "d_nb", 3000)
+    dma("S", T.cbs[:], T.cb[:], "", "cbs", "d_cb", 3500)
+    dma("D", T.bss[:], T.bs[:], "", "bss", "d_bs", 3500)
+    dma("S", T.fss[:], T.fs[:], "", "fss", "d_fs", 3500)
+    dma("D", T.ths[:, 0:1], T.th[:], "", "ths", "d_th", 3500)
+    dma("S", T.xfs[:, 0:4096], T.xf[:, 0:4096], "", "xfs", "d_xa", 9000)
+    dma("D", T.xfs[:, 4096:8192], T.xf[:, 4096:8192], "", "xfsb", "d_xb", 9000)
 
-    def gop(fn, R, W):
-        op("G", fn, R, W)
     ms(T.ONES[:], 1.0, "ONES")
-    ms(T.NB[:, 0:1], -8.5, "NB")
-    gop(lambda e: e.affine_select(T.SWT[:], T.ONES[:], [[-16, 8], [0, 16]], A.is_ge, 0.0, 0, 1), "ONES", "SWT")
-    gop(lambda e: e.affine_select(T.G16[:], T.SWT[:], [[16, 8], [0, 16]], A.is_ge, 0.0, 15, -1), "SWT", "G16")
-    gop(lambda e: e.affine_select(T.IDENT[:], T.ONES[:], [[-1, 128]], A.is_equal, 0.0, 0, 1), "ONES", "IDENT")
-    gop(lambda e: e.iota(T.PI[:, 0:1], [[1, 1]], 0, 1), "", "PI")
-    gop(lambda e: e.iota(T.LI[:], [[16, 16]], 0, 0), "", "LI")
-    gop(lambda e: e.iota(T.IOTC[:], [[1, 512]], -256, 0, allow_small_or_imprecise_dtypes=True), "", "IOTC")
-    for x in ("XB0", "XB1"):
-        for c in (0, 528):
-            gop(lambda e: e.iota(T[x][:, c:c + 16], [[0, 16]], 0, 0, allow_small_or_imprecise_dtypes=True), "", "+" + x)
-    for k in range(16):
-        gop(lambda e: e.affine_select(T.SELP[:, 128 * k:128 * k + 128], T.G16[:], [[0, 8], [1, 16]], A.is_equal, 0.0, -k, 0), "G16", "+SELP")
+    ms(T.TR[0:32, 0:128], -1024.0, "TR")
+    ms(T.SELW[:], 0.0, "SELW")
+    ms(T.LL[:], 0.0, "LL")
+    ms(T.EUW[:], 0.0, "EUW", 100)
+    ms(T.ESW[:], 0.0, "ESW", 100)
+    ms(T.ESW[:, 112:128], 1.0, "ESW")
+    ms(T.HALF[:], 0.5, "HALF")
+    ms(T.ACC[:, 4:5], 1.0 / 128, "ACC4")
+    ms(T.DF2[:, 0:16], 256.0, "DF2c")
+    ms(T.SB9[:], 1.0, "SB9")
+    ms(T.RTB[:], -1.0, "RTB")
+    for n in range(NXG):
+        ms(T.XG[:, 1024 * n:1024 * n + 1024:2], 0.0, "XG%d" % n, 256 * CYC)
+    iota(T.PI[:, 0:1], [[1, 1]], 0, 1, "PI")
+    sel(T.SWT[:], T.ONES[:], [[-16, 8], [0, 16]], A.is_ge, 0.0, 0, 1, "ONES", "SWT")
+    sel(T.G16[:], T.SWT[:], [[16, 8], [0, 16]], A.is_ge, 0.0, 15, -1, "SWT", "G16")
+    fiota(T.K16[:], [[0, 8], [1, 16]], 0, 0, "K16", 128)
+    fiota(T.IOTC[:], [[1, 512]], -256, 0, "IOTC", 512)
+    r32 = T.TR[0:32, 0:128]
+    sel(r32, r32, [[0, 16], [-1, 8]], A.not_equal, 0.0, -16, 1, "TR", "TR")
+    sel(r32, r32, [[0, 128]], A.is_ge, 0.0, -16, 1, "TR", "TR")
+    sel(r32, r32, [[-1, 8], [0, 16]], A.not_equal, 1.0, 0, 1, "TR", "TR")
+    sel(r32, r32, [[-1, 8], [0, 16]], A.not_equal, 1.0, -8, 1, "TR", "TR")
+    sel(T.IDENT[:], T.ONES[:], [[-1, 128]], A.is_equal, 0.0, 0, 1, "ONES", "IDENT")
+    sel(T.SELW[:, 0:128], T.G16[:], [[0, 8], [1, 16]], A.is_equal, 0.0, -15, 0, "G16", "SELW")
+    iota(T.LI[:], [[16, 16]], 0, 0, "LI")
+    iota(T.BASE[:], [[512, 16]], 64, 0, "BASE")
     for b in range(9):
-        for c, v in ((b, 2 ** (8 - b)), (16 + b, 2 ** b if b else 0), (32 + b, -2 ** b if b else 1)):
-            gop(lambda e: e.iota(T.PAB[:, c:c + 1], [[0, 1]], v, 0, allow_small_or_imprecise_dtypes=True), "", "+PAB")
-    gop(lambda e: e.iota(T.IDX1[:], [[1, 256]], 1, 0, allow_small_or_imprecise_dtypes=True), "", "IDX1")
-    for t in range(5):
-        for c in (8, 536):
-            gop(lambda e: e.iota(T["WO%d" % t][:, c:c + 8], [[0, 8]], 0, 0, allow_small_or_imprecise_dtypes=True), "", "WO%dp" % t)
-    cp(T.fsU[:], T.fss[:], "fss", "fsU")
-    cp(T.bsU[:], T.bss[:], "bss", "bsU")
+        fiota(T.PABI[:, b:b + 1], [[0, 1]], 2 ** (8 - b), 0, "+PABI", 1)
+        fiota(T.P2[:, b:b + 1], [[0, 1]], 2 ** b if b else 0, 0, "+P2", 1)
+    fiota(T.IDX[:], [[1, 256]], 0, 0, "IDX", 256)
+
+    tt(T.DF[:], T.pns[:], T.pfs[:], A.subtract, "pfs pns", "DF", 512 * CYC)
+    act(T.SG[:], T.DF[:], "DF", "SG", 256 * CYC, f=AF.Sign)
+    tt(T.HI[:], T.pns[:], T.pfs[:], A.max, "pfs pns", "HI", 512 * CYC)
+    tt(T.LO[:], T.pns[:], T.pfs[:], A.min, "pfs pns", "LO", 512 * CYC)
     cp(T.nbU[:], T.nbs[:], "nbs", "nbU")
-    cp(T.CBF[:], T.cbs[:], "cbs", "CBF")
-    cp(T.OH[:], T.CBF[:].indirect(T.nbU[:]), "CBF nbU", "OHa OHb")
-    act(T.CS[:], T.CBF[:].indirect(T.bsU[:]), "CBF bsU", "CS")
-    p = 32 * NSET[0]
-    tt(T.XN[:, 0:256 - p], T.pfs[:, p:256], T.pns[:, p:256], A.subtract, "pfs pns", "XN")
+    cp(T.CBF[:], T.cbs[:], "cbs", "CBF", 512 * CYC)
+    cp(T.bsU[:], T.bss[:], "bss", "bsU")
+    cp(T.fsU[:], T.fss[:], "fss", "fsU")
+    for k in range(4):
+        act(wi(0, HCOL[k], HCOL[k] + 64), T.CBF[:].indirect(T.nbU[:, 4 * k:4 * k + 4]), "CBF nbU", "WI0_%d" % k, gat(64))
     for k in range(16):
-        act(T.NNEG[:, k::16], T.pns[:, p:256], "pns", "+NNEG", scale=-1.0)
-        act(T.FMN[:, k::16], T.XN[:, 0:256 - p], "XN", "+FMN")
-    act(T.IDF[:], T.IDENT[:], "IDENT", "IDF")
-    act(T.NIDF[:], T.IDENT[:], "IDENT", "NIDF", scale=-1.0)
-    for k in range(16):
-        cp(T.F16[:, k::16], T.pfs[:], "pfs", "+F16")
-    for k in range(16):
-        cp(T.N16[:, k::16], T.pns[:], "pns", "+N16")
-    cp(T.OA[:], T.CS[:].indirect(T.fsU[:]), "CS fsU", "OA")
-    ts(T.GN8[:], T.G16[:, ::16], -1.0, None, A.mult, None, "G16", "GN8")
+        if k < 8:
+            act(T.D1[:, 2 * k::32], T.HI[:], "HI", "+D1", 256 * CYC)
+        else:
+            cp(T.D1[:, 2 * k::32], T.HI[:], "HI", "+D1", 128 * CYC)
+        cp(T.D1[:, 2 * k + 1::32], T.LO[:], "LO", "+D1", 128 * CYC)
+    act(T.CS[:], T.CBF[:].indirect(T.bsU[:]), "CBF bsU", "CS", gat(512))
+    act(T.AFL[:], T.CS[:].indirect(T.fsU[:]), "CS fsU", "AFL", gat(256))
+    for n in range(8):
+        ts(T.WH[:, :, n, :], T.SG[:], T.G16[:, 16 * n:16 * n + 1], -1.0, A.mult, A.mult, "SG G16", "+WH", 128 * CYC)
+    for n in range(4):
+        act(T.WA[:, 4 * n:4 * n + 4, :, :], T.WH[:, 4 * n:4 * n + 4, :, :], "WH", "+WA", 512 * CYC, scale=-1.0)
+    ts(T.PM[:, 0:1], T.PI[:, 0:1], 15, None, A.bitwise_and, None, "PI", "PM")
+    cp(T.PMF[:, 0:1], T.PM[:, 0:1], "PM", "PMF")
+    ts(T.KK[:], T.K16[:], T.PMF[:, 0:1], None, A.is_equal, None, "K16 PMF", "KK")
+    cp(T.LL[:, 40:48], T.G16[:, ::16], "G16", "+LL")
     for n, bits in enumerate((4032, 63)):
-        op("V", lambda e: e.tensor_scalar(T.TI[:, n:n + 1], T.ths[:, 0:1], 1, bits, A.arith_shift_right, A.bitwise_and), "ths", "TI%d" % n)
-    for n in range(2):
-        cp(T.thh[:, n:n + 1], T.TI[:, n:n + 1], "TI%d" % n, "thh%d" % n)
-    for n, c in enumerate(("THH", "THL")):
-        ts(T[c][:], T.ONES[:], T.thh[:, n:n + 1], -1.0, A.mult, A.mult, "ONES thh%d" % n, c)
+        ts(T.TH[:, n:n + 1], T.ths[:, 0:1], 1, bits, A.arith_shift_right, A.bitwise_and, "ths", "TH%d" % n)
+        ts(T.THN[:, n:n + 1], T.TH[:, n:n + 1], 0.5 * n, -1.0, A.add, A.mult, "TH%d" % n, "THN%d" % n)
+        ts(T.LL[:, 8 * n:8 * n + 8], T.G16[:, ::16], T.THN[:, n:n + 1], None, A.mult, None, "G16 THN%d" % n, "+LL")
+    cp(T.TR[0:32, 128:256], r32, "TR", "TRb")
+    cp(T.TR[0:32, 256:512], T.TR[0:32, 0:256], "TR TRb", "TRc", 128 * CYC)
+    mms([(T.PL[0:24, 0:128], T.LL[:, 0:24], T.KK[:], True, False), (T.PL[0:24, 0:128], T.LL[:, 24:48], T.G16[:], False, True)],
+        "LL KK G16", "PL", 256)
+    cp(T.TI[0:24, :], T.PL[0:24, 0:128], "PL", "TI", 128 * CYC)
+    act(T.IDF[:], T.IDENT[:], "IDENT", "IDF", 128 * CYC)
+    act(T.NIDF[:], T.IDENT[:], "IDENT", "NIDF", 128 * CYC, scale=-1.0)
+    ts(T.SELW[:], T.SELW[:], 0.0625, None, A.mult, None, "SELW", "SELW")
+    ts(T.EUW[:, 112:128], T.KK[:, 0:16], 32.0, 1.0, A.mult, A.add, "KK", "+EUW")
+    ts(T.L256[:], T.LI[:], T.PMF[:, 0:1], 256.0, A.add, A.add, "LI PMF", "L256")
+    ts(T.PMF[:, 1:2], T.PM[:, 0:1], 32.0, None, A.mult, None, "PM", "PMF1")
+    ts(T.NSELW[:], T.SELW[:], -1.0, None, A.mult, None, "SELW", "NSELW")
+    for t in range(4):
+        cp(mi(t, 0, 16), T.L256[:], "L256", "MIc%d" % t)
+    cp(mi(0, 32, 48), T.fss[:], "fss", "+MI0")
+    cp(fa(0, 0, 16), T.fss[:], "fss", "FA0")
+    cp(T.BROW4[:].indirect(T.bsU[:]), T.IOTC[:], "IOTC bsU", "BROW4", sca(512))
+    conv(T.PN[:, 0:16], T.pfs, 0, 16, "pfs", "PN")
+    ts(T.EI1[:], T.PN[:, 0:16], 16.0, None, A.mult, None, "PN", "EI1")
+    ts(T.EI2[:], T.EI1[:], 31, None, A.bitwise_and, None, "EI1", "EI2")
+    tt(T.ELS[:], T.EI2[:], T.BASE[:], A.add, "EI2 BASE", "ELS")
+    act(T.GROW[:], T.BROW4[:].indirect(T.nbU[:]), "BROW4 nbU", "GROW", gat(256))
+    conv(T.PN[:, 16:32], T.GROW, 0, 16, "GROW", "PN")
+    ts(mi(0, 16, 32), T.PN[:, 16:32], 256.0, None, A.add, None, "PN", "+MI0")
+    cp(T.PIF[:, 0:1], T.PI[:, 0:1], "PI", "PIF")
+    ts(T.PAB[:, 0:9], T.PABI[:, 0:9], 1.0 / 1024, None, A.mult, None, "PABI", "PAB")
+    ts(T.BI1[:, 0:5], T.PABI[:, 0:5], T.PIF[:, 0:1], None, A.mult, None, "PABI PIF", "BI1")
+    ts(T.BI2[:, 0:5], T.BI1[:, 0:5], 256, None, A.bitwise_and, None, "BI1", "BI2")
+    ts(T.SB9[:, 0:4], T.BI2[:, 0:4], -1.0 / 128, 1.0, A.mult, A.add, "BI2", "+SB9")
+    ts(T.RTB[:, 4:9], T.BI2[:, 0:5], 1.0 / 128, -1.0, A.mult, A.add, "BI2", "+RTB")
+    tt(T.LTB[:, 0:9], T.SB9[:, 0:9], T.P2[:, 0:9], A.mult, "SB9 P2", "LTB")
+    tt(T.LX1[:, 0:1], T.PMF[:, 0:1], T.SB9[:, 0:1], A.add, "PMF SB9", "LX1")
+    mms([(T.PD1[0:9, 0:128], T.LTB[:, 0:9], T.IDENT[:], True, True),
+         (T.PD1[0:9, 128:160], T.RTB[0:32, 0:9], T.IDENT[0:32, 0:32], True, True)], "LTB RTB IDENT", "PD1", 160)
+    act(T.LB[0:9, :], T.PD1[0:9, 0:128], "PD1", "LB", 128 * CYC)
+    act(T.RX[0:9, :], T.PD1[0:9, 128:160], "PD1", "RX")
+    act(T.BROW[:], T.IOTC[:].indirect(T.bsU[:]), "IOTC bsU", "BROW", gat(512))
+    act(T.XB0[:, 0:256], T.BROW[:].indirect(T.fsU[:]), "BROW fsU", "+XB0", gat(256))
+    act(T.XB0[:, 256:512], T.IOTC[:].indirect(T.nbU[:]), "IOTC nbU", "+XB0", gat(256))
 
-    def setup_lists():
-        op("V", lambda e: e.tensor_scalar(T.PM[:, 0:1], T.PI[:, 0:1], 15, None, A.bitwise_and), "PI", "PM")
-        cp(T.PMF[:, 0:1], T.PM[:, 0:1], "PM", "PMF")
-        ts(T.LIF[:], T.LI[:], T.PMF[:, 0:1], None, A.add, None, "LI PMF", "LIF")
-        ts(T.BASE[:], T.LI[:], 32.0, None, A.mult, None, "LI", "BASE")
-        ts(T.PMF[:, 1:2], T.PM[:, 0:1], 32.0, None, A.mult, None, "PM", "PMF1")
-        ts(T.LI1[:], T.LIF[:], 1.0, None, A.add, None, "LIF", "LI1")
-        ts(T.AB0[:], T.LIF[:], 144.0, None, A.add, None, "LIF", "AB0")
-        cp(T.BROW4[:].indirect(T.bsU[:]), T.IOTC[:], "IOTC bsU", "BROW4")
-        cp(T.MI0[:, 0:16], T.fss[:], "fss", "MI0")
+    ring = [0]
 
-    def setup_sums():
-        cp(T.OI1[:], T.PL[:, 0:16], "PL", "OI1")
-        op("V", lambda e: e.tensor_scalar(T.OI2[:], T.OI1[:], 31, None, A.bitwise_and), "OI1", "OI2")
-        tt(T.ELS[:], T.OI2[:], T.BASE[:], A.add, "OI2 BASE", "ELS")
-
-    def setup_sites():
-        ts(T.MI0[:, 16:32], T.PL[:, 16:32], 0.0625, 256.0, A.mult, A.add, "PL", "MI0")
-
-    def setup_xor():
+    def chunk(t, j):
+        c, n, m = j % 8, ring[0] % NXG, ring[0] % NCL
+        ring[0] += 1
+        off, key = (T.UH, "UH%d" % (c // 2)) if j < 8 else (T.UA, "UA%d" % (c // 4))
+        o, a = T.XG[:, 1024 * n + 1:1024 * n + 1024:2], T.xfs[:].indirect(off[:, 32 * c:32 * c + 32])
+        (cp if j in VG[t] else act)(o, a, "xfs xfsb " + key, "XG%d" % n, gat(512))
+        vec(lambda e: e.tensor_tensor_scan(T.CL[:, 1024 * m:1024 * m + 1024], T.XG[:, 1024 * n:1024 * n + 1024],
+                                           T.D1[:, 1024 * c:1024 * c + 1024], 0.0, A.min, A.max), "XG%d D1" % n, "CL%d" % m, 512 * CYC)
+        P, w = "PB%d" % (c // 2), ("WH", "WA")[j // 8]
+        if j < 8 and c % 2 == 0:
+            mms([(T[P][:], T.TI[0:24, :], T.TR[0:24, :], True, False)], "TI TR TRb TRc", P, 512)
+        l = []
         for b in range(4):
-            op("V", lambda e: e.tensor_scalar(T.BITS[:, b:b + 1], T.PM[:, 0:1], b, 1, A.arith_shift_right, A.bitwise_and), "PM", "+BITS")
-        for b in range(5):
-            op("V", lambda e: e.tensor_scalar(T.BITS[:, 4 + b:5 + b], T.PI[:, 0:1], b, 1, A.arith_shift_right, A.bitwise_and), "PI", "+BITS")
-        ms(T.LTB[:], 1.0, "LTB")
-        ms(T.RTB[:], 1.0, "RTB")
-        ts(T.LTB[:, 0:4], T.BITS[:, 0:4], -2.0, 1.0, A.mult, A.add, "BITS", "LTB")
-        ts(T.RTB[:, 4:9], T.BITS[:, 4:9], -2.0, 1.0, A.mult, A.add, "BITS", "RTB")
-        ms(T.C128[:, 0:1], 1.0 / 32768, "C128a")
-        ms(T.C128[:, 1:2], 1.0 / 256, "C128b")
+            col, s = 2 * c + b // 2, slice(8 * (b % 2), 8 * (b % 2) + 8)
+            a = 1024 * m + 256 * b + 1
+            l.append((T[P][:, col % 4, :, s], T.CL[:, a:a + 255:2], T[w][:, col, :, s], False, j >= 8 and c % 2 == 1 and b == 3))
+        mms(l, "CL%d %s" % (m, w), P, 256)
 
-    def setup_signs():
-        mm(T.PM2[0:9, 0:128], T.LTB[:, 0:9], T.IDENT[:], True, True, "LTB IDENT", "PM2")
-        mm(T.PM2[0:9, 128:160], T.RTB[0:32, 0:9], T.IDENT[0:32, 0:32], True, True, "RTB IDENT", "PM2")
-        mm(T.PM2[0:9, 160:161], T.PAB[:, 16:25], T.C128[:, 0:1], True, True, "PAB C128a", "PM2")
-        mm(T.PM2[0:9, 161:162], T.PAB[:, 32:41], T.C128[:, 1:2], True, True, "PAB C128b", "PM2")
+    def signs(k):
+        P, z = "PB%d" % k, "Z%d" % k
+        act(T.Z[:, 4 * k:4 * k + 4, :, :], T[P][:], P, z + " ACC%d" % k, 530 * CYC, f=AF.Sign, accum_out=T.ACC[:, k:k + 1])
+        mms([(T.PL[:, c:c + 17:16], T.Z[:, c, :, :], T.HALF[:], True, True) for c in range(4 * k, 4 * k + 4)], z + " HALF", "PL", 256)
 
-    def setup_signs2():
-        cp(T.LB[0:9, :], T.PM2[0:9, 0:128], "PM2", "LB")
-        cp(T.RC[0:9, :], T.PM2[0:9, 128:160], "PM2", "RC")
-        cp(T.AB[0:9, 0:2], T.PM2[0:9, 160:162], "PM2", "AB")
+    def total():
+        mms([(T.PN[0:9, 96:97], T.PAB[:, 0:9], T.ACC[:, k:k + 1], k == 4, k == 3) for k in (4, 0, 1, 2, 3)],
+            "PAB ACC0 ACC1 ACC2 ACC3 ACC4", "PN", 200)
 
-    def setup_boxes():
-        act(T.BROW[:], T.IOTC[:].indirect(T.bsU[:]), "IOTC bsU", "BROW")
-        act(T.XB0[:, 144:400], T.BROW[:].indirect(T.fsU[:]), "BROW fsU", "XB0")
-        act(T.XB0[:, 16:144], T.IOTC[:].indirect(T.nbU[:, 0:8]), "IOTC nbU", "XB0")
-        act(T.XB0[:, 400:528], T.IOTC[:].indirect(T.nbU[:, 8:16]), "IOTC nbU", "XB0")
+    def turned(t, k):
+        P, z, s = "PB%d" % k, "Z%d" % k, slice(64 * k, 64 * k + 64)
+        for n, e in enumerate(("EUW", "ESW")):
+            mms([(T[P][:, n, 0:4, :], T[e][:, 112 - 16 * x:240 - 16 * x], T.Z[:, 4 * k:4 * k + 4, x, :], x == 0, x == 7)
+                 for x in range(8)], z + " " + e, P, 512)
+        act(T.AB[:, s], T[P][:, 0, 0:4, :], P, "AB%d" % k, f=AF.Abs if t < 4 else AF.Identity, bias=343.0)
+        act(T.TROW[:, s], T[P][:, 1, 0:4, :], P, "TROW%d" % k, f=AF.Relu, scale=-512.0, bias=-56832.0)
 
-    def xg(j):
-        return T.XG[:, 512 * (j % NXG):512 * (j % NXG) + 512]
-
-    def gather(j):
-        off = T.OH if j < 8 else T.OA
-        key = ("OHa" if j < 4 else "OHb") if j < 8 else "OA"
-        c = j % 8
-        act(xg(j), T.xfs[:].indirect(off[:, 32 * c:32 * c + 32]), "xfs xfsb " + key, "XG%d" % (j % NXG))
-
-    def ident(j):
-        c, b = j % 8, "PX%d" % (j % 4)
-        x = "XG%d" % (j % NXG)
-        if c in NS[j // 8]:
-            n = NSET.index(c)
-            mm(T[b][:], T.IDENT[:], xg(j), True, False, "IDENT " + x, b)
-            mm(T[b][:], T.IDENT[:], T.NNEG[:, 512 * n:512 * n + 512], False, True, "IDENT NNEG", b)
-        else:
-            mm(T[b][:], T.IDENT[:], xg(j), True, True, "IDENT " + x, b)
-
-    def term_f(j):
-        c, b, n = j % 8, "PX%d" % (j % 4), (j // 4) % NT
-        o = T.TF[:, 512 * (j % 8):512 * (j % 8) + 512]
-        if c in NS[j // 8]:
-            tab, key, a = T.FMN, "FMN", NSET.index(c)
-        else:
-            tab, key, a = T.F16, "F16", c
-        tt(o, T[b][:], tab[:, 512 * a:512 * a + 512], A.max, b + " " + key, "TF%d_%d" % (n, j % 4))
-
-    def term_n(j):
-        c, b, n = j % 8, "PX%d" % (j % 4), (j // 4) % NT
-        o = T.TN[:, 512 * (j % 8):512 * (j % 8) + 512]
-        if c in NS[j // 8]:
-            act(o, T[b][:], b, "TN%d_%d" % (n, j % 4), f=AF.Relu)
-        else:
-            tt(o, T[b][:], T.N16[:, 512 * c:512 * c + 512], A.max, b + " N16", "TN%d_%d" % (n, j % 4))
-
-    def lanes(blk, which):
-        a, h = blk >= 2, blk % 2
-        nm = "%s%d" % (("TF", "TN")[which], blk % NT)
-        P = "PSC%d" % h
-        if not a and which == 0:
-            mm(T[P][:, 0:128], T.THH[:], T.IDENT[:], True, False, "THH IDENT", P)
-            mm(T[P][:, 0:128], T.THL[:], T.IDENT[:], False, False, "THL IDENT", P)
-        tab, key = (T.G16[:, ::16], "G16") if a == (which == 0) else (T.GN8[:], "GN8")
-        for k in range(16):
-            o = 2048 * (blk % NT)
-            mm(T[P][:, k:128:16], T[nm[0:2]][:, o + k:o + 2048:16], tab, False, a and which == 1 and k == 15,
-               "%s_0 %s_1 %s_2 %s_3 %s" % (nm, nm, nm, nm, key), P)
-
-    def half_cmp(h):
-        ts(T.SWT[:], T["PSC%d" % h][:, 0:128], 0.0, None, A.is_gt, None, "PSC%d" % h, "SWT")
-        mm(T.PM2[:, 256:384], T.SWT[:], T.IDENT[:], True, True, "SWT IDENT", "PM2")
-
-    def half_sum(h):
-        cp(T.SW[:, 128 * h:128 * h + 128], T.PM2[:, 256:384], "PM2", "SW%d" % h)
-        conv(T.PL[:, 8 * h:8 * h + 8], T.SW, 128 * h, 8, "SW%d" % h, "PL")
-        if h:
-            mm(T.PSC1[:, 128:384], T.G16[:], T.SW[:], True, True, "G16 SW0 SW1", "PSC1")
-            act(T.FLB[:], T.PSC1[:, 128:384], "PSC1 NB", "FLB", f=AF.Sign, bias=T.NB[:, 0:1])
-
-    def half_rows(t, h):
-        s = slice(128 * h, 128 * h + 128)
-        wo, key = T["WO%d" % t], "WO%d%s" % (t, "ab"[h])
-        p = T.PM2[:, 256:384]
-        tt(p, T.PM2[:, s], T.SW[:, s], A.mult, "PM2 SW%d" % h, "PM2")
-        a = slice(144 + 128 * h, 272 + 128 * h)
-        hh = slice(16 + 384 * h, 144 + 384 * h)
-        tt(wo[:, a], p, T.CAf[:, s], A.add, "PM2 CAf", "+" + key)
-        tt(wo[:, hh], T.CHf[:, s], p, A.subtract, "PM2 CHf%d" % h, "+" + key)
+    def rows(t, k):
+        P, s, hk = "PD%d" % (k % 2), slice(64 * k, 64 * k + 64), "WI%d_%d" % (t, k)
+        p, h = T[P][:, 0:64], wi(t, HCOL[k], HCOL[k] + 64)
+        mms([(p, T.IDF[:], h, True, False), (p, T.NIDF[:], T.AFL[:, s], False, True)], "IDF NIDF AFL " + hk, P, 512)
+        ts(T.MM[:, s], T.AB[:, s], 32.0 if t < 4 else 0.0, None, A.is_gt, None, "AB%d" % k, "MM%d" % k)
         if t < 4:
-            w = slice(16 + 256 * h, 272 + 256 * h)
-            send(T.cores[(rank + 1) % N], T["WI%d" % (t + 1)][:, w], wo[:, w], key, "a%d_%d" % (h, t + 1))
-
-    def half_off(h):
-        s = slice(8 * h, 8 * h + 8)
-        tt(T.OI1[:, s], T.PL[:, s], T.ELS[:, s], A.add, "PL ELS", "OI1")
-        op("V", lambda e: e.tensor_scalar(T.OI2[:, s], T.OI1[:, s], 8191 - 32, None, A.bitwise_and), "OI1", "OI2")
-        ts(T.OFFU[:, s], T.OI2[:, s], T.PMF[:, 1:2], None, A.add, None, "OI2 PMF1", "OFFU%d" % h)
-
-    def half_put(h):
-        s, r = slice(8 * h, 8 * h + 8), slice(128 * h, 128 * h + 128)
-        cp(T.xfs[:].indirect(T.OFFU[:, s]), T.pfs[:, r], "pfs OFFU%d" % h, "xfs xfsb")
-
-    def half_eta(t, h):
-        s = slice(8 * h, 8 * h + 8)
-        wo, key = T["WO%d" % t], "WO%d%s" % (t, "ab"[h])
-        e = slice(528 * h, 528 * h + 16)
-        ts(T.TD[:, s], T.PL[:, s], 4.5, (-128.0, 128.0)[h], A.is_lt, A.mult, "PL", "TD%d" % h)
-        tt(wo[:, 528 * h:528 * h + 8], T.LIF[:, s], T.TD[:, s], A.subtract, "LIF TD%d" % h, "WO%de%d" % (t, h))
-        if t < 4:
-            send(T.cores[(rank + 1) % N], T["WI%d" % (t + 1)][:, e], wo[:, e], "WO%de%d WO%dp" % (t, h, t), "a%d_%d" % (3 + h, t + 1))
-            act(T["MO%d" % t][:, 32 + 24 * h:40 + 24 * h], wo[:, 528 * h:528 * h + 8], "WO%de%d" % (t, h), "MO%de%d" % (t, h),
-                f=AF.Identity, bias=(16.0, 272.0)[h])
-
-    def win(t, h):
-        return T["WI%d" % t][:, 16 + 256 * h:272 + 256 * h]
-
-    def take_h(t, h):
-        s = slice(8 * h, 8 * h + 8)
-        cp(T.ETAU[:, s], T["WI%d" % t][:, 528 * h:528 * h + 8], "WI%de%d" % (t, h), "ETAU%d" % h)
-        cp(T.OH[:, 128 * h:128 * h + 128], win(t, h).indirect(T.ETAU[:, s]), "WI%d%s ETAU%d" % (t, "ab"[h], h), "OH" + "ab"[h])
-
-    def all_in(t):
-        return "WI%da WI%db WI%de0 WI%de1 " % (t, t, t, t)
-
-    def take_a(t):
-        cp(T.ALU[:], T["MI%d" % t][:, 40:56], "MI%d" % t, "ALU")
-        cp(T.OA[:], T["WI%d" % t][:].indirect(T.ALU[:]), all_in(t) + "ALU", "OA")
-
-    def floats(t, part):
-        if t == 0:
-            if part < 2:
-                h = part
-                act(T.CHf[:, 128 * h:128 * h + 128], T.CBF[:].indirect(T.nbU[:, 8 * h:8 * h + 8]), "CBF nbU", "CHf%d" % h)
-            else:
-                act(T.CAf[:], T.CS[:].indirect(T.fsU[:]), "CS fsU", "CAf")
-        elif part < 2:
-            h = part
-            act(T.CHf[:, 128 * h:128 * h + 128], win(t, h).indirect(T.ETAU[:, 8 * h:8 * h + 8]), "WI%d%s ETAU%d" % (t, "ab"[h], h), "CHf%d" % h)
+            tt(p, p, T.MM[:, s], A.mult, P + " MM%d" % k, P)
+            tt(wo(t, HCOL[k], HCOL[k] + 64), h, p, A.subtract, P + " " + hk, "WO%dh%d" % (t, k))
+            tt(wo(t, ACOL + 64 * k, ACOL + 64 + 64 * k), p, T.AFL[:, s], A.add, P + " AFL", "WO%da%d" % (t, k))
+            a, b, keys = SENDS[k]
+            send(1, wi(t + 1, a, b), wo(t, a, b), " ".join("WO%d%s" % (t, x) for x in keys.split()), "WI%d_%d" % (t + 1, k),
+                 "a%d_%d" % (k, t + 1), b - a)
         else:
-            act(T.CAf[:], T["WI%d" % t][:].indirect(T.ALU[:]), all_in(t) + "ALU", "CAf")
+            tt(T.PS[:, s], p, T.MM[:, s], A.mult, P + " MM%d" % k, "PS%d" % k)
+            tt(T.YC[:].indirect(T.YL[:, 4 * k:4 * k + 4]), T.AFL[:, s], T.PS[:, s], A.add, "AFL YL PS%d" % k, "YC", sca(64))
+            tt(T.YC[:].indirect(T.YL[:, 16 + 4 * k:20 + 4 * k]), h, T.PS[:, s], A.subtract, "YL PS%d %s" % (k, hk), "YC", sca(64))
 
-    def diff(h):
-        s = slice(128 * h, 128 * h + 128)
-        mm(T.PM2[:, s], T.IDF[:], T.CHf[:, s], True, False, "IDF CHf%d" % h, "PM2")
-        mm(T.PM2[:, s], T.NIDF[:], T.CAf[:, s], False, True, "NIDF CAf", "PM2")
+    def frames(a, b):
+        tt(T.OI1[:, a:b], T.PL[:, a:b], T.ELS[:, a:b], A.add, "PL ELS", "OI1%d" % a)
+        ts(T.OI2[:, a:b], T.OI1[:, a:b], 8191 - 32, None, A.bitwise_and, None, "OI1%d" % a, "OI2%d" % a)
+        ts(T.OFFU[:, a:b], T.OI2[:, a:b], T.PMF[:, 1:2], None, A.add, None, "PMF1 OI2%d" % a, "OFFU%d" % a)
+        cp(T.xfs[:].indirect(T.OFFU[:, a:b]), T.pfs[:, 16 * a:16 * b], "pfs OFFU%d" % a, "xfs xfsb", sca(16 * (b - a)))
 
-    def sites_in(t):
-        m = "MI%d" % t
-        cp(T.FU[:], T[m][:, 0:16], m, "FU")
-        tt(T.DFG[:], T[m][:, 16:32], T[m][:, 0:16], A.subtract, m, "DFG")
+    def flags(t, a, b):
+        keys = " ".join("TROW%d" % k for k in range(a // 4, b // 4))
+        tt(T.U[:, 0:512].indirect(fa(t, a, b)), T.TROW[:, 16 * a:16 * b], T.IDX[:, 16 * a:16 * b], A.add,
+           keys + " IDX FA%d" % (t % 2), "U0", sca(16 * (b - a)))
 
-    def chain(t):
-        op("V", lambda e: e.tensor_reduce(T.RTOT[:, 0:1], T.PL[:, 0:16], AxisListType.X, A.add), "PL", "RTOT")
-        mm(T.PM2[0:9, 384:385], T.PAB[:, 0:9], T.RTOT[:, 0:1], True, True, "PAB RTOT", "PM2")
-        ts(T.TRN[:], T.PL[:, 0:16], 4.5, None, A.is_lt, None, "PL", "TRN")
-        cp(T.UI[0:9, 0:1], T.PM2[0:9, 384:385], "PM2", "UI")
-        op("V", lambda e: e.tensor_scalar(T.UB[0:9, 0:1], T.UI[0:9, 0:1], 256, None, A.bitwise_and), "UI", "UB")
+    def take(t):
+        for k in range(4):
+            cp(T.UH[:, 64 * k:64 * k + 64], wi(t, HCOL[k], HCOL[k] + 64), "WI%d_%d" % (t, k), "UH%d" % k)
+        if t:
+            cp(fa(t, 0, 32), mi(t, 32, 64), "MI%d" % t, "FA%d" % (t % 2))
+            act(T.AFL[:], wi(t, ACOL, ACOL + 256).indirect(fa(t, 16, 32)), "WI%d_1 WI%d_3 FA%d" % (t, t, t % 2), "AFL", gat(256))
+        for h in range(2):
+            cp(T.UA[:, 128 * h:128 * h + 128], T.AFL[:, 128 * h:128 * h + 128], "AFL", "UA%d" % h, 128 * CYC)
+        tt(T.DF2[:, 16:32], mi(t, 16, 32), mi(t, 32, 48), A.subtract, "MI%d" % t, "DF2")
+        fiota(T.U[:, 0:512], [[0, 512]], 512, 0, "U0", 512)
+
+    def xor():
+        y = T.PN[0:9, 96:97]
+        cp(T.RI[0:9, 0:1], y, "PN", "RI")
+        tt(T.DD[0:9, 0:1], y, T.RI[0:9, 0:1], A.subtract, "PN RI", "DD")
+        ts(T.RS[0:9, :], T.RX[0:9, :], T.DD[0:9, 0:1], 0.0, A.mult, A.is_gt, "RX DD", "RS")
+        mms([(T.PN[:, 128:160], T.LB[0:9, :], T.RS[0:9, :], True, True)], "LB RS", "PN", 64)
+        ts(T.XLU[:], T.PN[:, 128:160], T.LX1[:, 0:1], None, A.add, None, "PN LX1", "XLU")
+
+    def turns(t):
+        ts(T.TRN[:], T.PL[:, 0:32], 4.5 - 64, None, A.is_lt, None, "PL", "TRN")
+        tt(T.XX[:], T.TRN[:], T.DF2[:], A.mult, "TRN DF2 DF2c", "XX")
         if t < 4:
-            ts(T.FL16[:], T.PL[:, 0:16], 8.5, 0.0625, A.is_gt, A.mult, "PL", "FL16")
-        ts(T.CF[0:9, 0:1], T.UB[0:9, 0:1], T.AB[0:9, 0:1], T.AB[0:9, 1:2], A.mult, A.add, "UB AB", "CF")
-        tt(T.XX[:], T.TRN[:], T.DFG[:], A.mult, "TRN DFG", "XX")
-        ts(T.RS[0:9, :], T.RC[0:9, :], T.CF[0:9, 0:1], None, A.mult, None, "RC CF", "RS")
-        mm(T.PM2[:, 400:432], T.LB[0:9, :], T.RS[0:9, :], True, True, "LB RS", "PM2")
-        m, mo = "MI%d" % t, "MO%d" % t
-        tt(T[mo][:, 0:16], T[m][:, 0:16], T.XX[:], A.add, m + " XX", mo)
-        ts(T.XLU[:], T.PM2[:, 400:432], 255.5, None, A.add, None, "PM2", "XLU")
-        tt(T.U[:, 0:512].indirect(T.FU[:]), T.FLB[:], T.IDX1[:], A.mult, "FLB IDX1 FU", "U0")
-        if t < 4:
-            tt(T[mo][:, 16:32], T[m][:, 16:32], T.XX[:], A.subtract, m + " XX", mo)
-            tt(T.ABS[:], T.AB0[:], T.TD[:], A.add, "AB0 TD0 TD1", "ABS")
-
-    def partner(t):
-        act(T.U[:, 512:1024], T.U[:, 0:512].indirect(T.XLU[:]), "U0 XLU", "U1")
-        act(T.MROW[:], T.U[:, 512:1024].indirect(T.FU[:]), "U1 FU", "MROW", f=AF.Relu)
-        conv(T.PL[:, 32:48], T.MROW, 0, 16, "MROW", "PL")
+            tt(mo(t, 48, 64), mi(t, 32, 48), T.XX[:, 16:32], A.add, "MI%d XX" % t, "MO%df" % t)
+            tt(mo(t, 16, 48), mi(t, 0, 32), T.XX[:], A.subtract, "MI%d MIc%d XX" % (t, t), "MO%dg" % t)
 
     def alpha(t):
-        mo = "MO%d" % t
-        tt(T.Z1[:], T.PL[:, 32:48], T.FL16[:], A.mult, "PL FL16", "Z1")
-        ts(T.Z2[:], T.Z1[:], 256.0, None, A.mult, None, "Z1", "Z2")
-        tt(T.Z1[:], T.Z1[:], T.ABS[:], A.add, "Z1 ABS", "Z1")
-        tt(T.Z3[:], T.Z2[:], T.LI1[:], A.min, "Z2 LI1", "Z3")
-        tt(T[mo][:, 40:56], T.Z1[:], T.Z3[:], A.subtract, "Z1 Z3", mo)
-        mo += " %se0 %se1" % (mo, mo)
-        send(T.cores[(rank + 1) % N], T["MI%d" % (t + 1)][:], T["MO%d" % t][:], mo, "a2_%d" % (t + 1))
-        if t in (1, 2):
-            send(T.cores[(rank - t) % N], T["HI%d" % t][:], T["MO%d" % t][:, 32:64], mo, "ah%d" % t)
+        conv(T.PN[:, 0:16], T.TROW, 0, 16, "TROW0 TROW1 TROW2 TROW3", "PN", sp=False)
+        act(T.U[:, 512:1024], T.U[:, 0:512].indirect(T.XLU[:]), "U0 XLU", "U1", gat(512))
+        act(T.MROW[:], T.U[:, 512:1024].indirect(fa(t, 0, 16)), "U1 FA%d" % (t % 2), "MROW", gat(256))
+        conv(T.PN[:, 0:16], T.MROW, 0, 16, "MROW", "PN", st=False)
+        tt(T.AL[:], T.PN[:, 0:16], T.L256[:], A.min, "PN L256", "AL")
+        ts(mo(t, 64, 80), T.AL[:], 255, None, A.bitwise_and, None, "AL", "MO%da" % t)
+        send(1, mi(t + 1, 16, 64), mo(t, 32, 80), "MO%da MO%df MO%dg" % (t, t, t), "MI%d" % (t + 1), "a4_%d" % (t + 1), 48)
+        tt(mo(t, 0, 16), mo(t, 64, 80), T.XX[:, 0:16], A.add, "MO%da XX" % t, "MO%db" % t)
+        if t:
+            send(-t, T.HM[:, 32 * t:32 * t + 32], mo(t, 0, 32), "MO%db MO%dg" % (t, t), "HM%d" % t, "ah%d" % t, 32)
 
-    def boxes(n, lists, key):
+    def boxes(n):
         a, b = "XB%d" % (n % 2), "XB%d" % (1 - n % 2)
-        cp(T.XLS[:], lists, key, "XLS")
-        act(T[b][:, 16:528], T[a][:].indirect(T.XLS[:]), a + " XLS", b)
+        if n:
+            cp(T.XLS[:], T.HM[:, 32 * n:32 * n + 32], "HM%d" % n, "XLS")
+        else:
+            cp(T.XLS[:], mo(0, 0, 32), "MO0b MO0g", "XLS")
+        act(T[b][:], T[a][:].indirect(T.XLS[:]), a + " XLS", b, gat(512))
 
     def box_lists():
-        ts(T.YL[:], T.PL[:, 64:96], 0.0625, 256.0, A.mult, A.add, "PL", "YL")
-        cp(T.GU[:, 0:8], T.MI4[:, 16:24], "MI4", "GU")
-        cp(T.GU[:, 8:24], T.MI4[:, 0:16], "MI4", "+GU")
-        cp(T.GU[:, 24:32], T.MI4[:, 24:32], "MI4", "+GU")
-        cp(T.BROW4[:].indirect(T.GU[:]), T.XB0[:, 16:528], "XB0 GU", "BROW4")
-        conv(T.PL[:, 128:160], T.BROW4, 0, 32, "BROW4", "PL")
+        conv(T.PN[:, 32:64], T.XB0, 0, 32, "XB0", "PN")
+        ts(T.YL[:], T.PN[:, 32:64], 256.0, None, A.add, None, "PN", "YL")
+        ts(T.YL32[:], T.PN[:, 32:64], 256.0, None, A.add, None, "PN", "YL32")
+        cp(T.GU[:], mi(4, 16, 32), "MI4", "GU")
+        tt(T.DA[:], T.YL32[:, 0:16], T.YL32[:, 16:32], A.subtract, "YL32", "DA")
+        cp(T.BROW4[:].indirect(fa(4, 0, 16)), T.XB0[:, 0:256], "XB0 FA0", "BROW4", sca(256))
+        cp(T.BROW4[:].indirect(T.GU[:]), T.XB0[:, 256:512], "XB0 GU", "BROW4", sca(256))
+        conv(T.PN[:, 64:96], T.BROW4, 0, 32, "BROW4", "PN")
+        ts(T.BL[:], T.PN[:, 64:96], 256.0, None, A.add, None, "PN", "BL")
 
-    def put_yc(h):
-        k = "WO4" + "ab"[h]
-        cp(T.YC[:].indirect(T.YL[:, 16 * h:16 * h + 16]), T.WO4[:, 16 + 256 * h:272 + 256 * h], k + " YL", "YC")
-
-    def main(t):
-        st = {"g": 0, "p": 0}
-
-        def ahead(j):
-            lim = 4 if not st.get("oh1") else (8 if not st.get("oa") else 16)
-            while st["g"] < min(lim, j + LG if j else 3):
-                gather(st["g"])
-                st["g"] += 1
-            while st["p"] < min(st["g"], j + LP + 1, 16):
-                ident(st["p"])
-                if st["p"] in NS[0]:
-                    term_n(st["p"])
-                st["p"] += 1
-        if t == 0:
-            st["oh1"] = st["oa"] = True
-        for j in range(16):
-            ahead(j)
-            if j == 0 and t:
-                partner(t - 1)
-            if j == 3 and t:
-                alpha(t - 1)
-            if j == 2 and t:
-                take_h(t, 1)
-                st["oh1"] = True
-                ahead(j)
-            if t == 0 and j == 4:
-                conv(T.PL[:, 0:16], T.pfs, 0, 16, "pfs", "PL")
-                act(T.GROW[:], T.BROW4[:].indirect(T.nbU[:]), "BROW4 nbU", "GROW")
-            if t == 0 and j == 6:
-                setup_sums()
-                conv(T.PL[:, 16:32], T.GROW, 0, 16, "GROW", "PL")
-                setup_signs()
-            if t == 0 and j == 9:
-                setup_sites()
-                setup_signs2()
-            if j == 7:
-                gop(lambda e: e.iota(T.U[:, 0:512], [[0, 512]], 0, 0, allow_small_or_imprecise_dtypes=True), "", "U0")
-            if j == 10:
-                floats(t, 0)
-                floats(t, 1)
-            if j == 6 and t:
-                take_a(t)
-                st["oa"] = True
-                ahead(j)
-            if j == JF:
-                floats(t, 2)
-            if j == 9:
-                sites_in(t)
-            if j == JD:
-                diff(0)
-            if t == 1 and j == 10:
-                boxes(0, T.MO0[:, 32:64], "MO0 MO0e0 MO0e1")
-            if t == 3 and j == 4:
-                boxes(1, T.HI1[:], "HI1")
-            if t == 4 and j == 3:
-                boxes(2, T.HI2[:], "HI2")
-            if t == 4 and j == 8:
-                boxes(3, T.MI4[:, 32:64], "MI4")
-            if t == 4 and j == 12:
-                conv(T.PL[:, 64:96], T.XB0, 16, 32, "XB0", "PL")
-            if t == 4 and j == 13:
-                box_lists()
-            if j == JC:
-                half_cmp(0)
-            term_f(j)
-            if j == JS:
-                half_sum(0)
-                half_rows(t, 0)
-                diff(1)
-            if j not in NS[0]:
-                term_n(j)
-            if j < 12:
-                if j % 4 == 3:
-                    lanes(j // 4, 0)
-                    lanes(j // 4, 1)
-        lanes(3, 0)
-        lanes(3, 1)
-        half_eta(t, 0)
-        if t < 4:
-            half_off(0)
-            half_put(0)
-        else:
-            put_yc(0)
-        half_cmp(1)
-        half_sum(1)
-        half_rows(t, 1)
-        if t < 4:
-            half_off(1)
-            half_eta(t, 1)
-            half_put(1)
-        else:
-            half_eta(t, 1)
-            put_yc(1)
-            dma("D", T.yc[:], T.YC[:], "YC", "yc", "o_yc")
-            ts(T.E4U[:, 0:8], T.WO4[:, 0:8], 16.0, None, A.add, None, "WO4e0", "E4U")
-            ts(T.E4U[:, 8:16], T.WO4[:, 528:536], 272.0, None, A.add, None, "WO4e1", "+E4U")
-            act(T.XN[:], T.XB0[:].indirect(T.E4U[:]), "XB0 E4U", "XN")
-        if t < 4:
-            take_h(t + 1, 0)
-        chain(t)
-
-    setup_lists()
-    setup_boxes()
-    setup_xor()
     for t in range(5):
-        main(t)
+        take(t)
+        if t:
+            boxes(t - 1)
+        if t == 4:
+            box_lists()
+        for j in range(16):
+            chunk(t, j)
+            if j > 8 and j % 2:
+                k = (j - 9) // 2
+                if k == 3 and t < 4:
+                    frames(*OFFS[0])
+                signs(k)
+                if k == 3:
+                    total()
+                    if t < 4:
+                        frames(*OFFS[1])
+                turned(t, k)
+                rows(t, k)
+        for a, b in FLAGS:
+            flags(t, a, b)
+        xor()
+        turns(t)
+        if t < 4:
+            alpha(t)
 
-    dma("D", T.yf[:], T.MO4[:, 0:16], "MO4", "yf", "o_yf")
-    conv(T.PL[:, 320:336], T.XN, 0, 16, "XN", "PL")
-    act(T.U[:, 1024:1536], T.BROW4[:].indirect(T.XLU[:]), "BROW4 XLU", "U2")
-    act(T.U[:, 512:1024], T.U[:, 0:512].indirect(T.XLU[:]), "U0 XLU", "U1")
-    ts(T.Z3[:], T.PL[:, 320:336], 0.0625, 256.0, A.mult, A.add, "PL", "Z3")
-    dma("D", T.yn[:], T.Z3[:], "Z3", "yn", "o_yn")
-    ts(T.BL[:], T.PL[:, 128:160], 0.0625, 256.0, A.mult, A.add, "PL", "BL")
-    conv(T.PL[:, 256:288], T.U, 1024, 32, "U2", "PL")
-    conv(T.PL[:, 192:224], T.U, 0, 32, "U0", "PL")
-    conv(T.PL[:, 224:256], T.U, 512, 32, "U1", "PL")
-    ts(T.B1[:], T.PL[:, 192:224], 0.5, None, A.is_gt, None, "PL", "B1")
-    ts(T.B2[:], T.PL[:, 224:256], 0.5, None, A.is_gt, None, "PL", "B2")
-    ts(T.B3[:], T.PL[:, 256:288], 0.0625, 256.0, A.mult, A.add, "PL", "B3")
-    tt(T.B1[:], T.B1[:], T.B2[:], A.mult, "B1 B2", "B1")
-    tt(T.B3[:], T.B3[:], T.BL[:], A.subtract, "B3 BL", "B3")
-    tt(T.B4[:], T.B3[:], T.B1[:], A.mult, "B3 B1", "B4")
-    tt(T.YB[:], T.BL[:], T.B4[:], A.add, "BL B4", "YB")
-    dma("D", T.yb[:], T.YB[:], "YB", "yb", "o_yb")
-    for q in ("V", "S", "P", "G"):
-        g.wait_ge(T.sem["q" + q], cnt[q])
+    dma("D", T.yc[:], T.YC[:], "YC", "yc", "o_yc", 3000)
+    conv(T.PD0[:, 0:32], T.BROW4, 0, 32, "BROW4", "PD0", sp=False, tab="NSELW")
+    conv(T.PN[:, 0:32], T.U, 0, 32, "U0", "PN", sp=False)
+    act(T.U[:, 512:1024], T.U[:, 0:512].indirect(T.XLU[:]), "U0 XLU", "U1", gat(512))
+    cp(T.U[:, 1024:1536], T.BROW4[:].indirect(T.XLU[:]), "BROW4 XLU", "U2", gat(512))
+    conv(T.PN[:, 0:32], T.U, 512, 32, "U1", "PN", st=False)
+    conv(T.PD0[:, 0:32], T.U, 1024, 32, "U2", "PD0", st=False)
+    ts(T.B1[:], T.PN[:, 0:32], 511.0, None, A.is_lt, None, "PN", "B1")
+    tt(T.B2[:], T.PD0[:, 0:32], T.B1[:], A.mult, "PD0 B1", "B2")
+    tt(T.YB[:], T.BL[:], T.B2[:], A.add, "BL B2", "YB")
+    dma("S", T.yb[:], T.YB[:], "YB", "yb", "o_yb")
+    tt(T.YF[:], mi(4, 32, 48), T.XX[:, 16:32], A.add, "MI4 XX", "YF")
+    dma("D", T.yf[:], T.YF[:], "YF", "yf", "o_yf")
+    tt(T.DA[:], T.DA[:], T.TRN[:, 0:16], A.mult, "DA TRN", "DA")
+    tt(T.YN[:], T.DA[:], T.YL32[:, 16:32], A.add, "DA YL32", "YN")
+    dma("S", T.yn[:], T.YN[:], "YN", "yn", "o_yn")
+    emit()
     for n in ("yc", "yb", "yf", "yn"):
         g.wait_ge(T.sem["o_" + n], 16)
     g.wait_ge(T.sem.loc, nloc[0])

@@ -1,13 +1,19 @@
-from concourse.mybir import AluOpType as A, ActivationFunctionType as AF
+from concourse.mybir import AluOpType as A, AxisListType, ActivationFunctionType as AF
 
-NXG, NCL = 6, 4
-VG = ((1, 5, 9, 12), (1, 6, 9, 12), (1, 6, 9, 12), (1, 6, 9, 12), (1, 6))
+NXG, NCL = 12, 8
+SCAN = 2
+MP = 4
+NQ, CC = 8 // MP, MP // 2
+PLAN = ("S1 V1 S2 V2 S2 S4 S4 V2 S2 S2 V2 S2 S2 S2 V1 S1", "S2 V2 S2 S2 S4 S4 S2 V2 S4 S4 S2 S2")
+EARLY = {}
 FLAGS = ((0, 8), (8, 12), (12, 16))
 OFFS = ((0, 12), (12, 16))
 HCOL, ACOL = (64, 128, 0, 448), 192
 SENDS = ((64, 128, "h0"), (128, 320, "h1 a0 a1"), (0, 64, "h2"), (320, 512, "a2 a3 h3"))
-CYC, GAT, SCA, PEC, HOP, FAR = 0.83, 1.3, 3.2, 0.5, 220, 3000
-PASSES = 4
+CYC, GAT, SCA, PEC, HOP, FAR = 0.83, 1.3, 3.2, 0.5, 180, 2200
+PASSES = 3
+LOOKS = (0.2, 0.3, 0.4, 0.5, 0.6)
+ORDER = []
 FL, BF, I32, U16 = "float32", "bfloat16", "int32", "uint16"
 
 
@@ -18,51 +24,64 @@ def _scratch():
         for n in names.split():
             s[n] = ("sbuf", [128, cols], dt)
     sb("xfs D1", 8192, BF)
-    sb("XG", 1024 * NXG, BF)
-    sb("CL", 1024 * NCL, BF)
-    for n in ("WH", "WA", "Z"):
+    sb("XG", 512 * NXG, BF)
+    sb("CL", 512 * NCL, BF)
+    for n in ("WH", "WA"):
         s[n] = ("sbuf", [128, 16, 8, 16], BF)
+    s["Z"] = ("sbuf", [128, 4 * CC, 8, 16], BF)
     sb("pfs pns LO HI DF SG AB MM TROW MROW IDX GROW", 256, BF)
     sb("cbs", 512, I32)
-    sb("CBF CS YC", 512, FL)
-    sb("AFL PS", 256, FL)
+    sb("CBF CS YC UF", 512, FL)
+    sb("AFL PS XF", 256, FL)
     sb("WI WO", 512 * 5, FL)
     sb("MI", 64 * 5, I32)
     sb("MO", 80 * 4, I32)
     sb("HM", 32 * 4, I32)
     sb("bss", 32, I32)
-    sb("fss nbs OI1 OI2 EI1 EI2 BASE LI ELS AL BI1 BI2", 16, I32)
+    sb("fss nbs OI1 OI2 EI1 BASE LI ELS AL BI1 BI2", 16, I32)
     sb("ths TH PI PM RI", 2, I32)
     sb("IDF NIDF", 128, FL)
     sb("THN PMF PIF DD LX1", 2, FL)
     sb("ACC", 8, FL)
-    sb("ONES IDENT G16 SWT KK K16 TI LB", 128, BF)
+    sb("ONES IDENT G16 KK K16 TI LB", 128, BF)
     sb("SELW NSELW", 144, BF)
-    sb("EUW ESW", 240, BF)
+    sb("EUW ESW", 48 * NQ, BF)
     sb("TR IOTC BROW BROW4 XB0 XB1", 512, BF)
-    sb("LL", 48, BF)
-    sb("HALF", 2, BF)
+    sb("LL", 24, BF)
+    sb("QS", 2 * NQ, BF)
+    sb("TWO OWN", 16, FL)
+    sb("HALF QUART", 128, FL)
+    sb("C16", 16, BF)
+    sb("TM", 128, BF)
     sb("LTB RTB SB9 P2", 16, BF)
     sb("RS RX", 32, BF)
     sb("UH UA", 256, U16)
     sb("bsU XLU XLS YL", 32, U16)
     sb("FA", 64, U16)
     sb("fsU nbU OFFU GU", 16, U16)
-    sb("L256 PABI PAB DA YF YN", 16, FL)
-    sb("TRN DF2 XX YL32 BL B1 B2 YB", 32, FL)
-    sb("U", 1536, BF)
+    sb("LIF DA YF YN", 16, FL)
+    sb("TRN DF2 XX YL32 BL B1 YB", 32, FL)
+    sb("U", 1024, BF)
     for n in ("PB0", "PB1", "PB2", "PB3"):
         s[n] = ("psum", [128, 4, 8, 16], FL)
-    for n in ("PD0", "PD1", "PL", "PN"):
+    sb("FB", 16, BF)
+    sb("X8", 8, BF)
+    sb("FT PABX", 128, BF)
+    sb("BT SBH", 256, BF)
+    sb("RB", 256, I32)
+    sb("PABW", 128, FL)
+    sb("C2", 2, FL)
+    for n in ("PT", "PD", "PN"):
         s[n] = ("psum", [128, 512], FL)
+    s["PL"] = ("psum", [128, 2, 256], FL)
     return s
 
 
 SCRATCH = _scratch()
-BANKS = ("PB0", "PB1", "PB2", "PB3", "PD0", "PD1", "PL", "PN")
+BANKS = ("PB0", "PB1", "PB2", "PB3", "PT", "PD", "PL", "PN")
 LOADS = ["pf", "pn", "fs", "bs", "nb", "th", "cb", "xa", "xb"]
 SEMAPHORES = (["qV", "qS", "qP", "qG", "loc"] + ["d_" + n for n in LOADS] + ["o_yc", "o_yb", "o_yf", "o_yn"]
-              + ["a%d_%d" % (k, t) for k in range(5) for t in range(1, 5)] + ["ah1", "ah2", "ah3"])
+              + ["a%d_%d" % (k, t) for k in range(6) for t in range(1, 5)] + ["ah1", "ah2", "ah3"])
 
 
 def issue_order(calls):
@@ -76,27 +95,31 @@ def issue_order(calls):
     def gap(i, j):
         return 0 if calls[i]["q"] == calls[j]["q"] == "P" else calls[min(i, j)]["late"]
 
-    def walk(before, behind, urgent, start):
+    def walk(before, behind, urgent, start, look):
         left = [len(b) for b in before]
         ready = {i: start(i) for i in range(n) if not left[i]}
         free, end, order = {}, [0.0] * n, []
         while ready:
-            t0, q = min((max(r, free.get(calls[i]["q"], 0.0)), calls[i]["q"]) for i, r in ready.items())
-            i = max((i for i, r in ready.items() if calls[i]["q"] == q and r <= t0 + HOP / 2), key=urgent)
-            end[i] = free[q] = max(t0, ready.pop(i)) + calls[i]["ns"]
+            t1, q = min((max(r, free.get(calls[i]["q"], 0.0)) + look * calls[i]["ns"], calls[i]["q"]) for i, r in ready.items())
+            i = max((i for i, r in ready.items() if calls[i]["q"] == q and r <= t1), key=urgent)
+            end[i] = free[q] = max(free.get(q, 0.0), ready.pop(i)) + calls[i]["ns"]
             order.append(i)
             for j in behind[i]:
                 left[j] -= 1
                 if not left[j]:
                     ready[j] = max(end[p] + gap(p, j) for p in before[j])
         return end, order
-    end, best = list(range(n)), None
-    for _ in range(PASSES):
-        back, _o = walk(after, pre, lambda i: end[i], lambda i: calls[i]["late"])
-        end, order = walk(pre, after, lambda i: (i < len(LOADS), -i if i < len(LOADS) else back[i]), lambda i: 0.0)
-        if best is None or max(end) < best[0]:
-            best = (max(end), order)
-    return best[1]
+    if not ORDER:
+        best = None
+        for look in LOOKS:
+            end = list(range(n))
+            for _ in range(PASSES):
+                back, _o = walk(after, pre, lambda i: end[i], lambda i: calls[i]["late"], look)
+                end, order = walk(pre, after, lambda i: (i < len(LOADS), -i if i < len(LOADS) else back[i] + calls[i].get("early", 0)),
+                                  lambda i: 0.0, look)
+                if best is None or max(end) < best:
+                    best, ORDER[:] = max(end), order
+    return ORDER
 
 
 def rank_program(g, core, T, topo):
@@ -212,6 +235,9 @@ def rank_program(g, core, T, topo):
         mms([(out, T[tab][:, 15 - l:143 - l], row[:, a + l:a + 16 * (n - 1) + l + 1:16], st and l == 0, sp and l == 15)
              for l in range(16)], R + " " + tab, W, 1024)
 
+    def part(q):
+        return slice(16 * MP * q, 16 * MP * (q + 1))
+
     def wi(t, a, b):
         return T.WI[:, 512 * t + a:512 * t + b]
 
@@ -241,33 +267,43 @@ def rank_program(g, core, T, topo):
     ms(T.TR[0:32, 0:128], -1024.0, "TR")
     ms(T.SELW[:], 0.0, "SELW")
     ms(T.LL[:], 0.0, "LL")
-    ms(T.EUW[:], 0.0, "EUW", 100)
-    ms(T.ESW[:], 0.0, "ESW", 100)
-    ms(T.ESW[:, 112:128], 1.0, "ESW")
-    ms(T.HALF[:], 0.5, "HALF")
+    ms(T.EUW[:], 0.0, "EUW")
+    ms(T.ESW[:], 0.0, "ESW")
+    ms(T.QS[:], 0.0, "QS")
+    for q in range(NQ):
+        ms(T.QS[part(q), q::NQ], 0.5, "+QS")
+        ms(T.ESW[part(q), 48 * q + 16:48 * q + 32], 1.0, "+ESW")
+    ms(T.TM[0:32, :], 16.0, "TM")
+    ms(T.HALF[:], 0.5, "HALF", 128 * CYC)
+    ms(T.QUART[:], 0.0, "QUART", 128 * CYC)
+    ms(T.HALF[:, ::16], 0.0, "+HALF")
+    ms(T.QUART[:, ::16], 0.25, "+QUART")
+    ms(T.TWO[:], 2.0, "TWO")
+    ms(T.LTB[:, 0:1], 0.0, "+LTB")
     ms(T.ACC[:, 4:5], 1.0 / 128, "ACC4")
     ms(T.DF2[:, 0:16], 256.0, "DF2c")
     ms(T.SB9[:], 1.0, "SB9")
+    ms(T.C16[:], 16.0, "C16")
+    ms(T.P2[:], 0.0, "P2")
+    ms(T.FT[0:32, :], 0.5, "FT")
     ms(T.RTB[:], -1.0, "RTB")
-    for n in range(NXG):
-        ms(T.XG[:, 1024 * n:1024 * n + 1024:2], 0.0, "XG%d" % n, 256 * CYC)
+    for n in range(0, NXG, 2):
+        ms(T.XG[:, 512 * n:512 * n + 1024:2], 0.0, "XG%d XG%d" % (n, n + 1), 256 * CYC)
     iota(T.PI[:, 0:1], [[1, 1]], 0, 1, "PI")
-    sel(T.SWT[:], T.ONES[:], [[-16, 8], [0, 16]], A.is_ge, 0.0, 0, 1, "ONES", "SWT")
-    sel(T.G16[:], T.SWT[:], [[16, 8], [0, 16]], A.is_ge, 0.0, 15, -1, "SWT", "G16")
+    sel(T.G16[:], T.ONES[:], [[-16, 8], [0, 16]], A.is_ge, 0.0, 0, 1, "ONES", "G16")
+    sel(T.G16[:], T.G16[:], [[16, 8], [0, 16]], A.is_ge, 0.0, 15, -1, "G16", "G16")
     fiota(T.K16[:], [[0, 8], [1, 16]], 0, 0, "K16", 128)
     fiota(T.IOTC[:], [[1, 512]], -256, 0, "IOTC", 512)
     r32 = T.TR[0:32, 0:128]
-    sel(r32, r32, [[0, 16], [-1, 8]], A.not_equal, 0.0, -16, 1, "TR", "TR")
+    sel(r32, r32, [[0, 128 // MP], [-1, MP]], A.not_equal, 0.0, -16, 1, "TR", "TR")
+    sel(T.TM[0:32, :], T.TM[0:32, :], [[0, NQ], [-1, MP], [0, 16]], A.is_equal, 0.0, -16, 1, "TM", "TM")
     sel(r32, r32, [[0, 128]], A.is_ge, 0.0, -16, 1, "TR", "TR")
     sel(r32, r32, [[-1, 8], [0, 16]], A.not_equal, 1.0, 0, 1, "TR", "TR")
     sel(r32, r32, [[-1, 8], [0, 16]], A.not_equal, 1.0, -8, 1, "TR", "TR")
     sel(T.IDENT[:], T.ONES[:], [[-1, 128]], A.is_equal, 0.0, 0, 1, "ONES", "IDENT")
     sel(T.SELW[:, 0:128], T.G16[:], [[0, 8], [1, 16]], A.is_equal, 0.0, -15, 0, "G16", "SELW")
     iota(T.LI[:], [[16, 16]], 0, 0, "LI")
-    iota(T.BASE[:], [[512, 16]], 64, 0, "BASE")
-    for b in range(9):
-        fiota(T.PABI[:, b:b + 1], [[0, 1]], 2 ** (8 - b), 0, "+PABI", 1)
-        fiota(T.P2[:, b:b + 1], [[0, 1]], 2 ** b if b else 0, 0, "+P2", 1)
+    iota(T.BASE[:], [[512, 16]], 8 * MP, 0, "BASE")
     fiota(T.IDX[:], [[1, 256]], 0, 0, "IDX", 256)
 
     tt(T.DF[:], T.pns[:], T.pfs[:], A.subtract, "pfs pns", "DF", 512 * CYC)
@@ -290,102 +326,140 @@ def rank_program(g, core, T, topo):
     act(T.AFL[:], T.CS[:].indirect(T.fsU[:]), "CS fsU", "AFL", gat(256))
     for n in range(8):
         ts(T.WH[:, :, n, :], T.SG[:], T.G16[:, 16 * n:16 * n + 1], -1.0, A.mult, A.mult, "SG G16", "+WH", 128 * CYC)
-    for n in range(4):
-        act(T.WA[:, 4 * n:4 * n + 4, :, :], T.WH[:, 4 * n:4 * n + 4, :, :], "WH", "+WA", 512 * CYC, scale=-1.0)
+        ts(T.WA[:, :, n, :], T.SG[:], T.G16[:, 16 * n:16 * n + 1], None, A.mult, None, "SG G16", "+WA", 128 * CYC)
     ts(T.PM[:, 0:1], T.PI[:, 0:1], 15, None, A.bitwise_and, None, "PI", "PM")
     cp(T.PMF[:, 0:1], T.PM[:, 0:1], "PM", "PMF")
     ts(T.KK[:], T.K16[:], T.PMF[:, 0:1], None, A.is_equal, None, "K16 PMF", "KK")
-    cp(T.LL[:, 40:48], T.G16[:, ::16], "G16", "+LL")
     for n, bits in enumerate((4032, 63)):
         ts(T.TH[:, n:n + 1], T.ths[:, 0:1], 1, bits, A.arith_shift_right, A.bitwise_and, "ths", "TH%d" % n)
         ts(T.THN[:, n:n + 1], T.TH[:, n:n + 1], 0.5 * n, -1.0, A.add, A.mult, "TH%d" % n, "THN%d" % n)
         ts(T.LL[:, 8 * n:8 * n + 8], T.G16[:, ::16], T.THN[:, n:n + 1], None, A.mult, None, "G16 THN%d" % n, "+LL")
-    cp(T.TR[0:32, 128:256], r32, "TR", "TRb")
-    cp(T.TR[0:32, 256:512], T.TR[0:32, 0:256], "TR TRb", "TRc", 128 * CYC)
-    mms([(T.PL[0:24, 0:128], T.LL[:, 0:24], T.KK[:], True, False), (T.PL[0:24, 0:128], T.LL[:, 24:48], T.G16[:], False, True)],
-        "LL KK G16", "PL", 256)
-    cp(T.TI[0:24, :], T.PL[0:24, 0:128], "PL", "TI", 128 * CYC)
+    for n in range(1, CC):
+        cp(T.TR[0:32, 128 * n:128 * n + 128], r32, "TR", "+TRb")
+    mms([(T.PL[0:24, 0, 0:128], T.LL[:, 0:24], T.KK[:], True, True)], "LL KK", "PL", 128)
+    tt(T.TI[0:24, :], T.PL[0:24, 0, 0:128], T.TM[0:24, :], A.add, "PL TM", "TI", 128 * CYC)
     act(T.IDF[:], T.IDENT[:], "IDENT", "IDF", 128 * CYC)
     act(T.NIDF[:], T.IDENT[:], "IDENT", "NIDF", 128 * CYC, scale=-1.0)
     ts(T.SELW[:], T.SELW[:], 0.0625, None, A.mult, None, "SELW", "SELW")
-    ts(T.EUW[:, 112:128], T.KK[:, 0:16], 32.0, 1.0, A.mult, A.add, "KK", "+EUW")
-    ts(T.L256[:], T.LI[:], T.PMF[:, 0:1], 256.0, A.add, A.add, "LI PMF", "L256")
+    for q in range(NQ):
+        ts(T.EUW[part(q), 48 * q + 16:48 * q + 32], T.KK[part(q), 0:16], 32.0, 1.0, A.mult, A.add, "KK", "+EUW")
+    ts(T.LIF[:], T.LI[:], T.PMF[:, 0:1], None, A.add, None, "LI PMF", "LIF")
     ts(T.PMF[:, 1:2], T.PM[:, 0:1], 32.0, None, A.mult, None, "PM", "PMF1")
     ts(T.NSELW[:], T.SELW[:], -1.0, None, A.mult, None, "SELW", "NSELW")
     for t in range(4):
-        cp(mi(t, 0, 16), T.L256[:], "L256", "MIc%d" % t)
+        ts(mi(t, 0, 16), T.LIF[:], 256.0, None, A.add, None, "LIF", "MIc%d" % t)
     cp(mi(0, 32, 48), T.fss[:], "fss", "+MI0")
     cp(fa(0, 0, 16), T.fss[:], "fss", "FA0")
-    cp(T.BROW4[:].indirect(T.bsU[:]), T.IOTC[:], "IOTC bsU", "BROW4", sca(512))
+    fiota(T.YC[:], [[1, 512]], 32, 0, "YC", 512)
+    act(T.UF[:].indirect(T.bsU[:]), T.YC[:], "YC bsU", "UF", sca(512) + 1300, f=AF.Silu)
     conv(T.PN[:, 0:16], T.pfs, 0, 16, "pfs", "PN")
     ts(T.EI1[:], T.PN[:, 0:16], 16.0, None, A.mult, None, "PN", "EI1")
-    ts(T.EI2[:], T.EI1[:], 31, None, A.bitwise_and, None, "EI1", "EI2")
-    tt(T.ELS[:], T.EI2[:], T.BASE[:], A.add, "EI2 BASE", "ELS")
-    act(T.GROW[:], T.BROW4[:].indirect(T.nbU[:]), "BROW4 nbU", "GROW", gat(256))
+    ts(T.EI1[:], T.EI1[:], 31, None, A.bitwise_and, None, "EI1", "EI1")
+    tt(T.ELS[:], T.EI1[:], T.BASE[:], A.add, "EI1 BASE", "ELS")
+    act(T.GROW[:], T.UF[:].indirect(T.nbU[:]), "UF nbU", "GROW", gat(256), f=AF.Identity, bias=-288.0)
     conv(T.PN[:, 16:32], T.GROW, 0, 16, "GROW", "PN")
     ts(mi(0, 16, 32), T.PN[:, 16:32], 256.0, None, A.add, None, "PN", "+MI0")
     cp(T.PIF[:, 0:1], T.PI[:, 0:1], "PI", "PIF")
-    ts(T.PAB[:, 0:9], T.PABI[:, 0:9], 1.0 / 1024, None, A.mult, None, "PABI", "PAB")
-    ts(T.BI1[:, 0:5], T.PABI[:, 0:5], T.PIF[:, 0:1], None, A.mult, None, "PABI PIF", "BI1")
+    vec(lambda e: e.tensor_tensor_scan(T.PABW[:], T.HALF[:], T.QUART[:], 0.0, A.mult, A.add), "HALF QUART", "PABW", 128 * CYC)
+    vec(lambda e: e.tensor_tensor_scan(T.P2[:, 0:9], T.TWO[:, 0:9], T.QUART[:, 1:10], 0.5, A.mult, A.add), "TWO QUART", "+P2", 0)
+    ts(T.BI1[:, 0:5], T.PABW[:, 0:5], T.PIF[:, 0:1], 1024.0, A.mult, A.mult, "PABW PIF", "BI1")
     ts(T.BI2[:, 0:5], T.BI1[:, 0:5], 256, None, A.bitwise_and, None, "BI1", "BI2")
     ts(T.SB9[:, 0:4], T.BI2[:, 0:4], -1.0 / 128, 1.0, A.mult, A.add, "BI2", "+SB9")
     ts(T.RTB[:, 4:9], T.BI2[:, 0:5], 1.0 / 128, -1.0, A.mult, A.add, "BI2", "+RTB")
-    tt(T.LTB[:, 0:9], T.SB9[:, 0:9], T.P2[:, 0:9], A.mult, "SB9 P2", "LTB")
+    tt(T.LTB[:, 1:9], T.SB9[:, 1:9], T.P2[:, 1:9], A.mult, "SB9 P2", "+LTB")
     tt(T.LX1[:, 0:1], T.PMF[:, 0:1], T.SB9[:, 0:1], A.add, "PMF SB9", "LX1")
-    mms([(T.PD1[0:9, 0:128], T.LTB[:, 0:9], T.IDENT[:], True, True),
-         (T.PD1[0:9, 128:160], T.RTB[0:32, 0:9], T.IDENT[0:32, 0:32], True, True)], "LTB RTB IDENT", "PD1", 160)
-    act(T.LB[0:9, :], T.PD1[0:9, 0:128], "PD1", "LB", 128 * CYC)
-    act(T.RX[0:9, :], T.PD1[0:9, 128:160], "PD1", "RX")
+    mms([(T.PT[0:9, 0:128], T.LTB[:, 0:9], T.IDENT[:], True, True),
+         (T.PT[0:9, 128:160], T.RTB[:, 0:9], T.IDENT[:, 0:32], True, True)], "LTB RTB IDENT", "PT", 160)
+    act(T.LB[0:9, :], T.PT[0:9, 0:128], "PT", "LB", 128 * CYC)
+    act(T.RX[0:9, :], T.PT[0:9, 128:160], "PT", "RX")
+    act(T.PABX[0:32, :], T.PABW[0:32, :], "PABW", "PABX", 128 * CYC, scale=2.0)
+    for h in range(2):
+        m = T.SBH[0:32, 128 * h:128 * h + 128]
+        sel(m, T.ONES[0:32, :], [[-1, 8], [0, 16]], A.is_equal, 0.0, -8 * h, 1, "ONES", "SBH%d" % h)
+        sel(m, m, [[0, 128]], A.not_equal, 1.0, -16, 1, "SBH%d" % h, "SBH%d" % h)
+        tt(m, m, T.PABX[0:32, :], A.mult, "PABX SBH%d" % h, "+SBH", 256 * CYC)
+    ts(T.P2[:, 8:9], T.P2[:, 8:9], -1.0, None, A.mult, None, "P2", "P2")
+    tt(T.P2[:], T.P2[:], T.KK[:, 0:16], A.mult, "P2 KK", "P2")
+    vec(lambda e: e.tensor_reduce(T.C2[:, 0:1], T.P2[:], AxisListType.X, A.add), "P2", "C2a", 0)
+    ts(T.C2[:, 1:2], T.C2[:, 0:1], -2.0, None, A.mult, None, "C2a", "C2")
+    ts(T.DD[:, 0:1], T.KK[:, 0:1], -1.0, -1.0, A.mult, A.add, "KK", "DD")
+    ts(T.X8[:], T.G16[:, ::16], T.DD[:, 0:1], 1.0, A.mult, A.add, "G16 DD", "X8")
     act(T.BROW[:], T.IOTC[:].indirect(T.bsU[:]), "IOTC bsU", "BROW", gat(512))
     act(T.XB0[:, 0:256], T.BROW[:].indirect(T.fsU[:]), "BROW fsU", "+XB0", gat(256))
     act(T.XB0[:, 256:512], T.IOTC[:].indirect(T.nbU[:]), "IOTC nbU", "+XB0", gat(256))
 
-    ring = [0]
+    ring = {"XG": 0, "CL": 0}
 
-    def chunk(t, j):
-        c, n, m = j % 8, ring[0] % NXG, ring[0] % NCL
-        ring[0] += 1
-        off, key = (T.UH, "UH%d" % (c // 2)) if j < 8 else (T.UA, "UA%d" % (c // 4))
-        o, a = T.XG[:, 1024 * n + 1:1024 * n + 1024:2], T.xfs[:].indirect(off[:, 32 * c:32 * c + 32])
-        (cp if j in VG[t] else act)(o, a, "xfs xfsb " + key, "XG%d" % n, gat(512))
-        vec(lambda e: e.tensor_tensor_scan(T.CL[:, 1024 * m:1024 * m + 1024], T.XG[:, 1024 * n:1024 * n + 1024],
-                                           T.D1[:, 1024 * c:1024 * c + 1024], 0.0, A.min, A.max), "XG%d D1" % n, "CL%d" % m, 512 * CYC)
-        P, w = "PB%d" % (c // 2), ("WH", "WA")[j // 8]
-        if j < 8 and c % 2 == 0:
-            mms([(T[P][:], T.TI[0:24, :], T.TR[0:24, :], True, False)], "TI TR TRb TRc", P, 512)
+    def slots(name, size, n):
+        a = ring[name] if ring[name] + n <= size else 0
+        ring[name] = a + n
+        return a, " ".join("%s%d" % (name, x) for x in range(a, a + n))
+
+    def early(name, step, *a):
+        n = len(calls)
+        step(*a)
+        for c in calls[n:]:
+            c["early"] = EARLY.get(name, 0)
+
+    def chunk(q, j, n):
+        c = j % 16
+        off, key = T[("UH", "UA")[j // 16]], [("UH%d", "UA%d")[j // 16] % ((c + x) // 4) for x in range(n)]
+        x, xk = slots("XG", NXG, n)
+        o, a = T.XG[:, 512 * x + 1:512 * (x + n):2], T.xfs[:].indirect(off[:, 16 * c:16 * (c + n)])
+        (cp if q == "V" else act)(o, a, "xfs xfsb " + " ".join(key), xk, gat(256 * n))
+        for u in range(0, n, SCAN):
+            clamp(j + u, x + u, min(SCAN, n - u))
+
+    def clamp(j, x, n):
+        c = j % 16
+        m, mk = slots("CL", NCL, n)
+        vec(lambda e: e.tensor_tensor_scan(T.CL[:, 512 * m:512 * (m + n)], T.XG[:, 512 * x:512 * (x + n)],
+                                           T.D1[:, 512 * c:512 * (c + n)], 0.0, A.min, A.max),
+            "D1 " + " ".join("XG%d" % y for y in range(x, x + n)), mk, 256 * n * CYC)
+        P, w = "PB%d" % (c // 4), ("WH", "WA")[j // 16]
+        if j < 16 and c % 4 == 0:
+            mms([(T[P][:, 0:CC, :, :], T.TI[0:24, :], T.TR[0:24, 0:128 * CC], True, False)], "TI TR TRb", P, 128 * CC)
         l = []
-        for b in range(4):
-            col, s = 2 * c + b // 2, slice(8 * (b % 2), 8 * (b % 2) + 8)
-            a = 1024 * m + 256 * b + 1
-            l.append((T[P][:, col % 4, :, s], T.CL[:, a:a + 255:2], T[w][:, col, :, s], False, j >= 8 and c % 2 == 1 and b == 3))
-        mms(l, "CL%d %s" % (m, w), P, 256)
+        for u in range(n):
+            for b in range(0, 16, MP):
+                a, s = 512 * (m + u) + 32 * b + 1, slice(b, b + MP)
+                l.append((T[P][part((c + u) % NQ), (c + u) % 4 // NQ, :, s], T.CL[:, a:a + 32 * MP - 1:2], T[w][:, c + u, :, s], False,
+                          j >= 16 and (c + u) % 4 >= 4 - NQ and b + MP == 16))
+        mms(l, mk + " " + w, P, n * (256 if MP < 8 else 128))
 
     def signs(k):
         P, z = "PB%d" % k, "Z%d" % k
-        act(T.Z[:, 4 * k:4 * k + 4, :, :], T[P][:], P, z + " ACC%d" % k, 530 * CYC, f=AF.Sign, accum_out=T.ACC[:, k:k + 1])
-        mms([(T.PL[:, c:c + 17:16], T.Z[:, c, :, :], T.HALF[:], True, True) for c in range(4 * k, 4 * k + 4)], z + " HALF", "PL", 256)
+        act(T.Z[:, CC * k:CC * k + CC, :, :], T[P][:, 0:CC, :, :], P, z + " ACC%d" % k, (128 * CC + 20) * CYC, f=AF.Sign,
+            accum_out=T.ACC[:, k:k + 1])
 
-    def total():
-        mms([(T.PN[0:9, 96:97], T.PAB[:, 0:9], T.ACC[:, k:k + 1], k == 4, k == 3) for k in (4, 0, 1, 2, 3)],
-            "PAB ACC0 ACC1 ACC2 ACC3 ACC4", "PN", 200)
+    def sums(k):
+        z = "Z%d" % k
+        mms([(T.PL[:, :, 4 * k + NQ * c:4 * k + NQ * (c + 1)], T.Z[:, CC * k + c, :, :], T.QS[:], True, True) for c in range(CC)],
+            z + " QS", "PL", 64 * CC)
+
+    def total(k):
+        mms([(T.PT[:, 0:1], T.PABW[:], T.ACC[:, k:k + 1], k == 4, k == 3)], "PABW ACC%d" % k, "PT", 256)
 
     def turned(t, k):
         P, z, s = "PB%d" % k, "Z%d" % k, slice(64 * k, 64 * k + 64)
         for n, e in enumerate(("EUW", "ESW")):
-            mms([(T[P][:, n, 0:4, :], T[e][:, 112 - 16 * x:240 - 16 * x], T.Z[:, 4 * k:4 * k + 4, x, :], x == 0, x == 7)
-                 for x in range(8)], z + " " + e, P, 512)
-        act(T.AB[:, s], T[P][:, 0, 0:4, :], P, "AB%d" % k, f=AF.Abs if t < 4 else AF.Identity, bias=343.0)
-        act(T.TROW[:, s], T[P][:, 1, 0:4, :], P, "TROW%d" % k, f=AF.Relu, scale=-512.0, bias=-56832.0)
+            mms([(T[P][32 * (x // 2):32 * (x // 2) + 32, n, q:4:NQ, :], T[e][:, 48 * q + 16 - 16 * (x % 2):48 * q + 48 - 16 * (x % 2)],
+                  T.Z[:, CC * k:CC * k + CC, x, :], x % 2 == 0, x % 2 == 1) for q in range(NQ) for x in range(8)],
+                z + " " + e, P, 8 * NQ * max(32, 16 * CC))
+        act(T.AB[:, s], T[P][:, 0, 0:4, :], P, "AB%d" % k, f=AF.Abs if t < 4 else AF.Identity, bias=48.0 * MP - 41)
+        act(T.TROW[:, s], T[P][:, 1, 0:4, :], P, "TROW%d" % k, f=AF.Relu, scale=-1024.0, bias=17408.0 - 16384 * MP)
+        x = T[P][:, 2, 0:4, :]
+        mms([(x, T.IDENT[:], T.TROW[:, s], True, False), (x, T.IDENT[:], T.IDX[:, s], False, True)], "IDENT IDX TROW%d" % k, P, 128)
+        act(T.XF[:, s], x, P, "XF%d" % k, f=AF.Identity, bias=32.0)
 
     def rows(t, k):
-        P, s, hk = "PD%d" % (k % 2), slice(64 * k, 64 * k + 64), "WI%d_%d" % (t, k)
-        p, h = T[P][:, 0:64], wi(t, HCOL[k], HCOL[k] + 64)
-        mms([(p, T.IDF[:], h, True, False), (p, T.NIDF[:], T.AFL[:, s], False, True)], "IDF NIDF AFL " + hk, P, 512)
+        P, s, hk = "PD", slice(64 * k, 64 * k + 64), "WI%d_%d" % (t, k)
+        p, h = T.PD[:, s], wi(t, HCOL[k], HCOL[k] + 64)
         ts(T.MM[:, s], T.AB[:, s], 32.0 if t < 4 else 0.0, None, A.is_gt, None, "AB%d" % k, "MM%d" % k)
         if t < 4:
-            tt(p, p, T.MM[:, s], A.mult, P + " MM%d" % k, P)
-            tt(wo(t, HCOL[k], HCOL[k] + 64), h, p, A.subtract, P + " " + hk, "WO%dh%d" % (t, k))
-            tt(wo(t, ACOL + 64 * k, ACOL + 64 + 64 * k), p, T.AFL[:, s], A.add, P + " AFL", "WO%da%d" % (t, k))
+            tt(p, p, T.MM[:, s], A.mult, "PD MM%d" % k, "pd%d" % k)
+            tt(wo(t, HCOL[k], HCOL[k] + 64), h, p, A.subtract, "PD pd%d %s" % (k, hk), "WO%dh%d" % (t, k))
+            tt(wo(t, ACOL + 64 * k, ACOL + 64 + 64 * k), p, T.AFL[:, s], A.add, "PD pd%d AFL" % k, "WO%da%d" % (t, k))
             a, b, keys = SENDS[k]
             send(1, wi(t + 1, a, b), wo(t, a, b), " ".join("WO%d%s" % (t, x) for x in keys.split()), "WI%d_%d" % (t + 1, k),
                  "a%d_%d" % (k, t + 1), b - a)
@@ -395,50 +469,76 @@ def rank_program(g, core, T, topo):
             tt(T.YC[:].indirect(T.YL[:, 16 + 4 * k:20 + 4 * k]), h, T.PS[:, s], A.subtract, "YL PS%d %s" % (k, hk), "YC", sca(64))
 
     def frames(a, b):
-        tt(T.OI1[:, a:b], T.PL[:, a:b], T.ELS[:, a:b], A.add, "PL ELS", "OI1%d" % a)
+        tt(T.OI1[:, a:b], T.PL[:, 0, a:b], T.ELS[:, a:b], A.add, "PL ELS", "OI1%d" % a)
         ts(T.OI2[:, a:b], T.OI1[:, a:b], 8191 - 32, None, A.bitwise_and, None, "OI1%d" % a, "OI2%d" % a)
         ts(T.OFFU[:, a:b], T.OI2[:, a:b], T.PMF[:, 1:2], None, A.add, None, "PMF1 OI2%d" % a, "OFFU%d" % a)
         cp(T.xfs[:].indirect(T.OFFU[:, a:b]), T.pfs[:, 16 * a:16 * b], "pfs OFFU%d" % a, "xfs xfsb", sca(16 * (b - a)))
 
     def flags(t, a, b):
-        keys = " ".join("TROW%d" % k for k in range(a // 4, b // 4))
-        tt(T.U[:, 0:512].indirect(fa(t, a, b)), T.TROW[:, 16 * a:16 * b], T.IDX[:, 16 * a:16 * b], A.add,
-           keys + " IDX FA%d" % (t % 2), "U0", sca(16 * (b - a)))
+        keys = " ".join("XF%d" % k for k in range(a // 4, b // 4))
+        act(T.UF[:].indirect(fa(t, a, b)), T.XF[:, 16 * a:16 * b], keys + " FA%d" % (t % 2), "UF", sca(16 * (b - a)), f=AF.Silu)
 
     def take(t):
         for k in range(4):
             cp(T.UH[:, 64 * k:64 * k + 64], wi(t, HCOL[k], HCOL[k] + 64), "WI%d_%d" % (t, k), "UH%d" % k)
         if t:
-            cp(fa(t, 0, 32), mi(t, 32, 64), "MI%d" % t, "FA%d" % (t % 2))
-            act(T.AFL[:], wi(t, ACOL, ACOL + 256).indirect(fa(t, 16, 32)), "WI%d_1 WI%d_3 FA%d" % (t, t, t % 2), "AFL", gat(256))
-        for h in range(2):
-            cp(T.UA[:, 128 * h:128 * h + 128], T.AFL[:, 128 * h:128 * h + 128], "AFL", "UA%d" % h, 128 * CYC)
+            cp(fa(t, 0, 16), mi(t, 32, 48), "MI%d" % t, "FA%d" % (t % 2))
+            cp(fa(t, 16, 32), mi(t, 48, 64), "MA%d" % t, "ALU")
+            act(T.AFL[:], wi(t, ACOL, ACOL + 256).indirect(fa(t, 16, 32)), "WI%d_1 WI%d_3 ALU" % (t, t), "AFL", gat(256))
+            cp(T.UA[:, 0:64], wi(t, ACOL, ACOL + 256).indirect(fa(t, 16, 20)), "WI%d_1 WI%d_3 ALU" % (t, t), "UA0", gat(64))
+        else:
+            cp(T.UA[:, 0:64], T.AFL[:, 0:64], "AFL", "UA0")
+        cp(T.UA[:, 64:256], T.AFL[:, 64:256], "AFL", "UA1 UA2 UA3", 192 * CYC)
+        for k in range(4):
+            s = slice(64 * k, 64 * k + 64)
+            mms([(T.PD[:, s], T.IDF[:], wi(t, HCOL[k], HCOL[k] + 64), True, False), (T.PD[:, s], T.NIDF[:], T.AFL[:, s], False, True)],
+                "IDF NIDF AFL WI%d_%d" % (t, k), "PD", 512)
+        if t < 4:
+            bits(t)
         tt(T.DF2[:, 16:32], mi(t, 16, 32), mi(t, 32, 48), A.subtract, "MI%d" % t, "DF2")
-        fiota(T.U[:, 0:512], [[0, 512]], 512, 0, "U0", 512)
+        fiota(T.UF[:], [[0, 512]], 1056, 0, "UF", 512)
 
-    def xor():
-        y = T.PN[0:9, 96:97]
-        cp(T.RI[0:9, 0:1], y, "PN", "RI")
-        tt(T.DD[0:9, 0:1], y, T.RI[0:9, 0:1], A.subtract, "PN RI", "DD")
-        ts(T.RS[0:9, :], T.RX[0:9, :], T.DD[0:9, 0:1], 0.0, A.mult, A.is_gt, "RX DD", "RS")
-        mms([(T.PN[:, 128:160], T.LB[0:9, :], T.RS[0:9, :], True, True)], "LB RS", "PN", 64)
-        ts(T.XLU[:], T.PN[:, 128:160], T.LX1[:, 0:1], None, A.add, None, "PN LX1", "XLU")
+    def bits(t):
+        ts(T.FB[:], mi(t, 32, 48), -256.0, None, A.add, None, "MI%d" % t, "FB")
+        mms([(T.PN[0:16, 128:256], T.FB[:], T.IDENT[:], True, True)], "FB IDENT", "PN", 128)
+        act(T.FT[0:16, :], T.PN[0:16, 128:256], "PN", "+FT", 128 * CYC)
+        mms([(T.PN[:, 256 + 128 * h:384 + 128 * h], T.SBH[0:17, 128 * h:128 * h + 128], T.FT[0:17, :], True, True) for h in range(2)],
+            "SBH FT", "PN", 256)
+        cp(T.RB[:], T.PN[:, 256:512], "PN", "RB", 256 * CYC)
+        tt(T.BT[:], T.PN[:, 256:512], T.RB[:], A.is_lt, "PN RB", "BT", 256 * CYC)
+        ts(T.BT[:], T.BT[:], T.C2[:, 1:2], T.C2[:, 0:1], A.mult, A.add, "BT C2", "BT", 128 * CYC)
+
+    def xor(t):
+        y = T.PT[:, 0:1]
+        cp(T.RI[:, 0:1], y, "PT", "RI")
+        tt(T.DD[:, 0:1], y, T.RI[:, 0:1], A.subtract, "PT RI", "DD")
+        if t < 4:
+            ts(T.RS[:, 0:8], T.X8[:], T.DD[:, 0:1], 0.0, A.add, A.is_lt, "X8 DD", "RS")
+            mms([(T.PT[:, 16:32], T.IDENT[:], T.FB[:], True, False), (T.PT[:, 16:24], T.BT[:, 0:128], T.RS[:, 0:8], False, False),
+                 (T.PT[:, 24:32], T.BT[:, 128:256], T.RS[:, 0:8], False, True)], "IDENT FB BT RS", "PT", 192)
+            ts(T.XLU[:, 0:16], T.PT[:, 16:32], 256.0, None, A.add, None, "PT", "XLU")
+        else:
+            ts(T.RS[0:9, :], T.RX[0:9, :], T.DD[0:9, 0:1], 0.0, A.mult, A.is_gt, "RX DD", "RS")
+            mms([(T.PT[:, 128:160], T.LB[0:9, :], T.RS[0:9, :], True, True)], "LB RS", "PT", 64)
+            ts(T.XLU[:], T.PT[:, 128:160], T.LX1[:, 0:1], None, A.add, None, "PT LX1", "XLU")
 
     def turns(t):
-        ts(T.TRN[:], T.PL[:, 0:32], 4.5 - 64, None, A.is_lt, None, "PL", "TRN")
+        ts(T.TRN[:], T.PL[:, :, 0:16], 4.5 - 8 * MP, None, A.is_lt, None, "PL", "TRN")
         tt(T.XX[:], T.TRN[:], T.DF2[:], A.mult, "TRN DF2 DF2c", "XX")
         if t < 4:
             tt(mo(t, 48, 64), mi(t, 32, 48), T.XX[:, 16:32], A.add, "MI%d XX" % t, "MO%df" % t)
             tt(mo(t, 16, 48), mi(t, 0, 32), T.XX[:], A.subtract, "MI%d MIc%d XX" % (t, t), "MO%dg" % t)
 
     def alpha(t):
-        conv(T.PN[:, 0:16], T.TROW, 0, 16, "TROW0 TROW1 TROW2 TROW3", "PN", sp=False)
-        act(T.U[:, 512:1024], T.U[:, 0:512].indirect(T.XLU[:]), "U0 XLU", "U1", gat(512))
-        act(T.MROW[:], T.U[:, 512:1024].indirect(fa(t, 0, 16)), "U1 FA%d" % (t % 2), "MROW", gat(256))
+        ts(T.OWN[:], T.PL[:, 0, 0:16], 8.5 - 8 * MP, 512.0, A.is_gt, A.mult, "PL", "OWN")
+        tt(T.OWN[:], T.OWN[:], T.LIF[:], A.add, "OWN LIF", "OWN")
+        mms([(T.PN[:, 0:16], T.G16[:], T.C16[:], True, False)], "G16 C16", "PN", 64)
+        act(T.MROW[:], T.UF[:].indirect(T.XLU[:, 0:16]), "UF XLU", "MROW", gat(256), f=AF.Identity, bias=-32.0)
         conv(T.PN[:, 0:16], T.MROW, 0, 16, "MROW", "PN", st=False)
-        tt(T.AL[:], T.PN[:, 0:16], T.L256[:], A.min, "PN L256", "AL")
+        tt(T.AL[:], T.PN[:, 0:16], T.OWN[:], A.min, "PN OWN", "AL")
         ts(mo(t, 64, 80), T.AL[:], 255, None, A.bitwise_and, None, "AL", "MO%da" % t)
-        send(1, mi(t + 1, 16, 64), mo(t, 32, 80), "MO%da MO%df MO%dg" % (t, t, t), "MI%d" % (t + 1), "a4_%d" % (t + 1), 48)
+        send(1, mi(t + 1, 48, 64), mo(t, 64, 80), "MO%da" % t, "MA%d" % (t + 1), "a5_%d" % (t + 1), 16)
+        send(1, mi(t + 1, 16, 48), mo(t, 32, 64), "MO%df MO%dg" % (t, t), "MI%d" % (t + 1), "a4_%d" % (t + 1), 32)
         tt(mo(t, 0, 16), mo(t, 64, 80), T.XX[:, 0:16], A.add, "MO%da XX" % t, "MO%db" % t)
         if t:
             send(-t, T.HM[:, 32 * t:32 * t + 32], mo(t, 0, 32), "MO%db MO%dg" % (t, t), "HM%d" % t, "ah%d" % t, 32)
@@ -468,36 +568,41 @@ def rank_program(g, core, T, topo):
             boxes(t - 1)
         if t == 4:
             box_lists()
-        for j in range(16):
-            chunk(t, j)
-            if j > 8 and j % 2:
-                k = (j - 9) // 2
+        j = 0
+        for w in PLAN[t // 4].split():
+            chunk(w[0], j, int(w[1:]))
+            j += int(w[1:])
+            if j > 16 and j % 4 == 0:
+                k = (j - 20) // 4
                 if k == 3 and t < 4:
-                    frames(*OFFS[0])
-                signs(k)
-                if k == 3:
-                    total()
-                    if t < 4:
-                        frames(*OFFS[1])
-                turned(t, k)
-                rows(t, k)
-        for a, b in FLAGS:
-            flags(t, a, b)
-        xor()
+                    early("frames", frames, *OFFS[0])
+                early("signs%d" % k, signs, k)
+                early("sums", sums, k)
+                if k == 0:
+                    total(4)
+                early("total", total, k)
+                if k == 3 and t < 4:
+                    early("frames", frames, *OFFS[1])
+                early("turned%d" % k, turned, t, k)
+                early("rows%d" % k, rows, t, k)
+                for a, b in FLAGS:
+                    if b == 4 * k + 4:
+                        early("flags%d" % k, flags, t, a, b)
+        early("xor", xor, t)
         turns(t)
         if t < 4:
-            alpha(t)
+            early("alpha", alpha, t)
 
     dma("D", T.yc[:], T.YC[:], "YC", "yc", "o_yc", 3000)
-    conv(T.PD0[:, 0:32], T.BROW4, 0, 32, "BROW4", "PD0", sp=False, tab="NSELW")
-    conv(T.PN[:, 0:32], T.U, 0, 32, "U0", "PN", sp=False)
-    act(T.U[:, 512:1024], T.U[:, 0:512].indirect(T.XLU[:]), "U0 XLU", "U1", gat(512))
-    cp(T.U[:, 1024:1536], T.BROW4[:].indirect(T.XLU[:]), "BROW4 XLU", "U2", gat(512))
-    conv(T.PN[:, 0:32], T.U, 512, 32, "U1", "PN", st=False)
-    conv(T.PD0[:, 0:32], T.U, 1024, 32, "U2", "PD0", st=False)
-    ts(T.B1[:], T.PN[:, 0:32], 511.0, None, A.is_lt, None, "PN", "B1")
-    tt(T.B2[:], T.PD0[:, 0:32], T.B1[:], A.mult, "PD0 B1", "B2")
-    tt(T.YB[:], T.BL[:], T.B2[:], A.add, "BL B2", "YB")
+    conv(T.PT[:, 0:32], T.BROW4, 0, 32, "BROW4", "PT", sp=False, tab="NSELW")
+    act(T.CS[:], T.UF[:], "UF", "CS", 512 * CYC)
+    tt(T.U[:, 0:512], T.UF[:].indirect(T.XLU[:]), T.CS[:], A.add, "UF CS XLU", "U1", gat(640))
+    act(T.U[:, 512:1024], T.BROW4[:].indirect(T.XLU[:]), "BROW4 XLU", "U2", gat(512))
+    conv(T.PT[:, 0:32], T.U, 512, 32, "U2", "PT", st=False)
+    conv(T.PN[:, 0:32], T.U, 0, 32, "U1", "PN")
+    ts(T.B1[:], T.PN[:, 0:32], 800.0, None, A.is_lt, None, "PN", "B1")
+    tt(T.B1[:], T.PT[:, 0:32], T.B1[:], A.mult, "PT B1", "B1")
+    tt(T.YB[:], T.BL[:], T.B1[:], A.add, "BL B1", "YB")
     dma("S", T.yb[:], T.YB[:], "YB", "yb", "o_yb")
     tt(T.YF[:], mi(4, 32, 48), T.XX[:, 16:32], A.add, "MI4 XX", "YF")
     dma("D", T.yf[:], T.YF[:], "YF", "yf", "o_yf")

@@ -1,18 +1,20 @@
 from concourse.mybir import AluOpType as A, AxisListType, ActivationFunctionType as AF
 
-NXG, NCL = 12, 8
+NXG, NCL = 10, 8
 SCAN = 2
 MP = 4
 NQ, CC = 8 // MP, MP // 2
-PLAN = ("S1 V1 S2 V2 S2 S4 S4 V2 S2 S2 V2 S2 S2 S2 V1 S1", "S2 V2 S2 S2 S4 S4 S2 V2 S4 S4 S2 S2")
-EARLY = {}
+PLAN = ("S1 V1 S2 V2 S2 S4 S4 V2 S2 V2 S2 S4 S2 V1 S1", "V2 S2 S2 V2 S4 S4 V2 S2 S4 S4 S2 V1 S1")
+NY = 6
+DS = 8
+EARLY = ({}, {})
 FLAGS = ((0, 8), (8, 12), (12, 16))
 OFFS = ((0, 12), (12, 16))
 HCOL, ACOL = (64, 128, 0, 448), 192
 SENDS = ((64, 128, "h0"), (128, 320, "h1 a0 a1"), (0, 64, "h2"), (320, 512, "a2 a3 h3"))
-CYC, GAT, SCA, PEC, HOP, FAR = 0.83, 1.3, 3.2, 0.5, 180, 2200
-PASSES = 3
-LOOKS = (0.2, 0.3, 0.4, 0.5, 0.6)
+CYC, GAT, SCA, PEC, HOP, FAR = 0.83, 1.3, 3.2, 0.47, 175, 2200
+XF, COL = 9100, 6.4
+PASSES = 800
 ORDER = []
 FL, BF, I32, U16 = "float32", "bfloat16", "int32", "uint16"
 
@@ -28,47 +30,51 @@ def _scratch():
     sb("CL", 512 * NCL, BF)
     for n in ("WH", "WA"):
         s[n] = ("sbuf", [128, 16, 8, 16], BF)
+    sb("YV CV", 256 * NY, BF)
     s["Z"] = ("sbuf", [128, 4 * CC, 8, 16], BF)
-    sb("pfs pns LO HI DF SG AB MM TROW MROW IDX GROW", 256, BF)
+    sb("pfs pns LO HI SG AB MM MROW", 256, BF)
+    sb("IDX", 256, FL)
+    sb("CX", 64, BF)
     sb("cbs", 512, I32)
-    sb("CBF CS YC UF", 512, FL)
+    sb("CBF YC UF", 512, FL)
     sb("AFL PS XF", 256, FL)
     sb("WI WO", 512 * 5, FL)
     sb("MI", 64 * 5, I32)
     sb("MO", 80 * 4, I32)
     sb("HM", 32 * 4, I32)
     sb("bss", 32, I32)
-    sb("fss nbs OI1 OI2 EI1 BASE LI ELS AL BI1 BI2", 16, I32)
+    sb("fss nbs OI1 OI2 BASE LI ELS AL BI1 BI2", 16, I32)
     sb("ths TH PI PM RI", 2, I32)
     sb("IDF NIDF", 128, FL)
     sb("THN PMF PIF DD LX1", 2, FL)
     sb("ACC", 8, FL)
-    sb("ONES IDENT G16 KK K16 TI LB", 128, BF)
+    sb("ONES IDENT G16 KK TI LB", 128, BF)
     sb("SELW NSELW", 144, BF)
     sb("EUW ESW", 48 * NQ, BF)
-    sb("TR IOTC BROW BROW4 XB0 XB1", 512, BF)
+    sb("TR IOTC XB0 XB1", 512, BF)
+    sb("BZ", 1024, BF)
     sb("LL", 24, BF)
     sb("QS", 2 * NQ, BF)
     sb("TWO OWN", 16, FL)
     sb("HALF QUART", 128, FL)
     sb("C16", 16, BF)
     sb("TM", 128, BF)
-    sb("LTB RTB SB9 P2", 16, BF)
+    sb("LTB RTB SB9", 16, BF)
     sb("RS RX", 32, BF)
     sb("UH UA", 256, U16)
     sb("bsU XLU XLS YL", 32, U16)
     sb("FA", 64, U16)
     sb("fsU nbU OFFU GU", 16, U16)
-    sb("LIF DA YF YN", 16, FL)
-    sb("TRN DF2 XX YL32 BL B1 YB", 32, FL)
+    sb("LIF DA YF", 16, FL)
+    sb("TRN DF2 XX YL32 BL B1", 32, FL)
     sb("U", 1024, BF)
     for n in ("PB0", "PB1", "PB2", "PB3"):
         s[n] = ("psum", [128, 4, 8, 16], FL)
     sb("FB", 16, BF)
-    sb("X8", 8, BF)
-    sb("FT PABX", 128, BF)
-    sb("BT SBH", 256, BF)
-    sb("RB", 256, I32)
+    sb("X16", 16, BF)
+    sb("P2", 18, BF)
+    sb("FT PABX BT SBH", 128, BF)
+    sb("RB", 128, I32)
     sb("PABW", 128, FL)
     sb("C2", 2, FL)
     for n in ("PT", "PD", "PN"):
@@ -79,46 +85,45 @@ def _scratch():
 
 SCRATCH = _scratch()
 BANKS = ("PB0", "PB1", "PB2", "PB3", "PT", "PD", "PL", "PN")
-LOADS = ["pf", "pn", "fs", "bs", "nb", "th", "cb", "xa", "xb"]
+LOADS = ["pf", "pn", "fs", "bs", "nb", "th", "cb", "xf"]
 SEMAPHORES = (["qV", "qS", "qP", "qG", "loc"] + ["d_" + n for n in LOADS] + ["o_yc", "o_yb", "o_yf", "o_yn"]
               + ["a%d_%d" % (k, t) for k in range(6) for t in range(1, 5)] + ["ah1", "ah2", "ah3"])
 
 
 def issue_order(calls):
+    if ORDER:
+        return ORDER
     n = len(calls)
-    pre = [c["pre"] for c in calls]
-    after = [[] for _ in range(n)]
-    for i in range(n):
-        for p in pre[i]:
-            after[p].append(i)
-
-    def gap(i, j):
-        return 0 if calls[i]["q"] == calls[j]["q"] == "P" else calls[min(i, j)]["late"]
+    qs, ns, late = [[c[k] for c in calls] for k in ("q", "ns", "late")]
+    pre, post = [[] for _ in range(n)], [[] for _ in range(n)]
+    for j, c in enumerate(calls):
+        for i in c["pre"]:
+            gap = 0 if qs[i] == qs[j] == "P" else late[i]
+            pre[j].append((i, gap))
+            post[i].append((j, gap))
 
     def walk(before, behind, urgent, start, look):
         left = [len(b) for b in before]
-        ready = {i: start(i) for i in range(n) if not left[i]}
-        free, end, order = {}, [0.0] * n, []
-        while ready:
-            t1, q = min((max(r, free.get(calls[i]["q"], 0.0)) + look * calls[i]["ns"], calls[i]["q"]) for i, r in ready.items())
-            i = max((i for i, r in ready.items() if calls[i]["q"] == q and r <= t1), key=urgent)
-            end[i] = free[q] = max(free.get(q, 0.0), ready.pop(i)) + calls[i]["ns"]
+        ready = {q: {i: start[i] for i in range(n) if qs[i] == q and not left[i]} for q in "VSPGD"}
+        free, end, order = dict.fromkeys(ready, 0.0), [0.0] * n, []
+        for _ in range(n):
+            t1, q = min((max(r, free[q]) + look * ns[i], q) for q in ready for i, r in ready[q].items())
+            i = max((i for i, r in ready[q].items() if r <= t1), key=lambda i: urgent[i])
+            end[i] = free[q] = max(free[q], ready[q].pop(i)) + ns[i]
             order.append(i)
-            for j in behind[i]:
+            for j, _g in behind[i]:
                 left[j] -= 1
                 if not left[j]:
-                    ready[j] = max(end[p] + gap(p, j) for p in before[j])
+                    ready[qs[j]][j] = max(end[p] + gap for p, gap in before[j])
         return end, order
-    if not ORDER:
-        best = None
-        for look in LOOKS:
-            end = list(range(n))
-            for _ in range(PASSES):
-                back, _o = walk(after, pre, lambda i: end[i], lambda i: calls[i]["late"], look)
-                end, order = walk(pre, after, lambda i: (i < len(LOADS), -i if i < len(LOADS) else back[i] + calls[i].get("early", 0)),
-                                  lambda i: 0.0, look)
-                if best is None or max(end) < best:
-                    best, ORDER[:] = max(end), order
+    end, now, best = list(range(n)), 1e18, 1e18
+    for k in range(PASSES):
+        back, _o = walk(post, pre, end, late, 0.1 + 0.8 * (0.618 * k % 1))
+        new, order = walk(pre, post, [1e18 - 1e3 * i if i < len(LOADS) else back[i] for i in range(n)], [0.0] * n, 0.1 + 0.8 * (0.414 * k % 1))
+        if max(new) < now + 2 * HOP:
+            end, now = new, max(new)
+        if max(new) < best:
+            best, ORDER[:] = max(new), order
     return ORDER
 
 
@@ -189,7 +194,7 @@ def rank_program(g, core, T, topo):
         dst, src = T.cores[(rank + hops) % N], T.cores[(rank - hops) % N]
         rid, pid, _s = topo.addr(dst)
         record("G", [lambda e: e.remote_dma(out, in_, T.sem[sem], T.sem.loc, pid, rid, topo.mask(core, dst))], R, W,
-               400, FAR + 6 * cols, (sem, len(topo.engines(src, core))), True)
+               max(300, COL * cols), FAR * (1 if nloc[0] else 2) + min(0, COL * cols - 300), (sem, len(topo.engines(src, core))), True)
         nloc[0] += len(topo.engines(core, dst))
 
     def vec(fn, R, W, n):
@@ -253,15 +258,14 @@ def rank_program(g, core, T, topo):
     def fa(t, a, b):
         return T.FA[:, 32 * (t % 2) + a:32 * (t % 2) + b]
 
-    dma("D", T.pfs[:], T.pf[:], "", "pfs", "d_pf")
-    dma("S", T.pns[:], T.pn[:], "", "pns", "d_pn")
-    dma("D", T.nbs[:], T.nb[:], "", "nbs", "d_nb", 3000)
-    dma("S", T.cbs[:], T.cb[:], "", "cbs", "d_cb", 3500)
-    dma("D", T.bss[:], T.bs[:], "", "bss", "d_bs", 3500)
-    dma("S", T.fss[:], T.fs[:], "", "fss", "d_fs", 3500)
-    dma("D", T.ths[:, 0:1], T.th[:], "", "ths", "d_th", 3500)
-    dma("S", T.xfs[:, 0:4096], T.xf[:, 0:4096], "", "xfs", "d_xa", 9000)
-    dma("D", T.xfs[:, 4096:8192], T.xf[:, 4096:8192], "", "xfsb", "d_xb", 9000)
+    dma("S", T.pns[:], T.pn[:], "", "pns", "d_pn", 1900)
+    dma("D", T.pfs[:], T.pf[:], "", "pfs", "d_pf", 2300)
+    dma("S", T.bss[:], T.bs[:], "", "bss", "d_bs", 2600)
+    dma("D", T.nbs[:], T.nb[:], "", "nbs", "d_nb", 2900)
+    dma("S", T.cbs[:], T.cb[:], "", "cbs", "d_cb", 3700)
+    dma("D", T.fss[:], T.fs[:], "", "fss", "d_fs", 4000)
+    dma("D", T.ths[:, 0:1], T.th[:], "", "ths", "d_th", 4300)
+    dma("D", T.xfs[:], T.xf[:], "", "xfs xfsb", "d_xf", XF)
 
     ms(T.ONES[:], 1.0, "ONES")
     ms(T.TR[0:32, 0:128], -1024.0, "TR")
@@ -272,19 +276,19 @@ def rank_program(g, core, T, topo):
     ms(T.QS[:], 0.0, "QS")
     for q in range(NQ):
         ms(T.QS[part(q), q::NQ], 0.5, "+QS")
-        ms(T.ESW[part(q), 48 * q + 16:48 * q + 32], 1.0, "+ESW")
+        ms(T.ESW[part(q), 48 * q + 16:48 * q + 32], -1024.0, "+ESW")
+    ms(T.CX[:], 1088.0 - 1024 * MP, "CX")
     ms(T.TM[0:32, :], 16.0, "TM")
     ms(T.HALF[:], 0.5, "HALF", 128 * CYC)
     ms(T.QUART[:], 0.0, "QUART", 128 * CYC)
-    ms(T.HALF[:, ::16], 0.0, "+HALF")
-    ms(T.QUART[:, ::16], 0.25, "+QUART")
+    ms(T.HALF[:, ::8], 0.0, "+HALF")
+    ms(T.QUART[:, ::8], 0.125, "+QUART")
+    ms(T.X16[:], 0.0, "X16")
     ms(T.TWO[:], 2.0, "TWO")
-    ms(T.LTB[:, 0:1], 0.0, "+LTB")
     ms(T.ACC[:, 4:5], 1.0 / 128, "ACC4")
     ms(T.DF2[:, 0:16], 256.0, "DF2c")
     ms(T.SB9[:], 1.0, "SB9")
     ms(T.C16[:], 16.0, "C16")
-    ms(T.P2[:], 0.0, "P2")
     ms(T.FT[0:32, :], 0.5, "FT")
     ms(T.RTB[:], -1.0, "RTB")
     for n in range(0, NXG, 2):
@@ -292,7 +296,7 @@ def rank_program(g, core, T, topo):
     iota(T.PI[:, 0:1], [[1, 1]], 0, 1, "PI")
     sel(T.G16[:], T.ONES[:], [[-16, 8], [0, 16]], A.is_ge, 0.0, 0, 1, "ONES", "G16")
     sel(T.G16[:], T.G16[:], [[16, 8], [0, 16]], A.is_ge, 0.0, 15, -1, "G16", "G16")
-    fiota(T.K16[:], [[0, 8], [1, 16]], 0, 0, "K16", 128)
+    fiota(T.KK[:], [[0, 8], [1, 16]], 0, 0, "KK", 128)
     fiota(T.IOTC[:], [[1, 512]], -256, 0, "IOTC", 512)
     r32 = T.TR[0:32, 0:128]
     sel(r32, r32, [[0, 128 // MP], [-1, MP]], A.not_equal, 0.0, -16, 1, "TR", "TR")
@@ -304,12 +308,14 @@ def rank_program(g, core, T, topo):
     sel(T.SELW[:, 0:128], T.G16[:], [[0, 8], [1, 16]], A.is_equal, 0.0, -15, 0, "G16", "SELW")
     iota(T.LI[:], [[16, 16]], 0, 0, "LI")
     iota(T.BASE[:], [[512, 16]], 8 * MP, 0, "BASE")
-    fiota(T.IDX[:], [[1, 256]], 0, 0, "IDX", 256)
+    fiota(T.IDX[:], [[1, 256]], 32, 0, "IDX", 256)
 
-    tt(T.DF[:], T.pns[:], T.pfs[:], A.subtract, "pfs pns", "DF", 512 * CYC)
-    act(T.SG[:], T.DF[:], "DF", "SG", 256 * CYC, f=AF.Sign)
-    tt(T.HI[:], T.pns[:], T.pfs[:], A.max, "pfs pns", "HI", 512 * CYC)
-    tt(T.LO[:], T.pns[:], T.pfs[:], A.min, "pfs pns", "LO", 512 * CYC)
+    pn = T.PD[:, 0:256]
+    mms([(pn, T.IDENT[:], T.pns[:], True, True)], "IDENT pns", "PD", 256)
+    tt(T.HI[:], pn, T.pfs[:], A.max, "pfs PD", "HI", 256 * CYC)
+    tt(T.LO[:], pn, T.pfs[:], A.min, "pfs PD", "LO", 256 * CYC)
+    tt(T.SG[:], pn, T.pfs[:], A.is_gt, "pfs PD", "SG", 256 * CYC)
+    ts(T.SG[:], T.SG[:], 2.0, -1.0, A.mult, A.add, "SG", "SG", 128 * CYC)
     cp(T.nbU[:], T.nbs[:], "nbs", "nbU")
     cp(T.CBF[:], T.cbs[:], "cbs", "CBF", 512 * CYC)
     cp(T.bsU[:], T.bss[:], "bss", "bsU")
@@ -317,19 +323,17 @@ def rank_program(g, core, T, topo):
     for k in range(4):
         act(wi(0, HCOL[k], HCOL[k] + 64), T.CBF[:].indirect(T.nbU[:, 4 * k:4 * k + 4]), "CBF nbU", "WI0_%d" % k, gat(64))
     for k in range(16):
-        if k < 8:
+        if k < DS:
             act(T.D1[:, 2 * k::32], T.HI[:], "HI", "+D1", 256 * CYC)
         else:
             cp(T.D1[:, 2 * k::32], T.HI[:], "HI", "+D1", 128 * CYC)
         cp(T.D1[:, 2 * k + 1::32], T.LO[:], "LO", "+D1", 128 * CYC)
-    act(T.CS[:], T.CBF[:].indirect(T.bsU[:]), "CBF bsU", "CS", gat(512))
-    act(T.AFL[:], T.CS[:].indirect(T.fsU[:]), "CS fsU", "AFL", gat(256))
     for n in range(8):
         ts(T.WH[:, :, n, :], T.SG[:], T.G16[:, 16 * n:16 * n + 1], -1.0, A.mult, A.mult, "SG G16", "+WH", 128 * CYC)
         ts(T.WA[:, :, n, :], T.SG[:], T.G16[:, 16 * n:16 * n + 1], None, A.mult, None, "SG G16", "+WA", 128 * CYC)
     ts(T.PM[:, 0:1], T.PI[:, 0:1], 15, None, A.bitwise_and, None, "PI", "PM")
     cp(T.PMF[:, 0:1], T.PM[:, 0:1], "PM", "PMF")
-    ts(T.KK[:], T.K16[:], T.PMF[:, 0:1], None, A.is_equal, None, "K16 PMF", "KK")
+    ts(T.KK[:], T.KK[:], T.PMF[:, 0:1], None, A.is_equal, None, "KK PMF", "KK")
     for n, bits in enumerate((4032, 63)):
         ts(T.TH[:, n:n + 1], T.ths[:, 0:1], 1, bits, A.arith_shift_right, A.bitwise_and, "ths", "TH%d" % n)
         ts(T.THN[:, n:n + 1], T.TH[:, n:n + 1], 0.5 * n, -1.0, A.add, A.mult, "TH%d" % n, "THN%d" % n)
@@ -353,60 +357,75 @@ def rank_program(g, core, T, topo):
     fiota(T.YC[:], [[1, 512]], 32, 0, "YC", 512)
     act(T.UF[:].indirect(T.bsU[:]), T.YC[:], "YC bsU", "UF", sca(512) + 1300, f=AF.Silu)
     conv(T.PN[:, 0:16], T.pfs, 0, 16, "pfs", "PN")
-    ts(T.EI1[:], T.PN[:, 0:16], 16.0, None, A.mult, None, "PN", "EI1")
-    ts(T.EI1[:], T.EI1[:], 31, None, A.bitwise_and, None, "EI1", "EI1")
-    tt(T.ELS[:], T.EI1[:], T.BASE[:], A.add, "EI1 BASE", "ELS")
-    act(T.GROW[:], T.UF[:].indirect(T.nbU[:]), "UF nbU", "GROW", gat(256), f=AF.Identity, bias=-288.0)
-    conv(T.PN[:, 16:32], T.GROW, 0, 16, "GROW", "PN")
+    ts(T.ELS[:], T.PN[:, 0:16], 16.0, None, A.mult, None, "PN", "ELS")
+    ts(T.ELS[:], T.ELS[:], 31, None, A.bitwise_and, None, "ELS", "ELS")
+    tt(T.ELS[:], T.ELS[:], T.BASE[:], A.add, "ELS BASE", "ELS")
+    act(T.MROW[:], T.UF[:].indirect(T.nbU[:]), "UF nbU", "MROW", gat(256), f=AF.Identity, bias=-288.0)
+    conv(T.PN[:, 16:32], T.MROW, 0, 16, "MROW", "PN")
     ts(mi(0, 16, 32), T.PN[:, 16:32], 256.0, None, A.add, None, "PN", "+MI0")
     cp(T.PIF[:, 0:1], T.PI[:, 0:1], "PI", "PIF")
     vec(lambda e: e.tensor_tensor_scan(T.PABW[:], T.HALF[:], T.QUART[:], 0.0, A.mult, A.add), "HALF QUART", "PABW", 128 * CYC)
-    vec(lambda e: e.tensor_tensor_scan(T.P2[:, 0:9], T.TWO[:, 0:9], T.QUART[:, 1:10], 0.5, A.mult, A.add), "TWO QUART", "+P2", 0)
-    ts(T.BI1[:, 0:5], T.PABW[:, 0:5], T.PIF[:, 0:1], 1024.0, A.mult, A.mult, "PABW PIF", "BI1")
+    vec(lambda e: e.tensor_tensor_scan(T.P2[:, 0:9], T.TWO[:, 0:9], T.X16[:, 0:9], 0.5, A.mult, A.add), "TWO X16", "P2", 0)
+    ts(T.BI1[:, 0:5], T.PABW[:, 0:5], T.PIF[:, 0:1], 2048.0, A.mult, A.mult, "PABW PIF", "BI1")
     ts(T.BI2[:, 0:5], T.BI1[:, 0:5], 256, None, A.bitwise_and, None, "BI1", "BI2")
     ts(T.SB9[:, 0:4], T.BI2[:, 0:4], -1.0 / 128, 1.0, A.mult, A.add, "BI2", "+SB9")
     ts(T.RTB[:, 4:9], T.BI2[:, 0:5], 1.0 / 128, -1.0, A.mult, A.add, "BI2", "+RTB")
     tt(T.LTB[:, 1:9], T.SB9[:, 1:9], T.P2[:, 1:9], A.mult, "SB9 P2", "+LTB")
     tt(T.LX1[:, 0:1], T.PMF[:, 0:1], T.SB9[:, 0:1], A.add, "PMF SB9", "LX1")
-    mms([(T.PT[0:9, 0:128], T.LTB[:, 0:9], T.IDENT[:], True, True),
-         (T.PT[0:9, 128:160], T.RTB[:, 0:9], T.IDENT[:, 0:32], True, True)], "LTB RTB IDENT", "PT", 160)
-    act(T.LB[0:9, :], T.PT[0:9, 0:128], "PT", "LB", 128 * CYC)
-    act(T.RX[0:9, :], T.PT[0:9, 128:160], "PT", "RX")
+    mms([(T.PT[0:8, 0:128], T.LTB[:, 1:9], T.IDENT[:], True, True),
+         (T.PT[0:8, 128:160], T.RTB[:, 1:9], T.IDENT[:, 0:32], True, True)], "LTB RTB IDENT", "PT", 160)
+    act(T.LB[0:8, :], T.PT[0:8, 0:128], "PT", "LB", 128 * CYC)
+    act(T.RX[0:8, :], T.PT[0:8, 128:160], "PT", "RX")
     act(T.PABX[0:32, :], T.PABW[0:32, :], "PABW", "PABX", 128 * CYC, scale=2.0)
-    for h in range(2):
-        m = T.SBH[0:32, 128 * h:128 * h + 128]
-        sel(m, T.ONES[0:32, :], [[-1, 8], [0, 16]], A.is_equal, 0.0, -8 * h, 1, "ONES", "SBH%d" % h)
-        sel(m, m, [[0, 128]], A.not_equal, 1.0, -16, 1, "SBH%d" % h, "SBH%d" % h)
-        tt(m, m, T.PABX[0:32, :], A.mult, "PABX SBH%d" % h, "+SBH", 256 * CYC)
+    m = T.SBH[0:32, :]
+    sel(m, T.ONES[0:32, :], [[-1, 16], [0, 8]], A.is_equal, 0.0, 0, 1, "ONES", "SBH")
+    sel(m, m, [[0, 128]], A.not_equal, 1.0, -16, 1, "SBH", "SBH")
+    tt(m, m, T.PABX[0:32, :], A.mult, "PABX SBH", "SBH", 256 * CYC)
     ts(T.P2[:, 8:9], T.P2[:, 8:9], -1.0, None, A.mult, None, "P2", "P2")
-    tt(T.P2[:], T.P2[:], T.KK[:, 0:16], A.mult, "P2 KK", "P2")
-    vec(lambda e: e.tensor_reduce(T.C2[:, 0:1], T.P2[:], AxisListType.X, A.add), "P2", "C2a", 0)
+    cp(T.P2[:, 9:17], T.P2[:, 1:9], "P2", "P2")
+    tt(T.P2[:, 1:17], T.P2[:, 1:17], T.KK[:, 0:16], A.mult, "P2 KK", "P2")
+    vec(lambda e: e.tensor_reduce(T.C2[:, 0:1], T.P2[:, 1:17], AxisListType.X, A.add), "P2", "C2a", 0)
     ts(T.C2[:, 1:2], T.C2[:, 0:1], -2.0, None, A.mult, None, "C2a", "C2")
-    ts(T.DD[:, 0:1], T.KK[:, 0:1], -1.0, -1.0, A.mult, A.add, "KK", "DD")
-    ts(T.X8[:], T.G16[:, ::16], T.DD[:, 0:1], 1.0, A.mult, A.add, "G16 DD", "X8")
-    act(T.BROW[:], T.IOTC[:].indirect(T.bsU[:]), "IOTC bsU", "BROW", gat(512))
-    act(T.XB0[:, 0:256], T.BROW[:].indirect(T.fsU[:]), "BROW fsU", "+XB0", gat(256))
+    sel(T.X16[:], T.X16[:], [[-8, 16]], A.is_ge, 1.0, 0, 1, "X16", "X16")
+    sel(T.X16[:], T.X16[:], [[8, 16]], A.is_ge, 1.0, 7, -1, "X16", "X16")
+    brow = T.BZ[:, 512:1024]
+    act(brow, T.IOTC[:].indirect(T.bsU[:]), "IOTC bsU", "BROW4", gat(512))
+    act(T.XB0[:, 0:256], brow.indirect(T.fsU[:]), "BROW4 fsU", "+XB0", gat(256))
+    conv(T.PN[:, 32:48], T.XB0, 0, 16, "XB0", "PN")
+    ts(T.GU[:], T.PN[:, 32:48], 256.0, None, A.add, None, "PN", "GU")
+    act(T.AFL[:], T.CBF[:].indirect(T.GU[:]), "CBF GU", "AFL", gat(256))
     act(T.XB0[:, 256:512], T.IOTC[:].indirect(T.nbU[:]), "IOTC nbU", "+XB0", gat(256))
 
-    ring = {"XG": 0, "CL": 0}
+    ring = {"XG": 0, "CL": 0, "YV": 0}
 
     def slots(name, size, n):
         a = ring[name] if ring[name] + n <= size else 0
         ring[name] = a + n
         return a, " ".join("%s%d" % (name, x) for x in range(a, a + n))
 
+    now = [0]
+
     def early(name, step, *a):
         n = len(calls)
         step(*a)
         for c in calls[n:]:
-            c["early"] = EARLY.get(name, 0)
+            c["early"] = EARLY[now[0] // 4].get(name, 0)
 
     def chunk(q, j, n):
         c = j % 16
         off, key = T[("UH", "UA")[j // 16]], [("UH%d", "UA%d")[j // 16] % ((c + x) // 4) for x in range(n)]
+        a, key = T.xfs[:].indirect(off[:, 16 * c:16 * (c + n)]), "xfs xfsb " + " ".join(key)
+        if q == "V":
+            x, xk = slots("YV", NY, n)
+            s, first = slice(256 * x, 256 * (x + n)), T.YV[:, 256 * x:256 * (x + n):16]
+            tt(T.YV[:, s], a, T.D1[:, 512 * c:512 * (c + n):2], A.min, "D1 " + key, xk, gat(256 * n))
+            tt(first, first, T.LO[:, 16 * c:16 * (c + n)], A.max, "LO " + xk, xk)
+            vec(lambda e: e.tensor_tensor_scan(T.CV[:, s], T.D1[:, 512 * c + 1:512 * (c + n):2], T.YV[:, s], 0.0, A.min, A.max),
+                "D1 " + xk, xk.replace("Y", "C"), 128 * n * CYC)
+            lanes(j, n, xk.replace("Y", "C"), lambda p: T.CV[:, 256 * x + 16 * p:256 * x + 16 * (p + MP)])
+            return
         x, xk = slots("XG", NXG, n)
-        o, a = T.XG[:, 512 * x + 1:512 * (x + n):2], T.xfs[:].indirect(off[:, 16 * c:16 * (c + n)])
-        (cp if q == "V" else act)(o, a, "xfs xfsb " + " ".join(key), xk, gat(256 * n))
+        act(T.XG[:, 512 * x + 1:512 * (x + n):2], a, key, xk, gat(256 * n))
         for u in range(0, n, SCAN):
             clamp(j + u, x + u, min(SCAN, n - u))
 
@@ -416,16 +435,16 @@ def rank_program(g, core, T, topo):
         vec(lambda e: e.tensor_tensor_scan(T.CL[:, 512 * m:512 * (m + n)], T.XG[:, 512 * x:512 * (x + n)],
                                            T.D1[:, 512 * c:512 * (c + n)], 0.0, A.min, A.max),
             "D1 " + " ".join("XG%d" % y for y in range(x, x + n)), mk, 256 * n * CYC)
+        lanes(j, n, mk, lambda p: T.CL[:, 512 * m + 32 * p + 1:512 * m + 32 * (p + MP):2])
+
+    def lanes(j, n, key, block):
+        c = j % 16
         P, w = "PB%d" % (c // 4), ("WH", "WA")[j // 16]
         if j < 16 and c % 4 == 0:
             mms([(T[P][:, 0:CC, :, :], T.TI[0:24, :], T.TR[0:24, 0:128 * CC], True, False)], "TI TR TRb", P, 128 * CC)
-        l = []
-        for u in range(n):
-            for b in range(0, 16, MP):
-                a, s = 512 * (m + u) + 32 * b + 1, slice(b, b + MP)
-                l.append((T[P][part((c + u) % NQ), (c + u) % 4 // NQ, :, s], T.CL[:, a:a + 32 * MP - 1:2], T[w][:, c + u, :, s], False,
-                          j >= 16 and (c + u) % 4 >= 4 - NQ and b + MP == 16))
-        mms(l, mk + " " + w, P, n * (256 if MP < 8 else 128))
+        mms([(T[P][part((c + u) % NQ), (c + u) % 4 // NQ, :, b:b + MP], block(16 * u + b), T[w][:, c + u, :, b:b + MP], False,
+              j >= 16 and (c + u) % 4 >= 4 - NQ and b + MP == 16) for u in range(n) for b in range(0, 16, MP)],
+            key + " " + w, P, n * (256 if MP < 8 else 128))
 
     def signs(k):
         P, z = "PB%d" % k, "Z%d" % k
@@ -443,20 +462,18 @@ def rank_program(g, core, T, topo):
     def turned(t, k):
         P, z, s = "PB%d" % k, "Z%d" % k, slice(64 * k, 64 * k + 64)
         for n, e in enumerate(("EUW", "ESW")):
-            mms([(T[P][32 * (x // 2):32 * (x // 2) + 32, n, q:4:NQ, :], T[e][:, 48 * q + 16 - 16 * (x % 2):48 * q + 48 - 16 * (x % 2)],
-                  T.Z[:, CC * k:CC * k + CC, x, :], x % 2 == 0, x % 2 == 1) for q in range(NQ) for x in range(8)],
-                z + " " + e, P, 8 * NQ * max(32, 16 * CC))
-        act(T.AB[:, s], T[P][:, 0, 0:4, :], P, "AB%d" % k, f=AF.Abs if t < 4 else AF.Identity, bias=48.0 * MP - 41)
-        act(T.TROW[:, s], T[P][:, 1, 0:4, :], P, "TROW%d" % k, f=AF.Relu, scale=-1024.0, bias=17408.0 - 16384 * MP)
-        x = T[P][:, 2, 0:4, :]
-        mms([(x, T.IDENT[:], T.TROW[:, s], True, False), (x, T.IDENT[:], T.IDX[:, s], False, True)], "IDENT IDX TROW%d" % k, P, 128)
-        act(T.XF[:, s], x, P, "XF%d" % k, f=AF.Identity, bias=32.0)
+            mms([(T[P][:, 1, 0:4, :], T.G16[:], T.CX[:], True, False)][:n]
+                + [(T[P][32 * (x // 2):32 * (x // 2) + 32, n, q:4:NQ, :], T[e][:, 48 * q + 16 - 16 * (x % 2):48 * q + 48 - 16 * (x % 2)],
+                    T.Z[:, CC * k:CC * k + CC, x, :], x % 2 == 0 and not n, x % 2 == 1 and (not n or q == NQ - 1))
+                   for q in range(NQ) for x in range(8)], z + " G16 CX " + e, P, 8 * NQ * max(32, 16 * CC) + 64 * n)
+        act(T.AB[:, s], T[P][:, 0, 0:4, :], P, "AB%d" % k, f=AF.Abs if t < 4 else AF.Sign, bias=48.0 * MP - 41)
+        tt(T.XF[:, s], T[P][:, 1, 0:4, :], T.IDX[:, s], A.max, P + " IDX", "XF%d" % k)
 
     def rows(t, k):
         P, s, hk = "PD", slice(64 * k, 64 * k + 64), "WI%d_%d" % (t, k)
         p, h = T.PD[:, s], wi(t, HCOL[k], HCOL[k] + 64)
-        ts(T.MM[:, s], T.AB[:, s], 32.0 if t < 4 else 0.0, None, A.is_gt, None, "AB%d" % k, "MM%d" % k)
         if t < 4:
+            ts(T.MM[:, s], T.AB[:, s], 32.0, None, A.is_gt, None, "AB%d" % k, "MM%d" % k)
             tt(p, p, T.MM[:, s], A.mult, "PD MM%d" % k, "pd%d" % k)
             tt(wo(t, HCOL[k], HCOL[k] + 64), h, p, A.subtract, "PD pd%d %s" % (k, hk), "WO%dh%d" % (t, k))
             tt(wo(t, ACOL + 64 * k, ACOL + 64 + 64 * k), p, T.AFL[:, s], A.add, "PD pd%d AFL" % k, "WO%da%d" % (t, k))
@@ -464,6 +481,7 @@ def rank_program(g, core, T, topo):
             send(1, wi(t + 1, a, b), wo(t, a, b), " ".join("WO%d%s" % (t, x) for x in keys.split()), "WI%d_%d" % (t + 1, k),
                  "a%d_%d" % (k, t + 1), b - a)
         else:
+            act(T.MM[:, s], T.AB[:, s], "AB%d" % k, "MM%d" % k, f=AF.Relu)
             tt(T.PS[:, s], p, T.MM[:, s], A.mult, P + " MM%d" % k, "PS%d" % k)
             tt(T.YC[:].indirect(T.YL[:, 4 * k:4 * k + 4]), T.AFL[:, s], T.PS[:, s], A.add, "AFL YL PS%d" % k, "YC", sca(64))
             tt(T.YC[:].indirect(T.YL[:, 16 + 4 * k:20 + 4 * k]), h, T.PS[:, s], A.subtract, "YL PS%d %s" % (k, hk), "YC", sca(64))
@@ -499,27 +517,28 @@ def rank_program(g, core, T, topo):
         fiota(T.UF[:], [[0, 512]], 1056, 0, "UF", 512)
 
     def bits(t):
-        ts(T.FB[:], mi(t, 32, 48), -256.0, None, A.add, None, "MI%d" % t, "FB")
+        ts(T.BI1[:], mi(t, 32, 48), 510, None, A.bitwise_and, None, "MI%d" % t, "BI1")
+        ts(T.BI2[:], T.BI1[:], 2.0, -255.0, A.mult, A.add, "BI1", "BI2")
+        tt(T.FB[:], T.BI2[:], mi(t, 32, 48), A.subtract, "BI2 MI%d" % t, "FB")
         mms([(T.PN[0:16, 128:256], T.FB[:], T.IDENT[:], True, True)], "FB IDENT", "PN", 128)
         act(T.FT[0:16, :], T.PN[0:16, 128:256], "PN", "+FT", 128 * CYC)
-        mms([(T.PN[:, 256 + 128 * h:384 + 128 * h], T.SBH[0:17, 128 * h:128 * h + 128], T.FT[0:17, :], True, True) for h in range(2)],
-            "SBH FT", "PN", 256)
-        cp(T.RB[:], T.PN[:, 256:512], "PN", "RB", 256 * CYC)
-        tt(T.BT[:], T.PN[:, 256:512], T.RB[:], A.is_lt, "PN RB", "BT", 256 * CYC)
-        ts(T.BT[:], T.BT[:], T.C2[:, 1:2], T.C2[:, 0:1], A.mult, A.add, "BT C2", "BT", 128 * CYC)
+        mms([(T.PN[:, 256:384], T.SBH[0:17, :], T.FT[0:17, :], True, True)], "SBH FT", "PN", 128)
+        cp(T.RB[:], T.PN[:, 256:384], "PN", "RB", 128 * CYC)
+        tt(T.BT[:], T.PN[:, 256:384], T.RB[:], A.is_lt, "PN RB", "BT", 128 * CYC)
+        ts(T.BT[:], T.BT[:], T.C2[:, 1:2], T.C2[:, 0:1], A.mult, A.add, "BT C2", "BT")
 
     def xor(t):
         y = T.PT[:, 0:1]
         cp(T.RI[:, 0:1], y, "PT", "RI")
         tt(T.DD[:, 0:1], y, T.RI[:, 0:1], A.subtract, "PT RI", "DD")
         if t < 4:
-            ts(T.RS[:, 0:8], T.X8[:], T.DD[:, 0:1], 0.0, A.add, A.is_lt, "X8 DD", "RS")
-            mms([(T.PT[:, 16:32], T.IDENT[:], T.FB[:], True, False), (T.PT[:, 16:24], T.BT[:, 0:128], T.RS[:, 0:8], False, False),
-                 (T.PT[:, 24:32], T.BT[:, 128:256], T.RS[:, 0:8], False, True)], "IDENT FB BT RS", "PT", 192)
+            ts(T.RS[:, 0:16], T.X16[:], T.DD[:, 0:1], 0.0, A.add, A.is_lt, "X16 DD", "RS")
+            mms([(T.PT[:, 16:32], T.IDENT[:], T.FB[:], True, False), (T.PT[:, 16:32], T.BT[:], T.RS[:, 0:16], False, True)],
+                "IDENT FB BT RS", "PT", 128)
             ts(T.XLU[:, 0:16], T.PT[:, 16:32], 256.0, None, A.add, None, "PT", "XLU")
         else:
-            ts(T.RS[0:9, :], T.RX[0:9, :], T.DD[0:9, 0:1], 0.0, A.mult, A.is_gt, "RX DD", "RS")
-            mms([(T.PT[:, 128:160], T.LB[0:9, :], T.RS[0:9, :], True, True)], "LB RS", "PT", 64)
+            ts(T.RS[0:8, :], T.RX[0:8, :], T.DD[0:8, 0:1], 0.0, A.mult, A.is_gt, "RX DD", "RS")
+            mms([(T.PT[:, 128:160], T.LB[0:8, :], T.RS[0:8, :], True, True)], "LB RS", "PT", 64)
             ts(T.XLU[:], T.PT[:, 128:160], T.LX1[:, 0:1], None, A.add, None, "PT LX1", "XLU")
 
     def turns(t):
@@ -557,17 +576,18 @@ def rank_program(g, core, T, topo):
         ts(T.YL32[:], T.PN[:, 32:64], 256.0, None, A.add, None, "PN", "YL32")
         cp(T.GU[:], mi(4, 16, 32), "MI4", "GU")
         tt(T.DA[:], T.YL32[:, 0:16], T.YL32[:, 16:32], A.subtract, "YL32", "DA")
-        cp(T.BROW4[:].indirect(fa(4, 0, 16)), T.XB0[:, 0:256], "XB0 FA0", "BROW4", sca(256))
-        cp(T.BROW4[:].indirect(T.GU[:]), T.XB0[:, 256:512], "XB0 GU", "BROW4", sca(256))
-        conv(T.PN[:, 64:96], T.BROW4, 0, 32, "BROW4", "PN")
+        cp(brow.indirect(fa(4, 0, 16)), T.XB0[:, 0:256], "XB0 FA0", "BROW4", sca(256))
+        cp(brow.indirect(T.GU[:]), T.XB0[:, 256:512], "XB0 GU", "BROW4", sca(256))
+        conv(T.PN[:, 64:96], T.BZ, 512, 32, "BROW4", "PN")
         ts(T.BL[:], T.PN[:, 64:96], 256.0, None, A.add, None, "PN", "BL")
 
     for t in range(5):
+        now[0] = t
         take(t)
         if t:
-            boxes(t - 1)
+            early("boxes", boxes, t - 1)
         if t == 4:
-            box_lists()
+            early("boxes", box_lists)
         j = 0
         for w in PLAN[t // 4].split():
             chunk(w[0], j, int(w[1:]))
@@ -594,21 +614,20 @@ def rank_program(g, core, T, topo):
             early("alpha", alpha, t)
 
     dma("D", T.yc[:], T.YC[:], "YC", "yc", "o_yc", 3000)
-    conv(T.PT[:, 0:32], T.BROW4, 0, 32, "BROW4", "PT", sp=False, tab="NSELW")
-    act(T.CS[:], T.UF[:], "UF", "CS", 512 * CYC)
-    tt(T.U[:, 0:512], T.UF[:].indirect(T.XLU[:]), T.CS[:], A.add, "UF CS XLU", "U1", gat(640))
-    act(T.U[:, 512:1024], T.BROW4[:].indirect(T.XLU[:]), "BROW4 XLU", "U2", gat(512))
-    conv(T.PT[:, 0:32], T.U, 512, 32, "U2", "PT", st=False)
-    conv(T.PN[:, 0:32], T.U, 0, 32, "U1", "PN")
+    act(T.BZ[:, 0:512], T.UF[:], "UF", "U0", 512 * CYC, scale=-1.0)
+    conv(T.PN[:, 0:64], T.BZ, 0, 64, "U0 BROW4", "PN", sp=False, tab="NSELW")
+    cp(T.U[:, 0:512], T.UF[:].indirect(T.XLU[:]), "UF XLU", "U1", gat(512))
+    act(T.U[:, 512:1024], brow.indirect(T.XLU[:]), "BROW4 XLU", "U2", gat(512))
+    conv(T.PN[:, 0:64], T.U, 0, 64, "U1 U2", "PN", st=False)
     ts(T.B1[:], T.PN[:, 0:32], 800.0, None, A.is_lt, None, "PN", "B1")
-    tt(T.B1[:], T.PT[:, 0:32], T.B1[:], A.mult, "PT B1", "B1")
-    tt(T.YB[:], T.BL[:], T.B1[:], A.add, "BL B1", "YB")
-    dma("S", T.yb[:], T.YB[:], "YB", "yb", "o_yb")
+    tt(T.B1[:], T.PN[:, 32:64], T.B1[:], A.mult, "PN B1", "B1")
+    tt(T.BL[:], T.BL[:], T.B1[:], A.add, "BL B1", "BL")
+    dma("S", T.yb[:], T.BL[:], "BL", "yb", "o_yb")
     tt(T.YF[:], mi(4, 32, 48), T.XX[:, 16:32], A.add, "MI4 XX", "YF")
     dma("D", T.yf[:], T.YF[:], "YF", "yf", "o_yf")
     tt(T.DA[:], T.DA[:], T.TRN[:, 0:16], A.mult, "DA TRN", "DA")
-    tt(T.YN[:], T.DA[:], T.YL32[:, 16:32], A.add, "DA YL32", "YN")
-    dma("S", T.yn[:], T.YN[:], "YN", "yn", "o_yn")
+    tt(T.DA[:], T.DA[:], T.YL32[:, 16:32], A.add, "DA YL32", "DA")
+    dma("S", T.yn[:], T.DA[:], "DA", "yn", "o_yn")
     emit()
     for n in ("yc", "yb", "yf", "yn"):
         g.wait_ge(T.sem["o_" + n], 16)

@@ -1,21 +1,26 @@
+import numpy as np
 from concourse.mybir import AluOpType as A, AxisListType, ActivationFunctionType as AF
 
-NXG, NCL = 10, 8
+NXG, NCL, NY = 12, 12, 8
 SCAN = 2
 MP = 4
 NQ, CC = 8 // MP, MP // 2
-PLAN = ("S1 V1 S2 V2 S2 S4 S4 V2 S2 V2 S2 S4 S2 V1 S1", "V2 S2 S2 V2 S4 S4 V2 S2 S4 S4 S2 V1 S1")
-NY = 6
-DS = 8
-EARLY = ({}, {})
+PLAN = ("S1 V1 S2 V2 S2 S4 V1 S3 V2 S2 S2 V2 S2 S2 S2 S1 V1", "V2 S2 S2 V2 S4 S4 V2 S2 S4 S4 S2 V1 S1")
+DS, WS = 8, 6
 FLAGS = ((0, 8), (8, 12), (12, 16))
 OFFS = ((0, 12), (12, 16))
 HCOL, ACOL = (64, 128, 0, 448), 192
-SENDS = ((64, 128, "h0"), (128, 320, "h1 a0 a1"), (0, 64, "h2"), (320, 512, "a2 a3 h3"))
-CYC, GAT, SCA, PEC, HOP, FAR = 0.83, 1.3, 3.2, 0.47, 175, 2200
-XF, COL = 9100, 6.4
-PASSES = 800
+SENDS = ((64, 128, "h0"), (128, 320, "h1 a0 a1"), (0, 64, "h2"), (320, 592, "a2 a3 h3 l"))
+MAGIC = 1.5 * 2 ** 23
+MODELS = ((0.83, 1.3, 3.2, 0.45, 215, 300, 1400, 8, 4.5), (1.1, 2.0, 4.6, 0.6, 240, 400, 2000, 12, 5.5),
+          (0.9, 1.15, 2.6, 0.49, 230, 550, 2300, 14, 6.0))
+CYC, GAT, SCA, PEC, HOP, ISSUE, FAR, ROW, COL = np.array(MODELS).T
+XF, FIRST = 9100, 2800
+MARK = "SPB|Z ACC"
+STARTS, PASSES, SHORT, LONG = 6, 50, 30, 380
+WIDE, PATIENCE, REACH, FREE, TENURE, SEED = 110, 60, 10, 600, 10, 1
 ORDER = []
+INFO = []
 FL, BF, I32, U16 = "float32", "bfloat16", "int32", "uint16"
 
 
@@ -28,58 +33,49 @@ def _scratch():
     sb("xfs D1", 8192, BF)
     sb("XG", 512 * NXG, BF)
     sb("CL", 512 * NCL, BF)
-    for n in ("WH", "WA"):
-        s[n] = ("sbuf", [128, 16, 8, 16], BF)
     sb("YV CV", 256 * NY, BF)
+    for n in ("WH", "WA", "SELB"):
+        s[n] = ("sbuf", [128, 16, 8, 16], BF)
     s["Z"] = ("sbuf", [128, 4 * CC, 8, 16], BF)
-    sb("pfs pns LO HI SG AB MM MROW", 256, BF)
-    sb("IDX", 256, FL)
-    sb("CX", 64, BF)
-    sb("cbs", 512, I32)
-    sb("CBF YC UF", 512, FL)
-    sb("AFL PS XF", 256, FL)
-    sb("WI WO", 512 * 5, FL)
-    sb("MI", 64 * 5, I32)
-    sb("MO", 80 * 4, I32)
-    sb("HM", 32 * 4, I32)
-    sb("bss", 32, I32)
-    sb("fss nbs OI1 OI2 BASE LI ELS AL BI1 BI2", 16, I32)
-    sb("ths TH PI PM RI", 2, I32)
-    sb("IDF NIDF", 128, FL)
-    sb("THN PMF PIF DD LX1", 2, FL)
-    sb("ACC", 8, FL)
-    sb("ONES IDENT G16 KK TI LB", 128, BF)
-    sb("SELW NSELW", 144, BF)
-    sb("EUW ESW", 48 * NQ, BF)
-    sb("TR IOTC XB0 XB1", 512, BF)
+    s["LO8"] = ("sbuf", [128, 8, 16], BF)
     sb("BZ", 1024, BF)
-    sb("LL", 24, BF)
-    sb("QS", 2 * NQ, BF)
-    sb("TWO OWN", 16, FL)
-    sb("HALF QUART", 128, FL)
-    sb("C16", 16, BF)
-    sb("TM", 128, BF)
-    sb("LTB RTB SB9", 16, BF)
+    sb("TR IOTC XB0 U", 512, BF)
+    sb("pfs pns LO HI SG AB MM MROW", 256, BF)
+    sb("SELW SELW2 SELW3", 144, BF)
+    sb("ONES IDENT I256 HB NHB G16 KK TI LB TM FT PABX BT SBH RB", 128, BF)
+    sb("BB", 96, BF)
+    sb("EUW", 48 * NQ, BF)
+    sb("C16", 64, BF)
     sb("RS RX", 32, BF)
+    sb("LL", 24, BF)
+    sb("P2", 18, BF)
+    sb("NF THR LTB RTB SB9 X16", 16, BF)
+    sb("QS", 6 * NQ, BF)
+    sb("WI WO", 608 * 5, FL)
+    sb("UF", 1536, FL)
+    sb("AFL", 256 * 5, FL)
+    sb("CBF YC", 512, FL)
+    sb("IDX PS", 256, FL)
+    sb("IDF NIDF HALF QUART PABW", 128, FL)
+    sb("XX TRN", 96, FL)
+    sb("YL32 BL B1", 32, FL)
+    sb("LI TWO", 16, FL)
+    sb("BC G8 ACC", 8, FL)
+    sb("THN PMF PIF DD LX1 C2", 2, FL)
+    sb("cbs", 512, I32)
+    sb("MA", 32 * 5, I32)
+    sb("DM", 32 * 4, I32)
+    sb("bss BI0 BI1 BI2 AL32", 32, I32)
+    sb("fss nbs OI1 OI2 BASE ELS AL", 16, I32)
+    sb("ths TH PI PM RI", 2, I32)
     sb("UH UA", 256, U16)
-    sb("bsU XLU XLS YL", 32, U16)
-    sb("FA", 64, U16)
-    sb("fsU nbU OFFU GU", 16, U16)
-    sb("LIF DA YF", 16, FL)
-    sb("TRN DF2 XX YL32 BL B1", 32, FL)
-    sb("U", 1024, BF)
+    sb("bsU XLU YL", 32, U16)
+    sb("fsU nbU OFFU GU FU ALU", 16, U16)
     for n in ("PB0", "PB1", "PB2", "PB3"):
         s[n] = ("psum", [128, 4, 8, 16], FL)
-    sb("FB", 16, BF)
-    sb("X16", 16, BF)
-    sb("P2", 18, BF)
-    sb("FT PABX BT SBH", 128, BF)
-    sb("RB", 128, I32)
-    sb("PABW", 128, FL)
-    sb("C2", 2, FL)
     for n in ("PT", "PD", "PN"):
         s[n] = ("psum", [128, 512], FL)
-    s["PL"] = ("psum", [128, 2, 256], FL)
+    s["PL"] = ("psum", [128, 8, 64], FL)
     return s
 
 
@@ -87,43 +83,237 @@ SCRATCH = _scratch()
 BANKS = ("PB0", "PB1", "PB2", "PB3", "PT", "PD", "PL", "PN")
 LOADS = ["pf", "pn", "fs", "bs", "nb", "th", "cb", "xf"]
 SEMAPHORES = (["qV", "qS", "qP", "qG", "loc"] + ["d_" + n for n in LOADS] + ["o_yc", "o_yb", "o_yf", "o_yn"]
-              + ["a%d_%d" % (k, t) for k in range(6) for t in range(1, 5)] + ["ah1", "ah2", "ah3"])
+              + ["a%s_%d" % (k, t) for k in list(range(len(SENDS))) + ["m"] for t in range(1, 5)])
 
 
 def issue_order(calls):
     if ORDER:
         return ORDER
-    n = len(calls)
-    qs, ns, late = [[c[k] for c in calls] for k in ("q", "ns", "late")]
-    pre, post = [[] for _ in range(n)], [[] for _ in range(n)]
+    n, K, first = len(calls), len(MODELS), len(LOADS)
+    qn = ["VSPGD".index(c["q"]) for c in calls]
+    NS, LATE, DUR = [np.array([c[k] + 0 * CYC for c in calls]).T for k in ("ns", "late", "far")]
+    NS, LATE = np.maximum(NS, DUR), LATE + np.minimum(NS, DUR)
+    reach, waited, need, serve = [0] * n, [0] * n, [], [[] for _ in range(n)]
     for j, c in enumerate(calls):
+        soft = {i for i in c["pre"] if qn[i] == qn[j] == 2}
         for i in c["pre"]:
-            gap = 0 if qs[i] == qs[j] == "P" else late[i]
-            pre[j].append((i, gap))
-            post[i].append((j, gap))
+            reach[j] |= reach[i]
+            waited[j] |= waited[i] if i in soft else reach[i]
+        need.append([i for i in c["pre"] if not (reach[j] if i in soft else waited[j]) >> i & 1])
+        for i in c["pre"]:
+            reach[j] |= 1 << i
+            waited[j] |= (i not in soft) << i
+        for i in need[j]:
+            serve[i].append(j)
+    sets = []
+    for ns, late in list(zip(NS.tolist(), LATE.tolist())) + [(NS.mean(0).tolist(), LATE.mean(0).tolist())]:
+        sets.append((ns, [[(i, 0.0 if qn[i] == qn[j] == 2 else late[i]) for i in need[j]] for j in range(n)],
+                     [[(j, 0.0 if qn[i] == qn[j] == 2 else late[i]) for j in serve[i]] for i in range(n)],
+                     [0.0 if serve[i] else late[i] for i in range(n)]))
+    names = sorted({c["name"][1:] for c in calls})
+    twin = {c["name"]: i for i, c in enumerate(calls)}
+    marks = [twin[t, MARK, 0] for t in range(5)]
+    seed = [SEED]
+
+    def draw(m):
+        seed[0] = (seed[0] * 1103515245 + 12345) % 2 ** 31
+        return (seed[0] >> 8) % m
 
     def walk(before, behind, urgent, start, look):
-        left = [len(b) for b in before]
-        ready = {q: {i: start[i] for i in range(n) if qs[i] == q and not left[i]} for q in "VSPGD"}
-        free, end, order = dict.fromkeys(ready, 0.0), [0.0] * n, []
+        ns, left = sets[K][0], [len(b) for b in before]
+        ready = [{i: start[i] for i in range(n) if qn[i] == q and not left[i]} for q in range(5)]
+        free, end, order = [0.0] * 5, [0.0] * n, []
         for _ in range(n):
-            t1, q = min((max(r, free[q]) + look * ns[i], q) for q in ready for i, r in ready[q].items())
+            t1, q = min((max(r, free[q]) + look * ns[i], q) for q in range(5) for i, r in ready[q].items())
             i = max((i for i, r in ready[q].items() if r <= t1), key=lambda i: urgent[i])
             end[i] = free[q] = max(free[q], ready[q].pop(i)) + ns[i]
             order.append(i)
             for j, _g in behind[i]:
                 left[j] -= 1
                 if not left[j]:
-                    ready[qs[j]][j] = max(end[p] + gap for p, gap in before[j])
+                    ready[qn[j]][j] = max(end[p] + gap for p, gap in before[j])
         return end, order
-    end, now, best = list(range(n)), 1e18, 1e18
-    for k in range(PASSES):
-        back, _o = walk(post, pre, end, late, 0.1 + 0.8 * (0.618 * k % 1))
-        new, order = walk(pre, post, [1e18 - 1e3 * i if i < len(LOADS) else back[i] for i in range(n)], [0.0] * n, 0.1 + 0.8 * (0.414 * k % 1))
-        if max(new) < now + 2 * HOP:
-            end, now = new, max(new)
-        if max(new) < best:
-            best, ORDER[:] = max(new), order
+
+    def fresh():
+        _n, pre, post, last = sets[K]
+        end, now, best, keep = list(range(n)), 1e18, 1e18, None
+        for _ in range(PASSES):
+            back, _o = walk(post, pre, end, last, 0.1 + 0.0008 * draw(1000))
+            push = {x: draw(1200) - 600 for x in names if not draw(20)}
+            new, order = walk(pre, post, [1e18 - 1e3 * i if i < first else back[i] + push.get(calls[i]["name"][1:], 0) for i in range(n)],
+                              [0.0] * n, 0.1 + 0.0008 * draw(1000))
+            if max(new) < now + 500:
+                end, now = new, max(new)
+            if max(new) < best:
+                best, keep = max(new), order
+        return keep
+
+    def sweep(part, free, links, base, ns, out, ready):
+        for i in part:
+            t = base[i]
+            for x, gap in links[i]:
+                if out[x] + gap > t:
+                    t = out[x] + gap
+            ready[i] = t
+            q = qn[i]
+            if free[q] > t:
+                t = free[q]
+            out[i] = free[q] = t + ns[i]
+
+    zero = [0.0] * n
+
+    def look(order):
+        got = []
+        for ns, pre, post, last in sets[:K]:
+            fin, rd, tail, qd = zero[:], zero[:], zero[:], zero[:]
+            sweep(order, [0.0] * 5, pre, zero, ns, fin, rd)
+            sweep(order[::-1], [0.0] * 5, post, last, ns, tail, qd)
+            got.append((fin, rd, tail, qd))
+        return got
+
+    def price(got):
+        return sum(max(x[2]) * s for x, s in zip(got, scale))
+
+    def starts(got):
+        return [f - x for f, x in zip(got[0][0], sets[0][0])]
+
+    def repeat(other, start, b, to):
+        lo, hi, lo2, hi2 = [0 if x < 0 else s[marks[x]] if x < 5 else 1e9 for s, x in ((other, b), (other, b + 1), (start, to), (start, to + 1))]
+        due = []
+        for i, c in enumerate(calls):
+            x = twin.get((c["name"][0] - to + b,) + c["name"][1:]) if b != to else i
+            if (c["name"][0] >= 0 or b == to) and i >= first and x is not None and (lo <= other[x] < hi or lo2 <= start[i] < hi2):
+                due.append(other[x] - lo + lo2)
+            else:
+                due.append(i - 1e9 if i < first else start[i] - (hi2 - lo2 - hi + lo) * min(1, max(0, (start[i] - lo2) / (hi2 - lo2))))
+        left, order = [len(x) for x in need], []
+        ready = [i for i in range(n) if not left[i]]
+        while ready:
+            i = min(ready, key=lambda i: due[i])
+            ready.remove(i)
+            order.append(i)
+            for j in serve[i]:
+                left[j] -= 1
+                if not left[j]:
+                    ready.append(j)
+        return order
+
+    def stretch(order, got, a0):
+        win, head, rest = order[a0:a0 + WIDE], order[:a0], order[a0 + WIDE:]
+        inside, before, after, past = set(win), [], [], []
+        for (fin, rd, tail, qd), (ns, pre, post, last) in zip(got, sets):
+            before.append([max([fin[i] for i in head[-200:] if qn[i] == q], default=0.0) for q in range(5)])
+            after.append([max([tail[i] for i in rest[:200] if qn[i] == q], default=0.0) for q in range(5)])
+            past.append(max([fin[i] + gap + tail[j] for i in head for j, gap in post[i] if j not in inside and tail[j] < tail[win[0]]]
+                            + [x + y for x, y in zip(before[-1], after[-1])], default=0.0))
+
+        def ends():
+            return [max(past[k], max(got[k][0][i] - sets[k][0][i] + got[k][2][i] for i in win)) for k in range(K)]
+        end, tabu, since, step = ends(), {}, 0, 0
+        best, keep = sum(x * s for x, s in zip(end, scale)), win
+        while since < PATIENCE:
+            since, step = since + 1, step + 1
+            line, at = [[] for _ in range(5)], {}
+            for i in win:
+                at[i] = len(line[qn[i]])
+                line[qn[i]].append(i)
+            k = draw(K)
+            (fin, rd, tail, qd), p, moves = got[k], sets[k][0], set()
+            for q in line:
+                run = []
+                for i in q + [None]:
+                    on = i is not None and fin[i] - p[i] + tail[i] > end[k] - 1e-6
+                    if on and (not run or fin[run[-1]] > fin[i] - p[i] - 1e-6):
+                        run.append(i)
+                        continue
+                    for d in range(1, min(len(run), REACH)):
+                        moves.update(((run[0], run[d], 1), (run[0], run[d], 0), (run[-1 - d], run[-1], 1), (run[-1 - d], run[-1], 0)))
+                    run = [i] if on else []
+            rated = []
+            for u, v, fore in sorted(moves):
+                q = line[qn[u]]
+                seg = q[at[u]:at[v] + 1]
+                if fore:
+                    seg = [v] + seg[:-1]
+                    if rd[v] > fin[u] + p[v] + FREE or any(reach[v] >> x & 1 for x in seg):
+                        continue
+                    bad = any(tabu.get((v, x), 0) > step for x in seg)
+                else:
+                    seg = seg[1:] + [u]
+                    if qd[u] > tail[v] + p[u] + FREE or any(reach[x] >> u & 1 for x in seg):
+                        continue
+                    bad = any(tabu.get((x, u), 0) > step for x in seg)
+                c = 0.0
+                for m in range(K):
+                    (f, r, w, s), pm, e = got[m], sets[m][0], end[m]
+                    t, top, on, heads = f[q[at[u] - 1]] if at[u] else before[m][qn[u]], 0.0, False, []
+                    for x in seg:
+                        t = max(t, r[x])
+                        heads.append(t)
+                        t += pm[x]
+                        on = on or f[x] - pm[x] + w[x] > e - 1e-6
+                    t = w[q[at[v] + 1]] if at[v] + 1 < len(q) else after[m][qn[u]]
+                    for x, h in zip(seg[::-1], heads[::-1]):
+                        t = max(t, s[x]) + pm[x]
+                        top = max(top, h + t)
+                    c += scale[m] * max(top, past[m] if on else e)
+                if not bad or c < best:
+                    rated.append((c + draw(1000) * 3e-7, u, v, fore))
+            for c, u, v, fore in sorted(rated):
+                a, b = win.index(u), win.index(v)
+                mid, go, held = win[a:b + 1], {v if fore else u}, set()
+                for x in mid[-2::-1] if fore else mid[1:]:
+                    if qn[x] in held or any(y in go for y in (serve if fore else need)[x]):
+                        go.add(x)
+                        held.add(qn[x])
+                if qn[u] in held:
+                    continue
+                stay, go = [x for x in mid if x not in go], [x for x in mid if x in go]
+                for x in stay:
+                    if qn[x] == qn[u]:
+                        tabu[(x, v) if fore else (u, x)] = step + TENURE + draw(TENURE)
+                win = win[:a] + (go + stay if fore else stay + go) + win[b + 1:]
+                for m in range(K):
+                    (f, r, w, s), (ns, pre, post, last) = got[m], sets[m]
+                    sweep(win, before[m][:], pre, zero, ns, f, r)
+                    sweep(win[::-1], after[m][:], post, last, ns, w, s)
+                break
+            else:
+                break
+            end = ends()
+            c = sum(x * s for x, s in zip(end, scale))
+            if c < best - 1e-9:
+                best, keep, since = c, win, 0
+        return head + keep + rest
+
+    def better(order, count, others):
+        got = look(order)
+        cost = price(got)
+        for step in range(count):
+            tries = [(None, 1, 2), (None, 1, 0), (None, 1, 3), (None, 2, 1)] if step % 8 == 7 else []
+            if step == 0:
+                tries = [(x, b, to) for x in others for to in range(-1, 5) for b in ({to, 1, 2} if 0 <= to < 4 else {to})]
+            for other, b, to in tries:
+                new = repeat(other or starts(got), starts(got), b, to)
+                g2 = look(new)
+                if price(g2) <= cost:
+                    order, got, cost = new, g2, price(g2)
+            start = starts(got)
+            order = sorted(order, key=lambda i: start[i] if i >= first else -1)
+            at = [first] + [order.index(x) for x in marks] + [n]
+            lo, hi = ((2, 3), (2, 3), (0, 2), (4, 6))[draw(4)]
+            new = stretch(order, got, max(first, min(n - WIDE, at[lo] + draw(at[hi] - at[lo]) - WIDE // 2)))
+            got = look(new)
+            if price(got) <= cost:
+                order, cost = new, price(got)
+            else:
+                got = look(order)
+        return cost, order, starts(got)
+    some = [fresh() for _ in range(STARTS)]
+    scale = [1.0 / max(x[2]) for x in look(some[0])]
+    some = sorted(better(x, SHORT, []) for x in some)
+    cost, ORDER[:], _s = better(some[0][1], LONG, [x[2] for x in some])
+    INFO.extend([cost] + [round(max(x[2])) for x in look(ORDER)] + [round(x[0], 4) for x in some])
     return ORDER
 
 
@@ -133,10 +323,12 @@ def rank_program(g, core, T, topo):
         return
     N = len(T.cores)
     Q = {"V": g.vector, "S": g.scalar, "P": g.tensor, "G": g, "D": g.sync}
-    calls = []
+    calls, count, now = [], {}, [-1]
     whole, parts, rd = {}, {}, {}
 
-    def record(q, fns, R, W, ns, late=HOP, tok=None, far=False):
+    def record(q, fns, R, W, ns, late=HOP, tok=None, far=0):
+        name = (now[0], q + "".join(x for x in R + "|" + W if not x.isdigit()))
+        count[name] = count.get(name, -1) + 1
         R, W, pre = R.split(), W.split(), set()
         for k in R:
             pre.update(parts.get(k, []))
@@ -146,7 +338,7 @@ def rank_program(g, core, T, topo):
             pre.update(parts.get(k, []) if k[0] != "+" else whole.get(k[1:], []))
             pre.update(rd.get(k.lstrip("+"), []))
         i = len(calls)
-        calls.append({"q": q, "fns": fns, "pre": pre, "ns": ns, "late": late, "tok": tok, "far": far})
+        calls.append({"q": q, "fns": fns, "pre": pre, "ns": ns, "late": late, "tok": tok, "far": far, "name": name + (count[name],)})
         for k in R:
             rd.setdefault(k, []).append(i)
         for k in W:
@@ -180,7 +372,7 @@ def rank_program(g, core, T, topo):
                     fn(Q[q]).then_inc(T.sem["q" + q], 1)
                     cnt[q] += 1
             tok[i] = c["tok"] or ("q" + q, cnt[q])
-            if not c["far"]:
+            if not np.any(c["far"]):
                 snap[tok[i]] = dict(seen[q])
         for q in cnt:
             g.wait_ge(T.sem["q" + q], cnt[q])
@@ -190,15 +382,15 @@ def rank_program(g, core, T, topo):
 
     nloc = [0]
 
-    def send(hops, out, in_, R, W, sem, cols):
-        dst, src = T.cores[(rank + hops) % N], T.cores[(rank - hops) % N]
+    def send(out, in_, R, W, sem, cols):
+        dst, src = T.cores[(rank + 1) % N], T.cores[(rank - 1) % N]
         rid, pid, _s = topo.addr(dst)
-        record("G", [lambda e: e.remote_dma(out, in_, T.sem[sem], T.sem.loc, pid, rid, topo.mask(core, dst))], R, W,
-               max(300, COL * cols), FAR * (1 if nloc[0] else 2) + min(0, COL * cols - 300), (sem, len(topo.engines(src, core))), True)
+        record("G", [lambda e: e.remote_dma(out, in_, T.sem[sem], T.sem.loc, pid, rid, topo.mask(core, dst))], R, W, ISSUE,
+               FAR + (0 if nloc[0] else FIRST), (sem, len(topo.engines(src, core))), 16 * ROW + COL * cols)
         nloc[0] += len(topo.engines(core, dst))
 
     def vec(fn, R, W, n):
-        record("V", [fn], R, W, max(n, 64 * CYC))
+        record("V", [fn], R, W, np.maximum(n, 64 * CYC))
 
     def tt(o, a, b, o_, R, W, n=0):
         vec(lambda e: e.tensor_tensor(o, a, b, o_), R, W, n)
@@ -216,19 +408,19 @@ def rank_program(g, core, T, topo):
         vec(lambda e: e.memset(o, c), "", W, n)
 
     def act(o, a, R, W, n=0, f=AF.Copy, **kw):
-        record("S", [lambda e: e.activation(o, a, f, **kw)], R, W, max(n, 64 * CYC))
+        record("S", [lambda e: e.activation(o, a, f, **kw)], R, W, np.maximum(n, 64 * CYC))
 
     def mms(l, R, W, n):
         record("P", [lambda e, m=m: e.matmul(*m) for m in l], R, W, n * PEC)
 
-    def iota(o, pat, base, cm, W, n=16, **kw):
-        record("G", [lambda e: e.iota(o, pat, base, cm, **kw)], "", W, 130 + 2 * n * CYC)
+    def iota(o, pat, base, cm, W, n=16, R="", **kw):
+        record("G", [lambda e: e.iota(o, pat, base, cm, **kw)], R, W, 130 + 2 * n * CYC)
 
-    def fiota(o, pat, base, cm, W, n=16):
-        iota(o, pat, base, cm, W, n, allow_small_or_imprecise_dtypes=True)
+    def fiota(o, pat, base, cm, W, n=16, R=""):
+        iota(o, pat, base, cm, W, n, R, allow_small_or_imprecise_dtypes=True)
 
-    def sel(o, a, pat, cmp_, fill, base, cm, R, W):
-        record("G", [lambda e: e.affine_select(o, a, pat, cmp_, fill, base, cm)], R, W, 170 + 256 * CYC)
+    def sel(o, a, pat, cmp_, fill, base, cm, R, W, n=128):
+        record("G", [lambda e: e.affine_select(o, a, pat, cmp_, fill, base, cm)], R, W, 170 + 2 * n * CYC)
 
     def gat(n):
         return 60 + GAT * n
@@ -236,27 +428,27 @@ def rank_program(g, core, T, topo):
     def sca(n):
         return 50 + SCA * n
 
-    def conv(out, row, a, n, R, W, st=True, sp=True, tab="SELW"):
-        mms([(out, T[tab][:, 15 - l:143 - l], row[:, a + l:a + 16 * (n - 1) + l + 1:16], st and l == 0, sp and l == 15)
+    def conv(out, row, a, n, R, W, st=True, tab="SELW"):
+        mms([(out, T[tab][:, 15 - l:143 - l], row[:, a + l:a + 16 * (n - 1) + l + 1:16], st and l == 0, l == 15)
              for l in range(16)], R + " " + tab, W, 1024)
 
     def part(q):
         return slice(16 * MP * q, 16 * MP * (q + 1))
 
     def wi(t, a, b):
-        return T.WI[:, 512 * t + a:512 * t + b]
+        return T.WI[:, 608 * t + a:608 * t + b]
 
     def wo(t, a, b):
-        return T.WO[:, 512 * t + a:512 * t + b]
+        return T.WO[:, 608 * t + a:608 * t + b]
 
-    def mi(t, a, b):
-        return T.MI[:, 64 * t + a:64 * t + b]
+    def afl(t, a, b):
+        return T.AFL[:, 256 * t + a:256 * t + b]
 
-    def mo(t, a, b):
-        return T.MO[:, 80 * t + a:80 * t + b]
+    def bb(a, b):
+        return T.BB[:, 16 * a:16 * b]
 
-    def fa(t, a, b):
-        return T.FA[:, 32 * (t % 2) + a:32 * (t % 2) + b]
+    def c16(n):
+        return T.C16[:, 16 * n:16 * n + 16]
 
     dma("S", T.pns[:], T.pn[:], "", "pns", "d_pn", 1900)
     dma("D", T.pfs[:], T.pf[:], "", "pfs", "d_pf", 2300)
@@ -272,12 +464,9 @@ def rank_program(g, core, T, topo):
     ms(T.SELW[:], 0.0, "SELW")
     ms(T.LL[:], 0.0, "LL")
     ms(T.EUW[:], 0.0, "EUW")
-    ms(T.ESW[:], 0.0, "ESW")
     ms(T.QS[:], 0.0, "QS")
     for q in range(NQ):
         ms(T.QS[part(q), q::NQ], 0.5, "+QS")
-        ms(T.ESW[part(q), 48 * q + 16:48 * q + 32], -1024.0, "+ESW")
-    ms(T.CX[:], 1088.0 - 1024 * MP, "CX")
     ms(T.TM[0:32, :], 16.0, "TM")
     ms(T.HALF[:], 0.5, "HALF", 128 * CYC)
     ms(T.QUART[:], 0.0, "QUART", 128 * CYC)
@@ -286,9 +475,10 @@ def rank_program(g, core, T, topo):
     ms(T.X16[:], 0.0, "X16")
     ms(T.TWO[:], 2.0, "TWO")
     ms(T.ACC[:, 4:5], 1.0 / 128, "ACC4")
-    ms(T.DF2[:, 0:16], 256.0, "DF2c")
     ms(T.SB9[:], 1.0, "SB9")
-    ms(T.C16[:], 16.0, "C16")
+    act(c16(1), T.ONES[:, 0:16], "ONES", "+C16", 1300, f=AF.Silu, scale=32768.0)
+    for n, x in ((0, 16.0), (2, 32.0), (3, 48.0)):
+        act(c16(n), T.ONES[:, 0:16], "ONES", "+C16", scale=x)
     ms(T.FT[0:32, :], 0.5, "FT")
     ms(T.RTB[:], -1.0, "RTB")
     for n in range(0, NXG, 2):
@@ -306,9 +496,10 @@ def rank_program(g, core, T, topo):
     sel(r32, r32, [[-1, 8], [0, 16]], A.not_equal, 1.0, -8, 1, "TR", "TR")
     sel(T.IDENT[:], T.ONES[:], [[-1, 128]], A.is_equal, 0.0, 0, 1, "ONES", "IDENT")
     sel(T.SELW[:, 0:128], T.G16[:], [[0, 8], [1, 16]], A.is_equal, 0.0, -15, 0, "G16", "SELW")
-    iota(T.LI[:], [[16, 16]], 0, 0, "LI")
+    fiota(T.LI[:], [[16, 16]], 1, 0, "LI")
     iota(T.BASE[:], [[512, 16]], 8 * MP, 0, "BASE")
-    fiota(T.IDX[:], [[1, 256]], 32, 0, "IDX", 256)
+    for w, x in (("IDF", 1.0), ("NIDF", -1.0), ("I256", 256.0), ("HB", 0.5), ("NHB", -0.5)):
+        act(T[w][:], T.IDENT[:], "IDENT", w, 128 * CYC, scale=x)
 
     pn = T.PD[:, 0:256]
     mms([(pn, T.IDENT[:], T.pns[:], True, True)], "IDENT pns", "PD", 256)
@@ -316,6 +507,7 @@ def rank_program(g, core, T, topo):
     tt(T.LO[:], pn, T.pfs[:], A.min, "pfs PD", "LO", 256 * CYC)
     tt(T.SG[:], pn, T.pfs[:], A.is_gt, "pfs PD", "SG", 256 * CYC)
     ts(T.SG[:], T.SG[:], 2.0, -1.0, A.mult, A.add, "SG", "SG", 128 * CYC)
+    act(T.G8[:], T.G16[:, ::16], "G16", "G8")
     cp(T.nbU[:], T.nbs[:], "nbs", "nbU")
     cp(T.CBF[:], T.cbs[:], "cbs", "CBF", 512 * CYC)
     cp(T.bsU[:], T.bss[:], "bss", "bsU")
@@ -330,7 +522,10 @@ def rank_program(g, core, T, topo):
         cp(T.D1[:, 2 * k + 1::32], T.LO[:], "LO", "+D1", 128 * CYC)
     for n in range(8):
         ts(T.WH[:, :, n, :], T.SG[:], T.G16[:, 16 * n:16 * n + 1], -1.0, A.mult, A.mult, "SG G16", "+WH", 128 * CYC)
-        ts(T.WA[:, :, n, :], T.SG[:], T.G16[:, 16 * n:16 * n + 1], None, A.mult, None, "SG G16", "+WA", 128 * CYC)
+        if n < WS:
+            act(T.WA[:, :, n, :], T.SG[:], "SG G8", "+WA", 256 * CYC, f=AF.Identity, scale=T.G8[:, n:n + 1])
+        else:
+            ts(T.WA[:, :, n, :], T.SG[:], T.G16[:, 16 * n:16 * n + 1], None, A.mult, None, "SG G16", "+WA", 128 * CYC)
     ts(T.PM[:, 0:1], T.PI[:, 0:1], 15, None, A.bitwise_and, None, "PI", "PM")
     cp(T.PMF[:, 0:1], T.PM[:, 0:1], "PM", "PMF")
     ts(T.KK[:], T.KK[:], T.PMF[:, 0:1], None, A.is_equal, None, "KK PMF", "KK")
@@ -340,29 +535,40 @@ def rank_program(g, core, T, topo):
         ts(T.LL[:, 8 * n:8 * n + 8], T.G16[:, ::16], T.THN[:, n:n + 1], None, A.mult, None, "G16 THN%d" % n, "+LL")
     for n in range(1, CC):
         cp(T.TR[0:32, 128 * n:128 * n + 128], r32, "TR", "+TRb")
-    mms([(T.PL[0:24, 0, 0:128], T.LL[:, 0:24], T.KK[:], True, True)], "LL KK", "PL", 128)
-    tt(T.TI[0:24, :], T.PL[0:24, 0, 0:128], T.TM[0:24, :], A.add, "PL TM", "TI", 128 * CYC)
-    act(T.IDF[:], T.IDENT[:], "IDENT", "IDF", 128 * CYC)
-    act(T.NIDF[:], T.IDENT[:], "IDENT", "NIDF", 128 * CYC, scale=-1.0)
+    mms([(T.PL[0:24, 0:2, :], T.LL[:, 0:24], T.KK[:], True, True)], "LL KK", "PL", 128)
+    tt(T.TI[0:24, :], T.PL[0:24, 0:2, :], T.TM[0:24, :], A.add, "PL TM", "TI", 128 * CYC)
     ts(T.SELW[:], T.SELW[:], 0.0625, None, A.mult, None, "SELW", "SELW")
     for q in range(NQ):
         ts(T.EUW[part(q), 48 * q + 16:48 * q + 32], T.KK[part(q), 0:16], 32.0, 1.0, A.mult, A.add, "KK", "+EUW")
-    ts(T.LIF[:], T.LI[:], T.PMF[:, 0:1], None, A.add, None, "LI PMF", "LIF")
+    ts(T.THR[:], T.LI[:], T.PMF[:, 0:1], 4.0, A.add, A.mult, "LI PMF", "THR")
     ts(T.PMF[:, 1:2], T.PM[:, 0:1], 32.0, None, A.mult, None, "PM", "PMF1")
-    ts(T.NSELW[:], T.SELW[:], -1.0, None, A.mult, None, "SELW", "NSELW")
-    for t in range(4):
-        ts(mi(t, 0, 16), T.LIF[:], 256.0, None, A.add, None, "LIF", "MIc%d" % t)
-    cp(mi(0, 32, 48), T.fss[:], "fss", "+MI0")
-    cp(fa(0, 0, 16), T.fss[:], "fss", "FA0")
+    cp(T.BI0[:, 0:16], T.fss[:], "fss", "+BI0")
+    ts(T.BC[:, 4:5], T.PMF[:, 0:1], 8.0, None, A.is_ge, None, "PMF", "BC4")
+    for n, (a, b) in enumerate(((256.0, 32.0), (-257.0, -31.0), (-2046.0, 2048.0), (2.0, 0.0))):
+        ts(T.BC[:, n:n + 1], T.BC[:, 4:5], a, b, A.mult, A.add, "BC4", "+BC")
+    ts(T.SELW2[:], T.SELW[:], T.BC[:, 2:3], None, A.mult, None, "SELW BC", "SELW2", 72 * CYC)
+    ts(T.SELW3[:], T.SELW[:], T.BC[:, 3:4], None, A.mult, None, "SELW BC", "SELW3", 72 * CYC)
+    fiota(T.SELB[:, :, :, 0:8], [[0, 1024]], 0, 0, "SELB", 1024)
+    sel(T.SELB[:, :, :, 8:16], T.SELB[:, :, :, 0:8], [[-1, 16], [-16, 8], [0, 8]], A.not_equal, 1.0, 0, 1, "SELB", "SELB", 1024)
+    ms(T.LO8[:, :, 0:8], 1.0 / 128, "+LO8")
+    ms(T.LO8[:, :, 8:16], 0.0, "+LO8")
+    ts(bb(4, 5), T.nbs[:], -256.0, None, A.add, None, "nbs", "+BH")
+    fiota(T.UF[:, 512:1536], [[0, 1024]], 16416, 0, "UFb", 1024)
     fiota(T.YC[:], [[1, 512]], 32, 0, "YC", 512)
-    act(T.UF[:].indirect(T.bsU[:]), T.YC[:], "YC bsU", "UF", sca(512) + 1300, f=AF.Silu)
+    act(T.UF[:, 0:512].indirect(T.bsU[:]), T.YC[:], "YC bsU C16", "UF", sca(512), f=AF.Silu)
     conv(T.PN[:, 0:16], T.pfs, 0, 16, "pfs", "PN")
     ts(T.ELS[:], T.PN[:, 0:16], 16.0, None, A.mult, None, "PN", "ELS")
     ts(T.ELS[:], T.ELS[:], 31, None, A.bitwise_and, None, "ELS", "ELS")
     tt(T.ELS[:], T.ELS[:], T.BASE[:], A.add, "ELS BASE", "ELS")
-    act(T.MROW[:], T.UF[:].indirect(T.nbU[:]), "UF nbU", "MROW", gat(256), f=AF.Identity, bias=-288.0)
+    act(T.MROW[:], T.UF[:, 0:512].indirect(T.nbU[:]), "UF nbU", "MROW", gat(256), f=AF.Identity, bias=-288.0)
     conv(T.PN[:, 16:32], T.MROW, 0, 16, "MROW", "PN")
-    ts(mi(0, 16, 32), T.PN[:, 16:32], 256.0, None, A.add, None, "PN", "+MI0")
+    ts(T.BI0[:, 16:32], T.PN[:, 16:32], 256.0, None, A.add, None, "PN", "+BI0")
+    ts(T.BI1[:], T.BI0[:], 510, None, A.bitwise_and, None, "BI0", "BI1")
+    ts(T.BI2[:], T.BI1[:], 2.0, -255.0, A.mult, A.add, "BI1", "BI2")
+    for n in range(2):
+        s = slice(16 * n, 16 * n + 16)
+        ts(bb(2 * n, 2 * n + 1), T.BI0[:, s], -256.0, None, A.add, None, "BI0", "+BH")
+        tt(bb(2 * n + 1, 2 * n + 2), T.BI2[:, s], T.BI0[:, s], A.subtract, "BI2 BI0", "+BH")
     cp(T.PIF[:, 0:1], T.PI[:, 0:1], "PI", "PIF")
     vec(lambda e: e.tensor_tensor_scan(T.PABW[:], T.HALF[:], T.QUART[:], 0.0, A.mult, A.add), "HALF QUART", "PABW", 128 * CYC)
     vec(lambda e: e.tensor_tensor_scan(T.P2[:, 0:9], T.TWO[:, 0:9], T.X16[:, 0:9], 0.5, A.mult, A.add), "TWO X16", "P2", 0)
@@ -381,35 +587,28 @@ def rank_program(g, core, T, topo):
     sel(m, T.ONES[0:32, :], [[-1, 16], [0, 8]], A.is_equal, 0.0, 0, 1, "ONES", "SBH")
     sel(m, m, [[0, 128]], A.not_equal, 1.0, -16, 1, "SBH", "SBH")
     tt(m, m, T.PABX[0:32, :], A.mult, "PABX SBH", "SBH", 256 * CYC)
+    sel(m, m, [[0, 128]], A.not_equal, 384.0, -17, 1, "SBH", "SBH")
     ts(T.P2[:, 8:9], T.P2[:, 8:9], -1.0, None, A.mult, None, "P2", "P2")
     cp(T.P2[:, 9:17], T.P2[:, 1:9], "P2", "P2")
     tt(T.P2[:, 1:17], T.P2[:, 1:17], T.KK[:, 0:16], A.mult, "P2 KK", "P2")
     vec(lambda e: e.tensor_reduce(T.C2[:, 0:1], T.P2[:, 1:17], AxisListType.X, A.add), "P2", "C2a", 0)
     ts(T.C2[:, 1:2], T.C2[:, 0:1], -2.0, None, A.mult, None, "C2a", "C2")
-    sel(T.X16[:], T.X16[:], [[-8, 16]], A.is_ge, 1.0, 0, 1, "X16", "X16")
-    sel(T.X16[:], T.X16[:], [[8, 16]], A.is_ge, 1.0, 7, -1, "X16", "X16")
+    sel(T.X16[:], T.X16[:], [[-8, 16]], A.is_ge, 1.0, 0, 1, "X16", "X16", 16)
+    sel(T.X16[:], T.X16[:], [[8, 16]], A.is_ge, 1.0, 7, -1, "X16", "X16", 16)
     brow = T.BZ[:, 512:1024]
-    act(brow, T.IOTC[:].indirect(T.bsU[:]), "IOTC bsU", "BROW4", gat(512))
-    act(T.XB0[:, 0:256], brow.indirect(T.fsU[:]), "BROW4 fsU", "+XB0", gat(256))
+    act(brow, T.IOTC[:].indirect(T.bsU[:]), "IOTC bsU", "BROW", gat(512))
+    act(T.XB0[:, 0:256], brow.indirect(T.fsU[:]), "BROW fsU", "XB0", gat(256))
     conv(T.PN[:, 32:48], T.XB0, 0, 16, "XB0", "PN")
     ts(T.GU[:], T.PN[:, 32:48], 256.0, None, A.add, None, "PN", "GU")
-    act(T.AFL[:], T.CBF[:].indirect(T.GU[:]), "CBF GU", "AFL", gat(256))
-    act(T.XB0[:, 256:512], T.IOTC[:].indirect(T.nbU[:]), "IOTC nbU", "+XB0", gat(256))
+    cp(bb(5, 6), T.PN[:, 32:48], "PN", "BA")
+    act(afl(0, 0, 256), T.CBF[:].indirect(T.GU[:]), "CBF GU", "AFL0", gat(256), scale=-1.0)
 
-    ring = {"XG": 0, "CL": 0, "YV": 0}
+    ring = {}
 
     def slots(name, size, n):
         a = ring[name] if ring[name] + n <= size else 0
         ring[name] = a + n
         return a, " ".join("%s%d" % (name, x) for x in range(a, a + n))
-
-    now = [0]
-
-    def early(name, step, *a):
-        n = len(calls)
-        step(*a)
-        for c in calls[n:]:
-            c["early"] = EARLY[now[0] // 4].get(name, 0)
 
     def chunk(q, j, n):
         c = j % 16
@@ -438,13 +637,16 @@ def rank_program(g, core, T, topo):
         lanes(j, n, mk, lambda p: T.CL[:, 512 * m + 32 * p + 1:512 * m + 32 * (p + MP):2])
 
     def lanes(j, n, key, block):
-        c = j % 16
-        P, w = "PB%d" % (c // 4), ("WH", "WA")[j // 16]
-        if j < 16 and c % 4 == 0:
-            mms([(T[P][:, 0:CC, :, :], T.TI[0:24, :], T.TR[0:24, 0:128 * CC], True, False)], "TI TR TRb", P, 128 * CC)
-        mms([(T[P][part((c + u) % NQ), (c + u) % 4 // NQ, :, b:b + MP], block(16 * u + b), T[w][:, c + u, :, b:b + MP], False,
-              j >= 16 and (c + u) % 4 >= 4 - NQ and b + MP == 16) for u in range(n) for b in range(0, 16, MP)],
-            key + " " + w, P, n * (256 if MP < 8 else 128))
+        for u0 in range(n):
+            c = (j + u0) % 16
+            P, w = "PB%d" % (c // 4), ("WH", "WA")[j // 16]
+            if u0 and c % 4:
+                continue
+            if j < 16 and c % 4 == 0:
+                mms([(T[P][:, 0:CC, :, :], T.TI[0:24, :], T.TR[0:24, 0:128 * CC], True, False)], "TI TR TRb", P, 128 * CC)
+            m = min(n - u0, 4 - c % 4)
+            mms([(T[P][part((c + u) % NQ), (c + u) % 4 // NQ, :, b:b + MP], block(16 * (u0 + u) + b), T[w][:, c + u, :, b:b + MP], False,
+                  j >= 16 and (c + u) % 4 >= 4 - NQ and b + MP == 16) for u in range(m) for b in range(0, 16, MP)], key + " " + w, P, 256 * m)
 
     def signs(k):
         P, z = "PB%d" % k, "Z%d" % k
@@ -452,182 +654,187 @@ def rank_program(g, core, T, topo):
             accum_out=T.ACC[:, k:k + 1])
 
     def sums(k):
-        z = "Z%d" % k
-        mms([(T.PL[:, :, 4 * k + NQ * c:4 * k + NQ * (c + 1)], T.Z[:, CC * k + c, :, :], T.QS[:], True, True) for c in range(CC)],
-            z + " QS", "PL", 64 * CC)
+        mms([(T.PL[:, 0, 4 * k + NQ * c:4 * k + NQ * (c + 1)], T.Z[:, CC * k + c, :, :], T.QS[:, 0:NQ], True, True) for c in range(CC)],
+            "Z%d QS" % k, "PL", 64 * CC)
+
+    def again(a, b):
+        mms([(T.PB0[:, 2, 0:6, NQ * c:NQ * (c + 1)], T.Z[:, c, :, :], T.QS[:], True, True) for c in range(a // NQ, b // NQ)],
+            " ".join("Z%d" % k for k in range(a // 4, b // 4)) + " QS", "PB0", 64 * (b - a) // NQ)
 
     def total(k):
         mms([(T.PT[:, 0:1], T.PABW[:], T.ACC[:, k:k + 1], k == 4, k == 3)], "PABW ACC%d" % k, "PT", 256)
 
-    def turned(t, k):
-        P, z, s = "PB%d" % k, "Z%d" % k, slice(64 * k, 64 * k + 64)
-        for n, e in enumerate(("EUW", "ESW")):
-            mms([(T[P][:, 1, 0:4, :], T.G16[:], T.CX[:], True, False)][:n]
-                + [(T[P][32 * (x // 2):32 * (x // 2) + 32, n, q:4:NQ, :], T[e][:, 48 * q + 16 - 16 * (x % 2):48 * q + 48 - 16 * (x % 2)],
-                    T.Z[:, CC * k:CC * k + CC, x, :], x % 2 == 0 and not n, x % 2 == 1 and (not n or q == NQ - 1))
-                   for q in range(NQ) for x in range(8)], z + " G16 CX " + e, P, 8 * NQ * max(32, 16 * CC) + 64 * n)
-        act(T.AB[:, s], T[P][:, 0, 0:4, :], P, "AB%d" % k, f=AF.Abs if t < 4 else AF.Sign, bias=48.0 * MP - 41)
-        tt(T.XF[:, s], T[P][:, 1, 0:4, :], T.IDX[:, s], A.max, P + " IDX", "XF%d" % k)
-
     def rows(t, k):
-        P, s, hk = "PD", slice(64 * k, 64 * k + 64), "WI%d_%d" % (t, k)
-        p, h = T.PD[:, s], wi(t, HCOL[k], HCOL[k] + 64)
+        P, s, hk, ak = "PB%d" % k, slice(64 * k, 64 * k + 64), "WI%d_%d" % (t, k), "AFL%d" % t
+        p, h, a = T.PD[:, s], wi(t, HCOL[k], HCOL[k] + 64), afl(t, 64 * k, 64 * k + 64)
+        mms([(T[P][32 * (x // 2):32 * (x // 2) + 32, 0, q:4:NQ, :], T.EUW[:, 48 * q + 16 - 16 * (x % 2):48 * q + 48 - 16 * (x % 2)],
+              T.Z[:, CC * k:CC * k + CC, x, :], x % 2 == 0, x % 2 == 1) for q in range(NQ) for x in range(8)],
+            "Z%d EUW" % k, P, 8 * NQ * max(32, 16 * CC))
+        act(T.AB[:, s], T[P][:, 0, 0:4, :], P, "AB%d" % k, f=AF.Abs if t < 4 else AF.Sign, bias=48.0 * MP - 41)
         if t < 4:
             ts(T.MM[:, s], T.AB[:, s], 32.0, None, A.is_gt, None, "AB%d" % k, "MM%d" % k)
             tt(p, p, T.MM[:, s], A.mult, "PD MM%d" % k, "pd%d" % k)
-            tt(wo(t, HCOL[k], HCOL[k] + 64), h, p, A.subtract, "PD pd%d %s" % (k, hk), "WO%dh%d" % (t, k))
-            tt(wo(t, ACOL + 64 * k, ACOL + 64 + 64 * k), p, T.AFL[:, s], A.add, "PD pd%d AFL" % k, "WO%da%d" % (t, k))
-            a, b, keys = SENDS[k]
-            send(1, wi(t + 1, a, b), wo(t, a, b), " ".join("WO%d%s" % (t, x) for x in keys.split()), "WI%d_%d" % (t + 1, k),
-                 "a%d_%d" % (k, t + 1), b - a)
+            tt(wo(t, HCOL[k], HCOL[k] + 64), p, h, A.add, "PD pd%d %s" % (k, hk), "WO%dh%d" % (t, k))
+            tt(wo(t, ACOL + 64 * k, ACOL + 64 + 64 * k), p, a, A.add, "PD pd%d %s" % (k, ak), "WO%da%d" % (t, k))
+            if k < 3:
+                leave(t, k)
         else:
             act(T.MM[:, s], T.AB[:, s], "AB%d" % k, "MM%d" % k, f=AF.Relu)
-            tt(T.PS[:, s], p, T.MM[:, s], A.mult, P + " MM%d" % k, "PS%d" % k)
-            tt(T.YC[:].indirect(T.YL[:, 4 * k:4 * k + 4]), T.AFL[:, s], T.PS[:, s], A.add, "AFL YL PS%d" % k, "YC", sca(64))
-            tt(T.YC[:].indirect(T.YL[:, 16 + 4 * k:20 + 4 * k]), h, T.PS[:, s], A.subtract, "YL PS%d %s" % (k, hk), "YC", sca(64))
+            tt(T.PS[:, s], p, T.MM[:, s], A.mult, "PD MM%d" % k, "PS%d" % k)
+            tt(T.YC[:].indirect(T.YL[:, 16 + 4 * k:20 + 4 * k]), a, T.PS[:, s], A.add, "YL PS%d %s" % (k, ak), "YC", sca(64))
+            tt(T.YC[:].indirect(T.YL[:, 4 * k:4 * k + 4]), h, T.PS[:, s], A.subtract, "YL PS%d %s" % (k, hk), "YC", sca(64))
+
+    def leave(t, k):
+        a, b, keys = SENDS[k]
+        send(wi(t + 1, a, b), wo(t, a, b), " ".join("WO%d%s" % (t, x) for x in keys.split()),
+             " ".join({"h": "WI%d_", "a": "WA%d_", "l": "MI%d"}[x[0]] % (t + 1) + x[1:] for x in keys.split()), "a%d_%d" % (k, t + 1), b - a)
 
     def frames(a, b):
         tt(T.OI1[:, a:b], T.PL[:, 0, a:b], T.ELS[:, a:b], A.add, "PL ELS", "OI1%d" % a)
         ts(T.OI2[:, a:b], T.OI1[:, a:b], 8191 - 32, None, A.bitwise_and, None, "OI1%d" % a, "OI2%d" % a)
-        ts(T.OFFU[:, a:b], T.OI2[:, a:b], T.PMF[:, 1:2], None, A.add, None, "PMF1 OI2%d" % a, "OFFU%d" % a)
-        cp(T.xfs[:].indirect(T.OFFU[:, a:b]), T.pfs[:, 16 * a:16 * b], "pfs OFFU%d" % a, "xfs xfsb", sca(16 * (b - a)))
+        ts(T.OFFU[:, a:b], T.OI2[:, a:b], T.PMF[:, 1:2], -512.0 * a, A.add, A.add, "PMF1 OI2%d" % a, "OFFU%d" % a)
+        cp(T.xfs[:, 512 * a:512 * b].indirect(T.OFFU[:, a:b]), T.pfs[:, 16 * a:16 * b], "pfs OFFU%d" % a, "xfsb" if a else "xfs",
+           sca(16 * (b - a)))
 
-    def flags(t, a, b):
-        keys = " ".join("XF%d" % k for k in range(a // 4, b // 4))
-        act(T.UF[:].indirect(fa(t, a, b)), T.XF[:, 16 * a:16 * b], keys + " FA%d" % (t % 2), "UF", sca(16 * (b - a)), f=AF.Silu)
+    def flags(a, b):
+        p = T.PB1[:, 2, 0, a:b]
+        again(a, b)
+        act(T.NF[:, a:b], T.PB0[:, 2, 0, a:b], "PB0", "NF%d" % a, f=AF.Sign, scale=-1.0, bias=8.5 - 8 * MP)
+        mms([(p, T.IDENT[:], T.BB[:, a:b], True, False), (p, T.G16[:], T.C16[:, 32 + a:32 + b], False, False)],
+            "IDENT G16 C16 BH", "PB1", 128)
+        mms([(p, T.I256[:], T.NF[:, a:b], False, True)], "I256 NF%d" % a, "PB1", 64)
+        cp(T.FU[:, a:b], p, "PB1", "FU%d" % a)
+        act(T.UF[:, 0:1024].indirect(T.FU[:, a:b]), T.IDX[:, 16 * a:16 * b], "IDX FU%d" % a, "UF", sca(16 * (b - a)), f=AF.Silu)
 
     def take(t):
         for k in range(4):
             cp(T.UH[:, 64 * k:64 * k + 64], wi(t, HCOL[k], HCOL[k] + 64), "WI%d_%d" % (t, k), "UH%d" % k)
+        sign, ak, a = (-1.0 if t < 4 else 1.0), "AFL%d" % t, 64 if t else 0
         if t:
-            cp(fa(t, 0, 16), mi(t, 32, 48), "MI%d" % t, "FA%d" % (t % 2))
-            cp(fa(t, 16, 32), mi(t, 48, 64), "MA%d" % t, "ALU")
-            act(T.AFL[:], wi(t, ACOL, ACOL + 256).indirect(fa(t, 16, 32)), "WI%d_1 WI%d_3 ALU" % (t, t), "AFL", gat(256))
-            cp(T.UA[:, 0:64], wi(t, ACOL, ACOL + 256).indirect(fa(t, 16, 20)), "WI%d_1 WI%d_3 ALU" % (t, t), "UA0", gat(64))
-        else:
-            cp(T.UA[:, 0:64], T.AFL[:, 0:64], "AFL", "UA0")
-        cp(T.UA[:, 64:256], T.AFL[:, 64:256], "AFL", "UA1 UA2 UA3", 192 * CYC)
+            win, keys = wi(t, ACOL, ACOL + 256), " ".join("WA%d_%d" % (t, k) for k in range(4)) + " ALU"
+            ts(T.ALU[:], T.MA[:, 32 * t:32 * t + 16], -1.0, None, A.add, None, "MA%d" % t, "ALU")
+            ts(bb(5, 6), T.MA[:, 32 * t + 16:32 * t + 32], -256.0, None, A.add, None, "MA%d" % t, "BA")
+            act(afl(t, 0, 256), win.indirect(T.ALU[:]), keys, ak, gat(256), scale=-sign)
+            ts(T.UA[:, 0:64], win.indirect(T.ALU[:, 0:4]), -1.0, None, A.mult, None, keys, "UA0", gat(64))
+            cp(T.BB[:, 0:80], wi(t, 512, 592), "MI%d" % t, "BH", 80 * CYC)
+        ts(T.UA[:, a:256], afl(t, a, 256), sign, None, A.mult, None, ak, "UA0 UA1 UA2 UA3"[a // 16:], (256 - a) * CYC)
         for k in range(4):
-            s = slice(64 * k, 64 * k + 64)
-            mms([(T.PD[:, s], T.IDF[:], wi(t, HCOL[k], HCOL[k] + 64), True, False), (T.PD[:, s], T.NIDF[:], T.AFL[:, s], False, True)],
-                "IDF NIDF AFL WI%d_%d" % (t, k), "PD", 512)
+            p = T.PD[:, 64 * k:64 * k + 64]
+            mms([(p, T["NIDF" if t < 4 else "IDF"][:], wi(t, HCOL[k], HCOL[k] + 64), True, False),
+                 (p, T.NIDF[:], afl(t, 64 * k, 64 * k + 64), False, True)], "IDF NIDF %s WI%d_%d" % (ak, t, k), "PD", 512)
+        for c, w in ((16, T.NHB[:]), (32, T.HB[:])):
+            more = [(5, T.I256[:], T.THR[:]), (5, T.G16[:], c16(1))] + [(x, T.G16[:], c16(0)) for x in ((5,), (0, 4))[t // 4]]
+            l = ([(T.PL[:, 0:6, c:c + 16], w, T.BB[:])] + [(T.PL[:, a:a + n, c:c + 16], T.HB[:], bb(b, b + n)) for a, b, n in
+                                                          ((0, 2, 2), (2, 0, 2), (4, 5, 1), (5, 4, 1))]
+                 + [(T.PL[:, x, c:c + 16], a, b) for x, a, b in more[:4 * (c // 32)]])
+            mms([m + (n == 0, n == len(l) - 1) for n, m in enumerate(l)], "HB NHB I256 BA BH G16 C16 THR", "PL", 64 * len(l) + 32)
+        a = 256 if t < 4 else 0
+        mms([(T.PT[:, a:512], T.LO8[:], T.IOTC[:, a:512], True, False)]
+            + [(T.PT[:, a + l:512:16], T.SELB[:, l, :, :], bb(4 + a // 256, 6), False, l == 15) for l in range(16)],
+            "LO8 IOTC SELB BA BH", "PT", 1536 - a)
+        act(T.IDX[:], T.PT[:, 256:512], "PT BC", "IDX", 256 * CYC, f=AF.Identity, bias=T.BC[:, 0:1])
         if t < 4:
-            bits(t)
-        tt(T.DF2[:, 16:32], mi(t, 16, 32), mi(t, 32, 48), A.subtract, "MI%d" % t, "DF2")
-        fiota(T.UF[:], [[0, 512]], 1056, 0, "UF", 512)
+            bits()
+        fiota(T.UF[:, 0:512], [[0, 512]], 16416, 0, "UF", 512, "UFb")
 
-    def bits(t):
-        ts(T.BI1[:], mi(t, 32, 48), 510, None, A.bitwise_and, None, "MI%d" % t, "BI1")
-        ts(T.BI2[:], T.BI1[:], 2.0, -255.0, A.mult, A.add, "BI1", "BI2")
-        tt(T.FB[:], T.BI2[:], mi(t, 32, 48), A.subtract, "BI2 MI%d" % t, "FB")
-        mms([(T.PN[0:16, 128:256], T.FB[:], T.IDENT[:], True, True)], "FB IDENT", "PN", 128)
+    def bits():
+        mms([(T.PN[0:16, 128:256], bb(0, 1), T.IDENT[:], True, True)], "IDENT BH", "PN", 128)
         act(T.FT[0:16, :], T.PN[0:16, 128:256], "PN", "+FT", 128 * CYC)
-        mms([(T.PN[:, 256:384], T.SBH[0:17, :], T.FT[0:17, :], True, True)], "SBH FT", "PN", 128)
-        cp(T.RB[:], T.PN[:, 256:384], "PN", "RB", 128 * CYC)
+        mms([(T.PN[:, 256:384], T.SBH[0:18, :], T.FT[0:18, :], True, True)], "SBH FT", "PN", 128)
+        act(T.RB[:], T.PN[:, 256:384], "PN", "RB", 128 * CYC)
         tt(T.BT[:], T.PN[:, 256:384], T.RB[:], A.is_lt, "PN RB", "BT", 128 * CYC)
         ts(T.BT[:], T.BT[:], T.C2[:, 1:2], T.C2[:, 0:1], A.mult, A.add, "BT C2", "BT")
+        mms([(T.PN[:, 16:32], T.IDENT[:], bb(1, 2), True, False), (T.PN[:, 16:32], T.G16[:], c16(3), False, False)],
+            "IDENT G16 C16 BH", "PN", 128)
 
     def xor(t):
         y = T.PT[:, 0:1]
-        cp(T.RI[:, 0:1], y, "PT", "RI")
-        tt(T.DD[:, 0:1], y, T.RI[:, 0:1], A.subtract, "PT RI", "DD")
         if t < 4:
-            ts(T.RS[:, 0:16], T.X16[:], T.DD[:, 0:1], 0.0, A.add, A.is_lt, "X16 DD", "RS")
-            mms([(T.PT[:, 16:32], T.IDENT[:], T.FB[:], True, False), (T.PT[:, 16:32], T.BT[:], T.RS[:, 0:16], False, True)],
-                "IDENT FB BT RS", "PT", 128)
-            ts(T.XLU[:, 0:16], T.PT[:, 16:32], 256.0, None, A.add, None, "PT", "XLU")
+            ts(T.DD[:, 0:1], y, MAGIC, MAGIC, A.add, A.subtract, "PT", "DD")
+            ts(T.RS[:, 0:16], T.X16[:], y, T.DD[:, 0:1], A.add, A.is_lt, "X16 PT DD", "RS")
+            mms([(T.PN[:, 16:32], T.I256[:], T.NF[:], False, False)] * 2, "I256 " + " ".join("NF%d" % a for a, b in FLAGS), "PN", 128)
+            mms([(T.PN[:, 16:32], T.BT[:], T.RS[:, 0:16], False, True)], "BT RS", "PN", 64)
+            cp(T.XLU[:, 0:16], T.PN[:, 16:32], "PN", "XLU")
         else:
+            cp(T.RI[:, 0:1], y, "PT", "RI")
+            tt(T.DD[:, 0:1], y, T.RI[:, 0:1], A.subtract, "PT RI", "DD")
             ts(T.RS[0:8, :], T.RX[0:8, :], T.DD[0:8, 0:1], 0.0, A.mult, A.is_gt, "RX DD", "RS")
             mms([(T.PT[:, 128:160], T.LB[0:8, :], T.RS[0:8, :], True, True)], "LB RS", "PT", 64)
             ts(T.XLU[:], T.PT[:, 128:160], T.LX1[:, 0:1], None, A.add, None, "PT LX1", "XLU")
 
     def turns(t):
-        ts(T.TRN[:], T.PL[:, :, 0:16], 4.5 - 8 * MP, None, A.is_lt, None, "PL", "TRN")
-        tt(T.XX[:], T.TRN[:], T.DF2[:], A.mult, "TRN DF2 DF2c", "XX")
+        act(T.TRN[:], T.PB0[:, 2, 0:6, :], "PB0", "TRN", 96 * CYC, f=AF.Sign, scale=-1.0, bias=4.5 - 8 * MP)
+        tt(T.XX[:], T.PL[:, 0:6, 16:32], T.TRN[:], A.mult, "TRN PL", "XX", 96 * CYC)
+        tt(wo(t, 512, 608), T.PL[:, 0:6, 32:48], T.XX[:], A.add, "PL XX", "WO%dl" % t, 96 * CYC)
         if t < 4:
-            tt(mo(t, 48, 64), mi(t, 32, 48), T.XX[:, 16:32], A.add, "MI%d XX" % t, "MO%df" % t)
-            tt(mo(t, 16, 48), mi(t, 0, 32), T.XX[:], A.subtract, "MI%d MIc%d XX" % (t, t), "MO%dg" % t)
+            for k in range(3, len(SENDS)):
+                leave(t, k)
 
     def alpha(t):
-        ts(T.OWN[:], T.PL[:, 0, 0:16], 8.5 - 8 * MP, 512.0, A.is_gt, A.mult, "PL", "OWN")
-        tt(T.OWN[:], T.OWN[:], T.LIF[:], A.add, "OWN LIF", "OWN")
-        mms([(T.PN[:, 0:16], T.G16[:], T.C16[:], True, False)], "G16 C16", "PN", 64)
-        act(T.MROW[:], T.UF[:].indirect(T.XLU[:, 0:16]), "UF XLU", "MROW", gat(256), f=AF.Identity, bias=-32.0)
-        conv(T.PN[:, 0:16], T.MROW, 0, 16, "MROW", "PN", st=False)
-        tt(T.AL[:], T.PN[:, 0:16], T.OWN[:], A.min, "PN OWN", "AL")
-        ts(mo(t, 64, 80), T.AL[:], 255, None, A.bitwise_and, None, "AL", "MO%da" % t)
-        send(1, mi(t + 1, 48, 64), mo(t, 64, 80), "MO%da" % t, "MA%d" % (t + 1), "a5_%d" % (t + 1), 16)
-        send(1, mi(t + 1, 16, 48), mo(t, 32, 64), "MO%df MO%dg" % (t, t), "MI%d" % (t + 1), "a4_%d" % (t + 1), 32)
-        tt(mo(t, 0, 16), mo(t, 64, 80), T.XX[:, 0:16], A.add, "MO%da XX" % t, "MO%db" % t)
-        if t:
-            send(-t, T.HM[:, 32 * t:32 * t + 32], mo(t, 0, 32), "MO%db MO%dg" % (t, t), "HM%d" % t, "ah%d" % t, 32)
-
-    def boxes(n):
-        a, b = "XB%d" % (n % 2), "XB%d" % (1 - n % 2)
-        if n:
-            cp(T.XLS[:], T.HM[:, 32 * n:32 * n + 32], "HM%d" % n, "XLS")
-        else:
-            cp(T.XLS[:], mo(0, 0, 32), "MO0b MO0g", "XLS")
-        act(T[b][:], T[a][:].indirect(T.XLS[:]), a + " XLS", b, gat(512))
+        d = T.DM[:, 32 * t:32 * t + 32]
+        mms([(T.PN[:, 0:16], T.G16[:], c16(0), True, False)], "G16 C16", "PN", 64)
+        act(T.MROW[:], T.UF[:].indirect(T.XLU[:, 0:16]), "UF XLU BC", "MROW", gat(256), f=AF.Identity, bias=T.BC[:, 1:2])
+        conv(T.PN[:, 0:16], T.MROW, 0, 16, "MROW", "PN", st=False, tab="SELW2")
+        tt(T.AL[:], T.PN[:, 0:16], wo(t, 592, 608), A.min, "PN WO%dl" % t, "AL")
+        ts(T.DM[:, 32 * t:32 * t + 16], T.AL[:], 10, 511, A.arith_shift_right, A.bitwise_and, "AL", "+DM%d" % t)
+        ts(T.DM[:, 32 * t + 16:32 * t + 32], T.AL[:], 511, None, A.bitwise_and, None, "AL", "+DM%d" % t)
+        send(T.MA[:, 32 * t + 32:32 * t + 64], d, "DM%d" % t, "MA%d" % (t + 1), "am_%d" % (t + 1), 32)
 
     def box_lists():
-        conv(T.PN[:, 32:64], T.XB0, 0, 32, "XB0", "PN")
-        ts(T.YL[:], T.PN[:, 32:64], 256.0, None, A.add, None, "PN", "YL")
-        ts(T.YL32[:], T.PN[:, 32:64], 256.0, None, A.add, None, "PN", "YL32")
-        cp(T.GU[:], mi(4, 16, 32), "MI4", "GU")
-        tt(T.DA[:], T.YL32[:, 0:16], T.YL32[:, 16:32], A.subtract, "YL32", "DA")
-        cp(brow.indirect(fa(4, 0, 16)), T.XB0[:, 0:256], "XB0 FA0", "BROW4", sca(256))
-        cp(brow.indirect(T.GU[:]), T.XB0[:, 256:512], "XB0 GU", "BROW4", sca(256))
-        conv(T.PN[:, 64:96], T.BZ, 512, 32, "BROW4", "PN")
+        act(T.XB0[:], T.PT[:, 0:512], "PT", "XB0", 512 * CYC)
+        ts(T.YL[:], bb(4, 6), 256.0, None, A.add, None, "BA BH", "YL")
+        ts(T.GU[:], bb(2, 3), 256.0, None, A.add, None, "BH", "GU")
+        ts(T.fsU[:], bb(0, 1), 256.0, None, A.add, None, "BH", "fsU")
+        cp(brow.indirect(T.fsU[:]), T.XB0[:, 256:512], "XB0 fsU", "BROW", sca(256))
+        cp(brow.indirect(T.GU[:]), T.XB0[:, 0:256], "XB0 GU", "BROW", sca(256))
+        conv(T.PN[:, 64:96], T.BZ, 512, 32, "BROW", "PN", tab="SELW3")
         ts(T.BL[:], T.PN[:, 64:96], 256.0, None, A.add, None, "PN", "BL")
 
     for t in range(5):
         now[0] = t
+        ring.update(XG=0, CL=0, YV=0)
         take(t)
-        if t:
-            early("boxes", boxes, t - 1)
         if t == 4:
-            early("boxes", box_lists)
+            box_lists()
         j = 0
         for w in PLAN[t // 4].split():
             chunk(w[0], j, int(w[1:]))
-            j += int(w[1:])
-            if j > 16 and j % 4 == 0:
-                k = (j - 20) // 4
+            for k in range(max(0, j // 4 - 4), (j + int(w[1:])) // 4 - 4):
                 if k == 3 and t < 4:
-                    early("frames", frames, *OFFS[0])
-                early("signs%d" % k, signs, k)
-                early("sums", sums, k)
+                    frames(*OFFS[0])
+                signs(k)
+                if t < 4:
+                    sums(k)
                 if k == 0:
                     total(4)
-                early("total", total, k)
+                total(k)
                 if k == 3 and t < 4:
-                    early("frames", frames, *OFFS[1])
-                early("turned%d" % k, turned, t, k)
-                early("rows%d" % k, rows, t, k)
+                    frames(*OFFS[1])
+                rows(t, k)
                 for a, b in FLAGS:
                     if b == 4 * k + 4:
-                        early("flags%d" % k, flags, t, a, b)
-        early("xor", xor, t)
+                        flags(a, b)
+            j += int(w[1:])
+        xor(t)
         turns(t)
         if t < 4:
-            early("alpha", alpha, t)
+            alpha(t)
 
     dma("D", T.yc[:], T.YC[:], "YC", "yc", "o_yc", 3000)
-    act(T.BZ[:, 0:512], T.UF[:], "UF", "U0", 512 * CYC, scale=-1.0)
-    conv(T.PN[:, 0:64], T.BZ, 0, 64, "U0 BROW4", "PN", sp=False, tab="NSELW")
-    cp(T.U[:, 0:512], T.UF[:].indirect(T.XLU[:]), "UF XLU", "U1", gat(512))
-    act(T.U[:, 512:1024], brow.indirect(T.XLU[:]), "BROW4 XLU", "U2", gat(512))
-    conv(T.PN[:, 0:64], T.U, 0, 64, "U1 U2", "PN", st=False)
-    ts(T.B1[:], T.PN[:, 0:32], 800.0, None, A.is_lt, None, "PN", "B1")
-    tt(T.B1[:], T.PN[:, 32:64], T.B1[:], A.mult, "PN B1", "B1")
-    tt(T.BL[:], T.BL[:], T.B1[:], A.add, "BL B1", "BL")
+    own = T.PB2[:, 2, 0:2, :]
+    ts(T.BZ[:, 0:512], T.UF[:, 0:512], -288.0, None, A.add, None, "UF", "U0", 512 * CYC)
+    conv(own, T.BZ, 0, 32, "U0", "PB2", tab="SELW3")
+    ts(T.YL32[:], own, -2.0, 600.0, A.mult, A.add, "PB2", "YL32")
+    mms([(T.PN[:, 0:32], T.NIDF[:], T.BL[:], True, False)] + [(T.PN[:, 16 * n:16 * n + 16], T.G16[:], c16(0), False, False) for n in range(2)],
+        "NIDF BL G16 C16", "PN", 384)
+    act(T.U[:], T.UF[:, 0:512].indirect(T.XLU[:]), "UF XLU", "U1", gat(512), f=AF.Identity, bias=-288.0)
+    conv(T.PN[:, 0:32], T.U, 0, 32, "U1", "PN", st=False, tab="SELW3")
+    tt(T.B1[:], T.PN[:, 0:32], T.YL32[:], A.is_lt, "PN YL32", "B1")
+    tt(T.AL32[:], T.PN[:, 0:32], T.B1[:], A.mult, "PN B1", "AL32")
+    tt(T.BL[:], T.BL[:], T.AL32[:], A.add, "BL AL32", "BL")
     dma("S", T.yb[:], T.BL[:], "BL", "yb", "o_yb")
-    tt(T.YF[:], mi(4, 32, 48), T.XX[:, 16:32], A.add, "MI4 XX", "YF")
-    dma("D", T.yf[:], T.YF[:], "YF", "yf", "o_yf")
-    tt(T.DA[:], T.DA[:], T.TRN[:, 0:16], A.mult, "DA TRN", "DA")
-    tt(T.DA[:], T.DA[:], T.YL32[:, 16:32], A.add, "DA YL32", "DA")
-    dma("S", T.yn[:], T.DA[:], "DA", "yn", "o_yn")
+    dma("D", T.yf[:], wo(4, 512, 528), "WO4l", "yf", "o_yf")
+    dma("S", T.yn[:], wo(4, 576, 592), "WO4l", "yn", "o_yn")
     emit()
     for n in ("yc", "yb", "yf", "yn"):
         g.wait_ge(T.sem["o_" + n], 16)

@@ -2,26 +2,37 @@ import numpy as np
 from concourse.mybir import AluOpType as A, AxisListType, ActivationFunctionType as AF
 
 NXG, NCL, NY = 12, 12, 8
-SCAN = 2
-MP = 4
+SCAN = 1
+MP = 2
+EACH, SWAP, FLAG, TURN = {4: (1.75, 32.0, 5.4375, 149.0 / 16384), 2: (1.390625, 32.109375, 17.0, 11.0 / 512)}[MP]
 NQ, CC = 8 // MP, MP // 2
-PLAN = ("S1 V1 S2 V2 S2 S4 V1 S3 V2 S2 S2 V2 S2 S2 S2 S1 V1", "V2 S2 S2 V2 S4 S4 V2 S2 S4 S4 S2 V1 S1")
-DS, WS = 8, 6
-FLAGS = ((0, 8), (8, 12), (12, 16))
-OFFS = ((0, 12), (12, 16))
-HCOL, ACOL = (64, 128, 0, 448), 192
-SENDS = ((64, 128, "h0"), (128, 320, "h1 a0 a1"), (0, 64, "h2"), (320, 592, "a2 a3 h3 l"))
+PLAN = ("S1 S1 V2 S2 V2 S2 V2 S2 S2 S2 V2 S2 V2 S2 S2 V2 S1 S1",
+        "S1 S1 V2 S2 S2 S2 V2 S2 S2 S2 V2 S2 V2 S2 S2 V2 S1 S1",
+        "V2 S2 V2 S2 S2 V2 S2 S2 S2 V1 S1 S2 S2 S2 S2 S1 S1 S1 S1")
+DS, WS = 10, 6
+RULES = ((), ("nurses c22",))
+DG = 4
+LATE = "S"
+QU = (0, 4, 8, 12, 16) if MP == 2 else (0, 4, 10, 14, 16)
+PART = [k for k in range(4) for _ in range(QU[k], QU[k + 1])]
+STAGES = ((0, QU[2]), (QU[2], QU[3]), (QU[3], 16))
+OFFS = STAGES
+XFS = " ".join("xf%d" % a for a, b in OFFS)
+HCOL, ACOL = (0, 16 * QU[1], 16 * QU[2], 16 * QU[3] + 256), 16 * QU[3]
+SENDS = ((0, HCOL[1], "h0", 0), (HCOL[1], HCOL[2], "h1", 1), (HCOL[2], ACOL, "h2", 2), (ACOL, 2 * ACOL, "a0 a1 a2", 2),
+         (2 * ACOL, 512, "a3 h3", 3))
 MAGIC = 1.5 * 2 ** 23
+MID = 288.0
 MODELS = ((0.83, 1.3, 3.2, 0.45, 215, 300, 1400, 8, 4.5), (1.1, 2.0, 4.6, 0.6, 240, 400, 2000, 12, 5.5),
-          (0.9, 1.15, 2.6, 0.49, 230, 550, 2300, 14, 6.0))
+          (0.9, 1.15, 2.6, 0.49, 230, 550, 2300, 14, 7.5), (0.86, 1.75, 4.3, 0.46, 220, 400, 1800, 10, 6.0))
 CYC, GAT, SCA, PEC, HOP, ISSUE, FAR, ROW, COL = np.array(MODELS).T
 XF, FIRST = 9100, 2800
 MARK = "SPB|Z ACC"
-STARTS, PASSES, SHORT, LONG = 6, 50, 30, 380
+STARTS, PASSES, SHORT, LONG = 8, 40, 25, 700
 WIDE, PATIENCE, REACH, FREE, TENURE, SEED = 110, 60, 10, 600, 10, 1
 ORDER = []
 INFO = []
-FL, BF, I32, U16 = "float32", "bfloat16", "int32", "uint16"
+FL, BF, HF, I32, U16 = "float32", "bfloat16", "float16", "int32", "uint16"
 
 
 def _scratch():
@@ -29,48 +40,53 @@ def _scratch():
 
     def sb(names, cols, dt):
         for n in names.split():
-            s[n] = ("sbuf", [128, cols], dt)
+            s[n] = ("sbuf", [128] + (cols if isinstance(cols, list) else [cols]), dt)
     sb("xfs D1", 8192, BF)
     sb("XG", 512 * NXG, BF)
     sb("CL", 512 * NCL, BF)
     sb("YV CV", 256 * NY, BF)
-    for n in ("WH", "WA", "SELB"):
-        s[n] = ("sbuf", [128, 16, 8, 16], BF)
-    s["Z"] = ("sbuf", [128, 4 * CC, 8, 16], BF)
-    s["LO8"] = ("sbuf", [128, 8, 16], BF)
-    sb("BZ", 1024, BF)
-    sb("TR IOTC XB0 U", 512, BF)
-    sb("pfs pns LO HI SG AB MM MROW", 256, BF)
-    sb("SELW SELW2 SELW3", 144, BF)
-    sb("ONES IDENT I256 HB NHB G16 KK TI LB TM FT PABX BT SBH RB", 128, BF)
-    sb("BB", 96, BF)
-    sb("EUW", 48 * NQ, BF)
-    sb("C16", 64, BF)
-    sb("RS RX", 32, BF)
+    sb("WH WA SELB", [16, 8, 16], BF)
+    sb("Z", [4 * CC, 8, 16], BF)
+    sb("LO8", [8, 16], BF)
+    sb("BB", [30, 16], BF)
+    sb("BO", [24, 16], BF)
+    sb("MC", [6, 16], BF)
+    sb("QA", [7, NQ], BF)
+    sb("EUW", [2, 48 * NQ], BF)
+    sb("UB", 1024, BF)
+    sb("TR IOTC XB0 U OWN", 512, BF)
+    sb("pfs pns LO HI SG MM", 256, BF)
+    sb("SELW SELJ SELX SELR", 144, BF)
+    sb("ONES NEG IDENT NID G16 KK TI LB TM FT PABX BT S1 S2 CM", 128, BF)
+    sb("RS RX SA SI", 32, BF)
     sb("LL", 24, BF)
-    sb("P2", 18, BF)
-    sb("NF THR LTB RTB SB9 X16", 16, BF)
-    sb("QS", 6 * NQ, BF)
-    sb("WI WO", 608 * 5, FL)
+    sb("P2 LTB", 18, BF)
+    sb("TA", [2, 16], BF)
+    sb("NI TB TC RTB SB9 X16", 16, BF)
+    sb("MROW", 256, HF)
+    sb("WI WO", 512 * 5, FL)
     sb("UF", 1536, FL)
     sb("AFL", 256 * 5, FL)
     sb("CBF YC", 512, FL)
     sb("IDX PS", 256, FL)
-    sb("IDF NIDF HALF QUART PABW", 128, FL)
-    sb("XX TRN", 96, FL)
-    sb("YL32 BL B1", 32, FL)
+    sb("HALF QUART", 128, BF)
+    sb("IDF NIDF PABW", 128, FL)
+    sb("XX DF", 48, FL)
+    sb("BL YO", 32, FL)
     sb("LI TWO", 16, FL)
-    sb("BC G8 ACC", 8, FL)
-    sb("THN PMF PIF DD LX1 C2", 2, FL)
+    sb("G8", 8, FL)
+    sb("ACC", 12, FL)
+    sb("THN PMF PIF DD LX1 C2 BC SC", 2, FL)
     sb("cbs", 512, I32)
-    sb("MA", 32 * 5, I32)
-    sb("DM", 32 * 4, I32)
-    sb("bss BI0 BI1 BI2 AL32", 32, I32)
-    sb("fss nbs OI1 OI2 BASE ELS AL", 16, I32)
-    sb("ths TH PI PM RI", 2, I32)
+    sb("bss BI1 BI2", 32, I32)
+    sb("fss nbs ELS BI0 BIT", 16, I32)
+    sb("ths TH PI PM", 2, I32)
     sb("UH UA", 256, U16)
-    sb("bsU XLU YL", 32, U16)
-    sb("fsU nbU OFFU GU FU ALU", 16, U16)
+    sb("AL", 16 * 5, U16)
+    sb("DM YL", 64, U16)
+    sb("OF", [2, 16], U16)
+    sb("bsU XLU", 32, U16)
+    sb("fsU nbU GU", 16, U16)
     for n in ("PB0", "PB1", "PB2", "PB3"):
         s[n] = ("psum", [128, 4, 8, 16], FL)
     for n in ("PT", "PD", "PN"):
@@ -83,7 +99,7 @@ SCRATCH = _scratch()
 BANKS = ("PB0", "PB1", "PB2", "PB3", "PT", "PD", "PL", "PN")
 LOADS = ["pf", "pn", "fs", "bs", "nb", "th", "cb", "xf"]
 SEMAPHORES = (["qV", "qS", "qP", "qG", "loc"] + ["d_" + n for n in LOADS] + ["o_yc", "o_yb", "o_yf", "o_yn"]
-              + ["a%s_%d" % (k, t) for k in list(range(len(SENDS))) + ["m"] for t in range(1, 5)])
+              + ["a%s_%d" % (k, t) for k in list(range(len(SENDS))) + ["m", "l"] for t in range(1, 5)])
 
 
 def issue_order(calls):
@@ -93,22 +109,23 @@ def issue_order(calls):
     qn = ["VSPGD".index(c["q"]) for c in calls]
     NS, LATE, DUR = [np.array([c[k] + 0 * CYC for c in calls]).T for k in ("ns", "late", "far")]
     NS, LATE = np.maximum(NS, DUR), LATE + np.minimum(NS, DUR)
-    reach, waited, need, serve = [0] * n, [0] * n, [], [[] for _ in range(n)]
+    reach, waited, need, serve, soft = [0] * n, [0] * n, [], [[] for _ in range(n)], []
     for j, c in enumerate(calls):
-        soft = {i for i in c["pre"] if qn[i] == qn[j] == 2}
-        for i in c["pre"]:
+        pre = c["pre"] | c["rule"]
+        soft.append({i for i in pre if qn[i] == qn[j] == 2 or i not in c["pre"]})
+        for i in pre:
             reach[j] |= reach[i]
-            waited[j] |= waited[i] if i in soft else reach[i]
-        need.append([i for i in c["pre"] if not (reach[j] if i in soft else waited[j]) >> i & 1])
-        for i in c["pre"]:
+            waited[j] |= waited[i] if i in soft[j] else reach[i]
+        need.append([i for i in pre if not (reach[j] if i in soft[j] else waited[j]) >> i & 1])
+        for i in pre:
             reach[j] |= 1 << i
-            waited[j] |= (i not in soft) << i
+            waited[j] |= (i not in soft[j]) << i
         for i in need[j]:
             serve[i].append(j)
     sets = []
     for ns, late in list(zip(NS.tolist(), LATE.tolist())) + [(NS.mean(0).tolist(), LATE.mean(0).tolist())]:
-        sets.append((ns, [[(i, 0.0 if qn[i] == qn[j] == 2 else late[i]) for i in need[j]] for j in range(n)],
-                     [[(j, 0.0 if qn[i] == qn[j] == 2 else late[i]) for j in serve[i]] for i in range(n)],
+        sets.append((ns, [[(i, 0.0 if i in soft[j] else late[i]) for i in need[j]] for j in range(n)],
+                     [[(j, 0.0 if i in soft[j] else late[i]) for j in serve[i]] for i in range(n)],
                      [0.0 if serve[i] else late[i] for i in range(n)]))
     names = sorted({c["name"][1:] for c in calls})
     twin = {c["name"]: i for i, c in enumerate(calls)}
@@ -324,9 +341,11 @@ def rank_program(g, core, T, topo):
     N = len(T.cores)
     Q = {"V": g.vector, "S": g.scalar, "P": g.tensor, "G": g, "D": g.sync}
     calls, count, now = [], {}, [-1]
-    whole, parts, rd = {}, {}, {}
+    whole, parts, rd, called = {}, {}, {}, {}
 
     def record(q, fns, R, W, ns, late=HOP, tok=None, far=0):
+        called.update(((now[0], k[1:]), len(calls)) for k in W.split() if k[0] == "#")
+        W, rule = " ".join(k for k in W.split() if k[0] != "#"), set()
         name = (now[0], q + "".join(x for x in R + "|" + W if not x.isdigit()))
         count[name] = count.get(name, -1) + 1
         R, W, pre = R.split(), W.split(), set()
@@ -338,7 +357,7 @@ def rank_program(g, core, T, topo):
             pre.update(parts.get(k, []) if k[0] != "+" else whole.get(k[1:], []))
             pre.update(rd.get(k.lstrip("+"), []))
         i = len(calls)
-        calls.append({"q": q, "fns": fns, "pre": pre, "ns": ns, "late": late, "tok": tok, "far": far, "name": name + (count[name],)})
+        calls.append({"q": q, "fns": fns, "pre": pre, "rule": rule, "ns": ns, "late": late, "tok": tok, "far": far, "name": name + (count[name],)})
         for k in R:
             rd.setdefault(k, []).append(i)
         for k in W:
@@ -347,7 +366,22 @@ def rank_program(g, core, T, topo):
             else:
                 whole[k], parts[k], rd[k] = [i], [i], []
 
+    def obey():
+        for t in range(5):
+            for line in RULES[t // 4]:
+                line = [called[t + (x[0] == "+"), x.lstrip("+")] for x in line.split()]
+                for a, b in zip(line, line[1:]):
+                    if a != b:
+                        calls[b]["rule"].add(a)
+        new, left = {}, list(range(len(calls)))
+        while left:
+            i = next(i for i in left if all(x in new for x in calls[i]["pre"] | calls[i]["rule"]))
+            left.remove(i)
+            new[i] = len(new)
+        calls[:] = [dict(calls[i], pre={new[x] for x in calls[i]["pre"]}, rule={new[x] for x in calls[i]["rule"]}) for i in new]
+
     def emit():
+        obey()
         cnt = {"V": 0, "S": 0, "P": 0, "G": 0}
         seen = {q: {} for q in Q}
         snap, tok = {}, {}
@@ -413,6 +447,9 @@ def rank_program(g, core, T, topo):
     def mms(l, R, W, n):
         record("P", [lambda e, m=m: e.matmul(*m) for m in l], R, W, n * PEC)
 
+    def group(l, R, W, n, st=True, stop=True):
+        mms([m + (st and x == 0, stop and x == len(l) - 1) for x, m in enumerate(l)], R, W, n)
+
     def iota(o, pat, base, cm, W, n=16, R="", **kw):
         record("G", [lambda e: e.iota(o, pat, base, cm, **kw)], R, W, 130 + 2 * n * CYC)
 
@@ -428,27 +465,49 @@ def rank_program(g, core, T, topo):
     def sca(n):
         return 50 + SCA * n
 
-    def conv(out, row, a, n, R, W, st=True, tab="SELW"):
-        mms([(out, T[tab][:, 15 - l:143 - l], row[:, a + l:a + 16 * (n - 1) + l + 1:16], st and l == 0, l == 15)
-             for l in range(16)], R + " " + tab, W, 1024)
+    def conv(out, row, a, n, R, W, st=True, stop=True, tab="SELW"):
+        group([(out, T[tab][:, 15 - l:143 - l], row[:, a + l:a + 16 * (n - 1) + l + 1:16]) for l in range(16)], R + " " + tab, W, 1024, st, stop)
 
     def part(q):
         return slice(16 * MP * q, 16 * MP * (q + 1))
 
+    def names(x, j, n):
+        return "".join(" #%s%d" % (x, j + y) for y in range(n))
+
+    def wide(k):
+        return 16 * (QU[k + 1] - QU[k])
+
+    def pairs(k):
+        return slice(16 * QU[k], 16 * QU[k + 1])
+
+    def blocks(k):
+        return range(QU[k] // NQ, QU[k + 1] // NQ)
+
+    def nurses(w, t, k):
+        return w[:, 512 * t + HCOL[k]:512 * t + HCOL[k] + wide(k)]
+
+    def fill(q, o, c, W, n, p=slice(0, 128), R=""):
+        if q == "V":
+            vec(lambda e: e.memset(o, c), R, W, 0)
+        elif q == "S":
+            act(o, T.ONES[p, 0:n], "ONES " + R, W, n * CYC, scale=c)
+        else:
+            sel(o, T.ONES[p, 0:n], [[0, n]], A.is_gt, c, 0, 0, "ONES " + R, W, n)
+
     def wi(t, a, b):
-        return T.WI[:, 608 * t + a:608 * t + b]
+        return T.WI[:, 512 * t + a:512 * t + b]
 
     def wo(t, a, b):
-        return T.WO[:, 608 * t + a:608 * t + b]
+        return T.WO[:, 512 * t + a:512 * t + b]
 
     def afl(t, a, b):
         return T.AFL[:, 256 * t + a:256 * t + b]
 
-    def bb(a, b):
-        return T.BB[:, 16 * a:16 * b]
+    def bb(t, a, b, step=1, c=slice(0, 16)):
+        return T.BB[:, 6 * t + a:6 * t + b:step, c]
 
-    def c16(n):
-        return T.C16[:, 16 * n:16 * n + 16]
+    def big(out, n, cols, w="ONES"):
+        return (out, T[w][0:n, :], T.CM[0:n, 0:cols])
 
     dma("S", T.pns[:], T.pn[:], "", "pns", "d_pn", 1900)
     dma("D", T.pfs[:], T.pf[:], "", "pfs", "d_pf", 2300)
@@ -457,30 +516,34 @@ def rank_program(g, core, T, topo):
     dma("S", T.cbs[:], T.cb[:], "", "cbs", "d_cb", 3700)
     dma("D", T.fss[:], T.fs[:], "", "fss", "d_fs", 4000)
     dma("D", T.ths[:, 0:1], T.th[:], "", "ths", "d_th", 4300)
-    dma("D", T.xfs[:], T.xf[:], "", "xfs xfsb", "d_xf", XF)
+    dma("D", T.xfs[:], T.xf[:], "", XFS, "d_xf", XF)
 
     ms(T.ONES[:], 1.0, "ONES")
+    low = slice(0, 32)
+    fill(LATE, T.NEG[low, :], -1.0, "NEG", 128, low)
+    fill(LATE, T.CM[:], MAGIC, "CM", 128)
     ms(T.TR[0:32, 0:128], -1024.0, "TR")
     ms(T.SELW[:], 0.0, "SELW")
     ms(T.LL[:], 0.0, "LL")
-    ms(T.EUW[:], 0.0, "EUW")
-    ms(T.QS[:], 0.0, "QS")
-    for q in range(NQ):
-        ms(T.QS[part(q), q::NQ], 0.5, "+QS")
+    ms(T.EUW[:], 0.0, "EUW0", 48 * NQ * CYC)
+    for a, b, w in ((0, 1, -0.5), (1, 2, -FLAG), (2, 3, 0.5), (3, 4, FLAG), (4, 7, -TURN)):
+        fill(LATE, T.QA[:, a:b, :], w, "+QA0", NQ * (b - a))
+    for a, b, x in ((0, 1, 32), (1, 2, 512), (2, 5, 1)):
+        fill(LATE, T.MC[low, a:b, :], x * MAGIC, "+MC", 16 * (b - a), low)
+    sel(T.QA[:], T.QA[:], [[0, 7], [-16 * MP, NQ]], A.is_ge, 0.0, 0, 1, "QA0", "QA", 7 * NQ)
+    sel(T.QA[:], T.QA[:], [[0, 7], [16 * MP, NQ]], A.is_ge, 0.0, 16 * MP - 1, -1, "QA", "QA", 7 * NQ)
     ms(T.TM[0:32, :], 16.0, "TM")
-    ms(T.HALF[:], 0.5, "HALF", 128 * CYC)
-    ms(T.QUART[:], 0.0, "QUART", 128 * CYC)
-    ms(T.HALF[:, ::8], 0.0, "+HALF")
+    ms(T.HALF[:], 0.5, "HALF")
+    ms(T.QUART[:], 0.0, "QUART")
     ms(T.QUART[:, ::8], 0.125, "+QUART")
     ms(T.X16[:], 0.0, "X16")
     ms(T.TWO[:], 2.0, "TWO")
-    ms(T.ACC[:, 4:5], 1.0 / 128, "ACC4")
+    fill(LATE, T.ACC[:, 0:1], 1.0 / 128, "ACC4", 1)
     ms(T.SB9[:], 1.0, "SB9")
-    act(c16(1), T.ONES[:, 0:16], "ONES", "+C16", 1300, f=AF.Silu, scale=32768.0)
-    for n, x in ((0, 16.0), (2, 32.0), (3, 48.0)):
-        act(c16(n), T.ONES[:, 0:16], "ONES", "+C16", scale=x)
-    ms(T.FT[0:32, :], 0.5, "FT")
-    ms(T.RTB[:], -1.0, "RTB")
+    act(T.SA[:, 0:16], T.ONES[:, 0:16], "ONES", "SA", 1300, f=AF.Silu, scale=32.0)
+    fill(LATE, T.FT[low, :], 0.5, "FT", 128, low)
+    fill(LATE, T.RTB[:, 0:8], 0.0, "+RTB0", 8)
+    fill(LATE, T.RTB[:, 8:16], 1.0, "+RTB0", 8)
     for n in range(0, NXG, 2):
         ms(T.XG[:, 512 * n:512 * n + 1024:2], 0.0, "XG%d XG%d" % (n, n + 1), 256 * CYC)
     iota(T.PI[:, 0:1], [[1, 1]], 0, 1, "PI")
@@ -495,10 +558,9 @@ def rank_program(g, core, T, topo):
     sel(r32, r32, [[-1, 8], [0, 16]], A.not_equal, 1.0, 0, 1, "TR", "TR")
     sel(r32, r32, [[-1, 8], [0, 16]], A.not_equal, 1.0, -8, 1, "TR", "TR")
     sel(T.IDENT[:], T.ONES[:], [[-1, 128]], A.is_equal, 0.0, 0, 1, "ONES", "IDENT")
-    sel(T.SELW[:, 0:128], T.G16[:], [[0, 8], [1, 16]], A.is_equal, 0.0, -15, 0, "G16", "SELW")
-    fiota(T.LI[:], [[16, 16]], 1, 0, "LI")
-    iota(T.BASE[:], [[512, 16]], 8 * MP, 0, "BASE")
-    for w, x in (("IDF", 1.0), ("NIDF", -1.0), ("I256", 256.0), ("HB", 0.5), ("NHB", -0.5)):
+    act(T.SELW[:, 15:128:16], T.G16[:, ::16], "G16", "SELW", scale=0.0625)
+    fiota(T.LI[:], [[16, 16]], 0, 0, "LI")
+    for w, x in (("IDF", 1.0), ("NIDF", -1.0), ("NID", -1.0)):
         act(T[w][:], T.IDENT[:], "IDENT", w, 128 * CYC, scale=x)
 
     pn = T.PD[:, 0:256]
@@ -513,13 +575,16 @@ def rank_program(g, core, T, topo):
     cp(T.bsU[:], T.bss[:], "bss", "bsU")
     cp(T.fsU[:], T.fss[:], "fss", "fsU")
     for k in range(4):
-        act(wi(0, HCOL[k], HCOL[k] + 64), T.CBF[:].indirect(T.nbU[:, 4 * k:4 * k + 4]), "CBF nbU", "WI0_%d" % k, gat(64))
+        act(nurses(T.WI, 0, k), T.CBF[:].indirect(T.nbU[:, QU[k]:QU[k + 1]]), "CBF nbU", "WI0_%d" % k, gat(wide(k)))
     for k in range(16):
         if k < DS:
             act(T.D1[:, 2 * k::32], T.HI[:], "HI", "+D1", 256 * CYC)
         else:
             cp(T.D1[:, 2 * k::32], T.HI[:], "HI", "+D1", 128 * CYC)
-        cp(T.D1[:, 2 * k + 1::32], T.LO[:], "LO", "+D1", 128 * CYC)
+        if k < DG:
+            sel(T.D1[:, 2 * k + 1::32], T.LO[:], [[0, 256]], A.is_ge, 0.0, 0, 0, "LO", "+D1", 256)
+        else:
+            cp(T.D1[:, 2 * k + 1::32], T.LO[:], "LO", "+D1", 128 * CYC)
     for n in range(8):
         ts(T.WH[:, :, n, :], T.SG[:], T.G16[:, 16 * n:16 * n + 1], -1.0, A.mult, A.mult, "SG G16", "+WH", 128 * CYC)
         if n < WS:
@@ -533,74 +598,87 @@ def rank_program(g, core, T, topo):
         ts(T.TH[:, n:n + 1], T.ths[:, 0:1], 1, bits, A.arith_shift_right, A.bitwise_and, "ths", "TH%d" % n)
         ts(T.THN[:, n:n + 1], T.TH[:, n:n + 1], 0.5 * n, -1.0, A.add, A.mult, "TH%d" % n, "THN%d" % n)
         ts(T.LL[:, 8 * n:8 * n + 8], T.G16[:, ::16], T.THN[:, n:n + 1], None, A.mult, None, "G16 THN%d" % n, "+LL")
-    for n in range(1, CC):
-        cp(T.TR[0:32, 128 * n:128 * n + 128], r32, "TR", "+TRb")
+    for n in range(1, max(len(blocks(k)) for k in range(4))):
+        act(T.TR[0:32, 128 * n:128 * n + 128], r32, "TR", "+TRb", 128 * CYC)
     mms([(T.PL[0:24, 0:2, :], T.LL[:, 0:24], T.KK[:], True, True)], "LL KK", "PL", 128)
     tt(T.TI[0:24, :], T.PL[0:24, 0:2, :], T.TM[0:24, :], A.add, "PL TM", "TI", 128 * CYC)
-    ts(T.SELW[:], T.SELW[:], 0.0625, None, A.mult, None, "SELW", "SELW")
     for q in range(NQ):
-        ts(T.EUW[part(q), 48 * q + 16:48 * q + 32], T.KK[part(q), 0:16], 32.0, 1.0, A.mult, A.add, "KK", "+EUW")
-    ts(T.THR[:], T.LI[:], T.PMF[:, 0:1], 4.0, A.add, A.mult, "LI PMF", "THR")
-    ts(T.PMF[:, 1:2], T.PM[:, 0:1], 32.0, None, A.mult, None, "PM", "PMF1")
-    cp(T.BI0[:, 0:16], T.fss[:], "fss", "+BI0")
-    ts(T.BC[:, 4:5], T.PMF[:, 0:1], 8.0, None, A.is_ge, None, "PMF", "BC4")
-    for n, (a, b) in enumerate(((256.0, 32.0), (-257.0, -31.0), (-2046.0, 2048.0), (2.0, 0.0))):
-        ts(T.BC[:, n:n + 1], T.BC[:, 4:5], a, b, A.mult, A.add, "BC4", "+BC")
-    ts(T.SELW2[:], T.SELW[:], T.BC[:, 2:3], None, A.mult, None, "SELW BC", "SELW2", 72 * CYC)
-    ts(T.SELW3[:], T.SELW[:], T.BC[:, 3:4], None, A.mult, None, "SELW BC", "SELW3", 72 * CYC)
-    fiota(T.SELB[:, :, :, 0:8], [[0, 1024]], 0, 0, "SELB", 1024)
-    sel(T.SELB[:, :, :, 8:16], T.SELB[:, :, :, 0:8], [[-1, 16], [-16, 8], [0, 8]], A.not_equal, 1.0, 0, 1, "SELB", "SELB", 1024)
-    ms(T.LO8[:, :, 0:8], 1.0 / 128, "+LO8")
-    ms(T.LO8[:, :, 8:16], 0.0, "+LO8")
-    ts(bb(4, 5), T.nbs[:], -256.0, None, A.add, None, "nbs", "+BH")
-    fiota(T.UF[:, 512:1536], [[0, 1024]], 16416, 0, "UFb", 1024)
-    fiota(T.YC[:], [[1, 512]], 32, 0, "YC", 512)
-    act(T.UF[:, 0:512].indirect(T.bsU[:]), T.YC[:], "YC bsU C16", "UF", sca(512), f=AF.Silu)
+        act(T.EUW[part(q), 0, 48 * q + 16:48 * q + 32], T.KK[part(q), 0:16], "KK EUW0", "+EUW", f=AF.Identity, scale=SWAP, bias=EACH)
+        act(T.EUW[part(q), 1, 48 * q + 16:48 * q + 32], T.KK[part(q), 0:16], "KK EUW0", "+EUW4")
+    tt(T.BC[:], T.KK[:, 0:16:8], T.KK[:, 4:16:8], A.subtract, "KK", "BC")
+    ts(T.SELJ[:], T.SELW[:], T.BC[:, 0:1], 16.0, A.mult, A.mult, "SELW BC", "SELJ", 72 * CYC)
+    ts(T.SELX[:], T.SELW[:], T.BC[:, 1:2], 16.0, A.mult, A.mult, "SELW BC", "SELX", 72 * CYC)
+    ts(T.SELR[:], T.SELW[:], T.KK[:, 8:9], -16.0, A.mult, A.mult, "SELW KK", "SELR", 72 * CYC)
+    ts(T.NI[:], T.LI[:], T.PMF[:, 0:1], -1.0, A.add, A.mult, "LI PMF", "NI")
+    for a, b in OFFS:
+        act(T.TB[:, a:b], T.NI[:, a:b], "NI", "+TB", f=AF.Identity, scale=-32.0, bias=-512.0 * a)
+
+    def sites(x, n, R, W):
+        s = slice(16 * (n // 3), 16 * (n // 3) + 16)
+        ts(T.BI1[:, s], x, 510, None, A.bitwise_and, None, R, "BI1%d" % n)
+        ts(T.BI2[:, s], T.BI1[:, s], 2.0, -255.0, A.mult, A.add, "BI1%d" % n, "BI2%d" % n)
+        ts(bb(0, n, n + 1), x, -256.0, None, A.add, None, R, W)
+        tt(bb(0, n + 1, n + 2), T.BI2[:, s], x, A.subtract, "BI2%d %s" % (n, R), W)
+
+    def nurses_sites():
+        fiota(T.YC[:], [[1, 512]], 32, 0, "YC", 512)
+        for a in range(0, 32, 8):
+            act(wo(4, 0, 512).indirect(T.bsU[:, a:a + 8]), T.YC[:, 16 * a:16 * a + 128], "YC bsU SA", "INV", sca(128), f=AF.Silu)
+        act(T.XB0[:, 256:512], wo(4, 0, 512).indirect(T.nbU[:]), "INV nbU", "XB1", gat(256), f=AF.Identity, bias=-288.0)
+        conv(T.PN[:, 256:272], T.XB0, 256, 16, "XB1", "PN")
+        ts(T.BI0[:], T.PN[:, 256:272], 256.0, None, A.add, None, "PN", "BI0")
+        sites(T.BI0[:], 3, "BI0", "+BG0")
+
+    sites(T.fss[:], 0, "fss", "+BB0")
+    ms(T.SELB[:, :, :, 0:8], 0.0, "SELB", 512 * CYC)
+    for a, x in ((8, 1.0), (12, -1.0)):
+        sel(T.SELB[:, :, :, a:a + 4], T.SELB[:, :, :, 0:4], [[-1, 16], [-16, 8], [0, 4]], A.not_equal, x, 0, 1, "SELB", "+SELBb", 512)
+    for a, b, x in ((0, 4, 1.0 / 128), (4, 8, -1.0 / 128), (8, 16, 0.0)):
+        fill(LATE, T.LO8[:, :, a:b], x, "+LO8", 8 * (b - a))
+    ts(bb(0, 5, 6), T.nbs[:], -256.0, None, A.add, None, "nbs", "+BB0")
+    fiota(T.UF[:, 0:512], [[0, 512]], 16416, 0, "UFb", 512)
     conv(T.PN[:, 0:16], T.pfs, 0, 16, "pfs", "PN")
     ts(T.ELS[:], T.PN[:, 0:16], 16.0, None, A.mult, None, "PN", "ELS")
     ts(T.ELS[:], T.ELS[:], 31, None, A.bitwise_and, None, "ELS", "ELS")
-    tt(T.ELS[:], T.ELS[:], T.BASE[:], A.add, "ELS BASE", "ELS")
-    act(T.MROW[:], T.UF[:, 0:512].indirect(T.nbU[:]), "UF nbU", "MROW", gat(256), f=AF.Identity, bias=-288.0)
-    conv(T.PN[:, 16:32], T.MROW, 0, 16, "MROW", "PN")
-    ts(T.BI0[:, 16:32], T.PN[:, 16:32], 256.0, None, A.add, None, "PN", "+BI0")
-    ts(T.BI1[:], T.BI0[:], 510, None, A.bitwise_and, None, "BI0", "BI1")
-    ts(T.BI2[:], T.BI1[:], 2.0, -255.0, A.mult, A.add, "BI1", "BI2")
-    for n in range(2):
-        s = slice(16 * n, 16 * n + 16)
-        ts(bb(2 * n, 2 * n + 1), T.BI0[:, s], -256.0, None, A.add, None, "BI0", "+BH")
-        tt(bb(2 * n + 1, 2 * n + 2), T.BI2[:, s], T.BI0[:, s], A.subtract, "BI2 BI0", "+BH")
+    fill(LATE, T.TA[:, 1, :], 0.0, "+TA", 16)
+    ts(T.TA[:, 0, :], T.ELS[:], -1.0, 15.5 - 8 * MP, A.mult, A.add, "ELS", "+TA")
+    ts(T.TC[:], T.ELS[:], 8.0 * MP - 256, None, A.add, None, "ELS", "TC")
     cp(T.PIF[:, 0:1], T.PI[:, 0:1], "PI", "PIF")
-    vec(lambda e: e.tensor_tensor_scan(T.PABW[:], T.HALF[:], T.QUART[:], 0.0, A.mult, A.add), "HALF QUART", "PABW", 128 * CYC)
+    vec(lambda e: e.tensor_tensor_scan(T.PABW[:], T.HALF[:], T.QUART[:], 0.0, A.mult, A.max), "HALF QUART", "PABW", 128 * CYC)
     vec(lambda e: e.tensor_tensor_scan(T.P2[:, 0:9], T.TWO[:, 0:9], T.X16[:, 0:9], 0.5, A.mult, A.add), "TWO X16", "P2", 0)
-    ts(T.BI1[:, 0:5], T.PABW[:, 0:5], T.PIF[:, 0:1], 2048.0, A.mult, A.mult, "PABW PIF", "BI1")
-    ts(T.BI2[:, 0:5], T.BI1[:, 0:5], 256, None, A.bitwise_and, None, "BI1", "BI2")
-    ts(T.SB9[:, 0:4], T.BI2[:, 0:4], -1.0 / 128, 1.0, A.mult, A.add, "BI2", "+SB9")
-    ts(T.RTB[:, 4:9], T.BI2[:, 0:5], 1.0 / 128, -1.0, A.mult, A.add, "BI2", "+RTB")
+    ts(T.BIT[:, 0:5], T.PABW[:, 0:5], T.PIF[:, 0:1], 2048.0, A.mult, A.mult, "PABW PIF", "BIT")
+    ts(T.BIT[:, 0:5], T.BIT[:, 0:5], 256, None, A.bitwise_and, None, "BIT", "BIT")
+    ts(T.SB9[:, 0:4], T.BIT[:, 0:4], -1.0 / 128, 1.0, A.mult, A.add, "BIT", "+SB9")
+    ts(T.RTB[:, 3:8], T.BIT[:, 0:5], -1.0 / 256, None, A.mult, None, "BIT RTB0", "+RTB")
+    ts(T.RTB[:, 11:16], T.BIT[:, 0:5], -1.0 / 256, 1.0, A.mult, A.add, "BIT RTB0", "+RTB")
     tt(T.LTB[:, 1:9], T.SB9[:, 1:9], T.P2[:, 1:9], A.mult, "SB9 P2", "+LTB")
+    ts(T.LTB[:, 9:17], T.P2[:, 1:9], -1.0, None, A.mult, None, "P2", "+LTB")
     tt(T.LX1[:, 0:1], T.PMF[:, 0:1], T.SB9[:, 0:1], A.add, "PMF SB9", "LX1")
-    mms([(T.PT[0:8, 0:128], T.LTB[:, 1:9], T.IDENT[:], True, True),
-         (T.PT[0:8, 128:160], T.RTB[:, 1:9], T.IDENT[:, 0:32], True, True)], "LTB RTB IDENT", "PT", 160)
-    act(T.LB[0:8, :], T.PT[0:8, 0:128], "PT", "LB", 128 * CYC)
-    act(T.RX[0:8, :], T.PT[0:8, 128:160], "PT", "RX")
-    act(T.PABX[0:32, :], T.PABW[0:32, :], "PABW", "PABX", 128 * CYC, scale=2.0)
-    m = T.SBH[0:32, :]
-    sel(m, T.ONES[0:32, :], [[-1, 16], [0, 8]], A.is_equal, 0.0, 0, 1, "ONES", "SBH")
-    sel(m, m, [[0, 128]], A.not_equal, 1.0, -16, 1, "SBH", "SBH")
-    tt(m, m, T.PABX[0:32, :], A.mult, "PABX SBH", "SBH", 256 * CYC)
-    sel(m, m, [[0, 128]], A.not_equal, 384.0, -17, 1, "SBH", "SBH")
-    ts(T.P2[:, 8:9], T.P2[:, 8:9], -1.0, None, A.mult, None, "P2", "P2")
-    cp(T.P2[:, 9:17], T.P2[:, 1:9], "P2", "P2")
+    ts(T.SC[:, 0:1], T.SB9[:, 0:1], -1.0, None, A.mult, None, "SB9", "+SC")
+    ts(T.SC[:, 1:2], T.SB9[:, 0:1], 512.0, 256.0, A.mult, A.add, "SB9", "+SC")
+    mms([(T.PT[0:16, 0:128], T.LTB[:, 1:17], T.IDENT[:], True, True),
+         (T.PT[0:16, 128:160], T.RTB[:], T.IDENT[:, 0:32], True, True)], "LTB RTB IDENT", "PT", 160)
+    act(T.LB[0:16, :], T.PT[0:16, 0:128], "PT", "LB", 128 * CYC)
+    act(T.RX[0:16, :], T.PT[0:16, 128:160], "PT", "RX")
+    act(T.PABX[0:32, :], T.PABW[0:32, :], "PABW", "PABX", 128 * CYC, scale=4.0)
+    m = T.S2[0:32, :]
+    sel(m, T.ONES[0:32, :], [[-1, 16], [0, 8]], A.is_equal, 0.0, 0, 1, "ONES", "S2")
+    sel(m, m, [[0, 128]], A.not_equal, 512.0, -16, 1, "S2", "S2")
+    sel(m, m, [[0, 128]], A.not_equal, 1.0, -17, 1, "S2", "S2")
+    tt(m, m, T.PABX[0:32, :], A.mult, "PABX S2", "S2", 256 * CYC)
+    ts(m, m, T.IDF[0:32, 16:17], None, A.subtract, None, "S2 IDF", "S2")
+    ts(T.S1[0:32, :], m, -1.0, T.IDF[0:32, 16:17], A.mult, A.add, "S2 IDF", "S1")
+    act(T.P2[:, 9:17], T.P2[:, 1:9], "P2", "P2")
     tt(T.P2[:, 1:17], T.P2[:, 1:17], T.KK[:, 0:16], A.mult, "P2 KK", "P2")
     vec(lambda e: e.tensor_reduce(T.C2[:, 0:1], T.P2[:, 1:17], AxisListType.X, A.add), "P2", "C2a", 0)
-    ts(T.C2[:, 1:2], T.C2[:, 0:1], -2.0, None, A.mult, None, "C2a", "C2")
+    act(T.C2[:, 1:2], T.C2[:, 0:1], "C2a", "C2", scale=-2.0)
     sel(T.X16[:], T.X16[:], [[-8, 16]], A.is_ge, 1.0, 0, 1, "X16", "X16", 16)
     sel(T.X16[:], T.X16[:], [[8, 16]], A.is_ge, 1.0, 7, -1, "X16", "X16", 16)
-    brow = T.BZ[:, 512:1024]
-    act(brow, T.IOTC[:].indirect(T.bsU[:]), "IOTC bsU", "BROW", gat(512))
-    act(T.XB0[:, 0:256], brow.indirect(T.fsU[:]), "BROW fsU", "XB0", gat(256))
+    act(T.U[:], T.IOTC[:].indirect(T.bsU[:]), "IOTC bsU", "U", gat(512))
+    act(T.XB0[:, 0:256], T.U[:].indirect(T.fsU[:]), "U fsU", "XB0", gat(256))
     conv(T.PN[:, 32:48], T.XB0, 0, 16, "XB0", "PN")
     ts(T.GU[:], T.PN[:, 32:48], 256.0, None, A.add, None, "PN", "GU")
-    cp(bb(5, 6), T.PN[:, 32:48], "PN", "BA")
+    cp(bb(0, 2, 3), T.PN[:, 32:48], "PN", "+BB0")
     act(afl(0, 0, 256), T.CBF[:].indirect(T.GU[:]), "CBF GU", "AFL0", gat(256), scale=-1.0)
 
     ring = {}
@@ -610,185 +688,191 @@ def rank_program(g, core, T, topo):
         ring[name] = a + n
         return a, " ".join("%s%d" % (name, x) for x in range(a, a + n))
 
-    def chunk(q, j, n):
+    def chunk(t, q, j, n):
         c = j % 16
-        off, key = T[("UH", "UA")[j // 16]], [("UH%d", "UA%d")[j // 16] % ((c + x) // 4) for x in range(n)]
-        a, key = T.xfs[:].indirect(off[:, 16 * c:16 * (c + n)]), "xfs xfsb " + " ".join(key)
+        off, key = T[("UH", "UA")[j // 16]], [("UH%d", "UA%d")[j // 16] % PART[c + x] for x in range(n)]
+        a, key = T.xfs[:].indirect(off[:, 16 * c:16 * (c + n)]), XFS + " " + " ".join(key)
         if q == "V":
             x, xk = slots("YV", NY, n)
             s, first = slice(256 * x, 256 * (x + n)), T.YV[:, 256 * x:256 * (x + n):16]
-            tt(T.YV[:, s], a, T.D1[:, 512 * c:512 * (c + n):2], A.min, "D1 " + key, xk, gat(256 * n))
-            tt(first, first, T.LO[:, 16 * c:16 * (c + n)], A.max, "LO " + xk, xk)
+            tt(T.YV[:, s], a, T.D1[:, 512 * c:512 * (c + n):2], A.min, "D1 " + key, xk + names("g", j, n), gat(256 * n))
+            tt(first, first, T.LO[:, 16 * c:16 * (c + n)], A.max, "LO " + xk, xk, 32 * n * CYC)
             vec(lambda e: e.tensor_tensor_scan(T.CV[:, s], T.D1[:, 512 * c + 1:512 * (c + n):2], T.YV[:, s], 0.0, A.min, A.max),
-                "D1 " + xk, xk.replace("Y", "C"), 128 * n * CYC)
-            lanes(j, n, xk.replace("Y", "C"), lambda p: T.CV[:, 256 * x + 16 * p:256 * x + 16 * (p + MP)])
+                "D1 " + xk, xk.replace("Y", "C") + names("c", j, n), 128 * n * CYC)
+            lanes(t, j, n, xk.replace("Y", "C"), lambda p: T.CV[:, 256 * x + 16 * p:256 * x + 16 * (p + MP)])
             return
         x, xk = slots("XG", NXG, n)
-        act(T.XG[:, 512 * x + 1:512 * (x + n):2], a, key, xk, gat(256 * n))
+        act(T.XG[:, 512 * x + 1:512 * (x + n):2], a, key, xk + names("g", j, n), gat(256 * n))
         for u in range(0, n, SCAN):
-            clamp(j + u, x + u, min(SCAN, n - u))
+            clamp(t, j + u, x + u, min(SCAN, n - u))
 
-    def clamp(j, x, n):
+    def clamp(t, j, x, n):
         c = j % 16
         m, mk = slots("CL", NCL, n)
         vec(lambda e: e.tensor_tensor_scan(T.CL[:, 512 * m:512 * (m + n)], T.XG[:, 512 * x:512 * (x + n)],
                                            T.D1[:, 512 * c:512 * (c + n)], 0.0, A.min, A.max),
-            "D1 " + " ".join("XG%d" % y for y in range(x, x + n)), mk, 256 * n * CYC)
-        lanes(j, n, mk, lambda p: T.CL[:, 512 * m + 32 * p + 1:512 * m + 32 * (p + MP):2])
+            "D1 " + " ".join("XG%d" % (x + y) for y in range(n)), mk + names("c", j, n), 256 * n * CYC)
+        lanes(t, j, n, mk, lambda p: T.CL[:, 512 * m + 32 * p + 1:512 * m + 32 * (p + MP):2])
 
-    def lanes(j, n, key, block):
+    def lanes(t, j, n, key, block):
         for u0 in range(n):
             c = (j + u0) % 16
-            P, w = "PB%d" % (c // 4), ("WH", "WA")[j // 16]
-            if u0 and c % 4:
+            k = PART[c]
+            P, w, cc = "PB%d" % k, ("WH", "WA")[j // 16], len(blocks(k))
+            if u0 and c != QU[k]:
                 continue
-            if j < 16 and c % 4 == 0:
-                mms([(T[P][:, 0:CC, :, :], T.TI[0:24, :], T.TR[0:24, 0:128 * CC], True, False)], "TI TR TRb", P, 128 * CC)
-            m = min(n - u0, 4 - c % 4)
-            mms([(T[P][part((c + u) % NQ), (c + u) % 4 // NQ, :, b:b + MP], block(16 * (u0 + u) + b), T[w][:, c + u, :, b:b + MP], False,
-                  j >= 16 and (c + u) % 4 >= 4 - NQ and b + MP == 16) for u in range(m) for b in range(0, 16, MP)], key + " " + w, P, 256 * m)
+            if j < 16 and c == QU[k]:
+                mms([(T[P][:, 0:cc, :, :], T.TI[0:24, :], T.TR[0:24, 0:128 * cc], True, False)], "TI TR TRb", P, 128 * cc)
+            m = min(n - u0, QU[k + 1] - c)
+            mms([(T[P][part((c + u) % NQ), (c + u - QU[k]) // NQ, :, b:b + MP], block(16 * (u0 + u) + b), T[w][:, c + u, :, b:b + MP], False,
+                  j >= 16 and c + u >= QU[k + 1] - NQ and b + MP == 16) for u in range(m) for b in range(0, 16, MP)], key + " " + w, P + names("l", j + u0, m), 256 * m)
 
     def signs(k):
-        P, z = "PB%d" % k, "Z%d" % k
-        act(T.Z[:, CC * k:CC * k + CC, :, :], T[P][:, 0:CC, :, :], P, z + " ACC%d" % k, (128 * CC + 20) * CYC, f=AF.Sign,
-            accum_out=T.ACC[:, k:k + 1])
-
-    def sums(k):
-        mms([(T.PL[:, 0, 4 * k + NQ * c:4 * k + NQ * (c + 1)], T.Z[:, CC * k + c, :, :], T.QS[:, 0:NQ], True, True) for c in range(CC)],
-            "Z%d QS" % k, "PL", 64 * CC)
-
-    def again(a, b):
-        mms([(T.PB0[:, 2, 0:6, NQ * c:NQ * (c + 1)], T.Z[:, c, :, :], T.QS[:], True, True) for c in range(a // NQ, b // NQ)],
-            " ".join("Z%d" % k for k in range(a // 4, b // 4)) + " QS", "PB0", 64 * (b - a) // NQ)
+        P, z, cc = "PB%d" % k, "Z%d" % k, len(blocks(k))
+        act(T.Z[:, QU[k] // NQ:QU[k + 1] // NQ, :, :], T[P][:, 0:cc, :, :], P, z + " ACC%d #sign%d" % (k, k), (128 * cc + 20) * CYC, f=AF.Sign,
+            accum_out=T.ACC[:, k + 1:k + 2])
 
     def total(k):
-        mms([(T.PT[:, 0:1], T.PABW[:], T.ACC[:, k:k + 1], k == 4, k == 3)], "PABW ACC%d" % k, "PT", 256)
+        if k == 2:
+            act(T.ACC[:, 8:12], T.ACC[:, 0:4], "ACC0 ACC1 ACC2 ACC4", "ACC5 #acc", accum_out=T.ACC[:, 5:6])
+        mms([(T.PT[:, 0:1], T.PABW[:], T.ACC[:, 7 - k:8 - k], k == 2, k == 3)], "PABW ACC%d" % (9 - 2 * k), "PT #total%d" % k, 256)
 
     def rows(t, k):
-        P, s, hk, ak = "PB%d" % k, slice(64 * k, 64 * k + 64), "WI%d_%d" % (t, k), "AFL%d" % t
-        p, h, a = T.PD[:, s], wi(t, HCOL[k], HCOL[k] + 64), afl(t, 64 * k, 64 * k + 64)
-        mms([(T[P][32 * (x // 2):32 * (x // 2) + 32, 0, q:4:NQ, :], T.EUW[:, 48 * q + 16 - 16 * (x % 2):48 * q + 48 - 16 * (x % 2)],
-              T.Z[:, CC * k:CC * k + CC, x, :], x % 2 == 0, x % 2 == 1) for q in range(NQ) for x in range(8)],
-            "Z%d EUW" % k, P, 8 * NQ * max(32, 16 * CC))
-        act(T.AB[:, s], T[P][:, 0, 0:4, :], P, "AB%d" % k, f=AF.Abs if t < 4 else AF.Sign, bias=48.0 * MP - 41)
+        P, s, hk, ak, n, u, c = "PB%d" % k, pairs(k), "WI%d_%d" % (t, k), "AFL%d" % t, wide(k), wide(k) // 16, 3 - k // 3
+        p, h, a, y = T.PD[:, s], nurses(T.WI, t, k), afl(t, s.start, s.stop), T[P][:, c, 0:u, :]
+        mms([big(y, 64, n) + (True, False)][t // 4:]
+            + [(T[P][32 * (x // 2):32 * (x // 2) + 32, c, q:u:NQ, :], T.EUW[:, t // 4, 48 * q + 16 - 16 * (x % 2):48 * q + 48 - 16 * (x % 2)],
+                T.Z[:, QU[k] // NQ:QU[k + 1] // NQ, x, :], t == 4 and x % 2 == 0, (t == 4 or q == NQ - 1) and x % 2 == 1)
+               for q in range(NQ) for x in range(8)], "Z%d ONES CM " % k + ("EUW", "EUW4")[t // 4], P + " #rows%d" % k,
+            8 * NQ * max(32, n // NQ) + max(64, n))
         if t < 4:
-            ts(T.MM[:, s], T.AB[:, s], 32.0, None, A.is_gt, None, "AB%d" % k, "MM%d" % k)
-            tt(p, p, T.MM[:, s], A.mult, "PD MM%d" % k, "pd%d" % k)
-            tt(wo(t, HCOL[k], HCOL[k] + 64), p, h, A.add, "PD pd%d %s" % (k, hk), "WO%dh%d" % (t, k))
-            tt(wo(t, ACOL + 64 * k, ACOL + 64 + 64 * k), p, a, A.add, "PD pd%d %s" % (k, ak), "WO%da%d" % (t, k))
-            if k < 3:
-                leave(t, k)
+            act(T.MM[:, s], y, P, "MM%d #mask%d" % (k, k), n * CYC, f=AF.Abs, scale=1.0 / 64, bias=MP - 1 - MAGIC)
+            tt(p, p, T.MM[:, s], A.mult, "PD MM%d" % k, "pd%d #p%d" % (k, k), n * CYC)
+            tt(nurses(T.WO, t, k), p, h, A.add, "PD pd%d %s" % (k, hk), "WO%dh%d #h%d" % (t, k, k), n * CYC)
+            tt(wo(t, ACOL + s.start, ACOL + s.stop), p, a, A.add, "PD pd%d %s" % (k, ak), "WO%da%d #a%d" % (t, k, k), n * CYC)
+            for n, (c0, c1, keys, after) in enumerate(SENDS):
+                if after == k:
+                    send(wi(t + 1, c0, c1), wo(t, c0, c1), " ".join("WO%d%s" % (t, x) for x in keys.split()),
+                         " ".join({"h": "WI%d_", "a": "WA%d_"}[x[0]] % (t + 1) + x[1:] for x in keys.split()), "a%d_%d" % (n, t + 1), c1 - c0)
         else:
-            act(T.MM[:, s], T.AB[:, s], "AB%d" % k, "MM%d" % k, f=AF.Relu)
-            tt(T.PS[:, s], p, T.MM[:, s], A.mult, "PD MM%d" % k, "PS%d" % k)
-            tt(T.YC[:].indirect(T.YL[:, 16 + 4 * k:20 + 4 * k]), a, T.PS[:, s], A.add, "YL PS%d %s" % (k, ak), "YC", sca(64))
-            tt(T.YC[:].indirect(T.YL[:, 4 * k:4 * k + 4]), h, T.PS[:, s], A.subtract, "YL PS%d %s" % (k, hk), "YC", sca(64))
+            act(T.MM[:, s], y, P, "MM%d #mask%d" % (k, k), n * CYC, f=AF.Identity, scale=0.5, bias=0.5 * MP)
+            tt(T.PS[:, s], p, T.MM[:, s], A.mult, "PD MM%d" % k, "PS%d #p%d" % (k, k), n * CYC)
+            tt(T.YC[:].indirect(T.YL[:, QU[k]:QU[k + 1]]), a, T.PS[:, s], A.add, "YL PS%d %s" % (k, ak), "YC #a%d" % k, sca(n))
+            tt(T.YC[:].indirect(T.YL[:, 48 + QU[k]:48 + QU[k + 1]]), h, T.PS[:, s], A.subtract, "YL PS%d %s" % (k, hk), "YC #h%d" % k, sca(n))
 
-    def leave(t, k):
-        a, b, keys = SENDS[k]
-        send(wi(t + 1, a, b), wo(t, a, b), " ".join("WO%d%s" % (t, x) for x in keys.split()),
-             " ".join({"h": "WI%d_", "a": "WA%d_", "l": "MI%d"}[x[0]] % (t + 1) + x[1:] for x in keys.split()), "a%d_%d" % (k, t + 1), b - a)
+    def sums(t, k):
+        n, (a, b) = [x for x in enumerate(STAGES) if x[1][0] <= QU[k] < x[1][1]][0]
+        P = "PB%d" % (n % 2)
+        if a == QU[k]:
+            group([(T[P][:, 0, 0:2, a:b], T.IDENT[:], T.TA[:, :, a:b]), (T[P][:, 0, 0, a:b], T.IDENT[:], T.TB[:, a:b])],
+                  "IDENT TA TB", P + " #open%d" % k, 128, True, False)
+        group([(T[P][:, 0, 0:2, NQ * c:NQ * (c + 1)], T.Z[:, c, :, :], T.QA[:, 0:2, :]) for c in blocks(k)],
+              "Z%d QA" % k, P + " #sums%d" % k, 64 * len(blocks(k)), False, False)
+        if b == QU[k + 1]:
+            stage(t, a, b, P)
+
+    def aside(t, k):
+        if k == 0:
+            group([(T.PL[:, 0:4, 0:16], T.ONES[0:1, :], T.MC[0:1, 1:5, :])], "ONES MC", "PL", 64, True, False)
+        group([(T.PL[:, 0:4, NQ * c:NQ * (c + 1)], T.Z[:, c, :, :], T.QA[:, 3:7, :]) for c in blocks(k)],
+              "Z%d QA" % k, "PL #aside%d" % k, 64 * len(blocks(k)), False, False)
+        if k == 3:
+            group([(T.PL[:, 0:4, 0:16], T.NEG[0:1, :], T.MC[0:1, 1:5, :]), (T.PL[:, 0, 0:16], T.IDENT[:], bb(t, 1, 2))],
+                  "NEG MC IDENT BB%d" % t, "PL #odd", 128, False, t == 4)
+
+    def stage(t, a, b, P):
+        zs, x, p = " ".join("Z%d" % k for k in range(PART[a], PART[b - 1] + 1)), t // 4, T[P]
+        k = PART[b - 1]
+        group([(p[:, 0, 0:2, a:b], T[w][0:1, :], T.MC[0:1, 0:2, a:b]) for w in ("ONES", "NEG")]
+              + [(p[:, 0, 1, a:b], T.IDENT[:], bb(t, 0, 1, 1, slice(a, b)))]
+              + ([(p[:, 0, 0, a:b], T.IDENT[:], T.TC[:, a:b])]
+                 + [(p[:, 0, 0, NQ * c:NQ * (c + 1)], T.Z[:, c, :, :], T.QA[:, 2, :]) for c in range(a // NQ, b // NQ)])[:99 * (1 - x)],
+              "ONES NEG MC IDENT TC QA BB%d %s" % (t, zs), P + " #stage%d" % k, 192 + (64 + 64 * (b - a) // NQ) * (1 - x), False)
+        ts(T.OF[:, x:2, a:b], p[:, 0, x:2, a:b], 256.0, None, A.add, None, P, "OF%d #of%d" % (a, k))
+        if t < 4:
+            act(T.UF[:, 512:1536].indirect(T.OF[:, 1, a:b]), T.IDX[:, 16 * a:16 * b], "IDX OF%d" % a, "UF #marks%d" % k, sca(16 * (b - a)), f=AF.Silu)
+        else:
+            cp(T.UB[:].indirect(T.OF[:, 1, a:b]), T.XB0[:, 16 * a:16 * b], "XB0 OF%d" % a, "UB #marks%d" % k, sca(16 * (b - a)))
 
     def frames(a, b):
-        tt(T.OI1[:, a:b], T.PL[:, 0, a:b], T.ELS[:, a:b], A.add, "PL ELS", "OI1%d" % a)
-        ts(T.OI2[:, a:b], T.OI1[:, a:b], 8191 - 32, None, A.bitwise_and, None, "OI1%d" % a, "OI2%d" % a)
-        ts(T.OFFU[:, a:b], T.OI2[:, a:b], T.PMF[:, 1:2], -512.0 * a, A.add, A.add, "PMF1 OI2%d" % a, "OFFU%d" % a)
-        cp(T.xfs[:, 512 * a:512 * b].indirect(T.OFFU[:, a:b]), T.pfs[:, 16 * a:16 * b], "pfs OFFU%d" % a, "xfsb" if a else "xfs",
-           sca(16 * (b - a)))
-
-    def flags(a, b):
-        p = T.PB1[:, 2, 0, a:b]
-        again(a, b)
-        act(T.NF[:, a:b], T.PB0[:, 2, 0, a:b], "PB0", "NF%d" % a, f=AF.Sign, scale=-1.0, bias=8.5 - 8 * MP)
-        mms([(p, T.IDENT[:], T.BB[:, a:b], True, False), (p, T.G16[:], T.C16[:, 32 + a:32 + b], False, False)],
-            "IDENT G16 C16 BH", "PB1", 128)
-        mms([(p, T.I256[:], T.NF[:, a:b], False, True)], "I256 NF%d" % a, "PB1", 64)
-        cp(T.FU[:, a:b], p, "PB1", "FU%d" % a)
-        act(T.UF[:, 0:1024].indirect(T.FU[:, a:b]), T.IDX[:, 16 * a:16 * b], "IDX FU%d" % a, "UF", sca(16 * (b - a)), f=AF.Silu)
+        cp(T.xfs[:, 512 * a:512 * b].indirect(T.OF[:, 0, a:b]), T.pfs[:, 16 * a:16 * b],
+           "pfs " + " ".join("OF%d" % x for x, y in STAGES if a <= x < b), "xf%d #frames%d" % (a, PART[b - 1]), sca(16 * (b - a)))
 
     def take(t):
         for k in range(4):
-            cp(T.UH[:, 64 * k:64 * k + 64], wi(t, HCOL[k], HCOL[k] + 64), "WI%d_%d" % (t, k), "UH%d" % k)
-        sign, ak, a = (-1.0 if t < 4 else 1.0), "AFL%d" % t, 64 if t else 0
+            cp(T.UH[:, pairs(k)], nurses(T.WI, t, k), "WI%d_%d" % (t, k), "UH%d #uh%d" % (k, k), wide(k) * CYC)
+        sign, ak, a, bk = (-1.0 if t < 4 else 1.0), "AFL%d" % t, wide(0) if t else 0, "BB%d" % t
         if t:
-            win, keys = wi(t, ACOL, ACOL + 256), " ".join("WA%d_%d" % (t, k) for k in range(4)) + " ALU"
-            ts(T.ALU[:], T.MA[:, 32 * t:32 * t + 16], -1.0, None, A.add, None, "MA%d" % t, "ALU")
-            ts(bb(5, 6), T.MA[:, 32 * t + 16:32 * t + 32], -256.0, None, A.add, None, "MA%d" % t, "BA")
-            act(afl(t, 0, 256), win.indirect(T.ALU[:]), keys, ak, gat(256), scale=-sign)
-            ts(T.UA[:, 0:64], win.indirect(T.ALU[:, 0:4]), -1.0, None, A.mult, None, keys, "UA0", gat(64))
-            cp(T.BB[:, 0:80], wi(t, 512, 592), "MI%d" % t, "BH", 80 * CYC)
-        ts(T.UA[:, a:256], afl(t, a, 256), sign, None, A.mult, None, ak, "UA0 UA1 UA2 UA3"[a // 16:], (256 - a) * CYC)
+            win, keys = wi(t, ACOL, ACOL + 256), " ".join("WA%d_%d" % (t, k) for k in range(4)) + " AL%d" % t
+            act(afl(t, 0, 256), win.indirect(T.AL[:, 16 * t:16 * t + 16]), keys, ak, gat(256), scale=-sign)
+            ts(T.UA[:, 0:a], win.indirect(T.AL[:, 16 * t:16 * t + QU[1]]), -1.0, None, A.mult, None, keys, "UA0", gat(a))
+        ts(T.UA[:, a:256], afl(t, a, 256), sign, None, A.mult, None, ak, "UA0 UA1 UA2 UA3"[4 * min(t, 1):], (256 - a) * CYC)
         for k in range(4):
-            p = T.PD[:, 64 * k:64 * k + 64]
-            mms([(p, T["NIDF" if t < 4 else "IDF"][:], wi(t, HCOL[k], HCOL[k] + 64), True, False),
-                 (p, T.NIDF[:], afl(t, 64 * k, 64 * k + 64), False, True)], "IDF NIDF %s WI%d_%d" % (ak, t, k), "PD", 512)
-        for c, w in ((16, T.NHB[:]), (32, T.HB[:])):
-            more = [(5, T.I256[:], T.THR[:]), (5, T.G16[:], c16(1))] + [(x, T.G16[:], c16(0)) for x in ((5,), (0, 4))[t // 4]]
-            l = ([(T.PL[:, 0:6, c:c + 16], w, T.BB[:])] + [(T.PL[:, a:a + n, c:c + 16], T.HB[:], bb(b, b + n)) for a, b, n in
-                                                          ((0, 2, 2), (2, 0, 2), (4, 5, 1), (5, 4, 1))]
-                 + [(T.PL[:, x, c:c + 16], a, b) for x, a, b in more[:4 * (c // 32)]])
-            mms([m + (n == 0, n == len(l) - 1) for n, m in enumerate(l)], "HB NHB I256 BA BH G16 C16 THR", "PL", 64 * len(l) + 32)
-        a = 256 if t < 4 else 0
-        mms([(T.PT[:, a:512], T.LO8[:], T.IOTC[:, a:512], True, False)]
-            + [(T.PT[:, a + l:512:16], T.SELB[:, l, :, :], bb(4 + a // 256, 6), False, l == 15) for l in range(16)],
-            "LO8 IOTC SELB BA BH", "PT", 1536 - a)
-        act(T.IDX[:], T.PT[:, 256:512], "PT BC", "IDX", 256 * CYC, f=AF.Identity, bias=T.BC[:, 0:1])
+            p = T.PD[:, pairs(k)]
+            group([(p, T["NIDF" if t < 4 else "IDF"][:], nurses(T.WI, t, k)), (p, T.NIDF[:], afl(t, 16 * QU[k], 16 * QU[k + 1]))],
+                  "IDF NIDF %s WI%d_%d" % (ak, t, k), "PD", 8 * max(64, wide(k)))
+        if t:
+            differences(t, "PN")
         if t < 4:
-            bits()
-        fiota(T.UF[:, 0:512], [[0, 512]], 16416, 0, "UF", 512, "UFb")
+            group([(T.PT[:, 256:512], T.LO8[:], T.IOTC[:, 256:512])]
+                  + [(T.PT[:, 256 + l:512:16], T.SELB[:, l, :, :], bb(t, 2, 3)) for l in range(16)], "LO8 IOTC SELB SELBb " + bk, "PT", 1280)
+            act(T.IDX[:], T.PT[:, 256:512], "PT", "IDX #idx", 256 * CYC, f=AF.Identity, bias=MID)
+            bits(t)
+            fiota(T.UF[:, 512:1024], [[0, 512]], 16416, 0, "UF", 512)
 
-    def bits():
-        mms([(T.PN[0:16, 128:256], bb(0, 1), T.IDENT[:], True, True)], "IDENT BH", "PN", 128)
-        act(T.FT[0:16, :], T.PN[0:16, 128:256], "PN", "+FT", 128 * CYC)
-        mms([(T.PN[:, 256:384], T.SBH[0:18, :], T.FT[0:18, :], True, True)], "SBH FT", "PN", 128)
-        act(T.RB[:], T.PN[:, 256:384], "PN", "RB", 128 * CYC)
-        tt(T.BT[:], T.PN[:, 256:384], T.RB[:], A.is_lt, "PN RB", "BT", 128 * CYC)
-        ts(T.BT[:], T.BT[:], T.C2[:, 1:2], T.C2[:, 0:1], A.mult, A.add, "BT C2", "BT")
-        mms([(T.PN[:, 16:32], T.IDENT[:], bb(1, 2), True, False), (T.PN[:, 16:32], T.G16[:], c16(3), False, False)],
-            "IDENT G16 C16 BH", "PN", 128)
+    def differences(t, P):
+        p = T[P][:, 400:448]
+        group([(p, T.IDENT[:], bb(t, 3, 6)), (p, T.NID[:], bb(t, 0, 3))], "IDENT NID BB%d BG%d" % (t, t), P, 128)
+        act(T.DF[:], p, P, "DF")
+
+    def bits(t):
+        p = T.PT[:, 0:128]
+        mms([(T.PN[0:16, 128:256], bb(t, 0, 1), T.IDENT[:], True, True)], "IDENT BB%d" % t, "PN", 128)
+        act(T.FT[0:16, :], T.PN[0:16, 128:256], "PN", "+FT #ft", 128 * CYC)
+        group([big(p, 2, 128), (p, T.S1[0:18, :], T.FT[0:18, :]), big(p, 2, 128, "NEG"), (p, T.S2[0:18, :], T.FT[0:18, :]),
+               big(p, 1, 128), big(p, 1, 128, "NEG")], "S1 S2 FT ONES NEG CM", "PT #bits", 768)
+        act(T.BT[:], p, "PT C2 C2a", "BT #bt", 128 * CYC, f=AF.Identity, scale=T.C2[:, 1:2], bias=T.C2[:, 0:1])
 
     def xor(t):
-        y = T.PT[:, 0:1]
+        y, n = T.PT[:, 0:1], 16 if t < 4 else 32
+        ts(T.DD[:, 0:1], y, MAGIC, MAGIC, A.add, A.subtract, "PT", "DD #dd")
         if t < 4:
-            ts(T.DD[:, 0:1], y, MAGIC, MAGIC, A.add, A.subtract, "PT", "DD")
-            ts(T.RS[:, 0:16], T.X16[:], y, T.DD[:, 0:1], A.add, A.is_lt, "X16 PT DD", "RS")
-            mms([(T.PN[:, 16:32], T.I256[:], T.NF[:], False, False)] * 2, "I256 " + " ".join("NF%d" % a for a, b in FLAGS), "PN", 128)
-            mms([(T.PN[:, 16:32], T.BT[:], T.RS[:, 0:16], False, True)], "BT RS", "PN", 64)
-            cp(T.XLU[:, 0:16], T.PN[:, 16:32], "PN", "XLU")
+            ts(T.RS[:, 0:16], T.X16[:], y, T.DD[:, 0:1], A.add, A.is_lt, "X16 PT DD", "RS #rs")
+            group([(T.PL[:, 0, 0:16], T.BT[:], T.RS[:, 0:16])], "BT RS", "PL #xor", 64, False)
+            ts(T.XLU[:, 0:16], T.PL[:, 0, 0:16], 768.0, None, A.add, None, "PL", "XLU #xl")
         else:
-            cp(T.RI[:, 0:1], y, "PT", "RI")
-            tt(T.DD[:, 0:1], y, T.RI[:, 0:1], A.subtract, "PT RI", "DD")
-            ts(T.RS[0:8, :], T.RX[0:8, :], T.DD[0:8, 0:1], 0.0, A.mult, A.is_gt, "RX DD", "RS")
-            mms([(T.PT[:, 128:160], T.LB[0:8, :], T.RS[0:8, :], True, True)], "LB RS", "PT", 64)
-            ts(T.XLU[:], T.PT[:, 128:160], T.LX1[:, 0:1], None, A.add, None, "PT LX1", "XLU")
-
-    def turns(t):
-        act(T.TRN[:], T.PB0[:, 2, 0:6, :], "PB0", "TRN", 96 * CYC, f=AF.Sign, scale=-1.0, bias=4.5 - 8 * MP)
-        tt(T.XX[:], T.PL[:, 0:6, 16:32], T.TRN[:], A.mult, "TRN PL", "XX", 96 * CYC)
-        tt(wo(t, 512, 608), T.PL[:, 0:6, 32:48], T.XX[:], A.add, "PL XX", "WO%dl" % t, 96 * CYC)
-        if t < 4:
-            for k in range(3, len(SENDS)):
-                leave(t, k)
+            ts(T.RS[0:16, :], T.RX[0:16, :], T.PT[0:16, 0:1], T.DD[0:16, 0:1], A.add, A.is_lt, "RX PT DD", "RS #rs")
+            mms([(T.PT[:, 128:160], T.LB[0:16, :], T.RS[0:16, :], True, True)], "LB RS", "PT #xor", 64)
+            ts(T.XLU[:], T.PT[:, 128:160], T.LX1[:, 0:1], None, A.add, None, "PT LX1", "XLU #xl")
 
     def alpha(t):
-        d = T.DM[:, 32 * t:32 * t + 32]
-        mms([(T.PN[:, 0:16], T.G16[:], c16(0), True, False)], "G16 C16", "PN", 64)
-        act(T.MROW[:], T.UF[:].indirect(T.XLU[:, 0:16]), "UF XLU BC", "MROW", gat(256), f=AF.Identity, bias=T.BC[:, 1:2])
-        conv(T.PN[:, 0:16], T.MROW, 0, 16, "MROW", "PN", st=False, tab="SELW2")
-        tt(T.AL[:], T.PN[:, 0:16], wo(t, 592, 608), A.min, "PN WO%dl" % t, "AL")
-        ts(T.DM[:, 32 * t:32 * t + 16], T.AL[:], 10, 511, A.arith_shift_right, A.bitwise_and, "AL", "+DM%d" % t)
-        ts(T.DM[:, 32 * t + 16:32 * t + 32], T.AL[:], 511, None, A.bitwise_and, None, "AL", "+DM%d" % t)
-        send(T.MA[:, 32 * t + 32:32 * t + 64], d, "DM%d" % t, "MA%d" % (t + 1), "am_%d" % (t + 1), 32)
+        tt(T.MROW[:], T.UF[:, 0:1024].indirect(T.XLU[:, 0:16]), T.IDX[:], A.min, "UF UFb XLU IDX", "MROW #mate", gat(256))
+        group([(T.PT[:, 0:16], T.IDENT[:], T.NI[:])], "IDENT NI", "PT", 64, True, False)
+        conv(T.PT[:, 0:16], T.MROW, 0, 16, "MROW", "PT", st=False, tab="SELJ")
+        cp(T.DM[:, 16 * t:16 * t + 16], T.PT[:, 0:16], "PT", "DM%d" % t)
+        send(T.AL[:, 16 * t + 16:16 * t + 32], T.DM[:, 16 * t:16 * t + 16], "DM%d" % t, "AL%d" % (t + 1), "am_%d" % (t + 1), 8)
+
+    def turns(t):
+        tt(T.XX[:], T.PL[:, 1:4, 0:16], T.DF[:], A.mult, "PL DF", "XX")
+        group([(T.PB3[:, 3, 0:2, :], T.IDENT[:], bb(t, 0, 2)), (T.PB3[:, 3, 2, :], T.NID[:], bb(t, 2, 3)),
+               (T.PB3[:, 3, 3:6, :], T.IDENT[:], bb(t, 3, 6)), (T.PB3[:, 3, 0:3, :], T.IDF[:], T.XX[:]),
+               (T.PB3[:, 3, 3:6, :], T.NIDF[:], T.XX[:])], "IDENT NID IDF NIDF XX BB%d BG%d" % (t, t), "PB3", 704, True, t == 4)
+        if t < 4:
+            conv(T.PB3[:, 3, 2, :], T.MROW, 0, 16, "MROW", "PB3", st=False, tab="SELX")
+            o = T.BO[:, 6 * t:6 * t + 6, :]
+            act(o, T.PB3[:, 3, 0:6, :], "PB3", "BO%d" % t, 96 * CYC)
+            send(bb(t + 1, 0, 6), o, "BO%d" % t, "BB%d BG%d" % (t + 1, t + 1), "al_%d" % (t + 1), 48)
+        else:
+            act(T.YO[:], T.PB3[:, 3, 0:6:5, :], "PB3", "YO", f=AF.Identity, bias=256.0)
 
     def box_lists():
-        act(T.XB0[:], T.PT[:, 0:512], "PT", "XB0", 512 * CYC)
-        ts(T.YL[:], bb(4, 6), 256.0, None, A.add, None, "BA BH", "YL")
-        ts(T.GU[:], bb(2, 3), 256.0, None, A.add, None, "BH", "GU")
-        ts(T.fsU[:], bb(0, 1), 256.0, None, A.add, None, "BH", "fsU")
-        cp(brow.indirect(T.fsU[:]), T.XB0[:, 256:512], "XB0 fsU", "BROW", sca(256))
-        cp(brow.indirect(T.GU[:]), T.XB0[:, 0:256], "XB0 GU", "BROW", sca(256))
-        conv(T.PN[:, 64:96], T.BZ, 512, 32, "BROW", "PN", tab="SELW3")
-        ts(T.BL[:], T.PN[:, 64:96], 256.0, None, A.add, None, "PN", "BL")
+        fiota(T.UB[:], [[0, 1024]], -512, 0, "UB", 1024)
+        ts(T.YL[:], bb(4, 2, 6), 256.0, None, A.add, None, "BB4", "YL")
+        tt(T.SI[:], bb(4, 1, 5, 3), bb(4, 0, 4, 3), A.subtract, "BB4", "SI")
+        tt(T.SA[:], T.SI[:], bb(4, 2, 6, 3), A.mult, "BB4 SI", "SA")
+        group([(T.PT[:, l:512:16], T.SELB[:, l, :, :], T.SA[:]) for l in range(16)], "SELB SELBb SA", "PT", 1024)
+        act(T.XB0[:], T.PT[:, 0:512], "PT", "XB0 XB1", 512 * CYC)
+        cp(T.UB[:, 512:1024].indirect(T.YL[:, 16:32]), T.XB0[:, 256:512], "XB1 YL", "UB #nurses", sca(256))
 
     for t in range(5):
         now[0] = t
@@ -797,44 +881,39 @@ def rank_program(g, core, T, topo):
         if t == 4:
             box_lists()
         j = 0
-        for w in PLAN[t // 4].split():
-            chunk(w[0], j, int(w[1:]))
-            for k in range(max(0, j // 4 - 4), (j + int(w[1:])) // 4 - 4):
-                if k == 3 and t < 4:
-                    frames(*OFFS[0])
+        for w in PLAN[(t + 2) // 3].split():
+            chunk(t, w[0], j, int(w[1:]))
+            for k in [k for k in range(4) if j < 16 + QU[k + 1] <= j + int(w[1:])]:
                 signs(k)
-                if t < 4:
-                    sums(k)
-                if k == 0:
-                    total(4)
-                total(k)
-                if k == 3 and t < 4:
-                    frames(*OFFS[1])
+                if k > 1:
+                    total(k)
+                aside(t, k)
                 rows(t, k)
-                for a, b in FLAGS:
-                    if b == 4 * k + 4:
-                        flags(a, b)
+                sums(t, k)
             j += int(w[1:])
+        if t < 4:
+            for a, b in OFFS:
+                frames(a, b)
         xor(t)
-        turns(t)
         if t < 4:
             alpha(t)
+        if t == 0:
+            nurses_sites()
+            differences(0, "PN")
+        turns(t)
 
     dma("D", T.yc[:], T.YC[:], "YC", "yc", "o_yc", 3000)
-    own = T.PB2[:, 2, 0:2, :]
-    ts(T.BZ[:, 0:512], T.UF[:, 0:512], -288.0, None, A.add, None, "UF", "U0", 512 * CYC)
-    conv(own, T.BZ, 0, 32, "U0", "PB2", tab="SELW3")
-    ts(T.YL32[:], own, -2.0, 600.0, A.mult, A.add, "PB2", "YL32")
-    mms([(T.PN[:, 0:32], T.NIDF[:], T.BL[:], True, False)] + [(T.PN[:, 16 * n:16 * n + 16], T.G16[:], c16(0), False, False) for n in range(2)],
-        "NIDF BL G16 C16", "PN", 384)
-    act(T.U[:], T.UF[:, 0:512].indirect(T.XLU[:]), "UF XLU", "U1", gat(512), f=AF.Identity, bias=-288.0)
-    conv(T.PN[:, 0:32], T.U, 0, 32, "U1", "PN", st=False, tab="SELW3")
-    tt(T.B1[:], T.PN[:, 0:32], T.YL32[:], A.is_lt, "PN YL32", "B1")
-    tt(T.AL32[:], T.PN[:, 0:32], T.B1[:], A.mult, "PN B1", "AL32")
-    tt(T.BL[:], T.BL[:], T.AL32[:], A.add, "BL AL32", "BL")
+    conv(T.PN[:, 0:32], T.UB, 0, 32, "UB", "PN", stop=False, tab="SELR")
+    conv(T.PN[:, 0:32], T.UB, 512, 32, "UB", "PN", st=False, stop=False, tab="SELR")
+    for n in range(2):
+        s = slice(256 * n, 256 * n + 256)
+        act(T.OWN[:, s], T.UB[:, s], "UB", "OWN%d" % n, 256 * CYC)
+        tt(T.U[:, s], T.UB[:, 0:512].indirect(T.XLU[:, 16 * n:16 * n + 16]), T.OWN[:, s], A.min, "UB XLU OWN%d" % n, "+U #mate%d" % n, gat(256))
+    conv(T.PN[:, 0:32], T.U, 0, 32, "U", "PN", st=False, tab="SELX")
+    act(T.BL[:], T.PN[:, 0:32], "PN SC", "BL", f=AF.Identity, scale=T.SC[:, 0:1], bias=T.SC[:, 1:2])
     dma("S", T.yb[:], T.BL[:], "BL", "yb", "o_yb")
-    dma("D", T.yf[:], wo(4, 512, 528), "WO4l", "yf", "o_yf")
-    dma("S", T.yn[:], wo(4, 576, 592), "WO4l", "yn", "o_yn")
+    dma("D", T.yf[:], T.YO[:, 0:16], "YO", "yf", "o_yf")
+    dma("D", T.yn[:], T.YO[:, 16:32], "YO", "yn", "o_yn")
     emit()
     for n in ("yc", "yb", "yf", "yn"):
         g.wait_ge(T.sem["o_" + n], 16)

import numpy as np
from concourse.mybir import AluOpType as A, AxisListType, ActivationFunctionType as AF

NXG, NCL, NY = 12, 12, 8
SCAN = 1
MP = 2
EACH, SWAP, FLAG, TURN = {4: (1.75, 32.0, 5.4375, 149.0 / 16384), 2: (1.390625, 32.109375, 17.0, 11.0 / 512)}[MP]
NQ, CC = 8 // MP, MP // 2
PLAN = ("S1 S1 V2 S2 V2 S2 V2 S2 S2 S2 V2 S2 V2 S2 S2 V2 S1 S1",
        "S1 S1 V2 S2 S2 S2 V2 S2 S2 S2 V2 S2 V2 S2 S2 V2 S1 S1",
        "V2 S2 V2 S2 S2 V2 S2 S2 S2 V1 S1 S2 S2 S2 S2 S1 S1 S1 S1")
DS, WS = 10, 6
RULES = ((), ("nurses c22",))
DG = 4
LATE = "S"
QU = (0, 4, 8, 12, 16) if MP == 2 else (0, 4, 10, 14, 16)
PART = [k for k in range(4) for _ in range(QU[k], QU[k + 1])]
STAGES = ((0, QU[2]), (QU[2], QU[3]), (QU[3], 16))
OFFS = STAGES
XFS = " ".join("xf%d" % a for a, b in OFFS)
HCOL, ACOL = (0, 16 * QU[1], 16 * QU[2], 16 * QU[3] + 256), 16 * QU[3]
SENDS = ((0, HCOL[1], "h0", 0), (HCOL[1], HCOL[2], "h1", 1), (HCOL[2], ACOL, "h2", 2), (ACOL, 2 * ACOL, "a0 a1 a2", 2),
         (2 * ACOL, 512, "a3 h3", 3))
MAGIC = 1.5 * 2 ** 23
MID = 288.0
MODELS = ((0.83, 1.3, 3.2, 0.45, 215, 300, 1400, 8, 4.5), (1.1, 2.0, 4.6, 0.6, 240, 400, 2000, 12, 5.5),
          (0.9, 1.15, 2.6, 0.49, 230, 550, 2300, 14, 7.5), (0.86, 1.75, 4.3, 0.46, 220, 400, 1800, 10, 6.0))
CYC, GAT, SCA, PEC, HOP, ISSUE, FAR, ROW, COL = np.array(MODELS).T
XF, FIRST = 9100, 2800
MARK = "SPB|Z ACC"
STARTS, PASSES, SHORT, LONG = 8, 40, 25, 700
WIDE, PATIENCE, REACH, FREE, TENURE, SEED = 110, 60, 10, 600, 10, 1
ORDER = []
INFO = []
FL, BF, HF, I32, U16 = "float32", "bfloat16", "float16", "int32", "uint16"


def _scratch():
    s = {}

    def sb(names, cols, dt):
        for n in names.split():
            s[n] = ("sbuf", [128] + (cols if isinstance(cols, list) else [cols]), dt)
    sb("xfs D1", 8192, BF)
    sb("XG", 512 * NXG, BF)
    sb("CL", 512 * NCL, BF)
    sb("YV CV", 256 * NY, BF)
    sb("WH WA SELB", [16, 8, 16], BF)
    sb("Z", [4 * CC, 8, 16], BF)
    sb("LO8", [8, 16], BF)
    sb("BB", [30, 16], BF)
    sb("BO", [24, 16], BF)
    sb("MC", [6, 16], BF)
    sb("QA", [7, NQ], BF)
    sb("EUW", [2, 48 * NQ], BF)
    sb("UB", 1024, BF)
    sb("TR IOTC XB0 U OWN", 512, BF)
    sb("pfs pns LO HI SG MM", 256, BF)
    sb("SELW SELJ SELX SELR", 144, BF)
    sb("ONES NEG IDENT NID G16 KK TI LB TM FT PABX BT S1 S2 CM", 128, BF)
    sb("RS RX SA SI", 32, BF)
    sb("LL", 24, BF)
    sb("P2 LTB", 18, BF)
    sb("TA", [2, 16], BF)
    sb("NI TB TC RTB SB9 X16", 16, BF)
    sb("MROW", 256, HF)
    sb("WI WO", 512 * 5, FL)
    sb("UF", 1536, FL)
    sb("AFL", 256 * 5, FL)
    sb("CBF YC", 512, FL)
    sb("IDX PS", 256, FL)
    sb("HALF QUART", 128, BF)
    sb("IDF NIDF PABW", 128, FL)
    sb("XX DF", 48, FL)
    sb("BL YO", 32, FL)
    sb("LI TWO", 16, FL)
    sb("G8", 8, FL)
    sb("ACC", 12, FL)
    sb("THN PMF PIF DD LX1 C2 BC SC", 2, FL)
    sb("cbs", 512, I32)
    sb("bss BI1 BI2", 32, I32)
    sb("fss nbs ELS BI0 BIT", 16, I32)
    sb("ths TH PI PM", 2, I32)
    sb("UH UA", 256, U16)
    sb("AL", 16 * 5, U16)
    sb("DM YL", 64, U16)
    sb("OF", [2, 16], U16)
    sb("bsU XLU", 32, U16)
    sb("fsU nbU GU", 16, U16)
    for n in ("PB0", "PB1", "PB2", "PB3"):
        s[n] = ("psum", [128, 4, 8, 16], FL)
    for n in ("PT", "PD", "PN"):
        s[n] = ("psum", [128, 512], FL)
    s["PL"] = ("psum", [128, 8, 64], FL)
    return s


SCRATCH = _scratch()
BANKS = ("PB0", "PB1", "PB2", "PB3", "PT", "PD", "PL", "PN")
LOADS = ["pf", "pn", "fs", "bs", "nb", "th", "cb", "xf"]
SEMAPHORES = (["qV", "qS", "qP", "qG", "loc"] + ["d_" + n for n in LOADS] + ["o_yc", "o_yb", "o_yf", "o_yn"]
              + ["a%s_%d" % (k, t) for k in list(range(len(SENDS))) + ["m", "l"] for t in range(1, 5)])


def issue_order(calls):
    if ORDER:
        return ORDER
    n, K, first = len(calls), len(MODELS), len(LOADS)
    qn = ["VSPGD".index(c["q"]) for c in calls]
    NS, LATE, DUR = [np.array([c[k] + 0 * CYC for c in calls]).T for k in ("ns", "late", "far")]
    NS, LATE = np.maximum(NS, DUR), LATE + np.minimum(NS, DUR)
    reach, waited, need, serve, soft = [0] * n, [0] * n, [], [[] for _ in range(n)], []
    for j, c in enumerate(calls):
        pre = c["pre"] | c["rule"]
        soft.append({i for i in pre if qn[i] == qn[j] == 2 or i not in c["pre"]})
        for i in pre:
            reach[j] |= reach[i]
            waited[j] |= waited[i] if i in soft[j] else reach[i]
        need.append([i for i in pre if not (reach[j] if i in soft[j] else waited[j]) >> i & 1])
        for i in pre:
            reach[j] |= 1 << i
            waited[j] |= (i not in soft[j]) << i
        for i in need[j]:
            serve[i].append(j)
    sets = []
    for ns, late in list(zip(NS.tolist(), LATE.tolist())) + [(NS.mean(0).tolist(), LATE.mean(0).tolist())]:
        sets.append((ns, [[(i, 0.0 if i in soft[j] else late[i]) for i in need[j]] for j in range(n)],
                     [[(j, 0.0 if i in soft[j] else late[i]) for j in serve[i]] for i in range(n)],
                     [0.0 if serve[i] else late[i] for i in range(n)]))
    names = sorted({c["name"][1:] for c in calls})
    twin = {c["name"]: i for i, c in enumerate(calls)}
    marks = [twin[t, MARK, 0] for t in range(5)]
    seed = [SEED]

    def draw(m):
        seed[0] = (seed[0] * 1103515245 + 12345) % 2 ** 31
        return (seed[0] >> 8) % m

    def walk(before, behind, urgent, start, look):
        ns, left = sets[K][0], [len(b) for b in before]
        ready = [{i: start[i] for i in range(n) if qn[i] == q and not left[i]} for q in range(5)]
        free, end, order = [0.0] * 5, [0.0] * n, []
        for _ in range(n):
            t1, q = min((max(r, free[q]) + look * ns[i], q) for q in range(5) for i, r in ready[q].items())
            i = max((i for i, r in ready[q].items() if r <= t1), key=lambda i: urgent[i])
            end[i] = free[q] = max(free[q], ready[q].pop(i)) + ns[i]
            order.append(i)
            for j, _g in behind[i]:
                left[j] -= 1
                if not left[j]:
                    ready[qn[j]][j] = max(end[p] + gap for p, gap in before[j])
        return end, order

    def fresh():
        _n, pre, post, last = sets[K]
        end, now, best, keep = list(range(n)), 1e18, 1e18, None
        for _ in range(PASSES):
            back, _o = walk(post, pre, end, last, 0.1 + 0.0008 * draw(1000))
            push = {x: draw(1200) - 600 for x in names if not draw(20)}
            new, order = walk(pre, post, [1e18 - 1e3 * i if i < first else back[i] + push.get(calls[i]["name"][1:], 0) for i in range(n)],
                              [0.0] * n, 0.1 + 0.0008 * draw(1000))
            if max(new) < now + 500:
                end, now = new, max(new)
            if max(new) < best:
                best, keep = max(new), order
        return keep

    def sweep(part, free, links, base, ns, out, ready):
        for i in part:
            t = base[i]
            for x, gap in links[i]:
                if out[x] + gap > t:
                    t = out[x] + gap
            ready[i] = t
            q = qn[i]
            if free[q] > t:
                t = free[q]
            out[i] = free[q] = t + ns[i]

    zero = [0.0] * n

    def look(order):
        got = []
        for ns, pre, post, last in sets[:K]:
            fin, rd, tail, qd = zero[:], zero[:], zero[:], zero[:]
            sweep(order, [0.0] * 5, pre, zero, ns, fin, rd)
            sweep(order[::-1], [0.0] * 5, post, last, ns, tail, qd)
            got.append((fin, rd, tail, qd))
        return got

    def price(got):
        return sum(max(x[2]) * s for x, s in zip(got, scale))

    def starts(got):
        return [f - x for f, x in zip(got[0][0], sets[0][0])]

    def repeat(other, start, b, to):
        lo, hi, lo2, hi2 = [0 if x < 0 else s[marks[x]] if x < 5 else 1e9 for s, x in ((other, b), (other, b + 1), (start, to), (start, to + 1))]
        due = []
        for i, c in enumerate(calls):
            x = twin.get((c["name"][0] - to + b,) + c["name"][1:]) if b != to else i
            if (c["name"][0] >= 0 or b == to) and i >= first and x is not None and (lo <= other[x] < hi or lo2 <= start[i] < hi2):
                due.append(other[x] - lo + lo2)
            else:
                due.append(i - 1e9 if i < first else start[i] - (hi2 - lo2 - hi + lo) * min(1, max(0, (start[i] - lo2) / (hi2 - lo2))))
        left, order = [len(x) for x in need], []
        ready = [i for i in range(n) if not left[i]]
        while ready:
            i = min(ready, key=lambda i: due[i])
            ready.remove(i)
            order.append(i)
            for j in serve[i]:
                left[j] -= 1
                if not left[j]:
                    ready.append(j)
        return order

    def stretch(order, got, a0):
        win, head, rest = order[a0:a0 + WIDE], order[:a0], order[a0 + WIDE:]
        inside, before, after, past = set(win), [], [], []
        for (fin, rd, tail, qd), (ns, pre, post, last) in zip(got, sets):
            before.append([max([fin[i] for i in head[-200:] if qn[i] == q], default=0.0) for q in range(5)])
            after.append([max([tail[i] for i in rest[:200] if qn[i] == q], default=0.0) for q in range(5)])
            past.append(max([fin[i] + gap + tail[j] for i in head for j, gap in post[i] if j not in inside and tail[j] < tail[win[0]]]
                            + [x + y for x, y in zip(before[-1], after[-1])], default=0.0))

        def ends():
            return [max(past[k], max(got[k][0][i] - sets[k][0][i] + got[k][2][i] for i in win)) for k in range(K)]
        end, tabu, since, step = ends(), {}, 0, 0
        best, keep = sum(x * s for x, s in zip(end, scale)), win
        while since < PATIENCE:
            since, step = since + 1, step + 1
            line, at = [[] for _ in range(5)], {}
            for i in win:
                at[i] = len(line[qn[i]])
                line[qn[i]].append(i)
            k = draw(K)
            (fin, rd, tail, qd), p, moves = got[k], sets[k][0], set()
            for q in line:
                run = []
                for i in q + [None]:
                    on = i is not None and fin[i] - p[i] + tail[i] > end[k] - 1e-6
                    if on and (not run or fin[run[-1]] > fin[i] - p[i] - 1e-6):
                        run.append(i)
                        continue
                    for d in range(1, min(len(run), REACH)):
                        moves.update(((run[0], run[d], 1), (run[0], run[d], 0), (run[-1 - d], run[-1], 1), (run[-1 - d], run[-1], 0)))
                    run = [i] if on else []
            rated = []
            for u, v, fore in sorted(moves):
                q = line[qn[u]]
                seg = q[at[u]:at[v] + 1]
                if fore:
                    seg = [v] + seg[:-1]
                    if rd[v] > fin[u] + p[v] + FREE or any(reach[v] >> x & 1 for x in seg):
                        continue
                    bad = any(tabu.get((v, x), 0) > step for x in seg)
                else:
                    seg = seg[1:] + [u]
                    if qd[u] > tail[v] + p[u] + FREE or any(reach[x] >> u & 1 for x in seg):
                        continue
                    bad = any(tabu.get((x, u), 0) > step for x in seg)
                c = 0.0
                for m in range(K):
                    (f, r, w, s), pm, e = got[m], sets[m][0], end[m]
                    t, top, on, heads = f[q[at[u] - 1]] if at[u] else before[m][qn[u]], 0.0, False, []
                    for x in seg:
                        t = max(t, r[x])
                        heads.append(t)
                        t += pm[x]
                        on = on or f[x] - pm[x] + w[x] > e - 1e-6
                    t = w[q[at[v] + 1]] if at[v] + 1 < len(q) else after[m][qn[u]]
                    for x, h in zip(seg[::-1], heads[::-1]):
                        t = max(t, s[x]) + pm[x]
                        top = max(top, h + t)
                    c += scale[m] * max(top, past[m] if on else e)
                if not bad or c < best:
                    rated.append((c + draw(1000) * 3e-7, u, v, fore))
            for c, u, v, fore in sorted(rated):
                a, b = win.index(u), win.index(v)
                mid, go, held = win[a:b + 1], {v if fore else u}, set()
                for x in mid[-2::-1] if fore else mid[1:]:
                    if qn[x] in held or any(y in go for y in (serve if fore else need)[x]):
                        go.add(x)
                        held.add(qn[x])
                if qn[u] in held:
                    continue
                stay, go = [x for x in mid if x not in go], [x for x in mid if x in go]
                for x in stay:
                    if qn[x] == qn[u]:
                        tabu[(x, v) if fore else (u, x)] = step + TENURE + draw(TENURE)
                win = win[:a] + (go + stay if fore else stay + go) + win[b + 1:]
                for m in range(K):
                    (f, r, w, s), (ns, pre, post, last) = got[m], sets[m]
                    sweep(win, before[m][:], pre, zero, ns, f, r)
                    sweep(win[::-1], after[m][:], post, last, ns, w, s)
                break
            else:
                break
            end = ends()
            c = sum(x * s for x, s in zip(end, scale))
            if c < best - 1e-9:
                best, keep, since = c, win, 0
        return head + keep + rest

    def better(order, count, others):
        got = look(order)
        cost = price(got)
        for step in range(count):
            tries = [(None, 1, 2), (None, 1, 0), (None, 1, 3), (None, 2, 1)] if step % 8 == 7 else []
            if step == 0:
                tries = [(x, b, to) for x in others for to in range(-1, 5) for b in ({to, 1, 2} if 0 <= to < 4 else {to})]
            for other, b, to in tries:
                new = repeat(other or starts(got), starts(got), b, to)
                g2 = look(new)
                if price(g2) <= cost:
                    order, got, cost = new, g2, price(g2)
            start = starts(got)
            order = sorted(order, key=lambda i: start[i] if i >= first else -1)
            at = [first] + [order.index(x) for x in marks] + [n]
            lo, hi = ((2, 3), (2, 3), (0, 2), (4, 6))[draw(4)]
            new = stretch(order, got, max(first, min(n - WIDE, at[lo] + draw(at[hi] - at[lo]) - WIDE // 2)))
            got = look(new)
            if price(got) <= cost:
                order, cost = new, price(got)
            else:
                got = look(order)
        return cost, order, starts(got)
    some = [fresh() for _ in range(STARTS)]
    scale = [1.0 / max(x[2]) for x in look(some[0])]
    some = sorted(better(x, SHORT, []) for x in some)
    cost, ORDER[:], _s = better(some[0][1], LONG, [x[2] for x in some])
    INFO.extend([cost] + [round(max(x[2])) for x in look(ORDER)] + [round(x[0], 4) for x in some])
    return ORDER


def rank_program(g, core, T, topo):
    rank = T.rank_of(core)
    if rank is None:
        return
    N = len(T.cores)
    Q = {"V": g.vector, "S": g.scalar, "P": g.tensor, "G": g, "D": g.sync}
    calls, count, now = [], {}, [-1]
    whole, parts, rd, called = {}, {}, {}, {}

    def record(q, fns, R, W, ns, late=HOP, tok=None, far=0):
        called.update(((now[0], k[1:]), len(calls)) for k in W.split() if k[0] == "#")
        W, rule = " ".join(k for k in W.split() if k[0] != "#"), set()
        name = (now[0], q + "".join(x for x in R + "|" + W if not x.isdigit()))
        count[name] = count.get(name, -1) + 1
        R, W, pre = R.split(), W.split(), set()
        for k in R:
            pre.update(parts.get(k, []))
            if k in BANKS:
                pre.update(i for i in rd.get(k, []) if calls[i]["q"] != q)
        for k in W:
            pre.update(parts.get(k, []) if k[0] != "+" else whole.get(k[1:], []))
            pre.update(rd.get(k.lstrip("+"), []))
        i = len(calls)
        calls.append({"q": q, "fns": fns, "pre": pre, "rule": rule, "ns": ns, "late": late, "tok": tok, "far": far, "name": name + (count[name],)})
        for k in R:
            rd.setdefault(k, []).append(i)
        for k in W:
            if k[0] == "+":
                parts.setdefault(k[1:], []).append(i)
            else:
                whole[k], parts[k], rd[k] = [i], [i], []

    def obey():
        for t in range(5):
            for line in RULES[t // 4]:
                line = [called[t + (x[0] == "+"), x.lstrip("+")] for x in line.split()]
                for a, b in zip(line, line[1:]):
                    if a != b:
                        calls[b]["rule"].add(a)
        new, left = {}, list(range(len(calls)))
        while left:
            i = next(i for i in left if all(x in new for x in calls[i]["pre"] | calls[i]["rule"]))
            left.remove(i)
            new[i] = len(new)
        calls[:] = [dict(calls[i], pre={new[x] for x in calls[i]["pre"]}, rule={new[x] for x in calls[i]["rule"]}) for i in new]

    def emit():
        obey()
        cnt = {"V": 0, "S": 0, "P": 0, "G": 0}
        seen = {q: {} for q in Q}
        snap, tok = {}, {}
        for i in issue_order(calls):
            c = calls[i]
            q, best = c["q"], {}
            for p in c["pre"]:
                if q != "P" or calls[p]["q"] != "P":
                    s, v = tok[p]
                    best[s] = max(best.get(s, 0), v)
            for s in sorted(best, key=lambda s: -best[s]):
                v = best[s]
                if v > seen[q].get(s, 0):
                    Q[q].wait_ge(T.sem[s], v)
                    for s2, v2 in snap.get((s, v), {}).items():
                        seen[q][s2] = max(seen[q].get(s2, 0), v2)
                    seen[q][s] = v
            for fn in c["fns"]:
                if c["tok"]:
                    fn(Q[q])
                else:
                    fn(Q[q]).then_inc(T.sem["q" + q], 1)
                    cnt[q] += 1
            tok[i] = c["tok"] or ("q" + q, cnt[q])
            if not np.any(c["far"]):
                snap[tok[i]] = dict(seen[q])
        for q in cnt:
            g.wait_ge(T.sem["q" + q], cnt[q])

    def dma(q, out, in_, R, W, sem, late=2500):
        record(q, [lambda e: e.dma_start(out, in_).then_inc(T.sem[sem], 16)], R, W, 60, late, (sem, 16))

    nloc = [0]

    def send(out, in_, R, W, sem, cols):
        dst, src = T.cores[(rank + 1) % N], T.cores[(rank - 1) % N]
        rid, pid, _s = topo.addr(dst)
        record("G", [lambda e: e.remote_dma(out, in_, T.sem[sem], T.sem.loc, pid, rid, topo.mask(core, dst))], R, W, ISSUE,
               FAR + (0 if nloc[0] else FIRST), (sem, len(topo.engines(src, core))), 16 * ROW + COL * cols)
        nloc[0] += len(topo.engines(core, dst))

    def vec(fn, R, W, n):
        record("V", [fn], R, W, np.maximum(n, 64 * CYC))

    def tt(o, a, b, o_, R, W, n=0):
        vec(lambda e: e.tensor_tensor(o, a, b, o_), R, W, n)

    def ts(o, a, s1, s2, o0, o1, R, W, n=0):
        if o1 is None:
            vec(lambda e: e.tensor_scalar(o, a, s1, None, o0), R, W, n)
        else:
            vec(lambda e: e.tensor_scalar(o, a, s1, s2, o0, o1), R, W, n)

    def cp(o, a, R, W, n=0):
        vec(lambda e: e.tensor_copy(o, a), R, W, n)

    def ms(o, c, W, n=0):
        vec(lambda e: e.memset(o, c), "", W, n)

    def act(o, a, R, W, n=0, f=AF.Copy, **kw):
        record("S", [lambda e: e.activation(o, a, f, **kw)], R, W, np.maximum(n, 64 * CYC))

    def mms(l, R, W, n):
        record("P", [lambda e, m=m: e.matmul(*m) for m in l], R, W, n * PEC)

    def group(l, R, W, n, st=True, stop=True):
        mms([m + (st and x == 0, stop and x == len(l) - 1) for x, m in enumerate(l)], R, W, n)

    def iota(o, pat, base, cm, W, n=16, R="", **kw):
        record("G", [lambda e: e.iota(o, pat, base, cm, **kw)], R, W, 130 + 2 * n * CYC)

    def fiota(o, pat, base, cm, W, n=16, R=""):
        iota(o, pat, base, cm, W, n, R, allow_small_or_imprecise_dtypes=True)

    def sel(o, a, pat, cmp_, fill, base, cm, R, W, n=128):
        record("G", [lambda e: e.affine_select(o, a, pat, cmp_, fill, base, cm)], R, W, 170 + 2 * n * CYC)

    def gat(n):
        return 60 + GAT * n

    def sca(n):
        return 50 + SCA * n

    def conv(out, row, a, n, R, W, st=True, stop=True, tab="SELW"):
        group([(out, T[tab][:, 15 - l:143 - l], row[:, a + l:a + 16 * (n - 1) + l + 1:16]) for l in range(16)], R + " " + tab, W, 1024, st, stop)

    def part(q):
        return slice(16 * MP * q, 16 * MP * (q + 1))

    def names(x, j, n):
        return "".join(" #%s%d" % (x, j + y) for y in range(n))

    def wide(k):
        return 16 * (QU[k + 1] - QU[k])

    def pairs(k):
        return slice(16 * QU[k], 16 * QU[k + 1])

    def blocks(k):
        return range(QU[k] // NQ, QU[k + 1] // NQ)

    def nurses(w, t, k):
        return w[:, 512 * t + HCOL[k]:512 * t + HCOL[k] + wide(k)]

    def fill(q, o, c, W, n, p=slice(0, 128), R=""):
        if q == "V":
            vec(lambda e: e.memset(o, c), R, W, 0)
        elif q == "S":
            act(o, T.ONES[p, 0:n], "ONES " + R, W, n * CYC, scale=c)
        else:
            sel(o, T.ONES[p, 0:n], [[0, n]], A.is_gt, c, 0, 0, "ONES " + R, W, n)

    def wi(t, a, b):
        return T.WI[:, 512 * t + a:512 * t + b]

    def wo(t, a, b):
        return T.WO[:, 512 * t + a:512 * t + b]

    def afl(t, a, b):
        return T.AFL[:, 256 * t + a:256 * t + b]

    def bb(t, a, b, step=1, c=slice(0, 16)):
        return T.BB[:, 6 * t + a:6 * t + b:step, c]

    def big(out, n, cols, w="ONES"):
        return (out, T[w][0:n, :], T.CM[0:n, 0:cols])

    dma("S", T.pns[:], T.pn[:], "", "pns", "d_pn", 1900)
    dma("D", T.pfs[:], T.pf[:], "", "pfs", "d_pf", 2300)
    dma("S", T.bss[:], T.bs[:], "", "bss", "d_bs", 2600)
    dma("D", T.nbs[:], T.nb[:], "", "nbs", "d_nb", 2900)
    dma("S", T.cbs[:], T.cb[:], "", "cbs", "d_cb", 3700)
    dma("D", T.fss[:], T.fs[:], "", "fss", "d_fs", 4000)
    dma("D", T.ths[:, 0:1], T.th[:], "", "ths", "d_th", 4300)
    dma("D", T.xfs[:], T.xf[:], "", XFS, "d_xf", XF)

    ms(T.ONES[:], 1.0, "ONES")
    low = slice(0, 32)
    fill(LATE, T.NEG[low, :], -1.0, "NEG", 128, low)
    fill(LATE, T.CM[:], MAGIC, "CM", 128)
    ms(T.TR[0:32, 0:128], -1024.0, "TR")
    ms(T.SELW[:], 0.0, "SELW")
    ms(T.LL[:], 0.0, "LL")
    ms(T.EUW[:], 0.0, "EUW0", 48 * NQ * CYC)
    for a, b, w in ((0, 1, -0.5), (1, 2, -FLAG), (2, 3, 0.5), (3, 4, FLAG), (4, 7, -TURN)):
        fill(LATE, T.QA[:, a:b, :], w, "+QA0", NQ * (b - a))
    for a, b, x in ((0, 1, 32), (1, 2, 512), (2, 5, 1)):
        fill(LATE, T.MC[low, a:b, :], x * MAGIC, "+MC", 16 * (b - a), low)
    sel(T.QA[:], T.QA[:], [[0, 7], [-16 * MP, NQ]], A.is_ge, 0.0, 0, 1, "QA0", "QA", 7 * NQ)
    sel(T.QA[:], T.QA[:], [[0, 7], [16 * MP, NQ]], A.is_ge, 0.0, 16 * MP - 1, -1, "QA", "QA", 7 * NQ)
    ms(T.TM[0:32, :], 16.0, "TM")
    ms(T.HALF[:], 0.5, "HALF")
    ms(T.QUART[:], 0.0, "QUART")
    ms(T.QUART[:, ::8], 0.125, "+QUART")
    ms(T.X16[:], 0.0, "X16")
    ms(T.TWO[:], 2.0, "TWO")
    fill(LATE, T.ACC[:, 0:1], 1.0 / 128, "ACC4", 1)
    ms(T.SB9[:], 1.0, "SB9")
    act(T.SA[:, 0:16], T.ONES[:, 0:16], "ONES", "SA", 1300, f=AF.Silu, scale=32.0)
    fill(LATE, T.FT[low, :], 0.5, "FT", 128, low)
    fill(LATE, T.RTB[:, 0:8], 0.0, "+RTB0", 8)
    fill(LATE, T.RTB[:, 8:16], 1.0, "+RTB0", 8)
    for n in range(0, NXG, 2):
        ms(T.XG[:, 512 * n:512 * n + 1024:2], 0.0, "XG%d XG%d" % (n, n + 1), 256 * CYC)
    iota(T.PI[:, 0:1], [[1, 1]], 0, 1, "PI")
    sel(T.G16[:], T.ONES[:], [[-16, 8], [0, 16]], A.is_ge, 0.0, 0, 1, "ONES", "G16")
    sel(T.G16[:], T.G16[:], [[16, 8], [0, 16]], A.is_ge, 0.0, 15, -1, "G16", "G16")
    fiota(T.KK[:], [[0, 8], [1, 16]], 0, 0, "KK", 128)
    fiota(T.IOTC[:], [[1, 512]], -256, 0, "IOTC", 512)
    r32 = T.TR[0:32, 0:128]
    sel(r32, r32, [[0, 128 // MP], [-1, MP]], A.not_equal, 0.0, -16, 1, "TR", "TR")
    sel(T.TM[0:32, :], T.TM[0:32, :], [[0, NQ], [-1, MP], [0, 16]], A.is_equal, 0.0, -16, 1, "TM", "TM")
    sel(r32, r32, [[0, 128]], A.is_ge, 0.0, -16, 1, "TR", "TR")
    sel(r32, r32, [[-1, 8], [0, 16]], A.not_equal, 1.0, 0, 1, "TR", "TR")
    sel(r32, r32, [[-1, 8], [0, 16]], A.not_equal, 1.0, -8, 1, "TR", "TR")
    sel(T.IDENT[:], T.ONES[:], [[-1, 128]], A.is_equal, 0.0, 0, 1, "ONES", "IDENT")
    act(T.SELW[:, 15:128:16], T.G16[:, ::16], "G16", "SELW", scale=0.0625)
    fiota(T.LI[:], [[16, 16]], 0, 0, "LI")
    for w, x in (("IDF", 1.0), ("NIDF", -1.0), ("NID", -1.0)):
        act(T[w][:], T.IDENT[:], "IDENT", w, 128 * CYC, scale=x)

    pn = T.PD[:, 0:256]
    mms([(pn, T.IDENT[:], T.pns[:], True, True)], "IDENT pns", "PD", 256)
    tt(T.HI[:], pn, T.pfs[:], A.max, "pfs PD", "HI", 256 * CYC)
    tt(T.LO[:], pn, T.pfs[:], A.min, "pfs PD", "LO", 256 * CYC)
    tt(T.SG[:], pn, T.pfs[:], A.is_gt, "pfs PD", "SG", 256 * CYC)
    ts(T.SG[:], T.SG[:], 2.0, -1.0, A.mult, A.add, "SG", "SG", 128 * CYC)
    act(T.G8[:], T.G16[:, ::16], "G16", "G8")
    cp(T.nbU[:], T.nbs[:], "nbs", "nbU")
    cp(T.CBF[:], T.cbs[:], "cbs", "CBF", 512 * CYC)
    cp(T.bsU[:], T.bss[:], "bss", "bsU")
    cp(T.fsU[:], T.fss[:], "fss", "fsU")
    for k in range(4):
        act(nurses(T.WI, 0, k), T.CBF[:].indirect(T.nbU[:, QU[k]:QU[k + 1]]), "CBF nbU", "WI0_%d" % k, gat(wide(k)))
    for k in range(16):
        if k < DS:
            act(T.D1[:, 2 * k::32], T.HI[:], "HI", "+D1", 256 * CYC)
        else:
            cp(T.D1[:, 2 * k::32], T.HI[:], "HI", "+D1", 128 * CYC)
        if k < DG:
            sel(T.D1[:, 2 * k + 1::32], T.LO[:], [[0, 256]], A.is_ge, 0.0, 0, 0, "LO", "+D1", 256)
        else:
            cp(T.D1[:, 2 * k + 1::32], T.LO[:], "LO", "+D1", 128 * CYC)
    for n in range(8):
        ts(T.WH[:, :, n, :], T.SG[:], T.G16[:, 16 * n:16 * n + 1], -1.0, A.mult, A.mult, "SG G16", "+WH", 128 * CYC)
        if n < WS:
            act(T.WA[:, :, n, :], T.SG[:], "SG G8", "+WA", 256 * CYC, f=AF.Identity, scale=T.G8[:, n:n + 1])
        else:
            ts(T.WA[:, :, n, :], T.SG[:], T.G16[:, 16 * n:16 * n + 1], None, A.mult, None, "SG G16", "+WA", 128 * CYC)
    ts(T.PM[:, 0:1], T.PI[:, 0:1], 15, None, A.bitwise_and, None, "PI", "PM")
    cp(T.PMF[:, 0:1], T.PM[:, 0:1], "PM", "PMF")
    ts(T.KK[:], T.KK[:], T.PMF[:, 0:1], None, A.is_equal, None, "KK PMF", "KK")
    for n, bits in enumerate((4032, 63)):
        ts(T.TH[:, n:n + 1], T.ths[:, 0:1], 1, bits, A.arith_shift_right, A.bitwise_and, "ths", "TH%d" % n)
        ts(T.THN[:, n:n + 1], T.TH[:, n:n + 1], 0.5 * n, -1.0, A.add, A.mult, "TH%d" % n, "THN%d" % n)
        ts(T.LL[:, 8 * n:8 * n + 8], T.G16[:, ::16], T.THN[:, n:n + 1], None, A.mult, None, "G16 THN%d" % n, "+LL")
    for n in range(1, max(len(blocks(k)) for k in range(4))):
        act(T.TR[0:32, 128 * n:128 * n + 128], r32, "TR", "+TRb", 128 * CYC)
    mms([(T.PL[0:24, 0:2, :], T.LL[:, 0:24], T.KK[:], True, True)], "LL KK", "PL", 128)
    tt(T.TI[0:24, :], T.PL[0:24, 0:2, :], T.TM[0:24, :], A.add, "PL TM", "TI", 128 * CYC)
    for q in range(NQ):
        act(T.EUW[part(q), 0, 48 * q + 16:48 * q + 32], T.KK[part(q), 0:16], "KK EUW0", "+EUW", f=AF.Identity, scale=SWAP, bias=EACH)
        act(T.EUW[part(q), 1, 48 * q + 16:48 * q + 32], T.KK[part(q), 0:16], "KK EUW0", "+EUW4")
    tt(T.BC[:], T.KK[:, 0:16:8], T.KK[:, 4:16:8], A.subtract, "KK", "BC")
    ts(T.SELJ[:], T.SELW[:], T.BC[:, 0:1], 16.0, A.mult, A.mult, "SELW BC", "SELJ", 72 * CYC)
    ts(T.SELX[:], T.SELW[:], T.BC[:, 1:2], 16.0, A.mult, A.mult, "SELW BC", "SELX", 72 * CYC)
    ts(T.SELR[:], T.SELW[:], T.KK[:, 8:9], -16.0, A.mult, A.mult, "SELW KK", "SELR", 72 * CYC)
    ts(T.NI[:], T.LI[:], T.PMF[:, 0:1], -1.0, A.add, A.mult, "LI PMF", "NI")
    for a, b in OFFS:
        act(T.TB[:, a:b], T.NI[:, a:b], "NI", "+TB", f=AF.Identity, scale=-32.0, bias=-512.0 * a)

    def sites(x, n, R, W):
        s = slice(16 * (n // 3), 16 * (n // 3) + 16)
        ts(T.BI1[:, s], x, 510, None, A.bitwise_and, None, R, "BI1%d" % n)
        ts(T.BI2[:, s], T.BI1[:, s], 2.0, -255.0, A.mult, A.add, "BI1%d" % n, "BI2%d" % n)
        ts(bb(0, n, n + 1), x, -256.0, None, A.add, None, R, W)
        tt(bb(0, n + 1, n + 2), T.BI2[:, s], x, A.subtract, "BI2%d %s" % (n, R), W)

    def nurses_sites():
        fiota(T.YC[:], [[1, 512]], 32, 0, "YC", 512)
        for a in range(0, 32, 8):
            act(wo(4, 0, 512).indirect(T.bsU[:, a:a + 8]), T.YC[:, 16 * a:16 * a + 128], "YC bsU SA", "INV", sca(128), f=AF.Silu)
        act(T.XB0[:, 256:512], wo(4, 0, 512).indirect(T.nbU[:]), "INV nbU", "XB1", gat(256), f=AF.Identity, bias=-288.0)
        conv(T.PN[:, 256:272], T.XB0, 256, 16, "XB1", "PN")
        ts(T.BI0[:], T.PN[:, 256:272], 256.0, None, A.add, None, "PN", "BI0")
        sites(T.BI0[:], 3, "BI0", "+BG0")

    sites(T.fss[:], 0, "fss", "+BB0")
    ms(T.SELB[:, :, :, 0:8], 0.0, "SELB", 512 * CYC)
    for a, x in ((8, 1.0), (12, -1.0)):
        sel(T.SELB[:, :, :, a:a + 4], T.SELB[:, :, :, 0:4], [[-1, 16], [-16, 8], [0, 4]], A.not_equal, x, 0, 1, "SELB", "+SELBb", 512)
    for a, b, x in ((0, 4, 1.0 / 128), (4, 8, -1.0 / 128), (8, 16, 0.0)):
        fill(LATE, T.LO8[:, :, a:b], x, "+LO8", 8 * (b - a))
    ts(bb(0, 5, 6), T.nbs[:], -256.0, None, A.add, None, "nbs", "+BB0")
    fiota(T.UF[:, 0:512], [[0, 512]], 16416, 0, "UFb", 512)
    conv(T.PN[:, 0:16], T.pfs, 0, 16, "pfs", "PN")
    ts(T.ELS[:], T.PN[:, 0:16], 16.0, None, A.mult, None, "PN", "ELS")
    ts(T.ELS[:], T.ELS[:], 31, None, A.bitwise_and, None, "ELS", "ELS")
    fill(LATE, T.TA[:, 1, :], 0.0, "+TA", 16)
    ts(T.TA[:, 0, :], T.ELS[:], -1.0, 15.5 - 8 * MP, A.mult, A.add, "ELS", "+TA")
    ts(T.TC[:], T.ELS[:], 8.0 * MP - 256, None, A.add, None, "ELS", "TC")
    cp(T.PIF[:, 0:1], T.PI[:, 0:1], "PI", "PIF")
    vec(lambda e: e.tensor_tensor_scan(T.PABW[:], T.HALF[:], T.QUART[:], 0.0, A.mult, A.max), "HALF QUART", "PABW", 128 * CYC)
    vec(lambda e: e.tensor_tensor_scan(T.P2[:, 0:9], T.TWO[:, 0:9], T.X16[:, 0:9], 0.5, A.mult, A.add), "TWO X16", "P2", 0)
    ts(T.BIT[:, 0:5], T.PABW[:, 0:5], T.PIF[:, 0:1], 2048.0, A.mult, A.mult, "PABW PIF", "BIT")
    ts(T.BIT[:, 0:5], T.BIT[:, 0:5], 256, None, A.bitwise_and, None, "BIT", "BIT")
    ts(T.SB9[:, 0:4], T.BIT[:, 0:4], -1.0 / 128, 1.0, A.mult, A.add, "BIT", "+SB9")
    ts(T.RTB[:, 3:8], T.BIT[:, 0:5], -1.0 / 256, None, A.mult, None, "BIT RTB0", "+RTB")
    ts(T.RTB[:, 11:16], T.BIT[:, 0:5], -1.0 / 256, 1.0, A.mult, A.add, "BIT RTB0", "+RTB")
    tt(T.LTB[:, 1:9], T.SB9[:, 1:9], T.P2[:, 1:9], A.mult, "SB9 P2", "+LTB")
    ts(T.LTB[:, 9:17], T.P2[:, 1:9], -1.0, None, A.mult, None, "P2", "+LTB")
    tt(T.LX1[:, 0:1], T.PMF[:, 0:1], T.SB9[:, 0:1], A.add, "PMF SB9", "LX1")
    ts(T.SC[:, 0:1], T.SB9[:, 0:1], -1.0, None, A.mult, None, "SB9", "+SC")
    ts(T.SC[:, 1:2], T.SB9[:, 0:1], 512.0, 256.0, A.mult, A.add, "SB9", "+SC")
    mms([(T.PT[0:16, 0:128], T.LTB[:, 1:17], T.IDENT[:], True, True),
         (T.PT[0:16, 128:160], T.RTB[:], T.IDENT[:, 0:32], True, True)], "LTB RTB IDENT", "PT", 160)
    act(T.LB[0:16, :], T.PT[0:16, 0:128], "PT", "LB", 128 * CYC)
    act(T.RX[0:16, :], T.PT[0:16, 128:160], "PT", "RX")
    act(T.PABX[0:32, :], T.PABW[0:32, :], "PABW", "PABX", 128 * CYC, scale=4.0)
    m = T.S2[0:32, :]
    sel(m, T.ONES[0:32, :], [[-1, 16], [0, 8]], A.is_equal, 0.0, 0, 1, "ONES", "S2")
    sel(m, m, [[0, 128]], A.not_equal, 512.0, -16, 1, "S2", "S2")
    sel(m, m, [[0, 128]], A.not_equal, 1.0, -17, 1, "S2", "S2")
    tt(m, m, T.PABX[0:32, :], A.mult, "PABX S2", "S2", 256 * CYC)
    ts(m, m, T.IDF[0:32, 16:17], None, A.subtract, None, "S2 IDF", "S2")
    ts(T.S1[0:32, :], m, -1.0, T.IDF[0:32, 16:17], A.mult, A.add, "S2 IDF", "S1")
    act(T.P2[:, 9:17], T.P2[:, 1:9], "P2", "P2")
    tt(T.P2[:, 1:17], T.P2[:, 1:17], T.KK[:, 0:16], A.mult, "P2 KK", "P2")
    vec(lambda e: e.tensor_reduce(T.C2[:, 0:1], T.P2[:, 1:17], AxisListType.X, A.add), "P2", "C2a", 0)
    act(T.C2[:, 1:2], T.C2[:, 0:1], "C2a", "C2", scale=-2.0)
    sel(T.X16[:], T.X16[:], [[-8, 16]], A.is_ge, 1.0, 0, 1, "X16", "X16", 16)
    sel(T.X16[:], T.X16[:], [[8, 16]], A.is_ge, 1.0, 7, -1, "X16", "X16", 16)
    act(T.U[:], T.IOTC[:].indirect(T.bsU[:]), "IOTC bsU", "U", gat(512))
    act(T.XB0[:, 0:256], T.U[:].indirect(T.fsU[:]), "U fsU", "XB0", gat(256))
    conv(T.PN[:, 32:48], T.XB0, 0, 16, "XB0", "PN")
    ts(T.GU[:], T.PN[:, 32:48], 256.0, None, A.add, None, "PN", "GU")
    cp(bb(0, 2, 3), T.PN[:, 32:48], "PN", "+BB0")
    act(afl(0, 0, 256), T.CBF[:].indirect(T.GU[:]), "CBF GU", "AFL0", gat(256), scale=-1.0)

    ring = {}

    def slots(name, size, n):
        a = ring[name] if ring[name] + n <= size else 0
        ring[name] = a + n
        return a, " ".join("%s%d" % (name, x) for x in range(a, a + n))

    def chunk(t, q, j, n):
        c = j % 16
        off, key = T[("UH", "UA")[j // 16]], [("UH%d", "UA%d")[j // 16] % PART[c + x] for x in range(n)]
        a, key = T.xfs[:].indirect(off[:, 16 * c:16 * (c + n)]), XFS + " " + " ".join(key)
        if q == "V":
            x, xk = slots("YV", NY, n)
            s, first = slice(256 * x, 256 * (x + n)), T.YV[:, 256 * x:256 * (x + n):16]
            tt(T.YV[:, s], a, T.D1[:, 512 * c:512 * (c + n):2], A.min, "D1 " + key, xk + names("g", j, n), gat(256 * n))
            tt(first, first, T.LO[:, 16 * c:16 * (c + n)], A.max, "LO " + xk, xk, 32 * n * CYC)
            vec(lambda e: e.tensor_tensor_scan(T.CV[:, s], T.D1[:, 512 * c + 1:512 * (c + n):2], T.YV[:, s], 0.0, A.min, A.max),
                "D1 " + xk, xk.replace("Y", "C") + names("c", j, n), 128 * n * CYC)
            lanes(t, j, n, xk.replace("Y", "C"), lambda p: T.CV[:, 256 * x + 16 * p:256 * x + 16 * (p + MP)])
            return
        x, xk = slots("XG", NXG, n)
        act(T.XG[:, 512 * x + 1:512 * (x + n):2], a, key, xk + names("g", j, n), gat(256 * n))
        for u in range(0, n, SCAN):
            clamp(t, j + u, x + u, min(SCAN, n - u))

    def clamp(t, j, x, n):
        c = j % 16
        m, mk = slots("CL", NCL, n)
        vec(lambda e: e.tensor_tensor_scan(T.CL[:, 512 * m:512 * (m + n)], T.XG[:, 512 * x:512 * (x + n)],
                                           T.D1[:, 512 * c:512 * (c + n)], 0.0, A.min, A.max),
            "D1 " + " ".join("XG%d" % (x + y) for y in range(n)), mk + names("c", j, n), 256 * n * CYC)
        lanes(t, j, n, mk, lambda p: T.CL[:, 512 * m + 32 * p + 1:512 * m + 32 * (p + MP):2])

    def lanes(t, j, n, key, block):
        for u0 in range(n):
            c = (j + u0) % 16
            k = PART[c]
            P, w, cc = "PB%d" % k, ("WH", "WA")[j // 16], len(blocks(k))
            if u0 and c != QU[k]:
                continue
            if j < 16 and c == QU[k]:
                mms([(T[P][:, 0:cc, :, :], T.TI[0:24, :], T.TR[0:24, 0:128 * cc], True, False)], "TI TR TRb", P, 128 * cc)
            m = min(n - u0, QU[k + 1] - c)
            mms([(T[P][part((c + u) % NQ), (c + u - QU[k]) // NQ, :, b:b + MP], block(16 * (u0 + u) + b), T[w][:, c + u, :, b:b + MP], False,
                  j >= 16 and c + u >= QU[k + 1] - NQ and b + MP == 16) for u in range(m) for b in range(0, 16, MP)], key + " " + w, P + names("l", j + u0, m), 256 * m)

    def signs(k):
        P, z, cc = "PB%d" % k, "Z%d" % k, len(blocks(k))
        act(T.Z[:, QU[k] // NQ:QU[k + 1] // NQ, :, :], T[P][:, 0:cc, :, :], P, z + " ACC%d #sign%d" % (k, k), (128 * cc + 20) * CYC, f=AF.Sign,
            accum_out=T.ACC[:, k + 1:k + 2])

    def total(k):
        if k == 2:
            act(T.ACC[:, 8:12], T.ACC[:, 0:4], "ACC0 ACC1 ACC2 ACC4", "ACC5 #acc", accum_out=T.ACC[:, 5:6])
        mms([(T.PT[:, 0:1], T.PABW[:], T.ACC[:, 7 - k:8 - k], k == 2, k == 3)], "PABW ACC%d" % (9 - 2 * k), "PT #total%d" % k, 256)

    def rows(t, k):
        P, s, hk, ak, n, u, c = "PB%d" % k, pairs(k), "WI%d_%d" % (t, k), "AFL%d" % t, wide(k), wide(k) // 16, 3 - k // 3
        p, h, a, y = T.PD[:, s], nurses(T.WI, t, k), afl(t, s.start, s.stop), T[P][:, c, 0:u, :]
        mms([big(y, 64, n) + (True, False)][t // 4:]
            + [(T[P][32 * (x // 2):32 * (x // 2) + 32, c, q:u:NQ, :], T.EUW[:, t // 4, 48 * q + 16 - 16 * (x % 2):48 * q + 48 - 16 * (x % 2)],
                T.Z[:, QU[k] // NQ:QU[k + 1] // NQ, x, :], t == 4 and x % 2 == 0, (t == 4 or q == NQ - 1) and x % 2 == 1)
               for q in range(NQ) for x in range(8)], "Z%d ONES CM " % k + ("EUW", "EUW4")[t // 4], P + " #rows%d" % k,
            8 * NQ * max(32, n // NQ) + max(64, n))
        if t < 4:
            act(T.MM[:, s], y, P, "MM%d #mask%d" % (k, k), n * CYC, f=AF.Abs, scale=1.0 / 64, bias=MP - 1 - MAGIC)
            tt(p, p, T.MM[:, s], A.mult, "PD MM%d" % k, "pd%d #p%d" % (k, k), n * CYC)
            tt(nurses(T.WO, t, k), p, h, A.add, "PD pd%d %s" % (k, hk), "WO%dh%d #h%d" % (t, k, k), n * CYC)
            tt(wo(t, ACOL + s.start, ACOL + s.stop), p, a, A.add, "PD pd%d %s" % (k, ak), "WO%da%d #a%d" % (t, k, k), n * CYC)
            for n, (c0, c1, keys, after) in enumerate(SENDS):
                if after == k:
                    send(wi(t + 1, c0, c1), wo(t, c0, c1), " ".join("WO%d%s" % (t, x) for x in keys.split()),
                         " ".join({"h": "WI%d_", "a": "WA%d_"}[x[0]] % (t + 1) + x[1:] for x in keys.split()), "a%d_%d" % (n, t + 1), c1 - c0)
        else:
            act(T.MM[:, s], y, P, "MM%d #mask%d" % (k, k), n * CYC, f=AF.Identity, scale=0.5, bias=0.5 * MP)
            tt(T.PS[:, s], p, T.MM[:, s], A.mult, "PD MM%d" % k, "PS%d #p%d" % (k, k), n * CYC)
            tt(T.YC[:].indirect(T.YL[:, QU[k]:QU[k + 1]]), a, T.PS[:, s], A.add, "YL PS%d %s" % (k, ak), "YC #a%d" % k, sca(n))
            tt(T.YC[:].indirect(T.YL[:, 48 + QU[k]:48 + QU[k + 1]]), h, T.PS[:, s], A.subtract, "YL PS%d %s" % (k, hk), "YC #h%d" % k, sca(n))

    def sums(t, k):
        n, (a, b) = [x for x in enumerate(STAGES) if x[1][0] <= QU[k] < x[1][1]][0]
        P = "PB%d" % (n % 2)
        if a == QU[k]:
            group([(T[P][:, 0, 0:2, a:b], T.IDENT[:], T.TA[:, :, a:b]), (T[P][:, 0, 0, a:b], T.IDENT[:], T.TB[:, a:b])],
                  "IDENT TA TB", P + " #open%d" % k, 128, True, False)
        group([(T[P][:, 0, 0:2, NQ * c:NQ * (c + 1)], T.Z[:, c, :, :], T.QA[:, 0:2, :]) for c in blocks(k)],
              "Z%d QA" % k, P + " #sums%d" % k, 64 * len(blocks(k)), False, False)
        if b == QU[k + 1]:
            stage(t, a, b, P)

    def aside(t, k):
        if k == 0:
            group([(T.PL[:, 0:4, 0:16], T.ONES[0:1, :], T.MC[0:1, 1:5, :])], "ONES MC", "PL", 64, True, False)
        group([(T.PL[:, 0:4, NQ * c:NQ * (c + 1)], T.Z[:, c, :, :], T.QA[:, 3:7, :]) for c in blocks(k)],
              "Z%d QA" % k, "PL #aside%d" % k, 64 * len(blocks(k)), False, False)
        if k == 3:
            group([(T.PL[:, 0:4, 0:16], T.NEG[0:1, :], T.MC[0:1, 1:5, :]), (T.PL[:, 0, 0:16], T.IDENT[:], bb(t, 1, 2))],
                  "NEG MC IDENT BB%d" % t, "PL #odd", 128, False, t == 4)

    def stage(t, a, b, P):
        zs, x, p = " ".join("Z%d" % k for k in range(PART[a], PART[b - 1] + 1)), t // 4, T[P]
        k = PART[b - 1]
        group([(p[:, 0, 0:2, a:b], T[w][0:1, :], T.MC[0:1, 0:2, a:b]) for w in ("ONES", "NEG")]
              + [(p[:, 0, 1, a:b], T.IDENT[:], bb(t, 0, 1, 1, slice(a, b)))]
              + ([(p[:, 0, 0, a:b], T.IDENT[:], T.TC[:, a:b])]
                 + [(p[:, 0, 0, NQ * c:NQ * (c + 1)], T.Z[:, c, :, :], T.QA[:, 2, :]) for c in range(a // NQ, b // NQ)])[:99 * (1 - x)],
              "ONES NEG MC IDENT TC QA BB%d %s" % (t, zs), P + " #stage%d" % k, 192 + (64 + 64 * (b - a) // NQ) * (1 - x), False)
        ts(T.OF[:, x:2, a:b], p[:, 0, x:2, a:b], 256.0, None, A.add, None, P, "OF%d #of%d" % (a, k))
        if t < 4:
            act(T.UF[:, 512:1536].indirect(T.OF[:, 1, a:b]), T.IDX[:, 16 * a:16 * b], "IDX OF%d" % a, "UF #marks%d" % k, sca(16 * (b - a)), f=AF.Silu)
        else:
            cp(T.UB[:].indirect(T.OF[:, 1, a:b]), T.XB0[:, 16 * a:16 * b], "XB0 OF%d" % a, "UB #marks%d" % k, sca(16 * (b - a)))

    def frames(a, b):
        cp(T.xfs[:, 512 * a:512 * b].indirect(T.OF[:, 0, a:b]), T.pfs[:, 16 * a:16 * b],
           "pfs " + " ".join("OF%d" % x for x, y in STAGES if a <= x < b), "xf%d #frames%d" % (a, PART[b - 1]), sca(16 * (b - a)))

    def take(t):
        for k in range(4):
            cp(T.UH[:, pairs(k)], nurses(T.WI, t, k), "WI%d_%d" % (t, k), "UH%d #uh%d" % (k, k), wide(k) * CYC)
        sign, ak, a, bk = (-1.0 if t < 4 else 1.0), "AFL%d" % t, wide(0) if t else 0, "BB%d" % t
        if t:
            win, keys = wi(t, ACOL, ACOL + 256), " ".join("WA%d_%d" % (t, k) for k in range(4)) + " AL%d" % t
            act(afl(t, 0, 256), win.indirect(T.AL[:, 16 * t:16 * t + 16]), keys, ak, gat(256), scale=-sign)
            ts(T.UA[:, 0:a], win.indirect(T.AL[:, 16 * t:16 * t + QU[1]]), -1.0, None, A.mult, None, keys, "UA0", gat(a))
        ts(T.UA[:, a:256], afl(t, a, 256), sign, None, A.mult, None, ak, "UA0 UA1 UA2 UA3"[4 * min(t, 1):], (256 - a) * CYC)
        for k in range(4):
            p = T.PD[:, pairs(k)]
            group([(p, T["NIDF" if t < 4 else "IDF"][:], nurses(T.WI, t, k)), (p, T.NIDF[:], afl(t, 16 * QU[k], 16 * QU[k + 1]))],
                  "IDF NIDF %s WI%d_%d" % (ak, t, k), "PD", 8 * max(64, wide(k)))
        if t:
            differences(t, "PN")
        if t < 4:
            group([(T.PT[:, 256:512], T.LO8[:], T.IOTC[:, 256:512])]
                  + [(T.PT[:, 256 + l:512:16], T.SELB[:, l, :, :], bb(t, 2, 3)) for l in range(16)], "LO8 IOTC SELB SELBb " + bk, "PT", 1280)
            act(T.IDX[:], T.PT[:, 256:512], "PT", "IDX #idx", 256 * CYC, f=AF.Identity, bias=MID)
            bits(t)
            fiota(T.UF[:, 512:1024], [[0, 512]], 16416, 0, "UF", 512)

    def differences(t, P):
        p = T[P][:, 400:448]
        group([(p, T.IDENT[:], bb(t, 3, 6)), (p, T.NID[:], bb(t, 0, 3))], "IDENT NID BB%d BG%d" % (t, t), P, 128)
        act(T.DF[:], p, P, "DF")

    def bits(t):
        p = T.PT[:, 0:128]
        mms([(T.PN[0:16, 128:256], bb(t, 0, 1), T.IDENT[:], True, True)], "IDENT BB%d" % t, "PN", 128)
        act(T.FT[0:16, :], T.PN[0:16, 128:256], "PN", "+FT #ft", 128 * CYC)
        group([big(p, 2, 128), (p, T.S1[0:18, :], T.FT[0:18, :]), big(p, 2, 128, "NEG"), (p, T.S2[0:18, :], T.FT[0:18, :]),
               big(p, 1, 128), big(p, 1, 128, "NEG")], "S1 S2 FT ONES NEG CM", "PT #bits", 768)
        act(T.BT[:], p, "PT C2 C2a", "BT #bt", 128 * CYC, f=AF.Identity, scale=T.C2[:, 1:2], bias=T.C2[:, 0:1])

    def xor(t):
        y, n = T.PT[:, 0:1], 16 if t < 4 else 32
        ts(T.DD[:, 0:1], y, MAGIC, MAGIC, A.add, A.subtract, "PT", "DD #dd")
        if t < 4:
            ts(T.RS[:, 0:16], T.X16[:], y, T.DD[:, 0:1], A.add, A.is_lt, "X16 PT DD", "RS #rs")
            group([(T.PL[:, 0, 0:16], T.BT[:], T.RS[:, 0:16])], "BT RS", "PL #xor", 64, False)
            ts(T.XLU[:, 0:16], T.PL[:, 0, 0:16], 768.0, None, A.add, None, "PL", "XLU #xl")
        else:
            ts(T.RS[0:16, :], T.RX[0:16, :], T.PT[0:16, 0:1], T.DD[0:16, 0:1], A.add, A.is_lt, "RX PT DD", "RS #rs")
            mms([(T.PT[:, 128:160], T.LB[0:16, :], T.RS[0:16, :], True, True)], "LB RS", "PT #xor", 64)
            ts(T.XLU[:], T.PT[:, 128:160], T.LX1[:, 0:1], None, A.add, None, "PT LX1", "XLU #xl")

    def alpha(t):
        tt(T.MROW[:], T.UF[:, 0:1024].indirect(T.XLU[:, 0:16]), T.IDX[:], A.min, "UF UFb XLU IDX", "MROW #mate", gat(256))
        group([(T.PT[:, 0:16], T.IDENT[:], T.NI[:])], "IDENT NI", "PT", 64, True, False)
        conv(T.PT[:, 0:16], T.MROW, 0, 16, "MROW", "PT", st=False, tab="SELJ")
        cp(T.DM[:, 16 * t:16 * t + 16], T.PT[:, 0:16], "PT", "DM%d" % t)
        send(T.AL[:, 16 * t + 16:16 * t + 32], T.DM[:, 16 * t:16 * t + 16], "DM%d" % t, "AL%d" % (t + 1), "am_%d" % (t + 1), 8)

    def turns(t):
        tt(T.XX[:], T.PL[:, 1:4, 0:16], T.DF[:], A.mult, "PL DF", "XX")
        group([(T.PB3[:, 3, 0:2, :], T.IDENT[:], bb(t, 0, 2)), (T.PB3[:, 3, 2, :], T.NID[:], bb(t, 2, 3)),
               (T.PB3[:, 3, 3:6, :], T.IDENT[:], bb(t, 3, 6)), (T.PB3[:, 3, 0:3, :], T.IDF[:], T.XX[:]),
               (T.PB3[:, 3, 3:6, :], T.NIDF[:], T.XX[:])], "IDENT NID IDF NIDF XX BB%d BG%d" % (t, t), "PB3", 704, True, t == 4)
        if t < 4:
            conv(T.PB3[:, 3, 2, :], T.MROW, 0, 16, "MROW", "PB3", st=False, tab="SELX")
            o = T.BO[:, 6 * t:6 * t + 6, :]
            act(o, T.PB3[:, 3, 0:6, :], "PB3", "BO%d" % t, 96 * CYC)
            send(bb(t + 1, 0, 6), o, "BO%d" % t, "BB%d BG%d" % (t + 1, t + 1), "al_%d" % (t + 1), 48)
        else:
            act(T.YO[:], T.PB3[:, 3, 0:6:5, :], "PB3", "YO", f=AF.Identity, bias=256.0)

    def box_lists():
        fiota(T.UB[:], [[0, 1024]], -512, 0, "UB", 1024)
        ts(T.YL[:], bb(4, 2, 6), 256.0, None, A.add, None, "BB4", "YL")
        tt(T.SI[:], bb(4, 1, 5, 3), bb(4, 0, 4, 3), A.subtract, "BB4", "SI")
        tt(T.SA[:], T.SI[:], bb(4, 2, 6, 3), A.mult, "BB4 SI", "SA")
        group([(T.PT[:, l:512:16], T.SELB[:, l, :, :], T.SA[:]) for l in range(16)], "SELB SELBb SA", "PT", 1024)
        act(T.XB0[:], T.PT[:, 0:512], "PT", "XB0 XB1", 512 * CYC)
        cp(T.UB[:, 512:1024].indirect(T.YL[:, 16:32]), T.XB0[:, 256:512], "XB1 YL", "UB #nurses", sca(256))

    for t in range(5):
        now[0] = t
        ring.update(XG=0, CL=0, YV=0)
        take(t)
        if t == 4:
            box_lists()
        j = 0
        for w in PLAN[(t + 2) // 3].split():
            chunk(t, w[0], j, int(w[1:]))
            for k in [k for k in range(4) if j < 16 + QU[k + 1] <= j + int(w[1:])]:
                signs(k)
                if k > 1:
                    total(k)
                aside(t, k)
                rows(t, k)
                sums(t, k)
            j += int(w[1:])
        if t < 4:
            for a, b in OFFS:
                frames(a, b)
        xor(t)
        if t < 4:
            alpha(t)
        if t == 0:
            nurses_sites()
            differences(0, "PN")
        turns(t)

    dma("D", T.yc[:], T.YC[:], "YC", "yc", "o_yc", 3000)
    conv(T.PN[:, 0:32], T.UB, 0, 32, "UB", "PN", stop=False, tab="SELR")
    conv(T.PN[:, 0:32], T.UB, 512, 32, "UB", "PN", st=False, stop=False, tab="SELR")
    for n in range(2):
        s = slice(256 * n, 256 * n + 256)
        act(T.OWN[:, s], T.UB[:, s], "UB", "OWN%d" % n, 256 * CYC)
        tt(T.U[:, s], T.UB[:, 0:512].indirect(T.XLU[:, 16 * n:16 * n + 16]), T.OWN[:, s], A.min, "UB XLU OWN%d" % n, "+U #mate%d" % n, gat(256))
    conv(T.PN[:, 0:32], T.U, 0, 32, "U", "PN", st=False, tab="SELX")
    act(T.BL[:], T.PN[:, 0:32], "PN SC", "BL", f=AF.Identity, scale=T.SC[:, 0:1], bias=T.SC[:, 1:2])
    dma("S", T.yb[:], T.BL[:], "BL", "yb", "o_yb")
    dma("D", T.yf[:], T.YO[:, 0:16], "YO", "yf", "o_yf")
    dma("D", T.yn[:], T.YO[:, 16:32], "YO", "yn", "o_yn")
    emit()
    for n in ("yc", "yb", "yf", "yn"):
        g.wait_ge(T.sem["o_" + n], 16)
    g.wait_ge(T.sem.loc, nloc[0])
